import numpy as np, ml_dtypes
CORES = [9,25,41,57]
N = 4
BF = ml_dtypes.bfloat16
M, L, CAP, VI, ST = 3584, 256, 192, 3, 4
W = M + (VI - 1) * L
def weights(rng):
    w = rng.integers(0, 64, (N, 8, 16)); o = np.argsort(rng.random((N, 8, 16)), axis=-1)
    a = o[..., :1] == np.arange(16); b = o[..., 1:2] == np.arange(16)
    return np.where(a, 1, np.where(b, 16, w)), a[:, :, None], b[:, :, None]
def aim(v, w, a, b, t):
    v = np.where(a | b, 0, v); need = (t - np.sum(v * w[:, :, None], axis=-1)) & 63
    return v + a * (need & 15)[..., None] + b * (need >> 4)[..., None]
def shake(rng, v, k, top):
    return np.clip(v + np.floor((2 * k + 1) * rng.random(v.shape)).astype(np.int64) - k, 0, top)
def homes(rng, e):
    t = (64 * rng.random((N, 8, M)) ** e).astype(np.int64)
    t = (t * (2 * rng.integers(0, 32, (N, 8, 1)) + 1) + rng.integers(0, 64, (N, 8, 1))) & 63
    t[:, :, 1:65] = np.arange(64); return t
def points(rng, w, a, b, top):
    tree = homes(rng, rng.choice(np.array([1.0, 1.5, 2.0, 3.0]), (N, 8, 1)))
    mid = rng.integers(0, top + 1, (N, 8, 64, 16)); k = rng.integers(0, 9, (N, 8, M, 1)); k[:, :, 1:65] = 0
    v = shake(rng, np.take_along_axis(mid, tree[..., None], 2), k, top)
    far = rng.random((N, 8, M, 1)) < 0.3; far[:, :, 1:65] = False
    return tree, aim(np.where(far, rng.integers(0, top + 1, v.shape), v), w, a, b, tree)
def grow(v, tree):
    x = v.astype(np.int32); c = np.zeros(N * 8 * M * 16, np.int64)
    R, g, n = np.nonzero(np.broadcast_to(np.arange(M) > 64, (N, 8, M))); at = tree[R, g, n] + 1
    for _ in range(24):
        if len(n) == 0: break
        band = np.add.reduce(np.abs(x[R, g, n] - x[R, g, at]), axis=-1) >> 4
        key = ((R * 8 + g) * M + at) * 16 + band
        u, i = np.unique(key, return_index=True); c[u] = n[i]
        more = np.ones(len(n), bool); more[i] = False
        R, g, n, at = R[more], g[more], n[more], c[key[more]]
    return c.reshape(N, 8, M, 16)
def queries(rng, v, tree, w, a, b):
    o = rng.integers(1, M, (N, 8, VI * L)); k = rng.integers(0, 7, (N, 8, VI * L, 1))
    s = shake(rng, np.take_along_axis(v, o[..., None], 2), k, 15)
    s = np.where(rng.random((N, 8, VI * L, 1)) < 0.25, rng.integers(0, 16, s.shape), s)
    return aim(s, w, a, b, np.take_along_axis(tree, o, 2))
def radii(rng):
    z = (N, 8, VI * L)
    return np.where(rng.random(z) < 0.7, rng.integers(100, 256, z), rng.integers(0, 100, z))
def full(v):
    return np.ascontiguousarray(v.transpose(0, 1, 3, 2)).reshape(N, 128, -1)
def pack(v, c, s, w, r0, th):
    return {"pt": full(v).astype(np.float32).astype(BF), "ch": full(c).astype(np.int32), "q": full(s).astype(np.float32).astype(BF),
            "w": np.ascontiguousarray(w.reshape(N, 128, 1)).astype(np.int32), "r0": r0.astype(np.int32), "th": np.repeat(th, 16, axis=1)[..., None].astype(np.int32)}
def setup_inputs(rng):
    w, a, b = weights(rng); tree, v = points(rng, w, a, b, 15)
    return pack(v, grow(v, tree), queries(rng, v, tree, w, a, b), w, radii(rng), rng.integers(20, 60, (N, 8)))
def setup_inputs_room(rng):
    w, a, b = weights(rng); tree, v = points(rng, w, a, b, 10); z = (N, 8, VI * L)
    n = rng.choice(np.array([0, 1, CAP - 1, CAP, CAP + 1, L]), (N, 8)); n[0] = (CAP, CAP + 1, L, CAP - 1, 1, 0, CAP, CAP + 1); n[:, 2] = L
    n = np.concatenate([n[:, :, None], np.full((N, 8, VI - 1), L // 2)], axis=2)
    hot = (np.argsort(rng.random((N, 8, VI, L)), axis=-1) < n[..., None]).reshape(z)
    s = np.where(hot[..., None], rng.integers(12, 16, z + (16,)), queries(rng, v, tree, w, a, b))
    r0 = np.where(hot, rng.choice(np.array([20, 21, 255, 255, 255]), z), rng.integers(0, 20, z))
    return pack(v, grow(v, tree), s, w, r0, np.full((N, 8), 20))
def setup_inputs_knots(rng):
    w, a, b = weights(rng); v = rng.integers(0, 16, (N, 8, M, 16)); v[:, 1::2] = v[:, 1::2][:, :, rng.integers(0, 37, M)]
    dens = rng.choice(np.array([1.0, 0.6, 0.2]), (N, 8, 1, 1)); dens[:, 0] = 1.0; dens[:, 1] = 0.2; dens[:, 2] = 0.3
    c = np.where(rng.random((N, 8, M, 16)) < dens, rng.integers(1, M, (N, 8, M, 16)), 0)
    c[:, 3] = rng.choice(np.array([0, 1, 64, 65, M - 1]), (N, M, 16))
    c[:, 5] = np.where(rng.random((N, M, 16)) < 0.5, np.arange(M)[:, None], c[:, 5])
    x = rng.integers(1, M, (N, M, 2)); e = np.arange(16) - rng.integers(1, 6, (N, M, 1)); j = rng.choice(np.array([-1, 3, 4]), (N, M, 1))
    some = rng.random((N, M, 1)) < 0.4; some[:, 1:65] = True
    c[:, 6] = some * np.where((e >= 0) & (e < 3), x[:, :, :1], np.where(e == j, x[:, :, 1:], 0)); c[:, :, 0] = 0
    return pack(v, c, queries(rng, v, rng.integers(0, 64, (N, 8, M)), w, a, b), w, radii(rng), rng.integers(20, 80, (N, 8)))
def setup_inputs_ties(rng):
    w = rng.integers(0, 64, (N, 8, 16)); v = 4 * rng.integers(0, 4, (N, 8, M, 16)); tree = homes(rng, 1.0); z = (N, 8, VI * L)
    s = np.take_along_axis(v, rng.integers(1, M, z)[..., None], 2); s = np.where(rng.random(s.shape) < 0.3, 4 * rng.integers(0, 4, s.shape), s)
    s = np.where(rng.random(s.shape) < 0.01, 15, s); s[:, ::2, 1::2] = s[:, ::2, ::2]
    r0 = np.where(rng.random(z) < 0.4, 16 * rng.integers(3, 9, z) + rng.choice(np.array([-1, 1]), z), 4 * rng.integers(10, 40, z))
    return pack(v, grow(v, tree), s, w, r0, 4 * rng.integers(8, 15, (N, 8)))
def setup_inputs_ends(rng):
    w, a, b = weights(rng); tree, v = points(rng, w, a, b, 15); n = np.arange(L)
    v[:, 4, 65:65 + L] = rng.integers(0, 16, (N, L, 16)); tree[:, 4, 65:65 + L] = n & 63; v = aim(v, w, a, b, tree)
    s = queries(rng, v, tree, w, a, b); s[:, 4, :L] = v[:, 4, 65:65 + L]
    w[:, 1] = 0; w[:, 2] = 63; v[:, :, 1] = 0; v[:, :, 64] = 15; v[:, :, M - 1] = 15; v[:, 3, 1:65] = 0
    c = grow(v, tree); c[:, :, 1, 15] = M - 1; c[:, 3] = 0; c[:, 4, 65:] = 0; c[:, 4, 1 + (n & 63), 4 * (n >> 6) + 2] = 65 + n
    R = np.arange(N); z = 1 + ((15 * np.sum(w[:, 7], axis=-1)) & 63)
    v[R, 7, z] = 0; v[:, 7, 65] = 0; v[:, 7, 66] = 15
    c[R, 7, z] = 0; c[R, 7, z, 9] = 65; c[:, 7, 65] = 0; c[:, 7, 65, 4] = 66
    s[:, 1, ::3] = 15; s[:, 3, ::2] = 15; s[:, 3, 1::4] = rng.integers(14, 16, s[:, 3, 1::4].shape); s[:, 7, ::4] = 15
    s[:, :, 0] = 15; s[:, :, L - 1] = 0
    r0 = rng.choice(np.array([0, 1, 15, 16, 17, 120, 254, 255]), (N, 8, VI * L)); high = np.array([240, 241, 255])
    r0[:, 3, ::2] = rng.choice(high, r0[:, 3, ::2].shape); r0[:, 3, 1::4] = rng.choice(np.array([191, 192, 239, 240, 241, 255]), r0[:, 3, 1::4].shape)
    r0[:, 4, :L] = 255; r0[:, 7, ::4] = rng.choice(high, r0[:, 7, ::4].shape); r0[:, :, 0] = 255; r0[:, :, L - 1] = 255
    th = rng.choice(np.array([0, 1, 16, 30, 240]), (N, 8)); th[:, 0] = 0; th[:, 3] = np.array([0, 240, 241, 255])[R & 3]; th[:, 4] = 0; th[:, 5] = 255; th[:, 6] = 240
    return pack(v, c, s, w, r0, th)
def setup_inputs_spread(rng):
    w = rng.integers(0, 64, (N, 8, 16)); e = rng.choice(np.array([0.25, 0.5, 1.0, 2.0, 4.0]), (N, 8, 1, 16))
    v = (16 * rng.random((N, 8, M, 16)) ** e).astype(np.int64); s = (16 * rng.random((N, 8, VI * L, 16)) ** e).astype(np.int64)
    c = grow(v, homes(rng, 4.0)); c = np.where(rng.random(c.shape) < 0.1, rng.integers(0, M, c.shape), c); c[:, :, 0] = 0
    th = np.exp2(7 * rng.random((N, 8))).astype(np.int64); th[:, 0] = 8
    return pack(np.clip(v, 0, 15), c, np.clip(s, 0, 15), w, rng.integers(0, 256, (N, 8, VI * L)), th)
def check_inputs(d):
    bad = []
    for k in ("pt", "q"):
        x = np.asarray(d[k]).astype(np.float32)
        if not (np.all(x >= 0) and np.all(x <= 15) and np.all(x == np.floor(x))): bad.append("whole numbers from 0 to 15 in " + k)
    for k, hi in (("ch", M - 1), ("w", 63), ("r0", 255), ("th", 255)):
        if np.min(d[k]) < 0 or np.max(d[k]) > hi: bad.append("range of " + k)
    if np.any(np.asarray(d["ch"])[:, :, 0] != 0): bad.append("column 0 of ch")
    x = np.asarray(d["th"]).reshape(-1, 16)
    if np.any(x != x[:, :1]): bad.append("one threshold a group")
    return bad
def dist(u, v):
    return np.add.reduce(np.abs(u - v), axis=-1)
def inside(D, rho):
    i = np.arange(16); return (16 * i <= (D + rho)[..., None]) & (16 * i + 15 >= (D - rho)[..., None])
def at(k, i):
    return np.take_along_axis(k, i[..., None], -1)[..., 0]
def reference(pt, ch, q, w, r0, th):
    X = np.zeros((N, 8, W, 16), np.int32); X[:, :, :M] = pt.astype(np.float32).astype(np.int32).reshape(N, 8, 16, M).transpose(0, 1, 3, 2)
    C = np.zeros((N, 8, W, 16), np.int32); C[:, :, :M] = ch.reshape(N, 8, 16, M).transpose(0, 1, 3, 2)
    Q = np.ascontiguousarray(q.astype(np.float32).astype(np.int32).reshape(N, 8, 16, VI * L).transpose(0, 1, 3, 2))
    wt = w.astype(np.int32).reshape(N, 8, 1, 16); lim = th.reshape(N, 8, 16)[:, :, :1]
    a, b, ln = np.ogrid[0:N, 0:8, 0:L]; far_off = 1000
    yr, yb, yp, held = [], [], [], None
    for t in range(VI):
        v = np.array(Q[:, :, t * L:(t + 1) * L]); rho = np.array(r0[:, :, t * L:(t + 1) * L]).astype(np.int32); best = np.zeros((N, 8, L), np.int32)
        if held is not None:
            hv, hr, hb, sent, place = held; h = np.nonzero(sent); to = ((h[0] + 1) % N, h[1], place[h])
            v[to] = hv[h]; rho[to] = hr[h]; best[to] = hb[h]
        kid = np.zeros((N, 8, ST + 1, L, 16), np.int32); far = np.zeros((N, 8, ST + 1, L, 16), np.int32); own = np.zeros((N, 8, ST + 1, L), np.int32)
        lev = np.zeros((N, 8, L), np.int64); push = np.ones((N, 8, L), bool)
        m = 1 + (np.add.reduce(wt * v, axis=-1) & 63); D = dist(X[a, b, m], v)
        for s in range(ST + 1):
            if s > 0:
                k = kid[a, b, lev, ln]; f = far[a, b, lev, ln]; ok = (k > 0) & inside(own[a, b, lev, ln], rho)
                i = np.argmin(np.where(ok, f, far_off), axis=-1); push = np.any(ok, axis=-1)
                m = np.where(push, at(k, i), 0); D = np.where(push, at(f, i), far_off)
                h = np.nonzero(push); kid[h[0], h[1], lev[h], h[2], i[h]] = 0
                lev = np.where(push, lev + 1, np.maximum(lev - 1, 0))
            P = np.where(inside(D, rho) & push[..., None], C[a, b, m], 0)
            F = dist(X[a[..., None], b[..., None], P], v[:, :, :, None])
            h = np.nonzero(push); e = (h[0], h[1], lev[h], h[2])
            kid[e] = P[h]; far[e] = F[h]; own[e] = D[h]
            key = np.concatenate([D[..., None], np.where(P > 0, F, far_off)], axis=-1); node = np.concatenate([m[..., None], P], axis=-1)
            i = np.argmin(key, axis=-1); least = at(key, i); better = least < rho
            best = np.where(better, 4096 * a + at(node, i), best); rho = np.where(better, least, rho)
        yr.append(rho); yb.append(best)
        if t == VI - 1: break
        goes = rho >= lim; here = (best > 0) & (best >> 12 == a); node = np.where(here, best & 4095, 0); row = rho >> 4
        can = goes & here & (C[a, b, node, row] == 0)
        earlier = np.arange(L)[None, :] < np.arange(L)[:, None]
        win = can & ~np.any((node[:, :, :, None] == node[:, :, None, :]) & can[:, :, None, :] & earlier, axis=-1)
        X[:, :, M + t * L:M + (t + 1) * L] = v; h = np.nonzero(win); C[h[0], h[1], node[h], row[h]] = M + t * L + h[2]
        yp.append(np.where(win, node, 0))
        place = np.add.accumulate(goes.astype(np.int64), axis=2) - 1
        held = (v, rho, best, goes & (place < CAP), place)
    return {"yr": np.concatenate(yr, axis=2).astype(np.float32), "yb": np.concatenate(yb, axis=2).astype(np.float32), "yp": np.concatenate(yp, axis=2).astype(np.float32)}

@@ -1,0 +1,608 @@
+from concourse.mybir import AluOpType as OP, ActivationFunctionType as AF
+
+N, L, CAP, M, VI = 4, 256, 192, 3584, 3
+B24 = float(2 ** 24)
+SC = float(2 ** 26)
+BIG = float(2 ** 60)
+GSC = (3, 6)
+NCH = 4
+SCH = ((1, 3), (1, 3))
+ROOM = 4096 + 256
+QSC = 16
+
+SCRATCH = {}
+PS = set()
+VIRT = {}
+POOL = {"float32": ["poolf", 0], "int32": ["pooli", 0], "bfloat16": ["poolb", 0], "uint16": ["poolu", 0]}
+
+
+def _own(name, cols, dt="float32"):
+    SCRATCH[name] = ("sbuf", [128, cols], dt)
+    VIRT[name] = (name, 0, cols)
+
+
+def _s(name, cols, dt="float32"):
+    p = POOL[dt]
+    VIRT[name] = (p[0], p[1], cols)
+    p[1] += (cols + 15) // 16 * 16
+
+
+for _n in ("VB", "KP0", "KP1", "LI0", "LI1", "MA", "MB", "MC"):
+    SCRATCH[_n] = ("psum", [128, 512], "float32")
+    VIRT[_n] = (_n, 0, 512)
+    PS.add(_n)
+_own("PT", 4096, "bfloat16"); _own("CHI", M, "int32"); _own("CH", ROOM); _own("QF", 768, "bfloat16")
+_own("wi", 8, "int32"); _own("thi", 8, "int32"); _own("r0i", 768, "int32")
+_own("Q16a", 4096, "bfloat16"); _own("Q16b", 4096, "bfloat16"); _own("DIFF", 4096, "bfloat16")
+for _t in "01":
+    _own("SND" + _t, CAP + L, "int32"); _own("RCV" + _t, L, "int32")
+for _t in "012":
+    _own("or" + _t, 256); _own("ob" + _t, 256); _own("op" + _t, 256)
+for _n, _c in (("r0f", 768), ("wf", 2), ("thf", 2), ("pf", 4), ("jf", 128), ("j15", 128), ("c8", 8), ("IDF", 128), ("DM", 256),
+               ("LC", 8), ("RAMP", 128), ("MX", 128), ("D0", 256), ("biasc", 2), ("biasr", 2), ("TH", 16), ("KI", 16), ("K192", 16),
+               ("K4096", 16), ("NID0", 256), ("NID1", 256), ("ONESF", 128), ("selj", 2048), ("SELR", 16), ("R0P1", 48),
+               ("C24", 8), ("BEST0", 16), ("VF", 112), ("VZ", 112), ("LF", 112), ("RHO", 16), ("ad", 16), ("bn", 16), ("BEST", 16),
+               ("pl", 16), ("go", 16), ("gd", 16), ("PN", 16), ("emp", 16), ("can", 16), ("win", 16), ("YP", 16), ("gq", 16),
+               ("LBD", 256), ("Z2", 256), ("PK", 256), ("X", 256), ("GC", 256), ("M1", 256), ("OHG", 256), ("OC", 256),
+               ("VAL", 256), ("LBD2", 256), ("Z3", 256), ("RV", 256), ("RT", 256), ("RF", 256), ("EF", 384)):
+    _s(_n, _c)
+for _n, _c in (("pi", 4), ("ji", 128), ("j15i", 128), ("V", 112), ("VI", 112), ("PI", 16), ("PJ", 16), ("hi6", 16), ("lo6", 16),
+               ("RI", 256), ("RS", 256)):
+    _s(_n, _c, "int32")
+for _n, _c in [("IDB", 128), ("NIDB", 128), ("BLK", 8), ("BLK0", 8), ("WB", 8), ("TRI", 128), ("LTRI", 128), ("ONESB", 128),
+               ("THM", 128), ("SELH", 2048), ("QV1", 256), ("QV2", 256), ("FARB", 16), ("NQ", 32), ("NQT", 128), ("RHT", 256),
+               ("BC0", 128), ("CANB", 16)] + [("EQ%d" % _e, 384) for _e in range(8)]:
+    _s(_n, _c, "bfloat16")
+for _n in ("OFFP", "GO1", "GO2"):
+    _s(_n, 16, "uint16")
+for _h in "01":
+    for _n, _c, _d in (("si", 8, "int32"), ("sj", 8, "int32"), ("RTL", 8, "float32"), ("SBD", 128, "float32"), ("RBD", 128, "float32"),
+                       ("Z", 128, "float32"), ("OFF", 8, "uint16"), ("DR", 128, "bfloat16"), ("FB0", 8, "float32"), ("FB1", 8, "float32"),
+                       ("E", 128, "float32"), ("A", 128, "float32"), ("Tf", 8, "int32"), ("u", 128, "float32"),
+                       ("Pf", 128, "float32"), ("PU", 128, "uint16"), ("KU", 128, "float32"), ("KS", 128, "float32"), ("u2", 128, "float32"),
+                       ("KM", 128, "float32"), ("MS", 128, "float32"), ("OH", 128, "float32"), ("FO", 128, "float32"), ("pm", 128, "float32"),
+                       ("lo", 8, "int32"), ("lp", 8, "int32"), ("ri", 8, "float32"), ("rx", 8, "float32"), ("rho", 8, "float32")):
+        _s(_n + _h, _c, _d)
+for _d in POOL:
+    SCRATCH[POOL[_d][0]] = ("sbuf", [128, POOL[_d][1]], _d)
+
+NDMA = 26
+SEMAPHORES = ["cv", "ct", "cs", "cg"] + ["d%d" % i for i in range(NDMA)] + ["arr0", "arr1", "sent0", "sent1"]
+
+
+def rank_program(g, core, T, topo):
+    rank = T.rank_of(core)
+    if rank is None:
+        return
+    ops = []
+    hist = {}
+    ndma = [0]
+    rot = [0]
+
+    def b(name, lo=0, hi=None, st=1, rows=None):
+        buf, o, c = VIRT[name]
+        hi = c if hi is None else hi
+        p = slice(None) if rows is None else slice(0, rows)
+        return (name, lo, hi, st, T[buf][p, o + lo:o + hi:st] if st > 1 else T[buf][p, o + lo:o + hi])
+
+    def ind(w, o):
+        return (w[0], w[1], w[2], 1, w[4].indirect(o[4]))
+
+    def clash(x, y):
+        if x[1] <= y[0] or y[1] <= x[0]:
+            return False
+        return not (x[2] == y[2] and x[2] > 1 and (x[0] - y[0]) % x[2])
+
+    def op(q, call, reads, writes, cost, kind="c", ext=None):
+        n = len(ops)
+        deps = set()
+        after = set()
+        both = [(False, o) for o in reads] + [(True, o) for o in writes]
+        for w, o in both:
+            r = (o[1], o[2], o[3])
+            for (r2, w2, n2) in hist.get(o[0], ()):
+                if o[0] in PS and q == "t" and ops[n2]["q"] == "t":
+                    after.add(n2)
+                elif (w or w2) and clash(r, r2):
+                    deps.add(n2)
+                elif o[0] in PS and ops[n2]["q"] != q:
+                    deps.add(n2)
+        for w, o in both:
+            r = (o[1], o[2], o[3])
+            h = hist.setdefault(o[0], [])
+            if w and o[0] not in PS:
+                h[:] = [e for e in h if not (r[2] == 1 and r[0] <= e[0][0] and e[0][1] <= r[1] and e[2] != n)]
+            h.append((r, w, n))
+            if len(h) > 400:
+                del h[:100]
+        d = {"q": q, "call": call, "deps": deps, "after": after - deps, "cost": cost, "kind": kind, "ext": ext}
+        if kind == "d":
+            d["sem"] = "d%d" % ndma[0]
+            ndma[0] += 1
+        ops.append(d)
+        return n
+
+    CY = 0.00083 * 1.15
+
+    def cols(o):
+        return (o[2] - o[1] + o[3] - 1) // o[3]
+
+    def vc(n, k=1.0):
+        return 0.06 + max(64, n * k) * CY
+
+    V, S, TE = g.vector, g.scalar, g.tensor
+
+    def isap(x):
+        return isinstance(x, tuple)
+
+    def tt(out, a, c, o):
+        k = 1.0 if (a[0] in PS or c[0] in PS) else 2.0
+        op("v", lambda: V.tensor_tensor(out[4], a[4], c[4], o), [a, c], [out], vc(cols(out), k))
+
+    def ts(out, a, s1, o1, s2=None, o2=None, ext=None):
+        x1 = s1[4] if isap(s1) else s1
+        x2 = s2[4] if isap(s2) else s2
+        rd = [a] + [s for s in (s1, s2) if isap(s)]
+        if o2 is None:
+            op("v", lambda: V.tensor_scalar(out[4], a[4], x1, None, o1), rd, [out], vc(cols(out)), "c", ext)
+        else:
+            op("v", lambda: V.tensor_scalar(out[4], a[4], x1, x2, o1, o2), rd, [out], vc(cols(out)), "c", ext)
+
+    def cp(out, a):
+        op("v", lambda: V.tensor_copy(out[4], a[4]), [a], [out], vc(cols(out)))
+
+    def scan(out, d0, d1, o0, o1):
+        op("v", lambda: V.tensor_tensor_scan(out[4], d0[4], d1[4], 0.0, o0, o1), [d0, d1], [out], vc(cols(out)))
+
+    def fill(out, x):
+        op("v", lambda: V.memset(out[4], x), [], [out], vc(cols(out)))
+
+    def act(out, a, f, bias=None, scale=1.0, extra=(), cost=None):
+        kw = {"scale": scale}
+        rd = [a] + list(extra)
+        if bias is not None:
+            kw["bias"] = bias[4] if isap(bias) else bias
+            if isap(bias):
+                rd.append(bias)
+        op("s", lambda: S.activation(out[4], a[4], f, **kw), rd, [out], cost or (0.06 + cols(out) * CY))
+
+    def mm(out, l, r, start=True, stop=True, f32=False):
+        n = max(min(64, cols(l)), cols(r))
+        op("t", lambda: TE.matmul(out[4], l[4], r[4], start, stop), [l, r], [out], 0.03 + n * (4 if f32 else 1) * 0.00083)
+
+    def dma(q, out, src, reads, writes, us):
+        eng = g.sync if q == "y" else g.scalar
+        op(q, lambda: eng.dma_start(out, src), reads, writes, 0.06, "d", us)
+
+    def iota(out, pat, base, cm, flag=False):
+        kw = {"allow_small_or_imprecise_dtypes": True} if flag else {}
+        op("g", lambda: g.iota(out[4], pat, base, cm, **kw), [], [out], 0.13 + 2 * cols(out) * CY)
+
+    def load(q, name, lo, hi, src, rows=None):
+        o = b(name, lo, hi, 1, rows)
+        dma(q, o[4], src, [], [o], 2.5)
+
+    load("y", "QF", 0, 768, T.q[:])
+    load("s", "wi", 0, 1, T.w[:])
+    load("y", "CHI", 0, 896, T.ch[:, 0:896])
+    load("s", "CHI", 896, 1792, T.ch[:, 896:1792])
+    load("y", "PT", 0, M, T.pt[:])
+    load("s", "CHI", 1792, 2688, T.ch[:, 1792:2688])
+    load("y", "r0i", 0, 768, T.r0[:], 8)
+    load("s", "CHI", 2688, M, T.ch[:, 2688:M])
+    load("y", "thi", 0, 1, T.th[:])
+
+    iota(b("pi", 0, 1), [[0, 1]], 0, 1)
+    iota(b("ji"), [[1, 128]], 0, 0)
+    iota(b("c8"), [[1, 8]], 0, 0, True)
+    ts(b("pi", 1, 2), b("pi", 0, 1), 15, OP.bitwise_and)
+    ts(b("pi", 2, 3), b("pi", 0, 1), 4, OP.arith_shift_right)
+    cp(b("pf", 0, 3), b("pi", 0, 3))
+    P, P15, P4 = b("pf", 0, 1), b("pf", 1, 2), b("pf", 2, 3)
+    cp(b("jf"), b("ji"))
+    ts(b("j15i"), b("ji"), 15, OP.bitwise_and)
+    cp(b("j15"), b("j15i"))
+    ts(b("LC"), b("c8"), P4, OP.is_equal)
+    ts(b("BLK"), b("LC"), 65536.0, OP.mult)
+    cp(b("wf", 0, 1), b("wi", 0, 1))
+    ts(b("WB"), b("LC"), b("wf", 0, 1), OP.mult)
+    ts(b("D0", 0, 128), b("j15"), 0.0, OP.is_gt)
+    ts(b("DM", 0, 128), b("j15"), P15, OP.is_equal)
+    ts(b("IDF"), b("jf"), P, OP.is_equal)
+    cp(b("IDB"), b("IDF"))
+    ts(b("NIDB"), b("IDF"), -1.0, OP.mult)
+    ts(b("RAMP"), b("j15"), 16.0 * 65536, OP.mult, 8.0 * 65536 - B24, OP.add)
+    ts(b("MX"), b("D0", 0, 128), -2 * BIG, OP.mult, BIG, OP.add)
+    ts(b("biasc", 0, 1), P15, 4096.0, OP.mult, -B24, OP.add)
+    fill(b("C24"), B24)
+    for h in "01":
+        fill(b("SBD" + h), 0.0)
+        fill(b("RBD" + h), 0.0)
+    fill(b("V"), 32768)
+    cp(b("r0f", rows=8), b("r0i", rows=8))
+    for t in range(VI):
+        for h in range(2):
+            k = t * 2 + h
+            mm(b("MC", 8 * k, 8 * k + 8), b("r0f", t * L + 128 * h, t * L + 128 * h + 128, rows=8), b("IDF", 0, 8, rows=8), f32=True)
+    ts(b("R0P1"), b("MC", 0, 48), 1.0, OP.add)
+    for k in range(4):
+        cp(b("CH", 896 * k, 896 * k + 896), b("CHI", 896 * k, 896 * k + 896))
+    fill(b("CH", M, ROOM), 0.0)
+    fill(b("PT", 0, 1), 2048.0)
+    cp(b("PT", M, M + L), b("QF", 0, L))
+    fill(b("PT", M + L, 4096), 0.0)
+
+    SBr = [b("VB", 0, 128), b("VB", 128, 256)]
+    RBr = [b("VB", 256, 384), b("VB", 384, 512)]
+
+    def lists(src, zt, mat, psum):
+        tt(zt, src, mat, OP.mult)
+        for x in range(cols(src) // 128):
+            mm(b(psum, 8 * x, 8 * x + 8), b(zt[0], 128 * x, 128 * x + 128), b("LC"), f32=True)
+
+    def radius(h):
+        n = lambda x, *a: b(x + str(h), *a)
+        ts(n("RBD", 0, 128, 16), n("Tf"), SC, OP.mult, (B24 + 524288) * SC, OP.add)
+        scan(RBr[h], b("D0", 0, 128), n("RBD"), OP.mult, OP.add)
+
+    def adopt(h, s, key):
+        ti = b("V", 56 * h + s, 56 * h + 56, 7)
+        tf = b("Tf%d" % h)
+        tt(ti, key, tf, OP.min)
+        ts(tf, ti, -65536, OP.bitwise_and)
+
+    def begin(t, h, Q, Q16):
+        hs = str(h)
+        n = lambda x, *a: b(x + hs, *a)
+        LI = "LI" + hs
+        q = b(Q[0], Q[1] + 128 * h, Q[1] + 128 * h + 128)
+        mm(b(LI, 8, 16), q, b("WB"))
+        cp(n("si"), b(LI, 8, 16))
+        ts(n("sj"), n("si"), 63, OP.bitwise_and)
+        ts(n("SBD", 0, 128, 16), n("sj"), 1.0, OP.add)
+        ts(n("RTL"), n("sj"), 32769.0, OP.add)
+        scan(SBr[h], b("D0", 0, 128), n("SBD"), OP.mult, OP.add)
+        lists(SBr[h], n("Z"), b("DM", 0, 128), LI)
+        cp(n("OFF"), b(LI, 0, 8))
+        for i in range(16):
+            o = b(Q16, 2048 * h + i, 2048 * h + 2048, 16)
+            if i < QSC:
+                act(o, q, AF.Copy)
+            else:
+                cp(o, q)
+        op("v", lambda: V.tensor_tensor(b("DR" + hs)[4], b("PT")[4].indirect(b("OFF" + hs)[4]), q[4], OP.subtract),
+           [b("PT"), n("OFF"), q], [n("DR")], 0.05 + 128 * 1.5 * CY)
+        act(n("DR"), n("DR"), AF.Abs)
+        mm(b(LI, 16, 24), n("DR"), b("BLK"))
+        tt(n("FB0"), b(LI, 16, 24), n("RTL"), OP.add)
+        r1 = b("R0P1", 8 * (t * 2 + h), 8 * (t * 2 + h) + 8)
+        if t == 0:
+            ts(n("Tf"), r1, 65536.0, OP.mult, -B24 - 65536, OP.add)
+        else:
+            mm(b(LI, 24, 40), b("RF", 128 * h, 128 * h + 128), b("SELR"), f32=True)
+            ts(n("ri"), b(LI, 24, 32), 0.0, OP.is_lt)
+            tt(n("rx"), n("ri"), r1, OP.mult)
+            tt(n("rho"), b(LI, 24, 32), n("rx"), OP.add)
+            ts(b("BEST0", 8 * h, 8 * h + 8), b(LI, 32, 40), 0.0, OP.max)
+            ts(n("Tf"), n("rho"), 65536.0, OP.mult, -B24, OP.add)
+        radius(h)
+        ts(n("SBD", 0, 128, 16), n("FB0"), -B24, OP.add)
+        scan(SBr[h], b("D0", 0, 128), n("SBD"), OP.mult, OP.add)
+        tt(n("E"), SBr[h], b("RAMP"), OP.subtract)
+        act(n("A"), n("E"), AF.Abs, scale=SC)
+
+    def push(t, h, s, Q16):
+        hs = str(h)
+        n = lambda x, *a: b(x + hs, *a)
+        KP, LI = "KP" + hs, "LI" + hs
+        kp = b(KP, 0, 128)
+        ch = b("CH", 0, 4096)
+        op("v", lambda: V.tensor_copy(n("PU")[4], ch[4].indirect(n("OFF")[4])), [ch, n("OFF")], [n("PU")], 0.05 + 128 * 1.5 * CY)
+        act(n("Pf"), ind(ch, n("OFF")), AF.Identity, bias=b("biasc", 0, 1), extra=[n("OFF")], cost=0.065 + 128 * 1.5 * CY)
+        tt(n("u"), n("A"), RBr[h], OP.subtract)
+        if s == 0:
+            adopt(h, 1, n("SBD", 0, 128, 16))
+        mm(kp, n("Pf"), b("IDF"), True, False, f32=True)
+        w = 2048 // NCH
+        for c in range(NCH):
+            lo = 2048 * h + w * c
+            d = b("DIFF", lo, lo + w)
+            o = n("PU", w // 16 * c, w // 16 * (c + 1))
+            qq = b(Q16, lo, lo + w)
+            if c in SCH[h]:
+                act(d, ind(b("PT"), o), AF.Copy, extra=[o], cost=0.065 + w * 1.5 * CY)
+                ps = ("MA", "MB", "MC")[rot[0] % 3]
+                rot[0] += 1
+                mm(b(ps, 0, w), b("IDB"), d, True, False)
+                mm(b(ps, 0, w), b("NIDB"), qq, False, True)
+                act(d, b(ps, 0, w), AF.Abs)
+            else:
+                op("v", lambda d=d, o=o, qq=qq: V.tensor_tensor(d[4], b("PT")[4].indirect(o[4]), qq[4], OP.subtract),
+                   [b("PT"), o, qq], [d], 0.05 + w * 1.5 * CY)
+                act(d, d, AF.Abs)
+        for i in range(16):
+            mm(b(KP, i, 128, 16), b("DIFF", 2048 * h + i, 2048 * h + 2048, 16), b("BLK"), False, i == 15)
+        tt(n("KU"), kp, n("u"), OP.max)
+        scan(n("KS"), b("MX"), n("KU"), OP.max, OP.min)
+        adopt(h, s + 2, n("KS", 15, 128, 16))
+        if s == 4:
+            ts(b("RHO", 8 * h, 8 * h + 8), n("Tf"), 2.0 ** -16, OP.mult, 256.0, OP.add)
+            return
+        radius(h)
+        tt(n("u2"), n("A"), RBr[h], OP.subtract)
+        tt(n("KM"), kp, n("u2"), OP.max)
+        scan(n("MS"), b("MX"), n("KM"), OP.max, OP.min)
+        fb = (b("C24"), n("FB0"), n("FB1"), b("C24"))[s]
+        tt(n("SBD", 0, 128, 16), n("MS", 15, 128, 16), fb, OP.min)
+        scan(SBr[h], b("D0", 0, 128), n("SBD"), OP.mult, OP.add)
+        lists(SBr[h], n("Z"), b("DM", 0, 128), LI)
+        cp(n("lo"), b(LI, 0, 8))
+        ts(n("lp"), n("lo"), 4095, OP.bitwise_and)
+        cp(n("OFF"), n("lp"))
+        if s in (0, 3):
+            tt(n("E"), SBr[h], b("RAMP"), OP.subtract)
+        else:
+            ts(n("pm"), SBr[h], 0.0, OP.is_ge, -B24, OP.mult)
+            tt(n("pm"), n("pm"), n("FO"), OP.mult)
+            tt(n("pm"), n("pm"), b("RAMP"), OP.subtract)
+            tt(n("E"), SBr[h], n("pm"), OP.add)
+        act(n("A"), n("E"), AF.Abs, scale=SC)
+        if s == 0:
+            ts(n("FB1"), n("SBD", 0, 128, 16), B24, OP.add)
+        if s in (0, 1):
+            tt(n("OH"), n("KM"), SBr[h], OP.is_equal)
+            act(n("FO"), n("OH"), AF.Identity, bias=1.0, scale=4096.0)
+
+    def out_rows(src, buf, psum, out, t):
+        for h in range(2):
+            mm(b(psum, 128 * h, 128 * h + 128, 1, 8), b(src, 8 * h, 8 * h + 8), b("IDF"), f32=True)
+        o = b(buf, 0, 256, 1, 8)
+        act(o, b(psum, 0, 256, 1, 8), AF.Copy)
+        dma("y", out[:, t * L:(t + 1) * L], o[4], [o], [], 2.0)
+
+    def wide(vals, dst):
+        vals(b("LBD2", 0, 256, 16))
+        scan(b("VB", 0, 256), b("D0"), b("LBD2"), OP.mult, OP.add)
+        lists(b("VB", 0, 256), b("Z3"), b("DM"), "MB")
+        cp(b(dst), b("MB", 0, 16))
+
+    def finish(t, Q):
+        ts(b("VI"), b("V"), 65535, OP.bitwise_and)
+        cp(b("VF"), b("VI"))
+        ts(b("VZ"), b("VI"), 0.0, OP.is_equal)
+        scan(b("LF"), b("VZ"), b("VF"), OP.mult, OP.add)
+        last = b("LF", 6, 112, 7)
+        if t < VI - 1:
+            tt(b("FARB"), b("RHO"), b("TH"), OP.is_ge)
+            mm(b("MA", 0, 8), b("LTRI"), b("FARB", 0, 8))
+            mm(b("MA", 8, 16), b("LTRI"), b("FARB", 8, 16), True, False)
+            mm(b("MA", 8, 16), b("ONESB"), b("FARB", 0, 8), False, True)
+            ts(b("pl"), b("MA", 0, 16), float(CAP), OP.is_lt)
+            tt(b("go"), b("pl"), b("FARB"), OP.mult)
+            tt(b("gd"), b("MA", 0, 16), b("K192"), OP.subtract)
+            tt(b("gd"), b("gd"), b("go"), OP.mult)
+            tt(b("LBD", 0, 256, 16), b("gd"), b("K192"), OP.add)
+            scan(b("VB", 256, 512), b("D0"), b("LBD"), OP.mult, OP.add)
+            lists(b("VB", 256, 512), b("Z2"), b("DM"), "MB")
+            cp(b("OFFP"), b("MB", 0, 16))
+        cp(b("PI"), last)
+        ts(b("PJ"), b("PI"), 4095, OP.bitwise_and)
+        ts(b("ad"), last, 32768.0, OP.not_equal)
+        ts(b("bn"), b("PJ"), 4096.0 * rank, OP.add)
+        if t:
+            tt(b("bn"), b("bn"), b("BEST0"), OP.subtract)
+        tt(b("BEST"), b("bn"), b("ad"), OP.mult)
+        if t:
+            tt(b("BEST"), b("BEST"), b("BEST0"), OP.add)
+        if t < VI - 1:
+            ts(b("PK", 0, 256, 16), b("RHO"), 16.0, OP.mult)
+            ts(b("PK", 1, 256, 16), b("BEST"), 16.0, OP.mult)
+            for h in range(2):
+                mm(b("MC", 128 * h, 128 * h + 128), b("PK", 128 * h, 128 * h + 128), b("IDF"), f32=True)
+            tt(b("X"), b("MC", 0, 256), Q, OP.add)
+            snd, rcv = "SND%d" % t, "RCV%d" % t
+            op("v", lambda: V.tensor_copy(b(snd)[4].indirect(b("OFFP")[4]), b("X")[4]), [b("X"), b("OFFP")], [b(snd)], 0.05 + 256 * 3 * CY)
+            dst = T.cores[(rank + 1) % N]
+            rid, pid, _x = topo.addr(dst)
+            op("g", lambda: g.remote_dma(T[rcv][:, 0:CAP], T[snd][:, 0:CAP], T.sem["arr%d" % t], T.sem["sent%d" % t], pid, rid, topo.mask(core, dst)),
+               [b(snd, 0, CAP)], [], 0.1, "r", t)
+        out_rows("RHO", "or%d" % t, "LI1", T.yr, t)
+        out_rows("BEST", "ob%d" % t, "KP1", T.yb, t)
+        if t == VI - 1:
+            return
+        cp(b("PN"), b("PJ"))
+        ts(b("hi6"), b("PJ"), 4032, OP.bitwise_and)
+        ts(b("lo6"), b("PJ"), 63, OP.bitwise_and)
+        cp(b("NQ", 0, 16), b("hi6"))
+        cp(b("NQ", 16, 32), b("lo6"))
+        mm(b("KP1", 0, 128, 1, 32), b("NQ"), b("IDB"))
+        act(b("NQT", 0, 128, 1, 32), b("KP1", 0, 128, 1, 32), AF.Copy)
+        wide(lambda o: cp(o, b("PJ")), "GO1")
+        act(b("GC"), ind(b("CH"), b("GO1")), AF.Copy, extra=[b("GO1")], cost=0.065 + 256 * 1.5 * CY)
+        act(b("RHT"), b("MC", 0, 256), AF.Copy)
+        for h in range(2):
+            mm(b("LI0", 128 * h, 128 * h + 128), b("BC0"), b("RHT", 128 * h, 128 * h + 128))
+        act(b("M1"), b("LI0", 0, 256), AF.Abs, bias=b("biasr", 0, 1))
+        act(b("M1"), b("M1"), AF.Sign, scale=-1.0, bias=8.0)
+        act(b("OHG"), b("M1"), AF.Relu)
+        tt(b("OC"), b("OHG"), b("GC"), OP.mult)
+        for h in range(2):
+            mm(b("LI1", 8 * h, 8 * h + 8), b("OC", 128 * h, 128 * h + 128), b("LC"), f32=True)
+        ts(b("emp"), b("LI1", 0, 16), 0.0, OP.is_equal)
+        tt(b("can"), b("ad"), b("FARB"), OP.mult)
+        tt(b("can"), b("can"), b("emp"), OP.mult)
+        cp(b("CANB"), b("can"))
+        for gg in range(8):
+            ps, eq = ("MA", "KP0")[gg % 2], "EQ%d" % gg
+            rw = [b("SELH", 128 * (8 * h + gg), 128 * (8 * h + gg) + 128, 1, 32) for h in range(2)]
+            nt = b("NQT", 0, 128, 1, 32)
+            mm(b(ps, 0, 128), rw[0], nt, True, False)
+            mm(b(ps, 0, 128), b("IDB"), b("TRI"), False, True)
+            mm(b(ps, 128, 256), rw[1], nt)
+            mm(b(ps, 256, 384), rw[1], nt, True, False)
+            mm(b(ps, 256, 384), b("IDB"), b("TRI"), False, True)
+            for lo, hi, cc in ((0, 256, gg), (256, 384, 8 + gg)):
+                if gg in GSC:
+                    act(b("EF", lo, hi), b(ps, lo, hi), AF.Abs, scale=-1.0, bias=b("PN", cc, cc + 1))
+                    act(b(eq, lo, hi), b("EF", lo, hi), AF.Relu, scale=-1.0, bias=1.0)
+                else:
+                    ts(b(eq, lo, hi), b(ps, lo, hi), b("PN", cc, cc + 1), OP.is_equal)
+        for gg in range(8):
+            eq = "EQ%d" % gg
+            mm(b("MC", gg, gg + 1), b(eq, 0, 128), b("CANB", gg, gg + 1))
+            mm(b("MC", 8 + gg, 9 + gg), b(eq, 128, 256), b("CANB", gg, gg + 1), True, False)
+            mm(b("MC", 8 + gg, 9 + gg), b(eq, 256, 384), b("CANB", 8 + gg, 9 + gg), False, True)
+        ts(b("win"), b("MC", 0, 16), 0.0, OP.is_equal)
+        tt(b("win"), b("win"), b("can"), OP.mult)
+        tt(b("YP"), b("win"), b("PN"), OP.mult)
+        tt(b("gq"), b("PN"), b("K4096"), OP.subtract)
+        tt(b("gq"), b("gq"), b("win"), OP.mult)
+        wide(lambda o: tt(o, b("gq"), b("K4096"), OP.add), "GO2")
+        tt(b("VAL"), b("OHG"), b("NID%d" % t), OP.mult)
+        tt(b("VAL"), b("VAL"), b("GC"), OP.add)
+        op("v", lambda: V.tensor_copy(b("CH")[4].indirect(b("GO2")[4]), b("VAL")[4]), [b("VAL"), b("GO2")], [b("CH")], 0.05 + 256 * 3 * CY)
+        if t == 1:
+            cp(b("PT", M + L, M + 2 * L), Q)
+        out_rows("YP", "op%d" % t, "MB", T.yp, t)
+
+    def receive(t):
+        r = b("RCV%d" % (t - 1))
+        ts(b("RV"), r, 0.0, OP.is_lt, ext=t - 1)
+        ts(b("RI"), r, 15, OP.bitwise_and, ext=t - 1)
+        tt(b("RT"), b("RV"), b("QF", L * t, L * t + L), OP.mult)
+        tt(b("QV%d" % t), b("RT"), b("RI"), OP.add)
+        ts(b("RS"), r, 4, OP.arith_shift_right, ext=t - 1)
+        cp(b("RF"), b("RS"))
+
+    def late_constants():
+        cp(b("D0", 128, 256), b("D0", 0, 128))
+        cp(b("DM", 128, 256), b("DM", 0, 128))
+        ts(b("LTRI"), b("jf"), P, OP.is_gt)
+        ts(b("TRI"), b("jf"), P, OP.is_le, 8192.0, OP.mult)
+        fill(b("ONESB"), 1.0)
+        fill(b("ONESF"), 1.0)
+        ts(b("pf", 3, 4), P15, 0.0, OP.is_equal)
+        ts(b("BLK0"), b("LC"), b("pf", 3, 4), OP.mult)
+        ts(b("biasr", 1, 2), P15, 1.0, OP.is_equal)
+        ts(b("SELR", 0, 8), b("LC"), b("pf", 3, 4), OP.mult)
+        ts(b("SELR", 8, 16), b("LC"), b("biasr", 1, 2), OP.mult)
+        ts(b("biasr", 0, 1), P15, -16.0, OP.mult, -7.5, OP.add)
+        cp(b("thf", 0, 1), b("thi", 0, 1))
+        ts(b("THM"), b("ONESF"), b("thf", 0, 1), OP.mult)
+        mm(b("MC", 64, 72), b("THM"), b("BLK0"))
+        cp(b("TH", 0, 8), b("MC", 64, 72))
+        cp(b("TH", 8, 16), b("MC", 64, 72))
+        iota(b("KI"), [[128, 2], [0, 8]], 0, 1, True)
+        ts(b("K192"), b("KI"), float(CAP), OP.add)
+        ts(b("K4096"), b("KI"), 4096.0, OP.add)
+        iota(b("NID0"), [[1, 256]], M, 0, True)
+        iota(b("NID1"), [[1, 256]], M + L, 0, True)
+        iota(b("selj"), [[1, 16], [0, 128]], 0, 0, True)
+        ts(b("SELH"), b("selj"), P15, OP.is_equal)
+        ts(b("j15i"), b("ji"), 4, OP.arith_shift_right)
+        cp(b("M1", 0, 128), b("j15i"))
+        ts(b("M1", 0, 128), b("M1", 0, 128), P4, OP.is_equal, 0.0625, OP.mult)
+        ts(b("BC0"), b("M1", 0, 128), b("pf", 3, 4), OP.mult)
+        for x in ("LBD", "LBD2", "PK"):
+            fill(b(x), 0.0)
+        for x in "01":
+            fill(b("SND" + x), -16)
+            fill(b("RCV" + x, CAP, L), -16)
+
+    for t in range(VI):
+        Q = b("QF", 0, L) if t == 0 else b("QV%d" % t)
+        Q16 = ("Q16a", "Q16b", "Q16a")[t]
+        if t:
+            receive(t)
+        for h in range(2):
+            begin(t, h, Q, Q16)
+        if t == 0:
+            late_constants()
+        for s in range(5):
+            for h in range(2):
+                push(t, h, s, Q16)
+        finish(t, Q)
+
+    n = len(ops)
+    WAKE = 0.06
+    lat = [o["cost"] + (o["ext"] if o["kind"] == "d" else 0) for o in ops]
+    succ = [[] for _ in range(n)]
+    cnt = [0] * n
+    for i, o in enumerate(ops):
+        dd = set(o["deps"])
+        if o["kind"] == "c" and o["ext"] is not None:
+            x = [j for j in range(n) if ops[j]["kind"] == "r" and ops[j]["ext"] == o["ext"]][0]
+            lat[x] = 4.0
+            dd.add(x)
+        for d in dd:
+            succ[d].append((i, WAKE))
+        for d in o["after"] - dd:
+            succ[d].append((i, None))
+        cnt[i] = len(dd | o["after"])
+    pri = [0.0] * n
+    for i in range(n - 1, -1, -1):
+        pri[i] = max([lat[i] + x + pri[j] if x is not None else ops[i]["cost"] + pri[j] for j, x in succ[i]] or [lat[i]])
+    rt = [0.0] * n
+    free = {}
+    order = []
+    byq = {}
+    for i in range(n):
+        if cnt[i] == 0:
+            byq.setdefault(ops[i]["q"], []).append(i)
+    while len(order) < n:
+        t0, qn = min((max(free.get(x, 0.0), min(rt[i] for i in lst)), x) for x, lst in byq.items() if lst)
+        i = max((i for i in byq[qn] if rt[i] <= t0), key=lambda i: pri[i])
+        byq[qn].remove(i)
+        order.append(i)
+        free[qn] = t0 + ops[i]["cost"]
+        for j, x in succ[i]:
+            if x is not None:
+                rt[j] = max(rt[j], t0 + lat[i] + x)
+            cnt[j] -= 1
+            if cnt[j] == 0:
+                byq.setdefault(ops[j]["q"], []).append(j)
+
+    QS = {"v": V, "t": TE, "s": S, "g": g, "y": g.sync}
+    CS = {"v": "cv", "t": "ct", "s": "cs", "g": "cg"}
+    done = {}
+    total = {"v": 0, "t": 0, "s": 0, "g": 0}
+    know = {x: {} for x in QS}
+    nout = len(topo.engines(core, T.cores[(rank + 1) % N]))
+    nin = len(topo.engines(T.cores[(rank - 1) % N], core))
+    for i in order:
+        o = ops[i]
+        qn = o["q"]
+        k = know[qn]
+        need = {}
+        for d in o["deps"]:
+            sem, val, kn = done[d]
+            if need.get(sem, (0,))[0] < val:
+                need[sem] = (val, kn)
+        if o["kind"] == "c" and o["ext"] is not None:
+            need["arr%d" % o["ext"]] = (nin, {})
+        for sem, (val, kn) in sorted(need.items(), key=lambda e: -len(e[1][1])):
+            if k.get(sem, 0) >= val:
+                continue
+            QS[qn].wait_ge(T.sem[sem], val)
+            k[sem] = val
+            for a, c in kn.items():
+                if k.get(a, 0) < c:
+                    k[a] = c
+        if o["kind"] == "c":
+            total[qn] += 1
+            o["call"]().then_inc(T.sem[CS[qn]], 1)
+            done[i] = (CS[qn], total[qn], dict(k))
+        elif o["kind"] == "d":
+            o["call"]().then_inc(T.sem[o["sem"]], 16)
+            done[i] = (o["sem"], 16, dict(k))
+        else:
+            o["call"]()
+            done[i] = ("sent%d" % o["ext"], nout, dict(k))
+    for x in "vtsg":
+        g.wait_ge(T.sem[CS[x]], total[x])
+    for i in range(ndma[0]):
+        g.wait_ge(T.sem["d%d" % i], 16)
+    for t in range(VI - 1):
+        g.wait_ge(T.sem["sent%d" % t], nout)
+        g.wait_ge(T.sem["arr%d" % t], nin)
+    return max(free.values())

@@ -1,14 +1,17 @@
 from concourse.mybir import AluOpType as OP, ActivationFunctionType as AF
 
 N, L, CAP, M, VI = 4, 256, 192, 3584, 3
-B24 = float(2 ** 24)
-SC = float(2 ** 26)
+U = 2.0 ** -26
 BIG = float(2 ** 60)
-GSC = (3, 6)
-NCH = 4
-SCH = ((1, 3), (1, 3))
+CO = 7.5 * 65536
+FLAG = float(2 ** 22)
 ROOM = 4096 + 256
-QSC = 16
+SNDW = 1280
+NV = ((70, 70), (70, 70), (70, 70), (70, 70), (80, 40))
+NVL = (88, 72)
+VP = 2
+QV = 10
+GSC = ((3, 6), (1, 3, 5, 7))
 
 SCRATCH = {}
 PS = set()
@@ -27,46 +30,46 @@ def _s(name, cols, dt="float32"):
     p[1] += (cols + 15) // 16 * 16
 
 
-for _n in ("VB", "KP0", "KP1", "LI0", "LI1", "MA", "MB", "MC"):
+for _n in ("KP0", "KP1", "MA", "MB", "SP0", "SP1", "SP2", "SP3"):
     SCRATCH[_n] = ("psum", [128, 512], "float32")
     VIRT[_n] = (_n, 0, 512)
     PS.add(_n)
-_own("PT", 4096, "bfloat16"); _own("CHI", M, "int32"); _own("CH", ROOM); _own("QF", 768, "bfloat16")
+_own("PT", M + VI * L, "bfloat16"); _own("CHI", M, "int32"); _own("CH", ROOM)
 _own("wi", 8, "int32"); _own("thi", 8, "int32"); _own("r0i", 768, "int32")
-_own("Q16a", 4096, "bfloat16"); _own("Q16b", 4096, "bfloat16"); _own("DIFF", 4096, "bfloat16")
+_own("Q16", 4096, "bfloat16"); _own("DIFF", 4096, "bfloat16")
 for _t in "01":
-    _own("SND" + _t, CAP + L, "int32"); _own("RCV" + _t, L, "int32")
+    _own("SND" + _t, SNDW); _own("RCV" + _t, L)
 for _t in "012":
-    _own("or" + _t, 256); _own("ob" + _t, 256); _own("op" + _t, 256)
-for _n, _c in (("r0f", 768), ("wf", 2), ("thf", 2), ("pf", 4), ("jf", 128), ("j15", 128), ("c8", 8), ("IDF", 128), ("DM", 256),
-               ("LC", 8), ("RAMP", 128), ("MX", 128), ("D0", 256), ("biasc", 2), ("biasr", 2), ("TH", 16), ("KI", 16), ("K192", 16),
-               ("K4096", 16), ("NID0", 256), ("NID1", 256), ("ONESF", 128), ("selj", 2048), ("SELR", 16), ("R0P1", 48),
-               ("C24", 8), ("BEST0", 16), ("VF", 112), ("VZ", 112), ("LF", 112), ("RHO", 16), ("ad", 16), ("bn", 16), ("BEST", 16),
-               ("pl", 16), ("go", 16), ("gd", 16), ("PN", 16), ("emp", 16), ("can", 16), ("win", 16), ("YP", 16), ("gq", 16),
-               ("LBD", 256), ("Z2", 256), ("PK", 256), ("X", 256), ("GC", 256), ("M1", 256), ("OHG", 256), ("OC", 256),
-               ("VAL", 256), ("LBD2", 256), ("Z3", 256), ("RV", 256), ("RT", 256), ("RF", 256), ("EF", 384)):
+    _own("OB" + _t, 256)
+for _n, _c in (("r0f", 768), ("wf", 2), ("thf", 2), ("pf", 8), ("jf", 128), ("j15", 128), ("c8", 8), ("IDF", 128), ("DM", 256),
+               ("LC", 8), ("RAMP", 256), ("MX", 128), ("ROWB", 128), ("D8", 64), ("bias", 8), ("THK", 8), ("K4096", 16), ("KL", 16),
+               ("SEL", 16), ("FR", 96), ("E", 256), ("A", 256), ("K0", 16), ("RTL", 16), ("B0C", 16), ("EF", 256), ("tmp", 128)):
     _s(_n, _c)
-for _n, _c in (("pi", 4), ("ji", 128), ("j15i", 128), ("V", 112), ("VI", 112), ("PI", 16), ("PJ", 16), ("hi6", 16), ("lo6", 16),
-               ("RI", 256), ("RS", 256)):
+for _n, _c in (("pi", 8), ("ji", 128), ("j15i", 128), ("li", 96), ("si", 16), ("sj", 16), ("DK", 16), ("MI", 192), ("QI", 192),
+               ("PM", 32), ("PD", 32)):
     _s(_n, _c, "int32")
-for _n, _c in [("IDB", 128), ("NIDB", 128), ("BLK", 8), ("BLK0", 8), ("WB", 8), ("TRI", 128), ("LTRI", 128), ("ONESB", 128),
-               ("THM", 128), ("SELH", 2048), ("QV1", 256), ("QV2", 256), ("FARB", 16), ("NQ", 32), ("NQT", 128), ("RHT", 256),
-               ("BC0", 128), ("CANB", 16)] + [("EQ%d" % _e, 384) for _e in range(8)]:
+for _n, _c in [("IDB", 128), ("NIDB", 128), ("WI", 128), ("BLKU", 8), ("BLK", 8), ("BLK0", 8), ("LCB", 8), ("WB", 8), ("TRI", 128),
+               ("LTD0", 128), ("LTD1", 128), ("ONES", 2048), ("R", 2048), ("THM", 128), ("selj", 1024), ("SELG", 1024), ("ZR", 256),
+               ("DRB", 256), ("NQT", 256), ("DGL", 128), ("DGB", 128 * 4)]:
     _s(_n, _c, "bfloat16")
-for _n in ("OFFP", "GO1", "GO2"):
-    _s(_n, 16, "uint16")
+_s("LI", 96, "uint16"); _s("OFF", 16, "uint16")
 for _h in "01":
-    for _n, _c, _d in (("si", 8, "int32"), ("sj", 8, "int32"), ("RTL", 8, "float32"), ("SBD", 128, "float32"), ("RBD", 128, "float32"),
-                       ("Z", 128, "float32"), ("OFF", 8, "uint16"), ("DR", 128, "bfloat16"), ("FB0", 8, "float32"), ("FB1", 8, "float32"),
-                       ("E", 128, "float32"), ("A", 128, "float32"), ("Tf", 8, "int32"), ("u", 128, "float32"),
-                       ("Pf", 128, "float32"), ("PU", 128, "uint16"), ("KU", 128, "float32"), ("KS", 128, "float32"), ("u2", 128, "float32"),
-                       ("KM", 128, "float32"), ("MS", 128, "float32"), ("OH", 128, "float32"), ("FO", 128, "float32"), ("pm", 128, "float32"),
-                       ("lo", 8, "int32"), ("lp", 8, "int32"), ("ri", 8, "float32"), ("rx", 8, "float32"), ("rho", 8, "float32")):
+    for _n, _c, _d in (("PU", 128, "uint16"), ("Pf", 128, "float32"), ("M1", 128, "bfloat16"), ("M2", 128, "bfloat16"),
+                       ("ST", 128, "bfloat16"), ("KS", 128, "float32"), ("KM", 128, "float32"), ("MS", 128, "float32"), ("SK", 32, "int32"), ("NN", 8, "int32"),
+                       ("Z", 128, "float32"), ("RB", 8, "int32"), ("RP", 8, "int32"), ("RKS", 64, "float32"),
+                       ("Tp", 8, "int32"), ("T3", 8, "int32"), ("thr", 8, "float32"), ("m", 64, "float32"), ("x", 64, "float32"),
+                       ("sc", 64, "float32"), ("ki", 8, "int32"), ("W", 16, "int32"), ("z3", 8, "float32"), ("V4", 8, "int32"),
+                       ("n4", 16, "int32"), ("z", 16, "float32"), ("RI", 24, "int32"), ("OUT", 32, "float32"), ("far", 8, "bfloat16"),
+                       ("dest", 8, "float32"), ("ZD", 128, "float32"), ("OP", 8, "uint16"), ("PK", 128, "float32"), ("XS", 128, "float32"),
+                       ("pre", 8, "float32"), ("gq", 8, "float32"), ("Z1", 128, "float32"), ("G1", 8, "uint16"), ("GC", 128, "float32"),
+                       ("bb", 8, "int32"), ("OH", 128, "bfloat16"), ("ON", 128, "float32"), ("OC", 128, "bfloat16"), ("can", 8, "bfloat16"),
+                       ("win", 8, "float32"), ("Z2", 128, "float32"), ("G2", 8, "uint16"), ("NI", 16, "int32"), ("NQ", 16, "bfloat16"),
+                       ("NT", 128, "bfloat16"), ("EQ", 2048, "bfloat16")):
         _s(_n + _h, _c, _d)
 for _d in POOL:
     SCRATCH[POOL[_d][0]] = ("sbuf", [128, POOL[_d][1]], _d)
 
-NDMA = 26
+NDMA = 24
 SEMAPHORES = ["cv", "ct", "cs", "cg"] + ["d%d" % i for i in range(NDMA)] + ["arr0", "arr1", "sent0", "sent1"]
 
 
@@ -78,15 +81,14 @@ def rank_program(g, core, T, topo):
     hist = {}
     ndma = [0]
     rot = [0]
+    tag = [""]
+    c0 = 4096.0 * rank
 
-    def b(name, lo=0, hi=None, st=1, rows=None):
+    def b(name, lo=0, hi=None, st=1, rows=None, row0=0):
         buf, o, c = VIRT[name]
         hi = c if hi is None else hi
-        p = slice(None) if rows is None else slice(0, rows)
+        p = slice(None) if rows is None else slice(row0, row0 + rows)
         return (name, lo, hi, st, T[buf][p, o + lo:o + hi:st] if st > 1 else T[buf][p, o + lo:o + hi])
-
-    def ind(w, o):
-        return (w[0], w[1], w[2], 1, w[4].indirect(o[4]))
 
     def clash(x, y):
         if x[1] <= y[0] or y[1] <= x[0]:
@@ -113,418 +115,445 @@ def rank_program(g, core, T, topo):
             if w and o[0] not in PS:
                 h[:] = [e for e in h if not (r[2] == 1 and r[0] <= e[0][0] and e[0][1] <= r[1] and e[2] != n)]
             h.append((r, w, n))
-            if len(h) > 400:
-                del h[:100]
-        d = {"q": q, "call": call, "deps": deps, "after": after - deps, "cost": cost, "kind": kind, "ext": ext}
+            if o[0] in PS and len(h) > 120:
+                del h[:40]
+        d = {"q": q, "call": call, "deps": deps, "after": after - deps, "cost": cost, "kind": kind, "ext": ext,
+             "tag": tag[0] + " " + (writes[0][0] if writes else "")}
         if kind == "d":
             d["sem"] = "d%d" % ndma[0]
             ndma[0] += 1
         ops.append(d)
         return n
 
-    CY = 0.00083 * 1.15
+    CY, GA, SCA = 0.00083 * 1.2, 1.56, 3.8
+    FV, FS, FT = 0.05, 0.065, 0.015
+    two = ("poolb", "poolu", "PT", "Q16", "DIFF")
 
     def cols(o):
         return (o[2] - o[1] + o[3] - 1) // o[3]
 
     def vc(n, k=1.0):
-        return 0.06 + max(64, n * k) * CY
+        return FV + max(64, n * k) * CY
+
+    def half(*xs):
+        return 0.5 if all(VIRT[x[0]][0] in two for x in xs) else 1.0
 
     V, S, TE = g.vector, g.scalar, g.tensor
 
     def isap(x):
         return isinstance(x, tuple)
 
-    def tt(out, a, c, o):
+    def tt(out, a, c, o, ext=None):
         k = 1.0 if (a[0] in PS or c[0] in PS) else 2.0
-        op("v", lambda: V.tensor_tensor(out[4], a[4], c[4], o), [a, c], [out], vc(cols(out), k))
+        op("v", lambda: V.tensor_tensor(out[4], a[4], c[4], o), [a, c], [out], vc(cols(out), k), "c", ext)
 
-    def ts(out, a, s1, o1, s2=None, o2=None, ext=None):
+    def tg(out, win, off, c, o):
+        op("v", lambda: V.tensor_tensor(out[4], win[4].indirect(off[4]), c[4], o), [win, off, c], [out], FV + cols(out) * GA * CY)
+
+    def ts(out, a, s1, o1, s2=None, o2=None):
         x1 = s1[4] if isap(s1) else s1
         x2 = s2[4] if isap(s2) else s2
         rd = [a] + [s for s in (s1, s2) if isap(s)]
         if o2 is None:
-            op("v", lambda: V.tensor_scalar(out[4], a[4], x1, None, o1), rd, [out], vc(cols(out)), "c", ext)
+            op("v", lambda: V.tensor_scalar(out[4], a[4], x1, None, o1), rd, [out], vc(cols(out), half(out, a)))
         else:
-            op("v", lambda: V.tensor_scalar(out[4], a[4], x1, x2, o1, o2), rd, [out], vc(cols(out)), "c", ext)
+            op("v", lambda: V.tensor_scalar(out[4], a[4], x1, x2, o1, o2), rd, [out], vc(cols(out), half(out, a)))
 
     def cp(out, a):
-        op("v", lambda: V.tensor_copy(out[4], a[4]), [a], [out], vc(cols(out)))
+        op("v", lambda: V.tensor_copy(out[4], a[4]), [a], [out], vc(cols(out), half(out, a)))
 
     def scan(out, d0, d1, o0, o1):
         op("v", lambda: V.tensor_tensor_scan(out[4], d0[4], d1[4], 0.0, o0, o1), [d0, d1], [out], vc(cols(out)))
 
     def fill(out, x):
-        op("v", lambda: V.memset(out[4], x), [], [out], vc(cols(out)))
+        op("v", lambda: V.memset(out[4], x), [], [out], vc(cols(out), half(out)))
 
-    def act(out, a, f, bias=None, scale=1.0, extra=(), cost=None):
+    def act(out, a, f, bias=None, scale=1.0, off=None):
         kw = {"scale": scale}
-        rd = [a] + list(extra)
+        rd = [a] if off is None else [a, off]
         if bias is not None:
             kw["bias"] = bias[4] if isap(bias) else bias
             if isap(bias):
                 rd.append(bias)
-        op("s", lambda: S.activation(out[4], a[4], f, **kw), rd, [out], cost or (0.06 + cols(out) * CY))
+        src = a[4] if off is None else a[4].indirect(off[4])
+        op("s", lambda: S.activation(out[4], src, f, **kw), rd, [out], FS + cols(out) * CY * (1 if off is None else GA))
 
-    def mm(out, l, r, start=True, stop=True, f32=False):
+    def mm(out, l, r, start=True, stop=True, f32=False, ext=None):
         n = max(min(64, cols(l)), cols(r))
-        op("t", lambda: TE.matmul(out[4], l[4], r[4], start, stop), [l, r], [out], 0.03 + n * (4 if f32 else 1) * 0.00083)
+        op("t", lambda: TE.matmul(out[4], l[4], r[4], start, stop), [l, r], [out], FT + n * (4 if f32 else 1) * CY, "c", ext)
 
     def dma(q, out, src, reads, writes, us):
         eng = g.sync if q == "y" else g.scalar
         op(q, lambda: eng.dma_start(out, src), reads, writes, 0.06, "d", us)
 
-    def iota(out, pat, base, cm, flag=False):
-        kw = {"allow_small_or_imprecise_dtypes": True} if flag else {}
+    def iota(out, pat, base, cm):
+        kw = {} if VIRT[out[0]][0] == "pooli" else {"allow_small_or_imprecise_dtypes": True}
         op("g", lambda: g.iota(out[4], pat, base, cm, **kw), [], [out], 0.13 + 2 * cols(out) * CY)
 
-    def load(q, name, lo, hi, src, rows=None):
+    def load(q, name, lo, hi, src, us, rows=None):
         o = b(name, lo, hi, 1, rows)
-        dma(q, o[4], src, [], [o], 2.5)
+        dma(q, o[4], src, [], [o], us)
 
-    load("y", "QF", 0, 768, T.q[:])
-    load("s", "wi", 0, 1, T.w[:])
-    load("y", "CHI", 0, 896, T.ch[:, 0:896])
-    load("s", "CHI", 896, 1792, T.ch[:, 896:1792])
-    load("y", "PT", 0, M, T.pt[:])
-    load("s", "CHI", 1792, 2688, T.ch[:, 1792:2688])
-    load("y", "r0i", 0, 768, T.r0[:], 8)
-    load("s", "CHI", 2688, M, T.ch[:, 2688:M])
-    load("y", "thi", 0, 1, T.th[:])
+    load("y", "PT", M, M + VI * L, T.q[:], 2.0)
+    load("s", "wi", 0, 1, T.w[:], 2.0)
+    load("y", "PT", 0, M, T.pt[:], 4.5)
+    load("s", "CHI", 0, 128, T.ch[:, 0:128], 2.2)
+    load("s", "r0i", 0, 768, T.r0[:], 2.2, 8)
+    CHP = (128, 1280, 2432, M)
+    for k in range(3):
+        load("y", "CHI", CHP[k], CHP[k + 1], T.ch[:, CHP[k]:CHP[k + 1]], 6.0 + 1.5 * k)
+    load("s", "thi", 0, 1, T.th[:], 2.5)
 
     iota(b("pi", 0, 1), [[0, 1]], 0, 1)
     iota(b("ji"), [[1, 128]], 0, 0)
-    iota(b("c8"), [[1, 8]], 0, 0, True)
+    iota(b("c8"), [[1, 8]], 0, 0)
+    iota(b("li", 0, 16), [[1, 16]], 0, 0)
+    iota(b("li", 16, 24), [[16, 8]], 15, 0)
+    iota(b("li", 24, 72), [[1, 6], [8, 8]], 0, 0)
+    iota(b("li", 72, 76), [[2, 4]], 0, 0)
+    iota(b("RAMP"), [[0, 16], [16, 16]], 0, 0)
     ts(b("pi", 1, 2), b("pi", 0, 1), 15, OP.bitwise_and)
     ts(b("pi", 2, 3), b("pi", 0, 1), 4, OP.arith_shift_right)
-    cp(b("pf", 0, 3), b("pi", 0, 3))
-    P, P15, P4 = b("pf", 0, 1), b("pf", 1, 2), b("pf", 2, 3)
+    ts(b("pi", 3, 4), b("pi", 0, 1), 3, OP.arith_shift_right, 1, OP.bitwise_and)
+    ts(b("pi", 4, 5), b("pi", 0, 1), 7, OP.bitwise_and)
+    cp(b("pf", 0, 5), b("pi", 0, 5))
+    P, P15, P4, P3, P7 = [b("pf", k, k + 1) for k in range(5)]
+    cp(b("LI", 0, 72), b("li", 0, 72))
+    ts(b("LI", 72, 76), b("li", 72, 76), P3, OP.add)
+    cp(b("LI", 76, 77), b("pi", 4, 5))
+    BC16, BC8, BC15, BH, DUP = b("LI", 0, 16), b("LI", 0, 8), b("LI", 16, 24), b("LI", 72, 76), b("LI", 76, 77)
+    BCS = [b("LI", 24 + 8 * s, 32 + 8 * s) for s in range(6)]
     cp(b("jf"), b("ji"))
     ts(b("j15i"), b("ji"), 15, OP.bitwise_and)
     cp(b("j15"), b("j15i"))
     ts(b("LC"), b("c8"), P4, OP.is_equal)
+    ts(b("LCB"), b("c8"), P4, OP.is_equal)
     ts(b("BLK"), b("LC"), 65536.0, OP.mult)
     cp(b("wf", 0, 1), b("wi", 0, 1))
     ts(b("WB"), b("LC"), b("wf", 0, 1), OP.mult)
-    ts(b("D0", 0, 128), b("j15"), 0.0, OP.is_gt)
     ts(b("DM", 0, 128), b("j15"), P15, OP.is_equal)
+    ts(b("DM", 128, 256), b("j15"), P15, OP.is_equal)
     ts(b("IDF"), b("jf"), P, OP.is_equal)
-    cp(b("IDB"), b("IDF"))
-    ts(b("NIDB"), b("IDF"), -1.0, OP.mult)
-    ts(b("RAMP"), b("j15"), 16.0 * 65536, OP.mult, 8.0 * 65536 - B24, OP.add)
-    ts(b("MX"), b("D0", 0, 128), -2 * BIG, OP.mult, BIG, OP.add)
-    ts(b("biasc", 0, 1), P15, 4096.0, OP.mult, -B24, OP.add)
-    fill(b("C24"), B24)
-    for h in "01":
-        fill(b("SBD" + h), 0.0)
-        fill(b("RBD" + h), 0.0)
-    fill(b("V"), 32768)
+    ts(b("IDB"), b("jf"), P, OP.is_equal)
+    ts(b("NIDB"), b("IDB"), -1.0, OP.mult)
+    ts(b("WI"), b("IDB"), 2.0 ** 26, OP.mult)
+    ts(b("RAMP"), b("RAMP"), 15.5, OP.add)
+    ts(b("MX"), b("j15"), 0.0, OP.is_gt, -2 * BIG, OP.mult)
+    ts(b("MX"), b("MX"), BIG, OP.add)
+    ts(b("BLKU"), b("LC"), 65536.0 * U, OP.mult)
+    ts(b("bias", 0, 1), P15, 4096.0 * U, OP.mult, CO * U, OP.add)
+    ts(b("bias", 1, 2), P15, 4096.0, OP.mult, CO + 32768, OP.add)
+    fill(b("ONES"), 1.0)
+    op("g", lambda: g.affine_select(b("R")[4], b("ONES")[4], [[-1, 128], [0, 16]], OP.is_equal, 0.0, 0, 1),
+       [b("ONES")], [b("R")], 0.17 + 2 * 2048 * CY)
+    fill(b("FR"), 0.0)
     cp(b("r0f", rows=8), b("r0i", rows=8))
-    for t in range(VI):
-        for h in range(2):
-            k = t * 2 + h
-            mm(b("MC", 8 * k, 8 * k + 8), b("r0f", t * L + 128 * h, t * L + 128 * h + 128, rows=8), b("IDF", 0, 8, rows=8), f32=True)
-    ts(b("R0P1"), b("MC", 0, 48), 1.0, OP.add)
-    for k in range(4):
-        cp(b("CH", 896 * k, 896 * k + 896), b("CHI", 896 * k, 896 * k + 896))
-    fill(b("CH", M, ROOM), 0.0)
+    for k in range(2 * VI):
+        mm(b("MB", 8 * k, 8 * k + 8), b("r0f", 128 * k, 128 * k + 128, rows=8), b("IDF", 0, 8, rows=8), f32=True)
+    for h in range(2):
+        fill(b("RKS%d" % h), 0.0)
+        ts(b("RKS%d" % h, 0, 64, 8), b("MB", 8 * h, 8 * h + 8), 65536.0 * U, OP.mult, CO * U, OP.add)
+    for t in (1, 2):
+        ts(b("FR", 32 * t, 32 * t + 16), b("MB", 16 * t, 16 * t + 16), 16.0, OP.mult, 128.0, OP.add)
+    cp(b("CH", 0, 128), b("CHI", 0, 128))
     fill(b("PT", 0, 1), 2048.0)
-    cp(b("PT", M, M + L), b("QF", 0, L))
-    fill(b("PT", M + L, 4096), 0.0)
 
-    SBr = [b("VB", 0, 128), b("VB", 128, 256)]
-    RBr = [b("VB", 256, 384), b("VB", 384, 512)]
-
-    def lists(src, zt, mat, psum):
-        tt(zt, src, mat, OP.mult)
-        for x in range(cols(src) // 128):
-            mm(b(psum, 8 * x, 8 * x + 8), b(zt[0], 128 * x, 128 * x + 128), b("LC"), f32=True)
-
-    def radius(h):
-        n = lambda x, *a: b(x + str(h), *a)
-        ts(n("RBD", 0, 128, 16), n("Tf"), SC, OP.mult, (B24 + 524288) * SC, OP.add)
-        scan(RBr[h], b("D0", 0, 128), n("RBD"), OP.mult, OP.add)
-
-    def adopt(h, s, key):
-        ti = b("V", 56 * h + s, 56 * h + 56, 7)
-        tf = b("Tf%d" % h)
-        tt(ti, key, tf, OP.min)
-        ts(tf, ti, -65536, OP.bitwise_and)
-
-    def begin(t, h, Q, Q16):
-        hs = str(h)
-        n = lambda x, *a: b(x + hs, *a)
-        LI = "LI" + hs
-        q = b(Q[0], Q[1] + 128 * h, Q[1] + 128 * h + 128)
-        mm(b(LI, 8, 16), q, b("WB"))
-        cp(n("si"), b(LI, 8, 16))
-        ts(n("sj"), n("si"), 63, OP.bitwise_and)
-        ts(n("SBD", 0, 128, 16), n("sj"), 1.0, OP.add)
-        ts(n("RTL"), n("sj"), 32769.0, OP.add)
-        scan(SBr[h], b("D0", 0, 128), n("SBD"), OP.mult, OP.add)
-        lists(SBr[h], n("Z"), b("DM", 0, 128), LI)
-        cp(n("OFF"), b(LI, 0, 8))
-        for i in range(16):
-            o = b(Q16, 2048 * h + i, 2048 * h + 2048, 16)
-            if i < QSC:
-                act(o, q, AF.Copy)
-            else:
-                cp(o, q)
-        op("v", lambda: V.tensor_tensor(b("DR" + hs)[4], b("PT")[4].indirect(b("OFF" + hs)[4]), q[4], OP.subtract),
-           [b("PT"), n("OFF"), q], [n("DR")], 0.05 + 128 * 1.5 * CY)
-        act(n("DR"), n("DR"), AF.Abs)
-        mm(b(LI, 16, 24), n("DR"), b("BLK"))
-        tt(n("FB0"), b(LI, 16, 24), n("RTL"), OP.add)
-        r1 = b("R0P1", 8 * (t * 2 + h), 8 * (t * 2 + h) + 8)
-        if t == 0:
-            ts(n("Tf"), r1, 65536.0, OP.mult, -B24 - 65536, OP.add)
-        else:
-            mm(b(LI, 24, 40), b("RF", 128 * h, 128 * h + 128), b("SELR"), f32=True)
-            ts(n("ri"), b(LI, 24, 32), 0.0, OP.is_lt)
-            tt(n("rx"), n("ri"), r1, OP.mult)
-            tt(n("rho"), b(LI, 24, 32), n("rx"), OP.add)
-            ts(b("BEST0", 8 * h, 8 * h + 8), b(LI, 32, 40), 0.0, OP.max)
-            ts(n("Tf"), n("rho"), 65536.0, OP.mult, -B24, OP.add)
-        radius(h)
-        ts(n("SBD", 0, 128, 16), n("FB0"), -B24, OP.add)
-        scan(SBr[h], b("D0", 0, 128), n("SBD"), OP.mult, OP.add)
-        tt(n("E"), SBr[h], b("RAMP"), OP.subtract)
-        act(n("A"), n("E"), AF.Abs, scale=SC)
-
-    def push(t, h, s, Q16):
-        hs = str(h)
-        n = lambda x, *a: b(x + hs, *a)
-        KP, LI = "KP" + hs, "LI" + hs
-        kp = b(KP, 0, 128)
-        ch = b("CH", 0, 4096)
-        op("v", lambda: V.tensor_copy(n("PU")[4], ch[4].indirect(n("OFF")[4])), [ch, n("OFF")], [n("PU")], 0.05 + 128 * 1.5 * CY)
-        act(n("Pf"), ind(ch, n("OFF")), AF.Identity, bias=b("biasc", 0, 1), extra=[n("OFF")], cost=0.065 + 128 * 1.5 * CY)
-        tt(n("u"), n("A"), RBr[h], OP.subtract)
-        if s == 0:
-            adopt(h, 1, n("SBD", 0, 128, 16))
-        mm(kp, n("Pf"), b("IDF"), True, False, f32=True)
-        w = 2048 // NCH
-        for c in range(NCH):
-            lo = 2048 * h + w * c
-            d = b("DIFF", lo, lo + w)
-            o = n("PU", w // 16 * c, w // 16 * (c + 1))
-            qq = b(Q16, lo, lo + w)
-            if c in SCH[h]:
-                act(d, ind(b("PT"), o), AF.Copy, extra=[o], cost=0.065 + w * 1.5 * CY)
-                ps = ("MA", "MB", "MC")[rot[0] % 3]
-                rot[0] += 1
-                mm(b(ps, 0, w), b("IDB"), d, True, False)
-                mm(b(ps, 0, w), b("NIDB"), qq, False, True)
-                act(d, b(ps, 0, w), AF.Abs)
-            else:
-                op("v", lambda d=d, o=o, qq=qq: V.tensor_tensor(d[4], b("PT")[4].indirect(o[4]), qq[4], OP.subtract),
-                   [b("PT"), o, qq], [d], 0.05 + w * 1.5 * CY)
-                act(d, d, AF.Abs)
-        for i in range(16):
-            mm(b(KP, i, 128, 16), b("DIFF", 2048 * h + i, 2048 * h + 2048, 16), b("BLK"), False, i == 15)
-        tt(n("KU"), kp, n("u"), OP.max)
-        scan(n("KS"), b("MX"), n("KU"), OP.max, OP.min)
-        adopt(h, s + 2, n("KS", 15, 128, 16))
-        if s == 4:
-            ts(b("RHO", 8 * h, 8 * h + 8), n("Tf"), 2.0 ** -16, OP.mult, 256.0, OP.add)
-            return
-        radius(h)
-        tt(n("u2"), n("A"), RBr[h], OP.subtract)
-        tt(n("KM"), kp, n("u2"), OP.max)
-        scan(n("MS"), b("MX"), n("KM"), OP.max, OP.min)
-        fb = (b("C24"), n("FB0"), n("FB1"), b("C24"))[s]
-        tt(n("SBD", 0, 128, 16), n("MS", 15, 128, 16), fb, OP.min)
-        scan(SBr[h], b("D0", 0, 128), n("SBD"), OP.mult, OP.add)
-        lists(SBr[h], n("Z"), b("DM", 0, 128), LI)
-        cp(n("lo"), b(LI, 0, 8))
-        ts(n("lp"), n("lo"), 4095, OP.bitwise_and)
-        cp(n("OFF"), n("lp"))
-        if s in (0, 3):
-            tt(n("E"), SBr[h], b("RAMP"), OP.subtract)
-        else:
-            ts(n("pm"), SBr[h], 0.0, OP.is_ge, -B24, OP.mult)
-            tt(n("pm"), n("pm"), n("FO"), OP.mult)
-            tt(n("pm"), n("pm"), b("RAMP"), OP.subtract)
-            tt(n("E"), SBr[h], n("pm"), OP.add)
-        act(n("A"), n("E"), AF.Abs, scale=SC)
-        if s == 0:
-            ts(n("FB1"), n("SBD", 0, 128, 16), B24, OP.add)
-        if s in (0, 1):
-            tt(n("OH"), n("KM"), SBr[h], OP.is_equal)
-            act(n("FO"), n("OH"), AF.Identity, bias=1.0, scale=4096.0)
-
-    def out_rows(src, buf, psum, out, t):
+    def late_constants():
+        for k in range(3):
+            cp(b("CH", CHP[k], CHP[k + 1]), b("CHI", CHP[k], CHP[k + 1]))
+        fill(b("CH", M, ROOM), 0.0)
+        ts(b("j15i"), b("ji"), 8, OP.add)
+        ts(b("j15i"), b("j15i"), 15, OP.bitwise_and)
+        ts(b("ROWB"), b("j15i"), 4096.0, OP.mult)
+        ts(b("li", 0, 64), b("ji", 0, 64), 7, OP.bitwise_and)
+        ts(b("D8"), b("li", 0, 64), 0.0, OP.is_gt)
+        ts(b("TRI"), b("jf"), P, OP.is_le, 8192.0, OP.mult)
+        ts(b("bias", 2, 3), P, 2.0, OP.mult, 256.0, OP.add)
+        ts(b("bias", 3, 4), P, 4.0, OP.mult, 512.0, OP.add)
+        ts(b("tmp"), b("jf"), P, OP.is_gt)
         for h in range(2):
-            mm(b(psum, 128 * h, 128 * h + 128, 1, 8), b(src, 8 * h, 8 * h + 8), b("IDF"), f32=True)
-        o = b(buf, 0, 256, 1, 8)
-        act(o, b(psum, 0, 256, 1, 8), AF.Copy)
-        dma("y", out[:, t * L:(t + 1) * L], o[4], [o], [], 2.0)
+            ts(b("Z1%d" % h), b("IDF"), b("bias", 2 + h, 3 + h), OP.mult)
+            tt(b("LTD%d" % h), b("tmp"), b("Z1%d" % h), OP.subtract)
+            fill(b("PK%d" % h), FLAG)
+            fill(b("SND%d" % h, 0, CAP), 0.0)
+            fill(b("RCV%d" % h, CAP, L), 0.0)
+        ts(b("bias", 5, 6), P15, 0.0, OP.is_equal)
+        ts(b("bias", 6, 7), P15, 1.0, OP.is_equal)
+        ts(b("BLK0"), b("BLK"), b("bias", 5, 6), OP.mult)
+        ts(b("SEL", 0, 8), b("LC"), b("bias", 5, 6), OP.mult)
+        ts(b("SEL", 8, 16), b("LC"), b("bias", 6, 7), OP.mult)
+        ts(b("bias", 7, 8), P, 8.0, OP.is_lt, -8.0 - c0, OP.mult)
+        ts(b("bias", 4, 5), P, 16.0, OP.is_lt, c0, OP.mult)
+        tt(b("bias", 4, 5), b("bias", 4, 5), b("bias", 7, 8), OP.add)
+        cp(b("thf", 0, 1), b("thi", 0, 1))
+        ts(b("THM"), b("ONES", 0, 128), b("thf", 0, 1), OP.mult)
+        mm(b("MB", 64, 72), b("THM"), b("BLK0"))
+        ts(b("THK"), b("MB", 64, 72), 8.0 * 65536, OP.add)
+        iota(b("K4096"), [[128, 2], [0, 8]], 4096, 1)
+        iota(b("KL"), [[16, 16]], 4096, 0)
+        ts(b("KL"), b("KL"), P15, OP.add)
+        iota(b("selj"), [[1, 8], [0, 128]], 0, 0)
+        ts(b("SELG"), b("selj"), P7, OP.is_equal)
+        ts(b("DGL"), b("IDB"), P, OP.mult)
+        for k in range(4):
+            ts(b("DGB", 128 * k, 128 * k + 128), b("IDB"), float(M + 128 * k), OP.mult)
 
-    def wide(vals, dst):
-        vals(b("LBD2", 0, 256, 16))
-        scan(b("VB", 0, 256), b("D0"), b("LBD2"), OP.mult, OP.add)
-        lists(b("VB", 0, 256), b("Z3"), b("DM"), "MB")
-        cp(b(dst), b("MB", 0, 16))
+    def share(t, p, h):
+        return NVL[h] if (t, p) == (VI - 1, 4) else NV[p][h]
 
-    def finish(t, Q):
-        ts(b("VI"), b("V"), 65535, OP.bitwise_and)
-        cp(b("VF"), b("VI"))
-        ts(b("VZ"), b("VI"), 0.0, OP.is_equal)
-        scan(b("LF"), b("VZ"), b("VF"), OP.mult, OP.add)
-        last = b("LF", 6, 112, 7)
-        if t < VI - 1:
-            tt(b("FARB"), b("RHO"), b("TH"), OP.is_ge)
-            mm(b("MA", 0, 8), b("LTRI"), b("FARB", 0, 8))
-            mm(b("MA", 8, 16), b("LTRI"), b("FARB", 8, 16), True, False)
-            mm(b("MA", 8, 16), b("ONESB"), b("FARB", 0, 8), False, True)
-            ts(b("pl"), b("MA", 0, 16), float(CAP), OP.is_lt)
-            tt(b("go"), b("pl"), b("FARB"), OP.mult)
-            tt(b("gd"), b("MA", 0, 16), b("K192"), OP.subtract)
-            tt(b("gd"), b("gd"), b("go"), OP.mult)
-            tt(b("LBD", 0, 256, 16), b("gd"), b("K192"), OP.add)
-            scan(b("VB", 256, 512), b("D0"), b("LBD"), OP.mult, OP.add)
-            lists(b("VB", 256, 512), b("Z2"), b("DM"), "MB")
-            cp(b("OFFP"), b("MB", 0, 16))
-        cp(b("PI"), last)
-        ts(b("PJ"), b("PI"), 4095, OP.bitwise_and)
-        ts(b("ad"), last, 32768.0, OP.not_equal)
-        ts(b("bn"), b("PJ"), 4096.0 * rank, OP.add)
+    def begin(t):
+        q0 = M + L * t
+        Q = b("PT", q0, q0 + L)
+        Qh = [b("PT", q0 + 128 * h, q0 + 128 * h + 128) for h in range(2)]
         if t:
-            tt(b("bn"), b("bn"), b("BEST0"), OP.subtract)
-        tt(b("BEST"), b("bn"), b("ad"), OP.mult)
+            r = "RCV%d" % (t - 1)
+            mm(b("KP0", 0, CAP), b("IDB"), b("PT", q0, q0 + CAP))
+            tt(b("MI"), b(r, 0, CAP), b("KP0", 0, CAP), OP.max, ext=t - 1)
+            ts(b("QI"), b("MI"), 15, OP.bitwise_and)
+            cp(b("PT", q0, q0 + CAP), b("QI"))
+        for h in range(2):
+            mm(b("KP0", 256 + 8 * h, 264 + 8 * h), Qh[h], b("WB"))
+        cp(b("si"), b("KP0", 256, 272))
+        ts(b("sj"), b("si"), 63, OP.bitwise_and)
+        tg(b("ZR"), b("sj"), BC16, b("DM"), OP.mult)
+        for h in range(2):
+            mm(b("KP0", 272 + 8 * h, 280 + 8 * h), b("ZR", 128 * h, 128 * h + 128), b("LCB"))
+        ts(b("OFF"), b("KP0", 272, 288), 1.0, OP.add)
+        lo = 128 - max(share(t, p, 0) for p in range(5))
+        hi = 128 + max(share(t, p, 1) for p in range(5))
+        for i in range(16):
+            o, q = b("Q16", 16 * lo + i, 16 * hi, 16), b("PT", q0 + lo, q0 + hi)
+            if i < QV:
+                cp(o, q)
+            else:
+                act(o, q, AF.Copy)
+        for h in range(2):
+            mm(b("SP2", 128 * h, 128 * h + 128), Qh[h], b("NIDB"))
+        act(b("NQT"), b("SP2", 0, 256), AF.Copy)
+        act(b("DRB"), b("PT", 0, 128), AF.Copy, off=b("OFF"))
+        mm(b("SP3", 0, 256), b("IDB"), b("DRB"), True, False)
+        mm(b("SP3", 0, 256), b("NIDB"), Q, False, True)
+        act(b("DRB"), b("SP3", 0, 256), AF.Abs)
         if t:
-            tt(b("BEST"), b("BEST"), b("BEST0"), OP.add)
-        if t < VI - 1:
-            ts(b("PK", 0, 256, 16), b("RHO"), 16.0, OP.mult)
-            ts(b("PK", 1, 256, 16), b("BEST"), 16.0, OP.mult)
+            for k in range(2):
+                for h in range(2):
+                    mm(b("MA", 16 * k + 8 * h, 16 * k + 8 * h + 8), b(r, 128 * h, 128 * h + 128), b("SEL", 8 * k, 8 * k + 8), f32=True, ext=t - 1)
+            tt(b("PM"), b("MA", 0, 32), b("FR", 32 * t, 32 * t + 32), OP.max)
+            ts(b("PD"), b("PM"), 4, OP.arith_shift_right, 2 ** 18 - 1, OP.bitwise_and)
             for h in range(2):
-                mm(b("MC", 128 * h, 128 * h + 128), b("PK", 128 * h, 128 * h + 128), b("IDF"), f32=True)
-            tt(b("X"), b("MC", 0, 256), Q, OP.add)
-            snd, rcv = "SND%d" % t, "RCV%d" % t
-            op("v", lambda: V.tensor_copy(b(snd)[4].indirect(b("OFFP")[4]), b("X")[4]), [b("X"), b("OFFP")], [b(snd)], 0.05 + 256 * 3 * CY)
+                ts(b("RKS%d" % h, 0, 64, 8), b("PD", 8 * h, 8 * h + 8), 65536.0 * U, OP.mult, -32768.0 * U, OP.add)
+            ts(b("B0C"), b("PD", 16, 32), -c0, OP.add)
+        for h in range(2):
+            mm(b("MA", 32 + 8 * h, 40 + 8 * h), b("DRB", 128 * h, 128 * h + 128), b("BLK"))
+        ts(b("RTL"), b("sj"), CO + 1, OP.add)
+        ts(b("DK"), b("MA", 32, 48), 2.0 ** -16, OP.mult, 8.0, OP.add)
+        tt(b("K0"), b("MA", 32, 48), b("RTL"), OP.add)
+        tg(b("E"), b("DK"), BC16, b("RAMP"), OP.subtract)
+        act(b("A"), b("E"), AF.Abs, scale=65536.0 * U)
+        ts(b("RTL"), b("K0"), U, OP.mult)
+        for h in range(2):
+            tt(b("RKS%d" % h, 1, 64, 8), b("RKS%d" % h, 0, 64, 8), b("RTL", 8 * h, 8 * h + 8), OP.min)
+
+    def push(t, h, p):
+        hs = str(h)
+        n = lambda x, *a: b(x + hs, *a)
+        KP = "KP" + hs
+        kp = b(KP, 0, 128)
+        ch = b("CH", 0, 128 if p == 0 else 4096)
+        off = b("OFF", 8 * h, 8 * h + 8)
+        A = b("A", 128 * h, 128 * h + 128)
+        pt = b("PT", 0, 4096)
+        op("v", lambda: V.tensor_copy(n("PU")[4], ch[4].indirect(off[4])), [ch, off], [n("PU")], FV + 128 * GA * CY)
+        act(n("Pf"), ch, AF.Identity, bias=b("bias", p // 4, p // 4 + 1), scale=1.0 if p == 4 else U, off=off)
+        tg(n("M1"), n("RKS"), BCS[p + 1 if p else 0], A, OP.is_lt)
+        mm(kp, n("Pf"), b("IDF"), True, False, f32=True)
+        mm(kp, b("WI" if p == 4 else "IDB"), n("M1"), False, False)
+        if p in (2, 3):
+            mm(kp, b("IDB"), n("ST"), False, False)
+        nv = share(t, p, h)
+        v0 = 128 - nv if h == 0 else 0
+        s0 = 0 if h == 0 else nv
+        ns = (128 - nv + 31) // 32
+        cut = [s0 + (128 - nv) * k // ns // 2 * 2 for k in range(ns)] + [s0 + 128 - nv]
+        for k in range(ns):
+            lo, hi = cut[k], cut[k + 1]
+            d = b("DIFF", 2048 * h + 16 * lo, 2048 * h + 16 * hi)
+            act(d, pt, AF.Copy, off=n("PU", lo, hi))
+            ps = b("SP%d" % (rot[0] % 4), 0, 16 * (hi - lo))
+            rot[0] += 1
+            mm(ps, b("IDB"), d, True, False)
+            mm(ps, b("NQT", 128 * h, 128 * h + 128), b("R", 16 * lo, 16 * hi), False, True)
+            act(d, ps, AF.Abs)
+        cut = [v0 + nv * k // VP // 2 * 2 for k in range(VP)] + [v0 + nv]
+        for k in range(VP if nv else 0):
+            lo, hi = cut[k], cut[k + 1]
+            d = b("DIFF", 2048 * h + 16 * lo, 2048 * h + 16 * hi)
+            tg(d, pt, n("PU", lo, hi), b("Q16", 2048 * h + 16 * lo, 2048 * h + 16 * hi), OP.subtract)
+            act(d, d, AF.Abs)
+        for i in range(16):
+            mm(b(KP, i, 128, 16), b("DIFF", 2048 * h + i, 2048 * h + 2048, 16), b("BLK" if p == 4 else "BLKU"), False, i == 15)
+        scan(n("KS"), b("MX"), kp, OP.max, OP.min)
+        if p == 4:
+            return
+        tt(n("RKS", p + 2, 64, 8), n("RKS", p + 1, 64, 8), n("KS", 15, 128, 16), OP.min)
+        if p == 0:
+            tg(n("M2"), n("RKS"), BCS[2], A, OP.is_lt)
+        else:
+            tg(n("M2"), n("KS"), BC15, A, OP.is_lt)
+        tt(n("KM"), kp, n("M2"), OP.add)
+        scan(n("MS"), b("MX"), n("KM"), OP.max, OP.min)
+        sk, dk = n("SK", 8 * p, 8 * p + 8), b("DK", 8 * h, 8 * h + 8)
+        if p in (0, 3):
+            ts(sk, n("MS", 15, 128, 16), 0.25, OP.min, 1 / U, OP.mult)
+        else:
+            ts(n("z3"), n("MS", 15, 128, 16), -0.25, OP.add, 1 / U, OP.mult)
+            tt(sk, n("z3"), b("K0", 8 * h, 8 * h + 8) if p == 1 else n("SK", 0, 8), OP.min)
+        ts(n("NN"), sk, 4095, OP.bitwise_and)
+        tg(n("Z"), n("NN"), BC8, b("DM", 0, 128), OP.mult)
+        mm(b(KP, 128, 136), n("Z"), b("LC"), f32=True)
+        cp(off, b(KP, 128, 136))
+        ts(dk, sk, 2.0 ** -16, OP.mult)
+        if p in (1, 2):
+            ts(dk, dk, 255, OP.bitwise_and)
+            ts(n("RB"), n("SK", 8 * p - 8, 8 * p), 0xF000, OP.bitwise_and)
+            tt(n("RP"), sk, n("RB"), OP.min)
+            tg(n("ST"), n("RP"), BC8, b("ROWB"), OP.is_equal)
+        e = b("E", 128 * h, 128 * h + 128)
+        tg(e, dk, BC8, b("RAMP", 0, 128), OP.subtract)
+        act(A, e, AF.Abs, scale=65536.0 * U)
+        if p == 3:
+            ts(n("Tp"), n("RKS", 5, 64, 8), 1 / U, OP.mult, 32768.0, OP.add)
+            ts(n("T3"), n("Tp"), -65536, OP.bitwise_and)
+            ts(n("thr"), n("T3"), 32768.0, OP.add, U, OP.mult)
+            tg(n("m"), n("thr"), BH, n("RKS"), OP.is_gt)
+            tt(n("x"), n("m"), n("RKS"), OP.mult)
+            scan(n("sc"), b("D8"), n("x"), OP.mult, OP.max)
+            ts(n("ki"), n("sc", 7, 64, 8), 1 / U, OP.mult)
+            ts(n("W", 8, 16), n("ki"), 4095, OP.bitwise_and)
+            if t:
+                ts(n("z3"), n("W", 8, 16), 0.0, OP.is_equal)
+                tt(n("z3"), n("z3"), b("B0C", 8 * h, 8 * h + 8), OP.mult)
+            else:
+                ts(n("z3"), n("W", 8, 16), 0.0, OP.is_equal, -c0, OP.mult)
+            tt(n("W", 0, 8), n("z3"), n("W", 8, 16), OP.add)
+
+    def lists(z, ps, out, add=None):
+        mm(ps, z, b("LC"), True, add is None, f32=True)
+        if add is not None:
+            mm(ps, b("IDF"), add, False, True, f32=True)
+        cp(out, ps)
+
+    def finish(t, h):
+        hs = str(h)
+        n = lambda x, *a: b(x + hs, *a)
+        pa, pb, pc, pg = (("KP0", "MA", "MB", "KP0"), ("KP1", "SP0", "SP1", "MB"))[h]
+        pairs = (("MB", "MA"), ("SP2", "SP3", "SP1"))[h]
+        q = b("PT", M + L * t + 128 * h, M + L * t + 128 * h + 128)
+        Rr, best, node = n("RI", 0, 8), n("RI", 8, 16), n("RI", 16, 24)
+        tt(n("V4"), n("KS", 15, 128, 16), n("T3"), OP.min)
+        if t < VI - 1:
+            tt(n("far"), n("V4"), b("THK"), OP.is_ge)
+            mm(b(pa, 136, 144), b("LTD" + hs), n("far"), True, h == 0)
+            if h:
+                mm(b(pa, 136, 144), b("ONES", 0, 128), b("far0"), False, True)
+            act(n("dest"), b(pa, 136, 144), AF.Identity, bias=b("bias", 2 + h, 3 + h))
+            tg(n("ZD"), n("dest"), BC8, b("DM", 0, 128), OP.mult)
+            lists(n("ZD"), b(pa, 144, 152), n("OP"))
+        ts(Rr, n("V4"), 16, OP.arith_shift_right)
+        op("v", lambda: V.tensor_scalar(n("n4")[4], n("V4")[4].indirect(DUP[4]), 4095, None, OP.bitwise_and),
+           [n("V4"), DUP], [n("n4")], FV + 16 * GA * CY)
+        ts(n("z"), n("n4"), 0.0, OP.is_equal)
+        tt(n("z"), n("z"), n("W"), OP.mult)
+        tt(n("RI", 8, 24), n("z"), n("n4"), OP.add)
+        ob = b("OB%d" % t, 128 * h, 128 * h + 128, 1, 32 if t < VI - 1 else 16)
+        if t == VI - 1:
+            cp(n("OUT", 0, 16), n("RI", 0, 16))
+            mm(b(pb, 0, 128, 1, 16), n("OUT", 0, 16), b("IDF"), f32=True)
+            act(ob, b(pb, 0, 128, 1, 16), AF.Identity, bias=b("bias", 4, 5, 1, 16))
+            for k, (qn, out) in enumerate((("y", T.yr), ("s" if h else "y", T.yb))):
+                o = b(ob[0], ob[1], ob[2], 1, 8, 8 * k)
+                dma(qn, out[:, t * L + 128 * h:t * L + 128 * h + 128], o[4], [o], [], 2.0)
+            return
+        ts(n("PK", 0, 128, 16), Rr, 16.0, OP.mult, FLAG, OP.add)
+        ts(n("PK", 1, 128, 16), best, 16.0, OP.mult, FLAG + 16 * c0, OP.add)
+        mm(b(pb, 0, 128), n("PK"), b("IDF"), True, False, f32=True)
+        mm(b(pb, 0, 128), b("IDB"), q, False, True)
+        act(n("XS"), b(pb, 0, 128), AF.Copy)
+        snd, rcv = "SND%d" % t, "RCV%d" % t
+        op("v", lambda: V.tensor_copy(b(snd)[4].indirect(n("OP")[4]), n("XS")[4]), [n("XS"), n("OP")], [b(snd)], FV + 128 * SCA * CY)
+        if h:
             dst = T.cores[(rank + 1) % N]
             rid, pid, _x = topo.addr(dst)
             op("g", lambda: g.remote_dma(T[rcv][:, 0:CAP], T[snd][:, 0:CAP], T.sem["arr%d" % t], T.sem["sent%d" % t], pid, rid, topo.mask(core, dst)),
                [b(snd, 0, CAP)], [], 0.1, "r", t)
-        out_rows("RHO", "or%d" % t, "LI1", T.yr, t)
-        out_rows("BEST", "ob%d" % t, "KP1", T.yb, t)
-        if t == VI - 1:
-            return
-        cp(b("PN"), b("PJ"))
-        ts(b("hi6"), b("PJ"), 4032, OP.bitwise_and)
-        ts(b("lo6"), b("PJ"), 63, OP.bitwise_and)
-        cp(b("NQ", 0, 16), b("hi6"))
-        cp(b("NQ", 16, 32), b("lo6"))
-        mm(b("KP1", 0, 128, 1, 32), b("NQ"), b("IDB"))
-        act(b("NQT", 0, 128, 1, 32), b("KP1", 0, 128, 1, 32), AF.Copy)
-        wide(lambda o: cp(o, b("PJ")), "GO1")
-        act(b("GC"), ind(b("CH"), b("GO1")), AF.Copy, extra=[b("GO1")], cost=0.065 + 256 * 1.5 * CY)
-        act(b("RHT"), b("MC", 0, 256), AF.Copy)
-        for h in range(2):
-            mm(b("LI0", 128 * h, 128 * h + 128), b("BC0"), b("RHT", 128 * h, 128 * h + 128))
-        act(b("M1"), b("LI0", 0, 256), AF.Abs, bias=b("biasr", 0, 1))
-        act(b("M1"), b("M1"), AF.Sign, scale=-1.0, bias=8.0)
-        act(b("OHG"), b("M1"), AF.Relu)
-        tt(b("OC"), b("OHG"), b("GC"), OP.mult)
-        for h in range(2):
-            mm(b("LI1", 8 * h, 8 * h + 8), b("OC", 128 * h, 128 * h + 128), b("LC"), f32=True)
-        ts(b("emp"), b("LI1", 0, 16), 0.0, OP.is_equal)
-        tt(b("can"), b("ad"), b("FARB"), OP.mult)
-        tt(b("can"), b("can"), b("emp"), OP.mult)
-        cp(b("CANB"), b("can"))
+        cp(n("OUT", 0, 24), n("RI"))
+        tt(n("gq"), node, b("K4096", 8 * h, 8 * h + 8), OP.subtract)
+        tg(n("Z1"), n("gq"), BC8, b("DM", 0, 128), OP.mult)
+        kl = b("KL", 8 * h, 8 * h + 8)
+        lists(n("Z1"), b(pg, 152, 160), n("G1"), kl)
+        act(n("GC"), b("CH", 0, 4096), AF.Copy, off=n("G1"))
+        ts(n("NI", 0, 8), node, 4032, OP.bitwise_and)
+        ts(n("NI", 8, 16), node, 63, OP.bitwise_and)
+        cp(n("NQ"), n("NI"))
+        mm(b(pc, 0, 128, 1, 16), n("NQ"), b("IDB"))
+        nt = b("NT" + hs, 0, 128, 1, 16)
+        act(nt, b(pc, 0, 128, 1, 16), AF.Copy)
+        ts(n("bb"), Rr, 0.0625, OP.mult, -0.96875, OP.add)
+        tg(n("OH"), n("bb"), BC8, b("j15"), OP.is_equal)
+        mm(b(pb, 128, 256), n("OH"), b("DGB", 128 * (2 * t + h), 128 * (2 * t + h) + 128), True, False)
+        mm(b(pb, 128, 256), n("OH"), b("DGL"), False, True)
+        act(n("ON"), b(pb, 128, 256), AF.Copy)
+        tt(n("pre"), node, n("far"), OP.min)
+        w = 128 * (h + 1)
         for gg in range(8):
-            ps, eq = ("MA", "KP0")[gg % 2], "EQ%d" % gg
-            rw = [b("SELH", 128 * (8 * h + gg), 128 * (8 * h + gg) + 128, 1, 32) for h in range(2)]
-            nt = b("NQT", 0, 128, 1, 32)
-            mm(b(ps, 0, 128), rw[0], nt, True, False)
-            mm(b(ps, 0, 128), b("IDB"), b("TRI"), False, True)
-            mm(b(ps, 128, 256), rw[1], nt)
-            mm(b(ps, 256, 384), rw[1], nt, True, False)
-            mm(b(ps, 256, 384), b("IDB"), b("TRI"), False, True)
-            for lo, hi, cc in ((0, 256, gg), (256, 384, 8 + gg)):
-                if gg in GSC:
-                    act(b("EF", lo, hi), b(ps, lo, hi), AF.Abs, scale=-1.0, bias=b("PN", cc, cc + 1))
-                    act(b(eq, lo, hi), b("EF", lo, hi), AF.Relu, scale=-1.0, bias=1.0)
+            ps = pairs[gg % len(pairs)]
+            sel = b("SELG", 128 * gg, 128 * gg + 128, 1, 16)
+            if h:
+                mm(b(ps, 256, 384), sel, nt)
+            mm(b(ps, 256 + w - 128, 256 + w), sel, nt, True, False)
+            mm(b(ps, 256 + w - 128, 256 + w), b("IDB"), b("TRI"), False, True)
+            for k in range(h + 1):
+                x, cc = b(ps, 256 + 128 * k, 384 + 128 * k), b("OUT%d" % k, 16 + gg, 17 + gg)
+                if gg in GSC[h]:
+                    act(b("EF", 128 * k, 128 * k + 128), x, AF.Abs, scale=-1.0, bias=cc)
                 else:
-                    ts(b(eq, lo, hi), b(ps, lo, hi), b("PN", cc, cc + 1), OP.is_equal)
+                    ts(n("EQ", 256 * gg + 128 * k, 256 * gg + 128 * k + 128), x, cc, OP.is_equal)
+            if gg in GSC[h]:
+                act(n("EQ", 256 * gg, 256 * gg + w), b("EF", 0, w), AF.Relu, scale=-1.0, bias=1.0)
+        tt(n("OC"), b(pb, 128, 256), n("GC"), OP.mult)
+        mm(b(pg, 160, 168), n("OC"), b("LCB"))
+        tt(n("can"), n("pre"), b(pg, 160, 168), OP.is_gt)
         for gg in range(8):
-            eq = "EQ%d" % gg
-            mm(b("MC", gg, gg + 1), b(eq, 0, 128), b("CANB", gg, gg + 1))
-            mm(b("MC", 8 + gg, 9 + gg), b(eq, 128, 256), b("CANB", gg, gg + 1), True, False)
-            mm(b("MC", 8 + gg, 9 + gg), b(eq, 256, 384), b("CANB", 8 + gg, 9 + gg), False, True)
-        ts(b("win"), b("MC", 0, 16), 0.0, OP.is_equal)
-        tt(b("win"), b("win"), b("can"), OP.mult)
-        tt(b("YP"), b("win"), b("PN"), OP.mult)
-        tt(b("gq"), b("PN"), b("K4096"), OP.subtract)
-        tt(b("gq"), b("gq"), b("win"), OP.mult)
-        wide(lambda o: tt(o, b("gq"), b("K4096"), OP.add), "GO2")
-        tt(b("VAL"), b("OHG"), b("NID%d" % t), OP.mult)
-        tt(b("VAL"), b("VAL"), b("GC"), OP.add)
-        op("v", lambda: V.tensor_copy(b("CH")[4].indirect(b("GO2")[4]), b("VAL")[4]), [b("VAL"), b("GO2")], [b("CH")], 0.05 + 256 * 3 * CY)
-        if t == 1:
-            cp(b("PT", M + L, M + 2 * L), Q)
-        out_rows("YP", "op%d" % t, "MB", T.yp, t)
-
-    def receive(t):
-        r = b("RCV%d" % (t - 1))
-        ts(b("RV"), r, 0.0, OP.is_lt, ext=t - 1)
-        ts(b("RI"), r, 15, OP.bitwise_and, ext=t - 1)
-        tt(b("RT"), b("RV"), b("QF", L * t, L * t + L), OP.mult)
-        tt(b("QV%d" % t), b("RT"), b("RI"), OP.add)
-        ts(b("RS"), r, 4, OP.arith_shift_right, ext=t - 1)
-        cp(b("RF"), b("RS"))
-
-    def late_constants():
-        cp(b("D0", 128, 256), b("D0", 0, 128))
-        cp(b("DM", 128, 256), b("DM", 0, 128))
-        ts(b("LTRI"), b("jf"), P, OP.is_gt)
-        ts(b("TRI"), b("jf"), P, OP.is_le, 8192.0, OP.mult)
-        fill(b("ONESB"), 1.0)
-        fill(b("ONESF"), 1.0)
-        ts(b("pf", 3, 4), P15, 0.0, OP.is_equal)
-        ts(b("BLK0"), b("LC"), b("pf", 3, 4), OP.mult)
-        ts(b("biasr", 1, 2), P15, 1.0, OP.is_equal)
-        ts(b("SELR", 0, 8), b("LC"), b("pf", 3, 4), OP.mult)
-        ts(b("SELR", 8, 16), b("LC"), b("biasr", 1, 2), OP.mult)
-        ts(b("biasr", 0, 1), P15, -16.0, OP.mult, -7.5, OP.add)
-        cp(b("thf", 0, 1), b("thi", 0, 1))
-        ts(b("THM"), b("ONESF"), b("thf", 0, 1), OP.mult)
-        mm(b("MC", 64, 72), b("THM"), b("BLK0"))
-        cp(b("TH", 0, 8), b("MC", 64, 72))
-        cp(b("TH", 8, 16), b("MC", 64, 72))
-        iota(b("KI"), [[128, 2], [0, 8]], 0, 1, True)
-        ts(b("K192"), b("KI"), float(CAP), OP.add)
-        ts(b("K4096"), b("KI"), 4096.0, OP.add)
-        iota(b("NID0"), [[1, 256]], M, 0, True)
-        iota(b("NID1"), [[1, 256]], M + L, 0, True)
-        iota(b("selj"), [[1, 16], [0, 128]], 0, 0, True)
-        ts(b("SELH"), b("selj"), P15, OP.is_equal)
-        ts(b("j15i"), b("ji"), 4, OP.arith_shift_right)
-        cp(b("M1", 0, 128), b("j15i"))
-        ts(b("M1", 0, 128), b("M1", 0, 128), P4, OP.is_equal, 0.0625, OP.mult)
-        ts(b("BC0"), b("M1", 0, 128), b("pf", 3, 4), OP.mult)
-        for x in ("LBD", "LBD2", "PK"):
-            fill(b(x), 0.0)
-        for x in "01":
-            fill(b("SND" + x), -16)
-            fill(b("RCV" + x, CAP, L), -16)
+            for k in range(h + 1):
+                mm(b(pg, 168 + gg, 169 + gg), n("EQ", 256 * gg + 128 * k, 256 * gg + 128 * k + 128), b("can%d" % k, gg, gg + 1), k == 0, k == h)
+        tt(n("win"), n("can"), b(pg, 168, 176), OP.is_gt)
+        tg(n("Z2"), n("win"), BC8, n("Z1"), OP.mult)
+        lists(n("Z2"), b(pg, 176, 184), n("G2"), kl)
+        op("v", lambda: V.tensor_tensor(b("CH")[4].indirect(n("G2")[4]), n("GC")[4], n("ON")[4], OP.add),
+           [n("GC"), n("ON"), n("G2")], [b("CH")], FV + 128 * SCA * CY)
+        tt(n("OUT", 24, 32), n("win"), node, OP.mult)
+        mm(b(pb, 0, 128, 1, 32), n("OUT"), b("IDF"), f32=True)
+        act(ob, b(pb, 0, 128, 1, 32), AF.Identity, bias=b("bias", 4, 5, 1, 32))
+        if h:
+            for k, out in ((0, T.yr), (1, T.yb), (3, T.yp)):
+                o = b(ob[0], 0, L, 1, 8, 8 * k)
+                dma("y", out[:, t * L:(t + 1) * L], o[4], [o], [], 2.0)
 
     for t in range(VI):
-        Q = b("QF", 0, L) if t == 0 else b("QV%d" % t)
-        Q16 = ("Q16a", "Q16b", "Q16a")[t]
-        if t:
-            receive(t)
-        for h in range(2):
-            begin(t, h, Q, Q16)
+        tag[0] = "b%d" % t
+        begin(t)
         if t == 0:
             late_constants()
-        for s in range(5):
+        for p in range(5):
             for h in range(2):
-                push(t, h, s, Q16)
-        finish(t, Q)
+                tag[0] = "%d%d%s" % (t, p, "AB"[h])
+                push(t, h, p)
+        for h in range(2):
+            tag[0] = "f%d%s" % (t, "AB"[h])
+            finish(t, h)
 
     n = len(ops)
-    WAKE = 0.06
+    WAKE, LOOK = 0.08, 0.1
     lat = [o["cost"] + (o["ext"] if o["kind"] == "d" else 0) for o in ops]
     succ = [[] for _ in range(n)]
     cnt = [0] * n
@@ -532,7 +561,7 @@ def rank_program(g, core, T, topo):
         dd = set(o["deps"])
         if o["kind"] == "c" and o["ext"] is not None:
             x = [j for j in range(n) if ops[j]["kind"] == "r" and ops[j]["ext"] == o["ext"]][0]
-            lat[x] = 4.0
+            lat[x] = 3.0
             dd.add(x)
         for d in dd:
             succ[d].append((i, WAKE))
@@ -551,13 +580,14 @@ def rank_program(g, core, T, topo):
             byq.setdefault(ops[i]["q"], []).append(i)
     while len(order) < n:
         t0, qn = min((max(free.get(x, 0.0), min(rt[i] for i in lst)), x) for x, lst in byq.items() if lst)
-        i = max((i for i in byq[qn] if rt[i] <= t0), key=lambda i: pri[i])
+        i = max((i for i in byq[qn] if rt[i] <= t0 + LOOK), key=lambda i: pri[i])
+        t0 = max(t0, rt[i])
         byq[qn].remove(i)
         order.append(i)
+        ops[i]["t0"] = t0
         free[qn] = t0 + ops[i]["cost"]
         for j, x in succ[i]:
-            if x is not None:
-                rt[j] = max(rt[j], t0 + lat[i] + x)
+            rt[j] = max(rt[j], t0 + lat[i] + x) if x is not None else max(rt[j], t0)
             cnt[j] -= 1
             if cnt[j] == 0:
                 byq.setdefault(ops[j]["q"], []).append(j)
@@ -605,4 +635,4 @@ def rank_program(g, core, T, topo):
     for t in range(VI - 1):
         g.wait_ge(T.sem["sent%d" % t], nout)
         g.wait_ge(T.sem["arr%d" % t], nin)
-    return max(free.values())
+    return ops, order

@@ -7,11 +7,19 @@ CO = 7.5 * 65536
 FLAG = float(2 ** 22)
 ROOM = 4096 + 256
 SNDW = 1280
-NV = ((70, 70), (70, 70), (70, 70), (70, 70), (80, 40))
-NVL = (88, 72)
+NV = ((64, 64), (64, 56), (56, 56), (56, 64), (64, 64))
+NVL = (72, 80)
 VP = 2
-QV = 10
-GSC = ((3, 6), (1, 3, 5, 7))
+QV = 8
+GSC = (4, 4)
+HALF, GAP, LOOK, EARLY = 4.72, 16.5, 0.04, 2.91
+WHEN = {'vPU0': -0.27, 'vvec0': 2.31, 'vvec1': 2.19, 'vM0': 2.4, 'vKS0': 4.94, 'vRKS0': 7.07, 'vM1': 3.4, 'vKM0': 8.1, 'vMS0': 7.01, 'vz0': 4.01, 'vSK0': 5.02, 'vNN0': 7.8, 'vZ0': 6.59, 'vDK0': 9.61, 'vE0': 10.37, 'vOFF0': 7.6, 'vRB0': 6.34, 'vRP0': 9.9, 'vST0': 5.59, 'vFB0': 10.57, 'sget0': -0.35, 'sget1': 1.68, 'sget2': -2.14, 'sPf0': 1.46, 'svec0': 3.84, 'sabs0': 4.05, 'sabs1': 3.38, 'svec1': 3.46, 'sabs2': 4.42, 'sA0': 10.9, 'tget0': 5.72, 'tabs0': 2.5, 'tget1': 1.97, 'tabs1': 4.48, 'tget2': 2.49, 'tabs2': 2.74, 'tPf': 4.06, 'tkey': 4.19, 'tlist': 4.56}
+WHEN0 = {"vPU0": 0.0, "vvec0": 0.25, "vvec1": 1.6, "vvec2": 2.0, "vvec3": 2.3, "vM0": 1.2, "vKS0": 5.9, "vRKS0": 6.1, "vM1": 6.2, "vKM0": 6.9, "vMS0": 7.2,
+        "vz0": 7.4, "vSK0": 7.5, "vNN0": 7.7, "vZ0": 7.9, "vDK0": 8.1, "vE0": 8.3, "vOFF0": 8.6, "vRB0": 7.3, "vRP0": 8.4, "vST0": 10.0,
+        "vFB0": 10.0, "sget0": 0.3, "sget1": 0.9, "sget2": 1.5, "sget3": 2.0, "sPf0": 2.0, "svec0": 2.2, "sabs0": 2.6, "sabs1": 3.0,
+        "svec1": 3.3, "svec2": 3.5, "svec3": 3.6, "sabs2": 3.8, "sabs3": 4.0, "sA0": 8.8,
+        "tget0": 1.4, "tabs0": 1.6, "tget1": 1.9, "tabs1": 2.1, "tget2": 2.4, "tabs2": 2.6, "tget3": 2.9, "tabs3": 3.0,
+        "tPf": 3.5, "tkey": 4.4, "tlist": 3.0}
 
 SCRATCH = {}
 PS = set()
@@ -35,35 +43,36 @@ for _n in ("KP0", "KP1", "MA", "MB", "SP0", "SP1", "SP2", "SP3"):
     VIRT[_n] = (_n, 0, 512)
     PS.add(_n)
 _own("PT", M + VI * L, "bfloat16"); _own("CHI", M, "int32"); _own("CH", ROOM)
-_own("wi", 8, "int32"); _own("thi", 8, "int32"); _own("r0i", 768, "int32")
+_own("wi", 8, "int32"); _own("thi", 8, "int32"); _own("r0i", 128, "int32")
 _own("Q16", 4096, "bfloat16"); _own("DIFF", 4096, "bfloat16")
 for _t in "01":
     _own("SND" + _t, SNDW); _own("RCV" + _t, L)
 for _t in "012":
     _own("OB" + _t, 256)
-for _n, _c in (("r0f", 768), ("wf", 2), ("thf", 2), ("pf", 8), ("jf", 128), ("j15", 128), ("c8", 8), ("IDF", 128), ("DM", 256),
-               ("LC", 8), ("RAMP", 256), ("MX", 128), ("ROWB", 128), ("D8", 64), ("bias", 8), ("THK", 8), ("K4096", 16), ("KL", 16),
-               ("SEL", 16), ("FR", 96), ("E", 256), ("A", 256), ("K0", 16), ("RTL", 16), ("B0C", 16), ("EF", 256), ("tmp", 128)):
+for _n, _c in (("r0f", 128), ("wf", 2), ("thf", 2), ("pf", 8), ("j15", 256), ("c8", 8), ("IDF", 128), ("DM", 256),
+               ("LC", 8), ("RAMP", 256), ("MX", 128), ("ROWB", 128), ("bias", 8), ("THK", 8), ("K4096", 16),
+               ("SEL", 16), ("FR", 96), ("E", 256), ("A", 256), ("K0", 16), ("K0U", 16), ("D0", 16), ("WL", 2), ("B0C", 32), ("EF", 1024)):
     _s(_n, _c)
-for _n, _c in (("pi", 8), ("ji", 128), ("j15i", 128), ("li", 96), ("si", 16), ("sj", 16), ("DK", 16), ("MI", 192), ("QI", 192),
-               ("PM", 32), ("PD", 32)):
+for _n, _c in (("pi", 8), ("li", 96), ("si", 16), ("sj", 16), ("DK", 16), ("MI", 192), ("QI", 192), ("PM", 32), ("PD", 32)):
     _s(_n, _c, "int32")
-for _n, _c in [("IDB", 128), ("NIDB", 128), ("WI", 128), ("BLKU", 8), ("BLK", 8), ("BLK0", 8), ("LCB", 8), ("WB", 8), ("TRI", 128),
-               ("LTD0", 128), ("LTD1", 128), ("ONES", 2048), ("R", 2048), ("THM", 128), ("selj", 1024), ("SELG", 1024), ("ZR", 256),
-               ("DRB", 256), ("NQT", 256), ("DGL", 128), ("DGB", 128 * 4)]:
+for _n, _c in [("IDB", 128), ("NIDB", 128), ("WI", 128), ("BLKU", 8), ("BLK", 8), ("LCB", 8), ("LC2", 8), ("WB", 8), ("WD", 128), ("RT", 16),
+               ("LTD0", 128), ("LTD1", 128), ("ONES", 2048), ("R", 2048), ("TB", 8), ("SELG", 1024), ("ZR", 256), ("D8", 64),
+               ("DRB", 256), ("NQT", 256), ("DGL", 128), ("DGB", 128 * 4), ("NONE", 128), ("KC", 16), ("CG", 128),
+               ("CL0", ROOM), ("CL1", ROOM)]:
     _s(_n, _c, "bfloat16")
 _s("LI", 96, "uint16"); _s("OFF", 16, "uint16")
 for _h in "01":
     for _n, _c, _d in (("PU", 128, "uint16"), ("Pf", 128, "float32"), ("M1", 128, "bfloat16"), ("M2", 128, "bfloat16"),
-                       ("ST", 128, "bfloat16"), ("KS", 128, "float32"), ("KM", 128, "float32"), ("MS", 128, "float32"), ("SK", 32, "int32"), ("NN", 8, "int32"),
+                       ("ST", 128, "bfloat16"), ("KS", 128, "float32"), ("KM", 128, "float32"), ("MS", 128, "float32"),
+                       ("SK", 32, "int32"), ("NN", 8, "int32"), ("FB", 8, "int32"),
                        ("Z", 128, "float32"), ("RB", 8, "int32"), ("RP", 8, "int32"), ("RKS", 64, "float32"),
                        ("Tp", 8, "int32"), ("T3", 8, "int32"), ("thr", 8, "float32"), ("m", 64, "float32"), ("x", 64, "float32"),
                        ("sc", 64, "float32"), ("ki", 8, "int32"), ("W", 16, "int32"), ("z3", 8, "float32"), ("V4", 8, "int32"),
-                       ("n4", 16, "int32"), ("z", 16, "float32"), ("RI", 24, "int32"), ("OUT", 32, "float32"), ("far", 8, "bfloat16"),
-                       ("dest", 8, "float32"), ("ZD", 128, "float32"), ("OP", 8, "uint16"), ("PK", 128, "float32"), ("XS", 128, "float32"),
-                       ("pre", 8, "float32"), ("gq", 8, "float32"), ("Z1", 128, "float32"), ("G1", 8, "uint16"), ("GC", 128, "float32"),
+                       ("n4", 16, "int32"), ("z", 16, "float32"), ("RI", 24, "int32"), ("OUT", 32, "float32"), ("near", 8, "bfloat16"),
+                       ("DG", 16, "float32"), ("ZZ", 256, "float32"), ("OG", 16, "uint16"), ("PK", 128, "float32"), ("XS", 128, "float32"),
+                       ("GC", 128, "float32"),
                        ("bb", 8, "int32"), ("OH", 128, "bfloat16"), ("ON", 128, "float32"), ("OC", 128, "bfloat16"), ("can", 8, "bfloat16"),
-                       ("win", 8, "float32"), ("Z2", 128, "float32"), ("G2", 8, "uint16"), ("NI", 16, "int32"), ("NQ", 16, "bfloat16"),
+                       ("win", 8, "float32"), ("Z2", 128, "float32"), ("G2", 8, "uint16"), ("NQ", 16, "bfloat16"),
                        ("NT", 128, "bfloat16"), ("EQ", 2048, "bfloat16")):
         _s(_n + _h, _c, _d)
 for _d in POOL:
@@ -82,6 +91,7 @@ def rank_program(g, core, T, topo):
     ndma = [0]
     rot = [0]
     tag = [""]
+    slot = [None, {}, ""]
     c0 = 4096.0 * rank
 
     def b(name, lo=0, hi=None, st=1, rows=None, row0=0):
@@ -119,6 +129,13 @@ def rank_program(g, core, T, topo):
                 del h[:40]
         d = {"q": q, "call": call, "deps": deps, "after": after - deps, "cost": cost, "kind": kind, "ext": ext,
              "tag": tag[0] + " " + (writes[0][0] if writes else "")}
+        d["slot"] = slot[0]
+        if slot[0] is not None:
+            lab = q + writes[0][0].rstrip("0123")
+            slot[1][lab] = slot[1].get(lab, -1) + 1
+            d["lab"] = lab + str(slot[1][lab])
+            if lab in ("tKP", "tSP", "sDIFF", "vDIFF"):
+                d["lab"] = q + slot[2]
         if kind == "d":
             d["sem"] = "d%d" % ndma[0]
             ndma[0] += 1
@@ -169,8 +186,8 @@ def rank_program(g, core, T, topo):
         op("v", lambda: V.memset(out[4], x), [], [out], vc(cols(out), half(out)))
 
     def act(out, a, f, bias=None, scale=1.0, off=None):
-        kw = {"scale": scale}
-        rd = [a] if off is None else [a, off]
+        kw = {"scale": scale[4] if isap(scale) else scale}
+        rd = ([a] if off is None else [a, off]) + ([scale] if isap(scale) else [])
         if bias is not None:
             kw["bias"] = bias[4] if isap(bias) else bias
             if isap(bias):
@@ -186,9 +203,15 @@ def rank_program(g, core, T, topo):
         eng = g.sync if q == "y" else g.scalar
         op(q, lambda: eng.dma_start(out, src), reads, writes, 0.06, "d", us)
 
-    def iota(out, pat, base, cm):
+    def iota(out, pat, base, cm=0):
         kw = {} if VIRT[out[0]][0] == "pooli" else {"allow_small_or_imprecise_dtypes": True}
         op("g", lambda: g.iota(out[4], pat, base, cm, **kw), [], [out], 0.13 + 2 * cols(out) * CY)
+
+    def const(out, x):
+        iota(out, [[0, cols(out)]], int(x))
+
+    def keep(out, a, pat, o, other, base=0, cm=1):
+        op("g", lambda: g.affine_select(out[4], a[4], pat, o, other, base, cm), [a], [out], 0.17 + 2 * cols(out) * CY)
 
     def load(q, name, lo, hi, src, us, rows=None):
         o = b(name, lo, hi, 1, rows)
@@ -198,105 +221,108 @@ def rank_program(g, core, T, topo):
     load("s", "wi", 0, 1, T.w[:], 2.0)
     load("y", "PT", 0, M, T.pt[:], 4.5)
     load("s", "CHI", 0, 128, T.ch[:, 0:128], 2.2)
-    load("s", "r0i", 0, 768, T.r0[:], 2.2, 8)
+    load("s", "r0i", 0, 128, T.r0[:], 2.2, 48)
     CHP = (128, 1280, 2432, M)
     for k in range(3):
         load("y", "CHI", CHP[k], CHP[k + 1], T.ch[:, CHP[k]:CHP[k + 1]], 6.0 + 1.5 * k)
     load("s", "thi", 0, 1, T.th[:], 2.5)
 
+    DIAG = [[-1, 128]]
+    fill(b("ONES"), 1.0)
     iota(b("pi", 0, 1), [[0, 1]], 0, 1)
-    iota(b("ji"), [[1, 128]], 0, 0)
-    iota(b("c8"), [[1, 8]], 0, 0)
-    iota(b("li", 0, 16), [[1, 16]], 0, 0)
-    iota(b("li", 16, 24), [[16, 8]], 15, 0)
-    iota(b("li", 24, 72), [[1, 6], [8, 8]], 0, 0)
-    iota(b("li", 72, 76), [[2, 4]], 0, 0)
-    iota(b("RAMP"), [[0, 16], [16, 16]], 0, 0)
+    iota(b("c8"), [[1, 8]], 0)
+    iota(b("li", 0, 16), [[1, 16]], 0)
+    iota(b("j15"), [[0, 16], [1, 16]], 0)
+    keep(b("IDB"), b("ONES", 0, 128), DIAG, OP.is_equal, 0.0)
+    iota(b("li", 16, 24), [[16, 8]], 15)
+    iota(b("li", 24, 72), [[1, 6], [8, 8]], 0)
+    iota(b("li", 72, 76), [[2, 4]], 0)
+    keep(b("R"), b("ONES"), [[-1, 128], [0, 16]], OP.is_equal, 0.0)
     ts(b("pi", 1, 2), b("pi", 0, 1), 15, OP.bitwise_and)
     ts(b("pi", 2, 3), b("pi", 0, 1), 4, OP.arith_shift_right)
     ts(b("pi", 3, 4), b("pi", 0, 1), 3, OP.arith_shift_right, 1, OP.bitwise_and)
-    ts(b("pi", 4, 5), b("pi", 0, 1), 7, OP.bitwise_and)
-    cp(b("pf", 0, 5), b("pi", 0, 5))
-    P, P15, P4, P3, P7 = [b("pf", k, k + 1) for k in range(5)]
-    cp(b("LI", 0, 72), b("li", 0, 72))
-    ts(b("LI", 72, 76), b("li", 72, 76), P3, OP.add)
-    cp(b("LI", 76, 77), b("pi", 4, 5))
+    cp(b("pf", 0, 4), b("pi", 0, 4))
+    P15, P4, P3 = [b("pf", k, k + 1) for k in range(1, 4)]
+    cp(b("LI", 0, 16), b("li", 0, 16))
+    cp(b("LI", 16, 72), b("li", 16, 72))
     BC16, BC8, BC15, BH, DUP = b("LI", 0, 16), b("LI", 0, 8), b("LI", 16, 24), b("LI", 72, 76), b("LI", 76, 77)
     BCS = [b("LI", 24 + 8 * s, 32 + 8 * s) for s in range(6)]
-    cp(b("jf"), b("ji"))
-    ts(b("j15i"), b("ji"), 15, OP.bitwise_and)
-    cp(b("j15"), b("j15i"))
     ts(b("LC"), b("c8"), P4, OP.is_equal)
-    ts(b("LCB"), b("c8"), P4, OP.is_equal)
-    ts(b("BLK"), b("LC"), 65536.0, OP.mult)
     cp(b("wf", 0, 1), b("wi", 0, 1))
     ts(b("WB"), b("LC"), b("wf", 0, 1), OP.mult)
-    ts(b("DM", 0, 128), b("j15"), P15, OP.is_equal)
-    ts(b("DM", 128, 256), b("j15"), P15, OP.is_equal)
-    ts(b("IDF"), b("jf"), P, OP.is_equal)
-    ts(b("IDB"), b("jf"), P, OP.is_equal)
-    ts(b("NIDB"), b("IDB"), -1.0, OP.mult)
-    ts(b("WI"), b("IDB"), 2.0 ** 26, OP.mult)
-    ts(b("RAMP"), b("RAMP"), 15.5, OP.add)
-    ts(b("MX"), b("j15"), 0.0, OP.is_gt, -2 * BIG, OP.mult)
-    ts(b("MX"), b("MX"), BIG, OP.add)
-    ts(b("BLKU"), b("LC"), 65536.0 * U, OP.mult)
-    ts(b("bias", 0, 1), P15, 4096.0 * U, OP.mult, CO * U, OP.add)
-    ts(b("bias", 1, 2), P15, 4096.0, OP.mult, CO + 32768, OP.add)
-    fill(b("ONES"), 1.0)
-    op("g", lambda: g.affine_select(b("R")[4], b("ONES")[4], [[-1, 128], [0, 16]], OP.is_equal, 0.0, 0, 1),
-       [b("ONES")], [b("R")], 0.17 + 2 * 2048 * CY)
-    fill(b("FR"), 0.0)
-    cp(b("r0f", rows=8), b("r0i", rows=8))
-    for k in range(2 * VI):
-        mm(b("MB", 8 * k, 8 * k + 8), b("r0f", 128 * k, 128 * k + 128, rows=8), b("IDF", 0, 8, rows=8), f32=True)
+    ts(b("DM"), b("j15"), P15, OP.is_equal)
+    for name, x in (("LCB", 1.0), ("BLK", 65536.0), ("BLKU", 65536.0 * U), ("LC2", 2.0)):
+        act(b(name), b("LC"), AF.Copy, scale=x)
+    act(b("NIDB"), b("IDB"), AF.Copy, scale=-1.0)
+    act(b("IDF"), b("IDB"), AF.Copy)
+    act(b("RAMP"), b("j15"), AF.Copy, scale=16.0)
+    fill(b("MX"), -BIG)
+    fill(b("MX", 0, 128, 16), BIG)
+    act(b("bias", 0, 1), P15, AF.Identity, scale=4096.0 * U, bias=CO * U)
+    act(b("bias", 1, 2), P15, AF.Identity, scale=4096.0, bias=CO + 32768)
+    cp(b("r0f", rows=48), b("r0i", rows=48))
+    mm(b("MB", 0, 48), b("r0f", rows=48), b("IDF", 0, 48, rows=48), f32=True)
+    const(b("FR"), 0)
     for h in range(2):
         fill(b("RKS%d" % h), 0.0)
-        ts(b("RKS%d" % h, 0, 64, 8), b("MB", 8 * h, 8 * h + 8), 65536.0 * U, OP.mult, CO * U, OP.add)
-    for t in (1, 2):
-        ts(b("FR", 32 * t, 32 * t + 16), b("MB", 16 * t, 16 * t + 16), 16.0, OP.mult, 128.0, OP.add)
+        act(b("RKS%d" % h, 0, 64, 8), b("MB", h, 48, 6), AF.Identity, scale=65536.0 * U, bias=CO * U)
+    for k in range(2, 6):
+        act(b("FR", 16 * k, 16 * k + 8), b("MB", k, 48, 6), AF.Identity, scale=16.0, bias=128.0)
     cp(b("CH", 0, 128), b("CHI", 0, 128))
     fill(b("PT", 0, 1), 2048.0)
 
     def late_constants():
         for k in range(3):
             cp(b("CH", CHP[k], CHP[k + 1]), b("CHI", CHP[k], CHP[k + 1]))
-        fill(b("CH", M, ROOM), 0.0)
-        ts(b("j15i"), b("ji"), 8, OP.add)
-        ts(b("j15i"), b("j15i"), 15, OP.bitwise_and)
-        ts(b("ROWB"), b("j15i"), 4096.0, OP.mult)
-        ts(b("li", 0, 64), b("ji", 0, 64), 7, OP.bitwise_and)
-        ts(b("D8"), b("li", 0, 64), 0.0, OP.is_gt)
-        ts(b("TRI"), b("jf"), P, OP.is_le, 8192.0, OP.mult)
-        ts(b("bias", 2, 3), P, 2.0, OP.mult, 256.0, OP.add)
-        ts(b("bias", 3, 4), P, 4.0, OP.mult, 512.0, OP.add)
-        ts(b("tmp"), b("jf"), P, OP.is_gt)
+        const(b("CH", M, ROOM), 0)
+        const(b("NONE"), -1)
+        iota(b("ROWB"), [[0, 8], [4096, 16]], 0)
+        keep(b("WI"), b("IDB"), DIAG, OP.not_equal, 2.0 ** 26)
+        keep(b("D8"), b("ONES", 0, 64), [[0, 8], [1, 8]], OP.is_gt, 0.0, 0, 0)
+        x = b("EF", 0, 128)
+        fill(x, 0.5)
+        op("v", lambda: V.tensor_tensor_scan(b("EF", 128, 256)[4], b("EF", 0, 128)[4], b("NONE")[4], 2.0 ** 64, OP.mult, OP.max),
+           [x, b("NONE")], [b("EF", 128, 256)], vc(128))
+        keep(b("EF", 256, 384), b("EF", 128, 256), DIAG, OP.is_equal, 0.0)
+        act(b("WD"), b("EF", 256, 384), AF.Copy, scale=-2.5)
+        mm(b("MB", 80, 81), b("WD"), b("ONES", 0, 1))
+        act(b("WL", 0, 1), b("MB", 80, 81), AF.Copy, scale=-0.4)
+        act(b("WL", 1, 2), b("MB", 80, 81), AF.Copy, scale=0.4)
         for h in range(2):
-            ts(b("Z1%d" % h), b("IDF"), b("bias", 2 + h, 3 + h), OP.mult)
-            tt(b("LTD%d" % h), b("tmp"), b("Z1%d" % h), OP.subtract)
-            fill(b("PK%d" % h), FLAG)
-            fill(b("SND%d" % h, 0, CAP), 0.0)
-            fill(b("RCV%d" % h, CAP, L), 0.0)
-        ts(b("bias", 5, 6), P15, 0.0, OP.is_equal)
-        ts(b("bias", 6, 7), P15, 1.0, OP.is_equal)
-        ts(b("BLK0"), b("BLK"), b("bias", 5, 6), OP.mult)
-        ts(b("SEL", 0, 8), b("LC"), b("bias", 5, 6), OP.mult)
-        ts(b("SEL", 8, 16), b("LC"), b("bias", 6, 7), OP.mult)
-        ts(b("bias", 7, 8), P, 8.0, OP.is_lt, -8.0 - c0, OP.mult)
-        ts(b("bias", 4, 5), P, 16.0, OP.is_lt, c0, OP.mult)
-        tt(b("bias", 4, 5), b("bias", 4, 5), b("bias", 7, 8), OP.add)
+            x = b("LTD%d" % h)
+            iota(x, [[0, 128]], 256 * (h + 1), 2 * (h + 1))
+            keep(x, x, DIAG, OP.is_equal, 0.0)
+            keep(x, x, DIAG, OP.is_ge, -1.0)
+            iota(b("bias", 6 + h, 7 + h), [[0, 1]], 128 * h, 1)
+            const(b("PK%d" % h), FLAG)
+            const(b("SND%d" % h, 0, CAP), 0)
+            const(b("RCV%d" % h, CAP, L), 0)
+        const(b("SEL"), 1)
+        keep(b("SEL"), b("SEL"), [[-1, 2], [-16, 8]], OP.is_equal, 0.0)
+        x = b("bias", 4, 5)
+        const(x, 0)
+        keep(x, x, [[0, 1]], OP.is_ge, c0, -16)
+        keep(x, x, [[0, 1]], OP.is_ge, -8.0, -8)
         cp(b("thf", 0, 1), b("thi", 0, 1))
-        ts(b("THM"), b("ONES", 0, 128), b("thf", 0, 1), OP.mult)
-        mm(b("MB", 64, 72), b("THM"), b("BLK0"))
-        ts(b("THK"), b("MB", 64, 72), 8.0 * 65536, OP.add)
+        ts(b("TB"), b("SEL", 0, 8), b("thf", 0, 1), OP.mult)
+        mm(b("MB", 64, 72), b("ONES", 0, 128), b("TB"))
+        act(b("THK"), b("MB", 64, 72), AF.Identity, scale=65536.0, bias=8.0 * 65536)
         iota(b("K4096"), [[128, 2], [0, 8]], 4096, 1)
-        iota(b("KL"), [[16, 16]], 4096, 0)
-        ts(b("KL"), b("KL"), P15, OP.add)
-        iota(b("selj"), [[1, 8], [0, 128]], 0, 0)
-        ts(b("SELG"), b("selj"), P7, OP.is_equal)
-        ts(b("DGL"), b("IDB"), P, OP.mult)
+        iota(b("KC"), [[16, 16]], 0)
+        act(b("bias", 5, 6), P15, AF.Identity, bias=4096.0)
+        for h in range(2):
+            act(b("bias", 2 + h, 3 + h), b("bias", 5, 6), AF.Identity, scale=-1.0, bias=b("bias", 6 + h, 7 + h))
+            const(b("CL%d" % h, 0, 4096), 0)
+        x = b("SELG", rows=16)
+        keep(x, b("ONES", 0, 1024, rows=16), [[-2, 8], [0, 128]], OP.is_ge, 0.0)
+        keep(x, x, [[2, 8], [0, 128]], OP.is_ge, 0.0, 1, -1)
+        iota(b("DGL"), [[0, 128]], 0, 1)
+        keep(b("DGL"), b("DGL"), DIAG, OP.is_equal, 0.0)
         for k in range(4):
-            ts(b("DGB", 128 * k, 128 * k + 128), b("IDB"), float(M + 128 * k), OP.mult)
+            keep(b("DGB", 128 * k, 128 * k + 128), b("IDB"), DIAG, OP.not_equal, float(M + 128 * k))
+        ts(b("LI", 72, 76), b("li", 72, 76), P3, OP.add)
+        ts(b("pi", 4, 5), b("pi", 0, 1), 7, OP.bitwise_and)
+        cp(b("LI", 76, 77), b("pi", 4, 5))
 
     def share(t, p, h):
         return NVL[h] if (t, p) == (VI - 1, 4) else NV[p][h]
@@ -335,24 +361,26 @@ def rank_program(g, core, T, topo):
         mm(b("SP3", 0, 256), b("NIDB"), Q, False, True)
         act(b("DRB"), b("SP3", 0, 256), AF.Abs)
         if t:
-            for k in range(2):
-                for h in range(2):
-                    mm(b("MA", 16 * k + 8 * h, 16 * k + 8 * h + 8), b(r, 128 * h, 128 * h + 128), b("SEL", 8 * k, 8 * k + 8), f32=True, ext=t - 1)
+            for h in range(2):
+                mm(b("MA", 16 * h, 16 * h + 16), b(r, 128 * h, 128 * h + 128), b("SEL"), f32=True, ext=t - 1)
             tt(b("PM"), b("MA", 0, 32), b("FR", 32 * t, 32 * t + 32), OP.max)
             ts(b("PD"), b("PM"), 4, OP.arith_shift_right, 2 ** 18 - 1, OP.bitwise_and)
+            ts(b("B0C"), b("PD"), -c0, OP.add)
             for h in range(2):
-                ts(b("RKS%d" % h, 0, 64, 8), b("PD", 8 * h, 8 * h + 8), 65536.0 * U, OP.mult, -32768.0 * U, OP.add)
-            ts(b("B0C"), b("PD", 16, 32), -c0, OP.add)
+                act(b("RKS%d" % h, 0, 64, 8), b("B0C", 16 * h, 16 * h + 8), AF.Identity, scale=65536.0 * U, bias=(c0 - 0.5) * 65536 * U)
+        cp(b("RT"), b("sj"))
         for h in range(2):
-            mm(b("MA", 32 + 8 * h, 40 + 8 * h), b("DRB", 128 * h, 128 * h + 128), b("BLK"))
-        ts(b("RTL"), b("sj"), CO + 1, OP.add)
-        ts(b("DK"), b("MA", 32, 48), 2.0 ** -16, OP.mult, 8.0, OP.add)
-        tt(b("K0"), b("MA", 32, 48), b("RTL"), OP.add)
-        tg(b("E"), b("DK"), BC16, b("RAMP"), OP.subtract)
-        act(b("A"), b("E"), AF.Abs, scale=65536.0 * U)
-        ts(b("RTL"), b("K0"), U, OP.mult)
+            mm(b("MA", 48 + 8 * h, 56 + 8 * h), b("DRB", 128 * h, 128 * h + 128), b("LCB"))
+        act(b("D0"), b("MA", 48, 64), AF.Copy)
         for h in range(2):
-            tt(b("RKS%d" % h, 1, 64, 8), b("RKS%d" % h, 0, 64, 8), b("RTL", 8 * h, 8 * h + 8), OP.min)
+            mm(b("MA", 32 + 8 * h, 40 + 8 * h), b("DRB", 128 * h, 128 * h + 128), b("BLK"), True, False)
+            mm(b("MA", 32 + 8 * h, 40 + 8 * h), b("IDB"), b("RT", 8 * h, 8 * h + 8), False, True)
+        act(b("K0U"), b("MA", 32, 48), AF.Identity, scale=U, bias=(CO + 1) * U)
+        act(b("K0"), b("MA", 32, 48), AF.Identity, bias=CO + 32768 + 1)
+        tg(b("E"), b("D0"), BC16, b("RAMP"), OP.subtract)
+        act(b("A"), b("E"), AF.Abs, scale=65536.0 * U, bias=-CO * U)
+        for h in range(2):
+            tt(b("RKS%d" % h, 1, 64, 8), b("RKS%d" % h, 0, 64, 8), b("K0U", 8 * h, 8 * h + 8), OP.min)
 
     def push(t, h, p):
         hs = str(h)
@@ -378,18 +406,22 @@ def rank_program(g, core, T, topo):
         for k in range(ns):
             lo, hi = cut[k], cut[k + 1]
             d = b("DIFF", 2048 * h + 16 * lo, 2048 * h + 16 * hi)
+            slot[2] = "get%d" % k
             act(d, pt, AF.Copy, off=n("PU", lo, hi))
             ps = b("SP%d" % (rot[0] % 4), 0, 16 * (hi - lo))
             rot[0] += 1
-            mm(ps, b("IDB"), d, True, False)
-            mm(ps, b("NQT", 128 * h, 128 * h + 128), b("R", 16 * lo, 16 * hi), False, True)
+            mm(ps, b("NQT", 128 * h, 128 * h + 128), b("R", 16 * lo, 16 * hi), True, False)
+            slot[2] = "abs%d" % k
+            mm(ps, b("IDB"), d, False, True)
             act(d, ps, AF.Abs)
         cut = [v0 + nv * k // VP // 2 * 2 for k in range(VP)] + [v0 + nv]
         for k in range(VP if nv else 0):
             lo, hi = cut[k], cut[k + 1]
             d = b("DIFF", 2048 * h + 16 * lo, 2048 * h + 16 * hi)
+            slot[2] = "vec%d" % k
             tg(d, pt, n("PU", lo, hi), b("Q16", 2048 * h + 16 * lo, 2048 * h + 16 * hi), OP.subtract)
             act(d, d, AF.Abs)
+        slot[2] = "key"
         for i in range(16):
             mm(b(KP, i, 128, 16), b("DIFF", 2048 * h + i, 2048 * h + 2048, 16), b("BLK" if p == 4 else "BLKU"), False, i == 15)
         scan(n("KS"), b("MX"), kp, OP.max, OP.min)
@@ -406,21 +438,25 @@ def rank_program(g, core, T, topo):
         if p in (0, 3):
             ts(sk, n("MS", 15, 128, 16), 0.25, OP.min, 1 / U, OP.mult)
         else:
-            ts(n("z3"), n("MS", 15, 128, 16), -0.25, OP.add, 1 / U, OP.mult)
-            tt(sk, n("z3"), b("K0", 8 * h, 8 * h + 8) if p == 1 else n("SK", 0, 8), OP.min)
+            ts(n("z3"), n("MS", 15, 128, 16), 32768.0 * U - 0.25, OP.add, 1 / U, OP.mult)
+            tt(sk, n("z3"), b("K0", 8 * h, 8 * h + 8) if p == 1 else n("FB"), OP.min)
         ts(n("NN"), sk, 4095, OP.bitwise_and)
         tg(n("Z"), n("NN"), BC8, b("DM", 0, 128), OP.mult)
+        slot[2] = "list"
         mm(b(KP, 128, 136), n("Z"), b("LC"), f32=True)
         cp(off, b(KP, 128, 136))
-        ts(dk, sk, 2.0 ** -16, OP.mult)
         if p in (1, 2):
-            ts(dk, dk, 255, OP.bitwise_and)
-            ts(n("RB"), n("SK", 8 * p - 8, 8 * p), 0xF000, OP.bitwise_and)
+            ts(dk, sk, 16, OP.arith_shift_right, 255, OP.bitwise_and)
+            ts(n("RB"), n("FB") if p == 1 else n("SK", 8, 16), 0xF000, OP.bitwise_and)
             tt(n("RP"), sk, n("RB"), OP.min)
             tg(n("ST"), n("RP"), BC8, b("ROWB"), OP.is_equal)
+        else:
+            ts(dk, sk, 2.0 ** -16, OP.mult)
+        if p == 0:
+            ts(n("FB"), sk, 32768.0, OP.add)
         e = b("E", 128 * h, 128 * h + 128)
         tg(e, dk, BC8, b("RAMP", 0, 128), OP.subtract)
-        act(A, e, AF.Abs, scale=65536.0 * U)
+        act(A, e, AF.Abs, scale=65536.0 * U, bias=-15.5 * 65536 * U)
         if p == 3:
             ts(n("Tp"), n("RKS", 5, 64, 8), 1 / U, OP.mult, 32768.0, OP.add)
             ts(n("T3"), n("Tp"), -65536, OP.bitwise_and)
@@ -432,33 +468,25 @@ def rank_program(g, core, T, topo):
             ts(n("W", 8, 16), n("ki"), 4095, OP.bitwise_and)
             if t:
                 ts(n("z3"), n("W", 8, 16), 0.0, OP.is_equal)
-                tt(n("z3"), n("z3"), b("B0C", 8 * h, 8 * h + 8), OP.mult)
+                tt(n("z3"), n("z3"), b("B0C", 16 * h + 8, 16 * h + 16), OP.mult)
             else:
                 ts(n("z3"), n("W", 8, 16), 0.0, OP.is_equal, -c0, OP.mult)
             tt(n("W", 0, 8), n("z3"), n("W", 8, 16), OP.add)
 
-    def lists(z, ps, out, add=None):
-        mm(ps, z, b("LC"), True, add is None, f32=True)
-        if add is not None:
-            mm(ps, b("IDF"), add, False, True, f32=True)
-        cp(out, ps)
-
     def finish(t, h):
         hs = str(h)
         n = lambda x, *a: b(x + hs, *a)
-        pa, pb, pc, pg = (("KP0", "MA", "MB", "KP0"), ("KP1", "SP0", "SP1", "MB"))[h]
-        pairs = (("MB", "MA"), ("SP2", "SP3", "SP1"))[h]
+        pa, pb, po, pg = (("KP0", "KP0", 256, "KP0"), ("KP1", "SP0", 0, "SP1"))[h]
+        pairs = (("MA", "MB"), ("SP2", "SP3"))[h]
         q = b("PT", M + L * t + 128 * h, M + L * t + 128 * h + 128)
-        Rr, best, node = n("RI", 0, 8), n("RI", 8, 16), n("RI", 16, 24)
+        Rr, node = n("RI", 0, 8), n("RI", 16, 24)
         tt(n("V4"), n("KS", 15, 128, 16), n("T3"), OP.min)
         if t < VI - 1:
-            tt(n("far"), n("V4"), b("THK"), OP.is_ge)
-            mm(b(pa, 136, 144), b("LTD" + hs), n("far"), True, h == 0)
+            tt(n("near"), n("V4"), b("THK"), OP.is_lt)
+            mm(b(pa, 136, 144), b("LTD" + hs), n("near"), True, h == 0)
             if h:
-                mm(b(pa, 136, 144), b("ONES", 0, 128), b("far0"), False, True)
-            act(n("dest"), b(pa, 136, 144), AF.Identity, bias=b("bias", 2 + h, 3 + h))
-            tg(n("ZD"), n("dest"), BC8, b("DM", 0, 128), OP.mult)
-            lists(n("ZD"), b(pa, 144, 152), n("OP"))
+                mm(b(pa, 136, 144), b("NONE"), b("near0"), False, True)
+            act(n("DG", 0, 8), b(pa, 136, 144), AF.Identity, bias=b("bias", 2 + h, 3 + h))
         ts(Rr, n("V4"), 16, OP.arith_shift_right)
         op("v", lambda: V.tensor_scalar(n("n4")[4], n("V4")[4].indirect(DUP[4]), 4095, None, OP.bitwise_and),
            [n("V4"), DUP], [n("n4")], FV + 16 * GA * CY)
@@ -468,72 +496,86 @@ def rank_program(g, core, T, topo):
         ob = b("OB%d" % t, 128 * h, 128 * h + 128, 1, 32 if t < VI - 1 else 16)
         if t == VI - 1:
             cp(n("OUT", 0, 16), n("RI", 0, 16))
-            mm(b(pb, 0, 128, 1, 16), n("OUT", 0, 16), b("IDF"), f32=True)
-            act(ob, b(pb, 0, 128, 1, 16), AF.Identity, bias=b("bias", 4, 5, 1, 16))
+            mm(b(pa, 256, 384, 1, 16), n("OUT", 0, 16), b("IDF"), f32=True)
+            act(ob, b(pa, 256, 384, 1, 16), AF.Identity, bias=b("bias", 4, 5, 1, 16))
             for k, (qn, out) in enumerate((("y", T.yr), ("s" if h else "y", T.yb))):
                 o = b(ob[0], ob[1], ob[2], 1, 8, 8 * k)
                 dma(qn, out[:, t * L + 128 * h:t * L + 128 * h + 128], o[4], [o], [], 2.0)
             return
-        ts(n("PK", 0, 128, 16), Rr, 16.0, OP.mult, FLAG, OP.add)
-        ts(n("PK", 1, 128, 16), best, 16.0, OP.mult, FLAG + 16 * c0, OP.add)
-        mm(b(pb, 0, 128), n("PK"), b("IDF"), True, False, f32=True)
-        mm(b(pb, 0, 128), b("IDB"), q, False, True)
-        act(n("XS"), b(pb, 0, 128), AF.Copy)
+        kc = b("KC", 8 * h, 8 * h + 8)
+        z1 = n("ZZ", 128, 256)
+        tt(n("DG", 8, 16), node, b("K4096", 8 * h, 8 * h + 8), OP.subtract)
+        tg(n("ZZ"), n("DG"), BC16, b("DM"), OP.mult)
+        mm(b(pa, 144, 152), n("ZZ", 0, 128), b("LC"), f32=True)
+        mm(b(pa, 152, 160), b("IDB"), kc, True, False)
+        mm(b(pa, 152, 160), z1, b("LC"), False, True, f32=True)
+        ts(n("OG"), b(pa, 144, 160), b("bias", 5, 6), OP.add)
+        cp(n("OUT", 0, 24), n("RI"))
+        act(n("PK", 0, 128, 16), n("OUT", 0, 8), AF.Identity, scale=16.0, bias=FLAG)
+        act(n("PK", 1, 128, 16), n("OUT", 8, 16), AF.Identity, scale=16.0, bias=FLAG + 16 * c0)
+        mm(b(pb, po, po + 128), b("IDB"), q, True, False)
+        mm(b(pb, po, po + 128), n("PK"), b("IDF"), False, True, f32=True)
+        act(n("XS"), b(pb, po, po + 128), AF.Copy)
         snd, rcv = "SND%d" % t, "RCV%d" % t
-        op("v", lambda: V.tensor_copy(b(snd)[4].indirect(n("OP")[4]), n("XS")[4]), [n("XS"), n("OP")], [b(snd)], FV + 128 * SCA * CY)
+        og = n("OG", 0, 8)
+        op("v", lambda: V.tensor_copy(b(snd)[4].indirect(og[4]), n("XS")[4]), [n("XS"), og], [b(snd)], FV + 128 * SCA * CY)
         if h:
             dst = T.cores[(rank + 1) % N]
             rid, pid, _x = topo.addr(dst)
             op("g", lambda: g.remote_dma(T[rcv][:, 0:CAP], T[snd][:, 0:CAP], T.sem["arr%d" % t], T.sem["sent%d" % t], pid, rid, topo.mask(core, dst)),
                [b(snd, 0, CAP)], [], 0.1, "r", t)
-        cp(n("OUT", 0, 24), n("RI"))
-        tt(n("gq"), node, b("K4096", 8 * h, 8 * h + 8), OP.subtract)
-        tg(n("Z1"), n("gq"), BC8, b("DM", 0, 128), OP.mult)
-        kl = b("KL", 8 * h, 8 * h + 8)
-        lists(n("Z1"), b(pg, 152, 160), n("G1"), kl)
-        act(n("GC"), b("CH", 0, 4096), AF.Copy, off=n("G1"))
-        ts(n("NI", 0, 8), node, 4032, OP.bitwise_and)
-        ts(n("NI", 8, 16), node, 63, OP.bitwise_and)
-        cp(n("NQ"), n("NI"))
-        mm(b(pc, 0, 128, 1, 16), n("NQ"), b("IDB"))
+        act(n("GC"), b("CH", 0, 4096), AF.Copy, off=n("OG", 8, 16))
+        cp(n("NQ", 0, 16, 2), node)
+        tt(n("NQ", 1, 16, 2), node, n("NQ", 0, 16, 2), OP.subtract)
+        mm(b(pg, 0, 128, 1, 16), n("NQ"), b("IDB"))
         nt = b("NT" + hs, 0, 128, 1, 16)
-        act(nt, b(pc, 0, 128, 1, 16), AF.Copy)
+        act(nt, b(pg, 0, 128, 1, 16), AF.Copy)
         ts(n("bb"), Rr, 0.0625, OP.mult, -0.96875, OP.add)
-        tg(n("OH"), n("bb"), BC8, b("j15"), OP.is_equal)
-        mm(b(pb, 128, 256), n("OH"), b("DGB", 128 * (2 * t + h), 128 * (2 * t + h) + 128), True, False)
-        mm(b(pb, 128, 256), n("OH"), b("DGL"), False, True)
-        act(n("ON"), b(pb, 128, 256), AF.Copy)
-        tt(n("pre"), node, n("far"), OP.min)
-        w = 128 * (h + 1)
+        tg(n("OH"), n("bb"), BC8, b("j15", 0, 128), OP.is_equal)
+        mm(b(pb, po + 128, po + 256), n("OH"), b("DGB", 128 * (2 * t + h), 128 * (2 * t + h) + 128), True, False)
+        mm(b(pb, po + 128, po + 256), n("OH"), b("DGL"), False, True)
+        act(n("ON"), b(pb, po + 128, po + 256), AF.Copy)
+        ns = GSC[h]
         for gg in range(8):
-            ps = pairs[gg % len(pairs)]
-            sel = b("SELG", 128 * gg, 128 * gg + 128, 1, 16)
-            if h:
-                mm(b(ps, 256, 384), sel, nt)
-            mm(b(ps, 256 + w - 128, 256 + w), sel, nt, True, False)
-            mm(b(ps, 256 + w - 128, 256 + w), b("IDB"), b("TRI"), False, True)
-            for k in range(h + 1):
-                x, cc = b(ps, 256 + 128 * k, 384 + 128 * k), b("OUT%d" % k, 16 + gg, 17 + gg)
-                if gg in GSC[h]:
-                    act(b("EF", 128 * k, 128 * k + 128), x, AF.Abs, scale=-1.0, bias=cc)
-                else:
-                    ts(n("EQ", 256 * gg + 128 * k, 256 * gg + 128 * k + 128), x, cc, OP.is_equal)
-            if gg in GSC[h]:
-                act(n("EQ", 256 * gg, 256 * gg + w), b("EF", 0, w), AF.Relu, scale=-1.0, bias=1.0)
-        tt(n("OC"), b(pb, 128, 256), n("GC"), OP.mult)
-        mm(b(pg, 160, 168), n("OC"), b("LCB"))
-        tt(n("can"), n("pre"), b(pg, 160, 168), OP.is_gt)
+            ps = b(pairs[gg // 4], 128 * (gg % 4), 128 * (gg % 4) + 128)
+            mm(ps, b("SELG", 128 * gg, 128 * gg + 128, 1, 16), nt)
+        wl, nwl = b("WL", 0, 1), b("WL", 1, 2)
         for gg in range(8):
-            for k in range(h + 1):
-                mm(b(pg, 168 + gg, 169 + gg), n("EQ", 256 * gg + 128 * k, 256 * gg + 128 * k + 128), b("can%d" % k, gg, gg + 1), k == 0, k == h)
-        tt(n("win"), n("can"), b(pg, 168, 176), OP.is_gt)
-        tg(n("Z2"), n("win"), BC8, n("Z1"), OP.mult)
-        lists(n("Z2"), b(pg, 176, 184), n("G2"), kl)
+            ps, cc = b(pairs[gg // 4], 128 * (gg % 4), 128 * (gg % 4) + 128), n("OUT", 16 + gg, 17 + gg)
+            if gg < ns:
+                act(b("EF", 128 * gg, 128 * gg + 128), ps, AF.Abs, scale=-1.0, bias=cc)
+            else:
+                ts(n("EQ", 128 * gg, 128 * gg + 128), ps, cc, OP.is_equal, wl, OP.mult)
+        act(n("EQ", 0, 128 * ns), b("EF", 0, 128 * ns), AF.Relu, scale=nwl, bias=wl)
+        tt(n("OC"), b(pb, po + 128, po + 256), n("GC"), OP.mult)
+        mm(b(pg, 160, 168), b("WI"), n("near"), True, False)
+        cl = b("CL%d" % t)
+        if h:
+            act(b("CG"), b(cl[0], 0, 4096), AF.Copy, off=n("OG", 8, 16))
+            mm(b(pg, 160, 168), b("CG"), b("BLK"), False, False)
+        mm(b(pg, 160, 168), n("OC"), b("LC2"), False, True)
+        tt(n("can"), node, b(pg, 160, 168), OP.is_gt)
+        mm(b(pg, 168, 176), b("WD"), n("can"), True, False)
+        for gg in range(8):
+            mm(b(pg, 168 + gg, 169 + gg), n("EQ", 128 * gg, 128 * gg + 128), n("can", gg, gg + 1), False, gg == 7)
+        if h:
+            mm(b(pa, 176, 184), b("IDB"), kc, True, False)
+        ts(n("win"), b(pg, 168, 176), 0.0, OP.is_lt)
+        if not h:
+            mm(b(pa, 176, 184), b("IDB"), kc, True, False)
+        tg(n("Z2"), n("win"), BC8, z1, OP.mult)
+        mm(b(pa, 176, 184), n("Z2"), b("LC"), False, True, f32=True)
+        ts(n("G2"), b(pa, 176, 184), b("bias", 5, 6), OP.add)
+        if h == 0:
+            one = b("ONES", 0, 128)
+            op("v", lambda: V.tensor_copy(cl[4].indirect(n("G2")[4]), one[4]), [one, n("G2")], [cl], FV + 128 * SCA * CY)
         op("v", lambda: V.tensor_tensor(b("CH")[4].indirect(n("G2")[4]), n("GC")[4], n("ON")[4], OP.add),
            [n("GC"), n("ON"), n("G2")], [b("CH")], FV + 128 * SCA * CY)
         tt(n("OUT", 24, 32), n("win"), node, OP.mult)
-        mm(b(pb, 0, 128, 1, 32), n("OUT"), b("IDF"), f32=True)
-        act(ob, b(pb, 0, 128, 1, 32), AF.Identity, bias=b("bias", 4, 5, 1, 32))
+        if h:
+            for k in range(2):
+                mm(b("MB", 128 * k, 128 * k + 128, 1, 32), b("OUT%d" % k), b("IDF"), f32=True)
+            act(b(ob[0], 0, L, 1, 32), b("MB", 0, L, 1, 32), AF.Identity, bias=b("bias", 4, 5, 1, 32))
         if h:
             for k, out in ((0, T.yr), (1, T.yb), (3, T.yp)):
                 o = b(ob[0], 0, L, 1, 8, 8 * k)
@@ -547,50 +589,68 @@ def rank_program(g, core, T, topo):
         for p in range(5):
             for h in range(2):
                 tag[0] = "%d%d%s" % (t, p, "AB"[h])
+                slot[:] = [(t, p, h), {}, "Pf"]
                 push(t, h, p)
+        slot[0] = None
         for h in range(2):
             tag[0] = "f%d%s" % (t, "AB"[h])
             finish(t, h)
 
     n = len(ops)
-    WAKE, LOOK = 0.08, 0.1
-    lat = [o["cost"] + (o["ext"] if o["kind"] == "d" else 0) for o in ops]
-    succ = [[] for _ in range(n)]
-    cnt = [0] * n
+    WAKE = 0.08
+    cost = [o["cost"] for o in ops]
+    more = [o["ext"] if o["kind"] == "d" else 3.0 if o["kind"] == "r" else 0.0 for o in ops]
+    fwd = [[] for _ in range(n)]
+    bwd = [[] for _ in range(n)]
     for i, o in enumerate(ops):
         dd = set(o["deps"])
         if o["kind"] == "c" and o["ext"] is not None:
-            x = [j for j in range(n) if ops[j]["kind"] == "r" and ops[j]["ext"] == o["ext"]][0]
-            lat[x] = 3.0
-            dd.add(x)
+            dd.add([j for j in range(n) if ops[j]["kind"] == "r" and ops[j]["ext"] == o["ext"]][0])
         for d in dd:
-            succ[d].append((i, WAKE))
+            fwd[d].append((i, cost[d] + more[d] + WAKE))
+            bwd[i].append((d, cost[i] + more[d] + WAKE))
         for d in o["after"] - dd:
-            succ[d].append((i, None))
-        cnt[i] = len(dd | o["after"])
-    pri = [0.0] * n
+            fwd[d].append((i, cost[d]))
+            bwd[i].append((d, cost[i]))
+
+    def place(succ, pri, first):
+        cnt = [0] * n
+        for lst in succ:
+            for j, x in lst:
+                cnt[j] += 1
+        rt, at, free, order, byq = list(first), [0.0] * n, {}, [], {}
+        for i in range(n):
+            if cnt[i] == 0:
+                byq.setdefault(ops[i]["q"], []).append(i)
+        while len(order) < n:
+            t0, qn = min((max(free.get(x, 0.0), min(rt[i] for i in lst)), x) for x, lst in byq.items() if lst)
+            i = max((i for i in byq[qn] if rt[i] <= t0 + LOOK), key=lambda i: pri[i])
+            at[i] = max(t0, rt[i])
+            byq[qn].remove(i)
+            order.append(i)
+            free[qn] = at[i] + cost[i]
+            for j, x in succ[i]:
+                rt[j] = max(rt[j], at[i] + x)
+                cnt[j] -= 1
+                if cnt[j] == 0:
+                    byq.setdefault(ops[j]["q"], []).append(j)
+        return order, at
+
+    seen = {}
+    due = [0.0] * n
     for i in range(n - 1, -1, -1):
-        pri[i] = max([lat[i] + x + pri[j] if x is not None else ops[i]["cost"] + pri[j] for j, x in succ[i]] or [lat[i]])
-    rt = [0.0] * n
-    free = {}
-    order = []
-    byq = {}
+        due[i] = min([due[j] - x for j, x in fwd[i]] or [1000.0])
+        o = ops[i]
+        if o["slot"] is not None:
+            t, p, h = o["slot"]
+            if o["lab"] in WHEN:
+                due[i] = (10 * HALF + GAP) * t + (2 * p + h) * HALF + WHEN[o["lab"]]
     for i in range(n):
-        if cnt[i] == 0:
-            byq.setdefault(ops[i]["q"], []).append(i)
-    while len(order) < n:
-        t0, qn = min((max(free.get(x, 0.0), min(rt[i] for i in lst)), x) for x, lst in byq.items() if lst)
-        i = max((i for i in byq[qn] if rt[i] <= t0 + LOOK), key=lambda i: pri[i])
-        t0 = max(t0, rt[i])
-        byq[qn].remove(i)
-        order.append(i)
-        ops[i]["t0"] = t0
-        free[qn] = t0 + ops[i]["cost"]
-        for j, x in succ[i]:
-            rt[j] = max(rt[j], t0 + lat[i] + x) if x is not None else max(rt[j], t0)
-            cnt[j] -= 1
-            if cnt[j] == 0:
-                byq.setdefault(ops[j]["q"], []).append(j)
+        if ops[i]["tag"][:1] == "f" and ops[i]["tag"][2] == "A":
+            due[i] -= EARLY
+    order, at = place(fwd, [-x for x in due], [0.0] * n)
+    for i in range(n):
+        ops[i]["t0"] = at[i]
 
     QS = {"v": V, "t": TE, "s": S, "g": g, "y": g.sync}
     CS = {"v": "cv", "t": "ct", "s": "cs", "g": "cg"}

@@ -3,17 +3,24 @@ from concourse.mybir import AluOpType as OP, ActivationFunctionType as AF
 N, L, CAP, M, VI = 4, 256, 192, 3584, 3
 U = 2.0 ** -26
 BIG = float(2 ** 60)
+RND = 1.5 * 2 ** 23
 CO = 7.5 * 65536
 FLAG = float(2 ** 22)
 ROOM = 4096 + 256
 SNDW = 1280
-NV = ((64, 64), (64, 56), (56, 56), (56, 64), (64, 64))
-NVL = (72, 80)
+NV = ((70, 62), (56, 52), (52, 52), (52, 54), (52, 64))
+NV0 = ((76, 66), (58, 52))
+DRV = True
+NVL = (72, 88)
 VP = 2
-QV = 8
-GSC = (4, 4)
-HALF, GAP, LOOK, EARLY = 4.72, 16.5, 0.04, 2.91
-WHEN = {'vPU0': -0.27, 'vvec0': 2.31, 'vvec1': 2.19, 'vM0': 2.4, 'vKS0': 4.94, 'vRKS0': 7.07, 'vM1': 3.4, 'vKM0': 8.1, 'vMS0': 7.01, 'vz0': 4.01, 'vSK0': 5.02, 'vNN0': 7.8, 'vZ0': 6.59, 'vDK0': 9.61, 'vE0': 10.37, 'vOFF0': 7.6, 'vRB0': 6.34, 'vRP0': 9.9, 'vST0': 5.59, 'vFB0': 10.57, 'sget0': -0.35, 'sget1': 1.68, 'sget2': -2.14, 'sPf0': 1.46, 'svec0': 3.84, 'sabs0': 4.05, 'sabs1': 3.38, 'svec1': 3.46, 'sabs2': 4.42, 'sA0': 10.9, 'tget0': 5.72, 'tabs0': 2.5, 'tget1': 1.97, 'tabs1': 4.48, 'tget2': 2.49, 'tabs2': 2.74, 'tPf': 4.06, 'tkey': 4.19, 'tlist': 4.56}
+SP = 2
+QV = 7
+GSC = (4, 6)
+HALF, GAP, LOOK, EARLY = 4.97, 18.0, 0.07, 2.3
+WHEN = {'vPU0': 0.83, 'vvec0': 2.6, 'vvec1': 2.85, 'vM0': 2.48, 'vKS0': 6.82, 'vRKS0': 7.81, 'vM1': 3.2, 'vKM0': 11.11, 'vMS0': 7.1, 'vz0': 7.44, 'vSK0': 5.26, 'vNN0': 7.1, 'vZ0': 5.7, 'vDK0': 8.03, 'vE0': 12.79, 'vOFF0': 8.24, 'vRB0': 7.77, 'vRP0': 9.84, 'vST0': 7.42, 'vFB0': 13.5, 'sget0': -0.16, 'sget1': 2.04, 'sPf0': 3.05, 'svec0': 2.69, 'sabs0': 3.0, 'sabs1': 1.92, 'svec1': 3.67, 'sA0': 12.3, 'tget0': 5.37, 'tabs0': 0.41, 'tget1': 2.4, 'tabs1': 5.16, 'tPf': 3.47, 'tkey': 2.85, 'tlist': 3.84, 'sD0': 4.51,
+        "vTp0": 8.0, "vT0": 8.0, "vthr0": 8.0, "vm0": 8.0, "vsc0": 8.0, "vki0": 8.0, "vW0": 8.0, "vy0": 8.0, "vy1": 8.0, "vW1": 8.0}
+ROUNDS = 15000
+FIX, WAKE = (0.07, 0.065, 0.01), 0.1
 WHEN0 = {"vPU0": 0.0, "vvec0": 0.25, "vvec1": 1.6, "vvec2": 2.0, "vvec3": 2.3, "vM0": 1.2, "vKS0": 5.9, "vRKS0": 6.1, "vM1": 6.2, "vKM0": 6.9, "vMS0": 7.2,
         "vz0": 7.4, "vSK0": 7.5, "vNN0": 7.7, "vZ0": 7.9, "vDK0": 8.1, "vE0": 8.3, "vOFF0": 8.6, "vRB0": 7.3, "vRP0": 8.4, "vST0": 10.0,
         "vFB0": 10.0, "sget0": 0.3, "sget1": 0.9, "sget2": 1.5, "sget3": 2.0, "sPf0": 2.0, "svec0": 2.2, "sabs0": 2.6, "sabs1": 3.0,
@@ -38,9 +45,14 @@ def _s(name, cols, dt="float32"):
     p[1] += (cols + 15) // 16 * 16
 
 
-for _n in ("KP0", "KP1", "MA", "MB", "SP0", "SP1", "SP2", "SP3"):
+for _n in ("KP0", "KP1"):
     SCRATCH[_n] = ("psum", [128, 512], "float32")
     VIRT[_n] = (_n, 0, 512)
+    PS.add(_n)
+RING = ("MA", "SP0", "SP1", "SP2", "SP3", "MB")
+SCRATCH["RING"] = ("psum", [128, 3072], "float32")
+for _k, _n in enumerate(RING):
+    VIRT[_n] = ("RING", 512 * _k, 512)
     PS.add(_n)
 _own("PT", M + VI * L, "bfloat16"); _own("CHI", M, "int32"); _own("CH", ROOM)
 _own("wi", 8, "int32"); _own("thi", 8, "int32"); _own("r0i", 128, "int32")
@@ -50,25 +62,25 @@ for _t in "01":
 for _t in "012":
     _own("OB" + _t, 256)
 for _n, _c in (("r0f", 128), ("wf", 2), ("thf", 2), ("pf", 8), ("j15", 256), ("c8", 8), ("IDF", 128), ("DM", 256),
-               ("LC", 8), ("RAMP", 256), ("MX", 128), ("ROWB", 128), ("bias", 8), ("THK", 8), ("K4096", 16),
-               ("SEL", 16), ("FR", 96), ("E", 256), ("A", 256), ("K0", 16), ("K0U", 16), ("D0", 16), ("WL", 2), ("B0C", 32), ("EF", 1024)):
+               ("LC", 8), ("RAMP", 256), ("RAMQ", 128), ("MX", 128), ("ROWB", 128), ("bias", 8), ("THK", 8), ("K4096", 16),
+               ("SEL", 16), ("FR", 96), ("E", 256), ("A", 256), ("K0", 16), ("K0U", 16), ("D0", 16), ("WL", 2), ("B0C", 32), ("EF", 1024),
+               ("RKS", 128), ("thr", 16), ("m", 136), ("sc", 128), ("y", 16)):
     _s(_n, _c)
-for _n, _c in (("pi", 8), ("li", 96), ("si", 16), ("sj", 16), ("DK", 16), ("MI", 192), ("QI", 192), ("PM", 32), ("PD", 32)):
+for _n, _c in (("pi", 8), ("li", 96), ("si", 16), ("sj", 16), ("DK", 16), ("MI", 192), ("QI", 192), ("PM", 32), ("PD", 32),
+               ("Tp", 16), ("T3", 16), ("ki", 16), ("W", 32)):
     _s(_n, _c, "int32")
 for _n, _c in [("IDB", 128), ("NIDB", 128), ("WI", 128), ("BLKU", 8), ("BLK", 8), ("LCB", 8), ("LC2", 8), ("WB", 8), ("WD", 128), ("RT", 16),
                ("LTD0", 128), ("LTD1", 128), ("ONES", 2048), ("R", 2048), ("TB", 8), ("SELG", 1024), ("ZR", 256), ("D8", 64),
-               ("DRB", 256), ("NQT", 256), ("DGL", 128), ("DGB", 128 * 4), ("NONE", 128), ("KC", 16), ("CG", 128),
-               ("CL0", ROOM), ("CL1", ROOM)]:
+               ("DRB", 256), ("NQT", 256), ("DGL", 128), ("DGB", 128 * 4), ("NONE", 128), ("KC", 16), ("CG", 128)]:
     _s(_n, _c, "bfloat16")
 _s("LI", 96, "uint16"); _s("OFF", 16, "uint16")
 for _h in "01":
     for _n, _c, _d in (("PU", 128, "uint16"), ("Pf", 128, "float32"), ("M1", 128, "bfloat16"), ("M2", 128, "bfloat16"),
                        ("ST", 128, "bfloat16"), ("KS", 128, "float32"), ("KM", 128, "float32"), ("MS", 128, "float32"),
                        ("SK", 32, "int32"), ("NN", 8, "int32"), ("FB", 8, "int32"),
-                       ("Z", 128, "float32"), ("RB", 8, "int32"), ("RP", 8, "int32"), ("RKS", 64, "float32"),
-                       ("Tp", 8, "int32"), ("T3", 8, "int32"), ("thr", 8, "float32"), ("m", 64, "float32"), ("x", 64, "float32"),
-                       ("sc", 64, "float32"), ("ki", 8, "int32"), ("W", 16, "int32"), ("z3", 8, "float32"), ("V4", 8, "int32"),
-                       ("n4", 16, "int32"), ("z", 16, "float32"), ("RI", 24, "int32"), ("OUT", 32, "float32"), ("near", 8, "bfloat16"),
+                       ("Z", 128, "float32"), ("RB", 8, "int32"), ("RP", 8, "int32"),
+                       ("z3", 8, "float32"), ("V4", 8, "int32"),
+                       ("n4", 16, "int32"), ("z", 16, "float32"), ("zw", 16, "float32"), ("RI", 24, "int32"), ("OUT", 32, "float32"), ("near", 8, "bfloat16"),
                        ("DG", 16, "float32"), ("ZZ", 256, "float32"), ("OG", 16, "uint16"), ("PK", 128, "float32"), ("XS", 128, "float32"),
                        ("GC", 128, "float32"),
                        ("bb", 8, "int32"), ("OH", 128, "bfloat16"), ("ON", 128, "float32"), ("OC", 128, "bfloat16"), ("can", 8, "bfloat16"),
@@ -80,6 +92,80 @@ for _d in POOL:
 
 NDMA = 24
 SEMAPHORES = ["cv", "ct", "cs", "cg"] + ["d%d" % i for i in range(NDMA)] + ["arr0", "arr1", "sent0", "sent1"]
+
+
+ORDER = {}
+
+
+def improve(order, q, cost, more, fwd):
+    n = len(order)
+    reach, pre, suc = [0] * n, [[] for _ in range(n)], [[] for _ in range(n)]
+    for i in range(n - 1, -1, -1):
+        for j, x in sorted(fwd[i]):
+            if not (reach[i] >> j) & 1 or more[i] > 0:
+                pre[j].append((i, x))
+                suc[i].append(j)
+                reach[i] |= reach[j] | (1 << j)
+
+    def run(order):
+        at, why, free, last, end = [0.0] * n, [None] * n, {}, {}, (0.0, 0)
+        for i in order:
+            t, w = 0.0, None
+            for d, x in pre[i]:
+                if at[d] + x > t:
+                    t, w = at[d] + x, (d, False)
+            if free.get(q[i], 0.0) > t + 1e-9:
+                t, w = free[q[i]], (last[q[i]], True)
+            at[i], why[i], free[q[i]], last[q[i]] = t, w, t + cost[i], i
+            if t + cost[i] + more[i] > end[0]:
+                end = (t + cost[i] + more[i], i)
+        return end, at, why
+
+    seed = [12345]
+
+    def draw(k):
+        seed[0] = (seed[0] * 1103515245 + 12345) % 2 ** 31
+        return (seed[0] >> 8) % k
+
+    cur = run(order)
+    best = (cur[0][0], order, cur[1])
+    for it in range(ROUNDS):
+        i, pairs = cur[0][1], []
+        while cur[2][i]:
+            if cur[2][i][1]:
+                pairs.append((cur[2][i][0], i))
+            i = cur[2][i][0]
+        x, y = pairs[draw(len(pairs))]
+        lo, hi, step = order.index(x), order.index(y), 2 * draw(2) - 1
+        k = lo if step < 0 else hi
+        for _ in range((0, 0, 1, 2, 4)[draw(5)]):
+            j = k + step
+            while 0 <= j < n and q[order[j]] != q[y]:
+                j += step
+            k = j if 0 <= j < n else k
+        if step < 0:
+            lo, go = k, {y}
+            seg = order[lo:hi + 1]
+            for v in reversed(seg):
+                if any(s in go for s in suc[v]):
+                    go.add(v)
+            new = [v for v in seg if v in go] + [v for v in seg if v not in go]
+        else:
+            hi, go = k, {x}
+            seg = order[lo:hi + 1]
+            for v in seg:
+                if any(d in go for d, _x in pre[v]):
+                    go.add(v)
+            new = [v for v in seg if v not in go] + [v for v in seg if v in go]
+        if x in go and y in go:
+            continue
+        new = order[:lo] + new + order[hi + 1:]
+        r = run(new)
+        if r[0][0] <= cur[0][0] + 0.0001 * draw(1000) * (1 - it / ROUNDS):
+            cur, order = r, new
+            if r[0][0] < best[0]:
+                best = (r[0][0], new, r[1])
+    return best[1], best[2]
 
 
 def rank_program(g, core, T, topo):
@@ -112,21 +198,29 @@ def rank_program(g, core, T, topo):
         both = [(False, o) for o in reads] + [(True, o) for o in writes]
         for w, o in both:
             r = (o[1], o[2], o[3])
+            if o[0] in PS:
+                runs = hist.setdefault(o[0], [])
+                if not runs or runs[-1][0] != q:
+                    runs.append((q, []))
+                if len(runs) > 1:
+                    deps.update(runs[-2][1][-1:] if runs[-2][0] == "t" else runs[-2][1])
+                if q == "t":
+                    after.update(runs[-1][1][-1:])
+                elif w:
+                    deps.update(runs[-1][1])
+                runs[-1][1].append(n)
+                continue
             for (r2, w2, n2) in hist.get(o[0], ()):
-                if o[0] in PS and q == "t" and ops[n2]["q"] == "t":
-                    after.add(n2)
-                elif (w or w2) and clash(r, r2):
-                    deps.add(n2)
-                elif o[0] in PS and ops[n2]["q"] != q:
+                if (w or w2) and clash(r, r2):
                     deps.add(n2)
         for w, o in both:
+            if o[0] in PS:
+                continue
             r = (o[1], o[2], o[3])
             h = hist.setdefault(o[0], [])
-            if w and o[0] not in PS:
-                h[:] = [e for e in h if not (r[2] == 1 and r[0] <= e[0][0] and e[0][1] <= r[1] and e[2] != n)]
+            if w:
+                h[:] = [e for e in h if not (e[2] != n and r[0] <= e[0][0] and e[0][1] <= r[1] and (r[2] == 1 or r == e[0]))]
             h.append((r, w, n))
-            if o[0] in PS and len(h) > 120:
-                del h[:40]
         d = {"q": q, "call": call, "deps": deps, "after": after - deps, "cost": cost, "kind": kind, "ext": ext,
              "tag": tag[0] + " " + (writes[0][0] if writes else "")}
         d["slot"] = slot[0]
@@ -134,8 +228,10 @@ def rank_program(g, core, T, topo):
             lab = q + writes[0][0].rstrip("0123")
             slot[1][lab] = slot[1].get(lab, -1) + 1
             d["lab"] = lab + str(slot[1][lab])
-            if lab in ("tKP", "tSP", "sDIFF", "vDIFF"):
+            if lab in ("tKP", "tSP", "tMA", "tMB", "sDIFF", "vDIFF"):
                 d["lab"] = q + slot[2]
+            if slot[2] == "out":
+                d["slot"] = None
         if kind == "d":
             d["sem"] = "d%d" % ndma[0]
             ndma[0] += 1
@@ -143,7 +239,7 @@ def rank_program(g, core, T, topo):
         return n
 
     CY, GA, SCA = 0.00083 * 1.2, 1.56, 3.8
-    FV, FS, FT = 0.05, 0.065, 0.015
+    FV, FS, FT = FIX
     two = ("poolb", "poolu", "PT", "Q16", "DIFF")
 
     def cols(o):
@@ -195,9 +291,9 @@ def rank_program(g, core, T, topo):
         src = a[4] if off is None else a[4].indirect(off[4])
         op("s", lambda: S.activation(out[4], src, f, **kw), rd, [out], FS + cols(out) * CY * (1 if off is None else GA))
 
-    def mm(out, l, r, start=True, stop=True, f32=False, ext=None):
+    def mm(out, l, r, start=True, stop=True, f32=False, ext=None, also=None):
         n = max(min(64, cols(l)), cols(r))
-        op("t", lambda: TE.matmul(out[4], l[4], r[4], start, stop), [l, r], [out], FT + n * (4 if f32 else 1) * CY, "c", ext)
+        op("t", lambda: TE.matmul(out[4], l[4], r[4], start, stop), [l, r] + ([also] if also else []), [out], FT + n * (4 if f32 else 1) * CY, "c", ext)
 
     def dma(q, out, src, reads, writes, us):
         eng = g.sync if q == "y" else g.scalar
@@ -222,7 +318,7 @@ def rank_program(g, core, T, topo):
     load("y", "PT", 0, M, T.pt[:], 4.5)
     load("s", "CHI", 0, 128, T.ch[:, 0:128], 2.2)
     load("s", "r0i", 0, 128, T.r0[:], 2.2, 48)
-    CHP = (128, 1280, 2432, M)
+    CHP = (128, 1536, 2944, M)
     for k in range(3):
         load("y", "CHI", CHP[k], CHP[k + 1], T.ch[:, CHP[k]:CHP[k + 1]], 6.0 + 1.5 * k)
     load("s", "thi", 0, 1, T.th[:], 2.5)
@@ -235,9 +331,10 @@ def rank_program(g, core, T, topo):
     iota(b("j15"), [[0, 16], [1, 16]], 0)
     keep(b("IDB"), b("ONES", 0, 128), DIAG, OP.is_equal, 0.0)
     iota(b("li", 16, 24), [[16, 8]], 15)
-    iota(b("li", 24, 72), [[1, 6], [8, 8]], 0)
-    iota(b("li", 72, 76), [[2, 4]], 0)
-    keep(b("R"), b("ONES"), [[-1, 128], [0, 16]], OP.is_equal, 0.0)
+    iota(b("li", 24, 72), [[1, 6], [8, 8]], 2)
+    iota(b("li", 72, 80), [[2, 8]], 0)
+    op("g", lambda: g.affine_select(b("R")[4], b("ONES")[4], [[-1, 128], [0, 16]], OP.is_equal, 0.0, 0, 1),
+       [b("ONES"), b("IDB"), b("li", 0, 72)], [b("R")], 0.17 + 2 * 2048 * CY)
     ts(b("pi", 1, 2), b("pi", 0, 1), 15, OP.bitwise_and)
     ts(b("pi", 2, 3), b("pi", 0, 1), 4, OP.arith_shift_right)
     ts(b("pi", 3, 4), b("pi", 0, 1), 3, OP.arith_shift_right, 1, OP.bitwise_and)
@@ -245,7 +342,8 @@ def rank_program(g, core, T, topo):
     P15, P4, P3 = [b("pf", k, k + 1) for k in range(1, 4)]
     cp(b("LI", 0, 16), b("li", 0, 16))
     cp(b("LI", 16, 72), b("li", 16, 72))
-    BC16, BC8, BC15, BH, DUP = b("LI", 0, 16), b("LI", 0, 8), b("LI", 16, 24), b("LI", 72, 76), b("LI", 76, 77)
+    BC16, BC8, BC15, BH, DUP = b("LI", 0, 16), b("LI", 0, 8), b("LI", 16, 24), b("LI", 72, 80), b("LI", 80, 81)
+    PICK = [b("LI", 82 + 2 * h, 83 + 2 * h) for h in range(2)]
     BCS = [b("LI", 24 + 8 * s, 32 + 8 * s) for s in range(6)]
     ts(b("LC"), b("c8"), P4, OP.is_equal)
     cp(b("wf", 0, 1), b("wi", 0, 1))
@@ -256,6 +354,7 @@ def rank_program(g, core, T, topo):
     act(b("NIDB"), b("IDB"), AF.Copy, scale=-1.0)
     act(b("IDF"), b("IDB"), AF.Copy)
     act(b("RAMP"), b("j15"), AF.Copy, scale=16.0)
+    act(b("RAMQ"), b("j15", 0, 128), AF.Identity, scale=16.0, bias=RND)
     fill(b("MX"), -BIG)
     fill(b("MX", 0, 128, 16), BIG)
     act(b("bias", 0, 1), P15, AF.Identity, scale=4096.0 * U, bias=CO * U)
@@ -263,22 +362,25 @@ def rank_program(g, core, T, topo):
     cp(b("r0f", rows=48), b("r0i", rows=48))
     mm(b("MB", 0, 48), b("r0f", rows=48), b("IDF", 0, 48, rows=48), f32=True)
     const(b("FR"), 0)
+    act(b("RKS"), b("ONES", 0, 128), AF.Copy)
     for h in range(2):
-        fill(b("RKS%d" % h), 0.0)
-        act(b("RKS%d" % h, 0, 64, 8), b("MB", h, 48, 6), AF.Identity, scale=65536.0 * U, bias=CO * U)
+        act(b("RKS", 64 * h + 2, 64 * h + 64, 8), b("MB", h, 48, 6), AF.Identity, scale=65536.0 * U, bias=CO * U)
     for k in range(2, 6):
-        act(b("FR", 16 * k, 16 * k + 8), b("MB", k, 48, 6), AF.Identity, scale=16.0, bias=128.0)
+        act(b("FR", 16 * k, 16 * k + 16, 2), b("MB", k, 48, 6), AF.Identity, scale=16.0, bias=128.0)
+    act(b("CH", M, ROOM), b("ONES", 0, ROOM - M), AF.Copy, scale=0.0)
     cp(b("CH", 0, 128), b("CHI", 0, 128))
     fill(b("PT", 0, 1), 2048.0)
 
     def late_constants():
         for k in range(3):
-            cp(b("CH", CHP[k], CHP[k + 1]), b("CHI", CHP[k], CHP[k + 1]))
-        const(b("CH", M, ROOM), 0)
+            if k == 2:
+                cp(b("CH", CHP[k], CHP[k + 1]), b("CHI", CHP[k], CHP[k + 1]))
+            else:
+                keep(b("CH", CHP[k], CHP[k + 1]), b("CHI", CHP[k], CHP[k + 1]), [[0, CHP[k + 1] - CHP[k]]], OP.is_ge, 0.0, 0, 0)
         const(b("NONE"), -1)
         iota(b("ROWB"), [[0, 8], [4096, 16]], 0)
         keep(b("WI"), b("IDB"), DIAG, OP.not_equal, 2.0 ** 26)
-        keep(b("D8"), b("ONES", 0, 64), [[0, 8], [1, 8]], OP.is_gt, 0.0, 0, 0)
+        const(b("m", 0, 8), 0)
         x = b("EF", 0, 128)
         fill(x, 0.5)
         op("v", lambda: V.tensor_tensor_scan(b("EF", 128, 256)[4], b("EF", 0, 128)[4], b("NONE")[4], 2.0 ** 64, OP.mult, OP.max),
@@ -298,21 +400,20 @@ def rank_program(g, core, T, topo):
             const(b("SND%d" % h, 0, CAP), 0)
             const(b("RCV%d" % h, CAP, L), 0)
         const(b("SEL"), 1)
-        keep(b("SEL"), b("SEL"), [[-1, 2], [-16, 8]], OP.is_equal, 0.0)
+        keep(b("SEL"), b("SEL"), [[-16, 8], [-1, 2]], OP.is_equal, 0.0)
         x = b("bias", 4, 5)
         const(x, 0)
         keep(x, x, [[0, 1]], OP.is_ge, c0, -16)
         keep(x, x, [[0, 1]], OP.is_ge, -8.0, -8)
         cp(b("thf", 0, 1), b("thi", 0, 1))
-        ts(b("TB"), b("SEL", 0, 8), b("thf", 0, 1), OP.mult)
+        ts(b("TB"), b("SEL", 0, 16, 2), b("thf", 0, 1), OP.mult)
         mm(b("MB", 64, 72), b("ONES", 0, 128), b("TB"))
         act(b("THK"), b("MB", 64, 72), AF.Identity, scale=65536.0, bias=8.0 * 65536)
-        iota(b("K4096"), [[128, 2], [0, 8]], 4096, 1)
+        iota(b("K4096", 0, 2), [[-128, 2]], -4096, -1)
         iota(b("KC"), [[16, 16]], 0)
         act(b("bias", 5, 6), P15, AF.Identity, bias=4096.0)
         for h in range(2):
             act(b("bias", 2 + h, 3 + h), b("bias", 5, 6), AF.Identity, scale=-1.0, bias=b("bias", 6 + h, 7 + h))
-            const(b("CL%d" % h, 0, 4096), 0)
         x = b("SELG", rows=16)
         keep(x, b("ONES", 0, 1024, rows=16), [[-2, 8], [0, 128]], OP.is_ge, 0.0)
         keep(x, x, [[2, 8], [0, 128]], OP.is_ge, 0.0, 1, -1)
@@ -320,12 +421,14 @@ def rank_program(g, core, T, topo):
         keep(b("DGL"), b("DGL"), DIAG, OP.is_equal, 0.0)
         for k in range(4):
             keep(b("DGB", 128 * k, 128 * k + 128), b("IDB"), DIAG, OP.not_equal, float(M + 128 * k))
-        ts(b("LI", 72, 76), b("li", 72, 76), P3, OP.add)
+        ts(BH, b("li", 72, 80), P3, OP.add)
         ts(b("pi", 4, 5), b("pi", 0, 1), 7, OP.bitwise_and)
-        cp(b("LI", 76, 77), b("pi", 4, 5))
+        cp(DUP, b("pi", 4, 5))
+        act(b("pf", 4, 5), P3, AF.Identity, scale=8.0, bias=P15)
+        ts(b("LI", 82, 86), b("li", 72, 76), 2.0, OP.mult, b("pf", 4, 5), OP.add)
 
     def share(t, p, h):
-        return NVL[h] if (t, p) == (VI - 1, 4) else NV[p][h]
+        return NVL[h] if (t, p) == (VI - 1, 4) else NV0[p][h] if t == 0 and p < 2 else NV[p][h]
 
     def begin(t):
         q0 = M + L * t
@@ -356,18 +459,21 @@ def rank_program(g, core, T, topo):
         for h in range(2):
             mm(b("SP2", 128 * h, 128 * h + 128), Qh[h], b("NIDB"))
         act(b("NQT"), b("SP2", 0, 256), AF.Copy)
-        act(b("DRB"), b("PT", 0, 128), AF.Copy, off=b("OFF"))
-        mm(b("SP3", 0, 256), b("IDB"), b("DRB"), True, False)
-        mm(b("SP3", 0, 256), b("NIDB"), Q, False, True)
-        act(b("DRB"), b("SP3", 0, 256), AF.Abs)
+        if DRV:
+            tg(b("DRB"), b("PT", 0, 128), b("OFF"), Q, OP.subtract)
+            act(b("DRB"), b("DRB"), AF.Abs)
+        else:
+            act(b("DRB"), b("PT", 0, 128), AF.Copy, off=b("OFF"))
+            mm(b("SP3", 0, 256), b("NIDB"), Q, True, False)
+            mm(b("SP3", 0, 256), b("IDB"), b("DRB"), False, True)
+            act(b("DRB"), b("SP3", 0, 256), AF.Abs)
         if t:
             for h in range(2):
                 mm(b("MA", 16 * h, 16 * h + 16), b(r, 128 * h, 128 * h + 128), b("SEL"), f32=True, ext=t - 1)
             tt(b("PM"), b("MA", 0, 32), b("FR", 32 * t, 32 * t + 32), OP.max)
             ts(b("PD"), b("PM"), 4, OP.arith_shift_right, 2 ** 18 - 1, OP.bitwise_and)
             ts(b("B0C"), b("PD"), -c0, OP.add)
-            for h in range(2):
-                act(b("RKS%d" % h, 0, 64, 8), b("B0C", 16 * h, 16 * h + 8), AF.Identity, scale=65536.0 * U, bias=(c0 - 0.5) * 65536 * U)
+            act(b("RKS", 2, 128, 8), b("B0C", 0, 32, 2), AF.Identity, scale=65536.0 * U, bias=(c0 - 0.5) * 65536 * U)
         cp(b("RT"), b("sj"))
         for h in range(2):
             mm(b("MA", 48 + 8 * h, 56 + 8 * h), b("DRB", 128 * h, 128 * h + 128), b("LCB"))
@@ -379,8 +485,7 @@ def rank_program(g, core, T, topo):
         act(b("K0"), b("MA", 32, 48), AF.Identity, bias=CO + 32768 + 1)
         tg(b("E"), b("D0"), BC16, b("RAMP"), OP.subtract)
         act(b("A"), b("E"), AF.Abs, scale=65536.0 * U, bias=-CO * U)
-        for h in range(2):
-            tt(b("RKS%d" % h, 1, 64, 8), b("RKS%d" % h, 0, 64, 8), b("K0U", 8 * h, 8 * h + 8), OP.min)
+        tt(b("RKS", 3, 128, 8), b("RKS", 2, 128, 8), b("K0U"), OP.min)
 
     def push(t, h, p):
         hs = str(h)
@@ -393,7 +498,8 @@ def rank_program(g, core, T, topo):
         pt = b("PT", 0, 4096)
         op("v", lambda: V.tensor_copy(n("PU")[4], ch[4].indirect(off[4])), [ch, off], [n("PU")], FV + 128 * GA * CY)
         act(n("Pf"), ch, AF.Identity, bias=b("bias", p // 4, p // 4 + 1), scale=1.0 if p == 4 else U, off=off)
-        tg(n("M1"), n("RKS"), BCS[p + 1 if p else 0], A, OP.is_lt)
+        rks = b("RKS", 64 * h, 64 * h + 64)
+        tg(n("M1"), rks, BCS[p + 1 if p else 0], A, OP.is_lt)
         mm(kp, n("Pf"), b("IDF"), True, False, f32=True)
         mm(kp, b("WI" if p == 4 else "IDB"), n("M1"), False, False)
         if p in (2, 3):
@@ -401,19 +507,26 @@ def rank_program(g, core, T, topo):
         nv = share(t, p, h)
         v0 = 128 - nv if h == 0 else 0
         s0 = 0 if h == 0 else nv
-        ns = (128 - nv + 31) // 32
-        cut = [s0 + (128 - nv) * k // ns // 2 * 2 for k in range(ns)] + [s0 + 128 - nv]
-        for k in range(ns):
-            lo, hi = cut[k], cut[k + 1]
-            d = b("DIFF", 2048 * h + 16 * lo, 2048 * h + 16 * hi)
+        c = 16 * (128 - nv)
+        r0 = 1536 - c if h == 0 else 1536
+        cut = [r0] + [x for x in range(512, 3072, 512) if r0 < x < r0 + c] + [r0 + c]
+        parts = [[k] for k in range(len(cut) - 1)] if SP > 2 else [list(range(len(cut) - 1))] if SP == 1 else [[0], list(range(1, len(cut) - 1))]
+        if h == 0 and SP == 2:
+            parts = [list(range(len(cut) - 2)), [len(cut) - 2]]
+        for k, part in enumerate(x for x in parts if x):
+            at = lambda x: 16 * s0 + x - r0
+            lo, hi = cut[part[0]], cut[part[-1] + 1]
+            d = b("DIFF", 2048 * h + at(lo), 2048 * h + at(hi))
             slot[2] = "get%d" % k
-            act(d, pt, AF.Copy, off=n("PU", lo, hi))
-            ps = b("SP%d" % (rot[0] % 4), 0, 16 * (hi - lo))
-            rot[0] += 1
-            mm(ps, b("NQT", 128 * h, 128 * h + 128), b("R", 16 * lo, 16 * hi), True, False)
+            act(d, pt, AF.Copy, off=n("PU", at(lo) // 16, at(hi) // 16))
+            banks = [b(RING[cut[j] // 512], cut[j] % 512, cut[j] % 512 + cut[j + 1] - cut[j]) for j in part]
+            for j, ps in zip(part, banks):
+                slot[2] = "get%d" % k
+                mm(ps, b("NQT", 128 * h, 128 * h + 128), b("R", at(cut[j]), at(cut[j + 1])), True, False)
             slot[2] = "abs%d" % k
-            mm(ps, b("IDB"), d, False, True)
-            act(d, ps, AF.Abs)
+            for j, ps in zip(part, banks):
+                mm(ps, b("IDB"), b("DIFF", 2048 * h + at(cut[j]), 2048 * h + at(cut[j + 1])), False, True)
+            op("s", lambda d=d, lo=lo, hi=hi: S.activation(d[4], T.RING[:, lo:hi], AF.Abs), banks, [d], FS + (hi - lo) * CY)
         cut = [v0 + nv * k // VP // 2 * 2 for k in range(VP)] + [v0 + nv]
         for k in range(VP if nv else 0):
             lo, hi = cut[k], cut[k + 1]
@@ -427,9 +540,9 @@ def rank_program(g, core, T, topo):
         scan(n("KS"), b("MX"), kp, OP.max, OP.min)
         if p == 4:
             return
-        tt(n("RKS", p + 2, 64, 8), n("RKS", p + 1, 64, 8), n("KS", 15, 128, 16), OP.min)
+        tt(b("RKS", 64 * h + p + 4, 64 * h + 64, 8), b("RKS", 64 * h + p + 3, 64 * h + 64, 8), n("KS", 15, 128, 16), OP.min)
         if p == 0:
-            tg(n("M2"), n("RKS"), BCS[2], A, OP.is_lt)
+            tg(n("M2"), rks, BCS[2], A, OP.is_lt)
         else:
             tg(n("M2"), n("KS"), BC15, A, OP.is_lt)
         tt(n("KM"), kp, n("M2"), OP.add)
@@ -451,36 +564,47 @@ def rank_program(g, core, T, topo):
             tt(n("RP"), sk, n("RB"), OP.min)
             tg(n("ST"), n("RP"), BC8, b("ROWB"), OP.is_equal)
         else:
-            ts(dk, sk, 2.0 ** -16, OP.mult)
+            dk = b("D0", 8 * h, 8 * h + 8)
+            act(dk, n("MS", 15, 128, 16), AF.Identity, scale=1 / (65536 * U), bias=RND)
         if p == 0:
             ts(n("FB"), sk, 32768.0, OP.add)
         e = b("E", 128 * h, 128 * h + 128)
-        tg(e, dk, BC8, b("RAMP", 0, 128), OP.subtract)
+        tg(e, dk, BC8, b("RAMP", 0, 128) if p in (1, 2) else b("RAMQ"), OP.subtract)
         act(A, e, AF.Abs, scale=65536.0 * U, bias=-15.5 * 65536 * U)
-        if p == 3:
-            ts(n("Tp"), n("RKS", 5, 64, 8), 1 / U, OP.mult, 32768.0, OP.add)
-            ts(n("T3"), n("Tp"), -65536, OP.bitwise_and)
-            ts(n("thr"), n("T3"), 32768.0, OP.add, U, OP.mult)
-            tg(n("m"), n("thr"), BH, n("RKS"), OP.is_gt)
-            tt(n("x"), n("m"), n("RKS"), OP.mult)
-            scan(n("sc"), b("D8"), n("x"), OP.mult, OP.max)
-            ts(n("ki"), n("sc", 7, 64, 8), 1 / U, OP.mult)
-            ts(n("W", 8, 16), n("ki"), 4095, OP.bitwise_and)
+        if (p, h) == (3, 1):
+            ts(b("Tp"), b("RKS", 7, 128, 8), 1 / U, OP.mult, 32768.0, OP.add)
+            ts(b("T3"), b("Tp"), -65536, OP.bitwise_and)
+            ts(b("thr"), b("T3"), 32768.0, OP.add, U, OP.mult)
+            tg(b("m", 8, 136), b("thr"), BH, b("RKS"), OP.is_gt)
+            scan(b("sc"), b("m", 7, 135), b("RKS"), OP.mult, OP.max)
+            ts(b("ki"), b("sc", 7, 128, 8), 1 / U, OP.mult)
+            ts(b("W", 16, 32), b("ki"), 4095, OP.bitwise_and)
             if t:
-                ts(n("z3"), n("W", 8, 16), 0.0, OP.is_equal)
-                tt(n("z3"), n("z3"), b("B0C", 16 * h + 8, 16 * h + 16), OP.mult)
+                ts(b("y"), b("W", 16, 32), 0.0, OP.is_equal)
+                tt(b("y"), b("y"), b("B0C", 1, 32, 2), OP.mult)
             else:
-                ts(n("z3"), n("W", 8, 16), 0.0, OP.is_equal, -c0, OP.mult)
-            tt(n("W", 0, 8), n("z3"), n("W", 8, 16), OP.add)
+                ts(b("y"), b("W", 16, 32), 0.0, OP.is_equal, -c0, OP.mult)
+            tt(b("W", 0, 16), b("y"), b("W", 16, 32), OP.add)
+        if (p, h) == (1, 0) and t:
+            outputs(t - 1)
+
+    def outputs(t):
+        slot[2] = "out"
+        for k in range(2):
+            mm(b("MB", 128 * k, 128 * k + 128, 1, 32), b("OUT%d" % k), b("IDF"), f32=True, also=b("KS0"))
+        act(b("OB%d" % t, 0, L, 1, 32), b("MB", 0, L, 1, 32), AF.Identity, bias=b("bias", 4, 5, 1, 32))
+        for k, out in ((0, T.yr), (1, T.yb), (3, T.yp)):
+            o = b("OB%d" % t, 0, L, 1, 8, 8 * k)
+            dma("y", out[:, t * L:(t + 1) * L], o[4], [o], [o], 2.0)
 
     def finish(t, h):
         hs = str(h)
         n = lambda x, *a: b(x + hs, *a)
-        pa, pb, po, pg = (("KP0", "KP0", 256, "KP0"), ("KP1", "SP0", 0, "SP1"))[h]
-        pairs = (("MA", "MB"), ("SP2", "SP3"))[h]
+        pa, pb, po, pg = (("KP0", "SP0", 0, "SP1"), ("KP1", "SP2", 0, "SP3"))[h]
+        pairs = ("MA", "MB")
         q = b("PT", M + L * t + 128 * h, M + L * t + 128 * h + 128)
-        Rr, node = n("RI", 0, 8), n("RI", 16, 24)
-        tt(n("V4"), n("KS", 15, 128, 16), n("T3"), OP.min)
+        Rr, node = n("RI", 0, 8), n("OUT", 16, 24)
+        tt(n("V4"), n("KS", 15, 128, 16), b("T3", 8 * h, 8 * h + 8), OP.min)
         if t < VI - 1:
             tt(n("near"), n("V4"), b("THK"), OP.is_lt)
             mm(b(pa, 136, 144), b("LTD" + hs), n("near"), True, h == 0)
@@ -491,11 +615,11 @@ def rank_program(g, core, T, topo):
         op("v", lambda: V.tensor_scalar(n("n4")[4], n("V4")[4].indirect(DUP[4]), 4095, None, OP.bitwise_and),
            [n("V4"), DUP], [n("n4")], FV + 16 * GA * CY)
         ts(n("z"), n("n4"), 0.0, OP.is_equal)
-        tt(n("z"), n("z"), n("W"), OP.mult)
-        tt(n("RI", 8, 24), n("z"), n("n4"), OP.add)
+        tg(n("zw"), b("W"), PICK[h], n("z"), OP.mult)
+        tt(n("OUT", 8, 24), n("zw"), n("n4"), OP.add)
+        cp(n("OUT", 0, 8), Rr)
         ob = b("OB%d" % t, 128 * h, 128 * h + 128, 1, 32 if t < VI - 1 else 16)
         if t == VI - 1:
-            cp(n("OUT", 0, 16), n("RI", 0, 16))
             mm(b(pa, 256, 384, 1, 16), n("OUT", 0, 16), b("IDF"), f32=True)
             act(ob, b(pa, 256, 384, 1, 16), AF.Identity, bias=b("bias", 4, 5, 1, 16))
             for k, (qn, out) in enumerate((("y", T.yr), ("s" if h else "y", T.yb))):
@@ -504,13 +628,12 @@ def rank_program(g, core, T, topo):
             return
         kc = b("KC", 8 * h, 8 * h + 8)
         z1 = n("ZZ", 128, 256)
-        tt(n("DG", 8, 16), node, b("K4096", 8 * h, 8 * h + 8), OP.subtract)
+        act(n("DG", 8, 16), node, AF.Identity, bias=b("K4096", h, h + 1))
         tg(n("ZZ"), n("DG"), BC16, b("DM"), OP.mult)
         mm(b(pa, 144, 152), n("ZZ", 0, 128), b("LC"), f32=True)
         mm(b(pa, 152, 160), b("IDB"), kc, True, False)
         mm(b(pa, 152, 160), z1, b("LC"), False, True, f32=True)
         ts(n("OG"), b(pa, 144, 160), b("bias", 5, 6), OP.add)
-        cp(n("OUT", 0, 24), n("RI"))
         act(n("PK", 0, 128, 16), n("OUT", 0, 8), AF.Identity, scale=16.0, bias=FLAG)
         act(n("PK", 1, 128, 16), n("OUT", 8, 16), AF.Identity, scale=16.0, bias=FLAG + 16 * c0)
         mm(b(pb, po, po + 128), b("IDB"), q, True, False)
@@ -524,8 +647,9 @@ def rank_program(g, core, T, topo):
             rid, pid, _x = topo.addr(dst)
             op("g", lambda: g.remote_dma(T[rcv][:, 0:CAP], T[snd][:, 0:CAP], T.sem["arr%d" % t], T.sem["sent%d" % t], pid, rid, topo.mask(core, dst)),
                [b(snd, 0, CAP)], [], 0.1, "r", t)
+        tag[0] = "g" + tag[0][1:]
         act(n("GC"), b("CH", 0, 4096), AF.Copy, off=n("OG", 8, 16))
-        cp(n("NQ", 0, 16, 2), node)
+        act(n("NQ", 0, 16, 2), node, AF.Copy)
         tt(n("NQ", 1, 16, 2), node, n("NQ", 0, 16, 2), OP.subtract)
         mm(b(pg, 0, 128, 1, 16), n("NQ"), b("IDB"))
         nt = b("NT" + hs, 0, 128, 1, 16)
@@ -546,40 +670,27 @@ def rank_program(g, core, T, topo):
                 act(b("EF", 128 * gg, 128 * gg + 128), ps, AF.Abs, scale=-1.0, bias=cc)
             else:
                 ts(n("EQ", 128 * gg, 128 * gg + 128), ps, cc, OP.is_equal, wl, OP.mult)
-        act(n("EQ", 0, 128 * ns), b("EF", 0, 128 * ns), AF.Relu, scale=nwl, bias=wl)
+        for lo in range(0, ns, 4):
+            hi = min(ns, lo + 4)
+            act(n("EQ", 128 * lo, 128 * hi), b("EF", 128 * lo, 128 * hi), AF.Relu, scale=nwl, bias=wl)
         tt(n("OC"), b(pb, po + 128, po + 256), n("GC"), OP.mult)
         mm(b(pg, 160, 168), b("WI"), n("near"), True, False)
-        cl = b("CL%d" % t)
         if h:
-            act(b("CG"), b(cl[0], 0, 4096), AF.Copy, off=n("OG", 8, 16))
+            act(b("CG"), n("GC"), AF.Relu, bias=1.0 - M - L * t)
             mm(b(pg, 160, 168), b("CG"), b("BLK"), False, False)
         mm(b(pg, 160, 168), n("OC"), b("LC2"), False, True)
         tt(n("can"), node, b(pg, 160, 168), OP.is_gt)
         mm(b(pg, 168, 176), b("WD"), n("can"), True, False)
         for gg in range(8):
             mm(b(pg, 168 + gg, 169 + gg), n("EQ", 128 * gg, 128 * gg + 128), n("can", gg, gg + 1), False, gg == 7)
-        if h:
-            mm(b(pa, 176, 184), b("IDB"), kc, True, False)
+        mm(b(pa, 176, 184), b("IDB"), kc, True, False)
         ts(n("win"), b(pg, 168, 176), 0.0, OP.is_lt)
-        if not h:
-            mm(b(pa, 176, 184), b("IDB"), kc, True, False)
         tg(n("Z2"), n("win"), BC8, z1, OP.mult)
         mm(b(pa, 176, 184), n("Z2"), b("LC"), False, True, f32=True)
         ts(n("G2"), b(pa, 176, 184), b("bias", 5, 6), OP.add)
-        if h == 0:
-            one = b("ONES", 0, 128)
-            op("v", lambda: V.tensor_copy(cl[4].indirect(n("G2")[4]), one[4]), [one, n("G2")], [cl], FV + 128 * SCA * CY)
         op("v", lambda: V.tensor_tensor(b("CH")[4].indirect(n("G2")[4]), n("GC")[4], n("ON")[4], OP.add),
            [n("GC"), n("ON"), n("G2")], [b("CH")], FV + 128 * SCA * CY)
         tt(n("OUT", 24, 32), n("win"), node, OP.mult)
-        if h:
-            for k in range(2):
-                mm(b("MB", 128 * k, 128 * k + 128, 1, 32), b("OUT%d" % k), b("IDF"), f32=True)
-            act(b(ob[0], 0, L, 1, 32), b("MB", 0, L, 1, 32), AF.Identity, bias=b("bias", 4, 5, 1, 32))
-        if h:
-            for k, out in ((0, T.yr), (1, T.yb), (3, T.yp)):
-                o = b(ob[0], 0, L, 1, 8, 8 * k)
-                dma("y", out[:, t * L:(t + 1) * L], o[4], [o], [], 2.0)
 
     for t in range(VI):
         tag[0] = "b%d" % t
@@ -597,7 +708,6 @@ def rank_program(g, core, T, topo):
             finish(t, h)
 
     n = len(ops)
-    WAKE = 0.08
     cost = [o["cost"] for o in ops]
     more = [o["ext"] if o["kind"] == "d" else 3.0 if o["kind"] == "r" else 0.0 for o in ops]
     fwd = [[] for _ in range(n)]
@@ -646,11 +756,14 @@ def rank_program(g, core, T, topo):
             if o["lab"] in WHEN:
                 due[i] = (10 * HALF + GAP) * t + (2 * p + h) * HALF + WHEN[o["lab"]]
     for i in range(n):
-        if ops[i]["tag"][:1] == "f" and ops[i]["tag"][2] == "A":
+        if ops[i]["tag"][:1] in ("f", "g") and ops[i]["tag"][2] == "A":
             due[i] -= EARLY
-    order, at = place(fwd, [-x for x in due], [0.0] * n)
+    if "order" not in ORDER:
+        at = place(fwd, [-x for x in due], [0.0] * n)[1]
+        ORDER["order"], ORDER["at"] = improve(sorted(range(n), key=lambda i: (at[i], i)), [o["q"] for o in ops], cost, more, fwd)
+    order = ORDER["order"]
     for i in range(n):
-        ops[i]["t0"] = at[i]
+        ops[i]["t0"] = ORDER["at"][i]
 
     QS = {"v": V, "t": TE, "s": S, "g": g, "y": g.sync}
     CS = {"v": "cv", "t": "ct", "s": "cs", "g": "cg"}

@@ -2,25 +2,32 @@ from concourse.mybir import AluOpType as OP, ActivationFunctionType as AF
 
 N, L, CAP, M, VI = 4, 256, 192, 3584, 3
 U = 2.0 ** -26
+WIDE = 17.0 * 4096
 BIG = float(2 ** 60)
-RND = 1.5 * 2 ** 23
 CO = 7.5 * 65536
 FLAG = float(2 ** 22)
 ROOM = 4096 + 256
 SNDW = 1280
-NV = ((70, 62), (56, 52), (52, 52), (52, 54), (52, 64))
-NV0 = ((76, 66), (58, 52))
+NV = ((60, 52), (46, 42), (42, 42), (42, 46), (40, 64))
+NV0 = ((66, 54), (46, 42))
 DRV = True
-NVL = (72, 88)
+PUS = False
+OFS = False
+NVL = (50, 76)
+VA, KSP, KG = 2, False, 8
 VP = 2
 SP = 2
-QV = 7
+QV = 8
 GSC = (4, 6)
 HALF, GAP, LOOK, EARLY = 4.97, 18.0, 0.07, 2.3
 WHEN = {'vPU0': 0.83, 'vvec0': 2.6, 'vvec1': 2.85, 'vM0': 2.48, 'vKS0': 6.82, 'vRKS0': 7.81, 'vM1': 3.2, 'vKM0': 11.11, 'vMS0': 7.1, 'vz0': 7.44, 'vSK0': 5.26, 'vNN0': 7.1, 'vZ0': 5.7, 'vDK0': 8.03, 'vE0': 12.79, 'vOFF0': 8.24, 'vRB0': 7.77, 'vRP0': 9.84, 'vST0': 7.42, 'vFB0': 13.5, 'sget0': -0.16, 'sget1': 2.04, 'sPf0': 3.05, 'svec0': 2.69, 'sabs0': 3.0, 'sabs1': 1.92, 'svec1': 3.67, 'sA0': 12.3, 'tget0': 5.37, 'tabs0': 0.41, 'tget1': 2.4, 'tabs1': 5.16, 'tPf': 3.47, 'tkey': 2.85, 'tlist': 3.84, 'sD0': 4.51,
-        "vTp0": 8.0, "vT0": 8.0, "vthr0": 8.0, "vm0": 8.0, "vsc0": 8.0, "vki0": 8.0, "vW0": 8.0, "vy0": 8.0, "vy1": 8.0, "vW1": 8.0}
-ROUNDS = 15000
-FIX, WAKE = (0.07, 0.065, 0.01), 0.1
+        "tkez": 2.8, "vvec2": 3.0, "vvec3": 3.2, "vvec4": 3.4, "vvec5": 3.6, "svec2": 3.8, "sDK0": 8.0, "sDS0": 8.5, "sOFF0": 8.2, "sy0": 8.0, "sFB0": 12.0, "vTp0": 6.0, "vT0": 6.0, "vthr0": 6.0, "vm0": 6.0, "vsc0": 6.0, "vki0": 6.0, "vW0": 6.0, "vy0": 6.0, "vy1": 6.0, "vW1": 6.0}
+WHEN = {'sA0': 14.05, 'sPf0': 2.05, 'sabs0': 3.39, 'sabs1': -15.79, 'sget0': -2.15, 'sget1': 3.3, 'svec0': 2.89, 'tPf': 2.12, 'tabs0': 1.27, 'tabs1': 6.58, 'tget0': 2.43, 'tget1': -0.73, 'tkey': 3.6, 'tlist': -1.05, 'vDK0': 9.61, 'vDS0': 9.82, 'vE0': 23.88, 'vFB0': 24.54, 'vKM0': 10.8, 'vKS0': 9.72, 'vM0': 1.82, 'vM1': -12.36, 'vMS0': -17.94, 'vNN0': 8.71, 'vOFF0': -19.34, 'vPU0': -1.82, 'vRB0': 11.03, 'vRKS0': 2.41, 'vRP0': 24.86, 'vSK0': 1.07, 'vST0': 11.0, 'vT0': 8.99, 'vTp0': 0.57, 'vW0': 9.0, 'vY0': 9.24, 'vZ0': 0.62, 'vki0': -8.34, 'vm0': -13.12, 'vsc0': 5.83, 'vthr0': 9.0, 'vvec0': 2.73, 'vvec1': 3.79, 'vy0': 9.0, 'vz0': 12.31}
+WHEN = {'sA0': 10.3, 'sPf0': -2.94, 'sabs0': 5.99, 'sabs1': -16.03, 'sget0': -3.36, 'sget1': 0.91, 'svec0': 4.87, 'tPf': 1.92, 'tabs0': 5.5, 'tabs1': 9.09, 'tget0': 1.71, 'tget1': 0.33, 'tkey': -0.55, 'tlist': 2.81, 'vDK0': 12.77, 'vDS0': 9.52, 'vE0': 17.18, 'vFB0': 36.43, 'vKM0': 5.46, 'vKS0': 12.54, 'vM0': 0.41, 'vM1': -6.44, 'vMS0': -19.19, 'vNN0': 12.0, 'vOFF0': -36.48, 'vPU0': -0.93, 'vRB0': 17.61, 'vRKS0': 2.22, 'vRP0': 36.68, 'vSK0': 2.61, 'vST0': 5.41, 'vT0': 10.68, 'vTp0': 5.99, 'vW0': 19.94, 'vY0': 19.51, 'vZ0': 3.84, 'vki0': -30.94, 'vm0': -18.97, 'vsc0': 0.84, 'vthr0': 17.12, 'vvec0': 4.0, 'vvec1': 2.9, 'vy0': 1.69, 'vz0': 17.89}
+HALF, GAP, LOOK, EARLY = 9.66, 46.6, 0.1, -2.05
+ROUNDS = 30000
+CY, GA, GT, SCA, CS, CT, FI = 0.00089, 1.56, 1.6, 3.8, 0.83, 0.88, 0.065
+FIX, WAKE, FAR = (0.05, 0.09, 0.0), 0.145, 3.0
 WHEN0 = {"vPU0": 0.0, "vvec0": 0.25, "vvec1": 1.6, "vvec2": 2.0, "vvec3": 2.3, "vM0": 1.2, "vKS0": 5.9, "vRKS0": 6.1, "vM1": 6.2, "vKM0": 6.9, "vMS0": 7.2,
         "vz0": 7.4, "vSK0": 7.5, "vNN0": 7.7, "vZ0": 7.9, "vDK0": 8.1, "vE0": 8.3, "vOFF0": 8.6, "vRB0": 7.3, "vRP0": 8.4, "vST0": 10.0,
         "vFB0": 10.0, "sget0": 0.3, "sget1": 0.9, "sget2": 1.5, "sget3": 2.0, "sPf0": 2.0, "svec0": 2.2, "sabs0": 2.6, "sabs1": 3.0,
@@ -55,33 +62,33 @@ for _k, _n in enumerate(RING):
     VIRT[_n] = ("RING", 512 * _k, 512)
     PS.add(_n)
 _own("PT", M + VI * L, "bfloat16"); _own("CHI", M, "int32"); _own("CH", ROOM)
-_own("wi", 8, "int32"); _own("thi", 8, "int32"); _own("r0i", 128, "int32")
+_own("wi", 8, "int32"); _own("wn", 8, "int32"); _own("thi", 8, "int32"); _own("r0i", 128, "int32")
 _own("Q16", 4096, "bfloat16"); _own("DIFF", 4096, "bfloat16")
 for _t in "01":
     _own("SND" + _t, SNDW); _own("RCV" + _t, L)
 for _t in "012":
     _own("OB" + _t, 256)
 for _n, _c in (("r0f", 128), ("wf", 2), ("thf", 2), ("pf", 8), ("j15", 256), ("c8", 8), ("IDF", 128), ("DM", 256),
-               ("LC", 8), ("RAMP", 256), ("RAMQ", 128), ("MX", 128), ("ROWB", 128), ("bias", 8), ("THK", 8), ("K4096", 16),
-               ("SEL", 16), ("FR", 96), ("E", 256), ("A", 256), ("K0", 16), ("K0U", 16), ("D0", 16), ("WL", 2), ("B0C", 32), ("EF", 1024),
-               ("RKS", 128), ("thr", 16), ("m", 136), ("sc", 128), ("y", 16)):
+               ("LC", 8), ("MX", 128), ("ROWB", 128), ("bias", 8), ("THK", 8), ("K4096", 16),
+               ("SEL", 32), ("FR", 192), ("THX", 384), ("A", 256), ("K0", 16), ("K0U", 16), ("WL", 2), ("B0C", 16), ("EF", 1024),
+               ("RKS", 128), ("thr", 16), ("m", 136), ("sc", 128), ("y", 16), ("Y", 16)):
     _s(_n, _c)
-for _n, _c in (("pi", 8), ("li", 96), ("si", 16), ("sj", 16), ("DK", 16), ("MI", 192), ("QI", 192), ("PM", 32), ("PD", 32),
-               ("Tp", 16), ("T3", 16), ("ki", 16), ("W", 32)):
+for _n, _c in (("pi", 8), ("li", 120), ("sm", 16), ("sn", 16), ("DK", 16), ("MI", 192), ("QI", 192), ("PM", 64), ("PD", 64),
+               ("Tp", 16), ("T3", 16), ("ki", 16), ("W", 16)):
     _s(_n, _c, "int32")
-for _n, _c in [("IDB", 128), ("NIDB", 128), ("WI", 128), ("BLKU", 8), ("BLK", 8), ("LCB", 8), ("LC2", 8), ("WB", 8), ("WD", 128), ("RT", 16),
-               ("LTD0", 128), ("LTD1", 128), ("ONES", 2048), ("R", 2048), ("TB", 8), ("SELG", 1024), ("ZR", 256), ("D8", 64),
+for _n, _c in [("IDB", 128), ("NIDB", 128), ("WI", 128), ("BLKU", 8), ("BLKW", 8), ("BLK", 8), ("LCB", 8), ("LC2", 8), ("WB", 8), ("WD", 128), ("RT", 16),
+               ("RL", 32), ("WN", 8), ("ONES", 2048), ("R", 2048), ("TB", 8), ("SELG", 1024), ("ZR", 256), ("E", 256), ("GO", 256), ("DS", 256),
                ("DRB", 256), ("NQT", 256), ("DGL", 128), ("DGB", 128 * 4), ("NONE", 128), ("KC", 16), ("CG", 128)]:
     _s(_n, _c, "bfloat16")
-_s("LI", 96, "uint16"); _s("OFF", 16, "uint16")
+_s("LI", 136, "uint16"); _s("OFF", 16, "uint16")
 for _h in "01":
     for _n, _c, _d in (("PU", 128, "uint16"), ("Pf", 128, "float32"), ("M1", 128, "bfloat16"), ("M2", 128, "bfloat16"),
                        ("ST", 128, "bfloat16"), ("KS", 128, "float32"), ("KM", 128, "float32"), ("MS", 128, "float32"),
                        ("SK", 32, "int32"), ("NN", 8, "int32"), ("FB", 8, "int32"),
                        ("Z", 128, "float32"), ("RB", 8, "int32"), ("RP", 8, "int32"),
                        ("z3", 8, "float32"), ("V4", 8, "int32"),
-                       ("n4", 16, "int32"), ("z", 16, "float32"), ("zw", 16, "float32"), ("RI", 24, "int32"), ("OUT", 32, "float32"), ("near", 8, "bfloat16"),
-                       ("DG", 16, "float32"), ("ZZ", 256, "float32"), ("OG", 16, "uint16"), ("PK", 128, "float32"), ("XS", 128, "float32"),
+                       ("n4", 8, "int32"), ("z", 8, "float32"), ("RI", 16, "int32"), ("OUT", 32, "float32"), ("NB", 384, "bfloat16"),
+                       ("gq", 8, "float32"), ("Z1", 128, "float32"), ("OP", 8, "uint16"), ("G1", 8, "uint16"), ("PK", 128, "float32"), ("XS", 128, "float32"),
                        ("GC", 128, "float32"),
                        ("bb", 8, "int32"), ("OH", 128, "bfloat16"), ("ON", 128, "float32"), ("OC", 128, "bfloat16"), ("can", 8, "bfloat16"),
                        ("win", 8, "float32"), ("Z2", 128, "float32"), ("G2", 8, "uint16"), ("NQ", 16, "bfloat16"),
@@ -91,7 +98,7 @@ for _d in POOL:
     SCRATCH[POOL[_d][0]] = ("sbuf", [128, POOL[_d][1]], _d)
 
 NDMA = 24
-SEMAPHORES = ["cv", "ct", "cs", "cg"] + ["d%d" % i for i in range(NDMA)] + ["arr0", "arr1", "sent0", "sent1"]
+SEMAPHORES = ["cv", "ct", "cs", "cg"] + ["d%d" % i for i in range(NDMA)] + ["arr0", "arr1", "arr2", "sent0", "sent1", "sent2"]
 
 
 ORDER = {}
@@ -238,7 +245,6 @@ def rank_program(g, core, T, topo):
         ops.append(d)
         return n
 
-    CY, GA, SCA = 0.00083 * 1.2, 1.56, 3.8
     FV, FS, FT = FIX
     two = ("poolb", "poolu", "PT", "Q16", "DIFF")
 
@@ -261,7 +267,7 @@ def rank_program(g, core, T, topo):
         op("v", lambda: V.tensor_tensor(out[4], a[4], c[4], o), [a, c], [out], vc(cols(out), k), "c", ext)
 
     def tg(out, win, off, c, o):
-        op("v", lambda: V.tensor_tensor(out[4], win[4].indirect(off[4]), c[4], o), [win, off, c], [out], FV + cols(out) * GA * CY)
+        op("v", lambda: V.tensor_tensor(out[4], win[4].indirect(off[4]), c[4], o), [win, off, c], [out], FV + cols(out) * GT * CY)
 
     def ts(out, a, s1, o1, s2=None, o2=None):
         x1 = s1[4] if isap(s1) else s1
@@ -276,7 +282,7 @@ def rank_program(g, core, T, topo):
         op("v", lambda: V.tensor_copy(out[4], a[4]), [a], [out], vc(cols(out), half(out, a)))
 
     def scan(out, d0, d1, o0, o1):
-        op("v", lambda: V.tensor_tensor_scan(out[4], d0[4], d1[4], 0.0, o0, o1), [d0, d1], [out], vc(cols(out)))
+        op("v", lambda: V.tensor_tensor_scan(out[4], d0[4], d1[4], 0.0, o0, o1), [d0, d1], [out], vc(cols(out), half(out, d0, d1)))
 
     def fill(out, x):
         op("v", lambda: V.memset(out[4], x), [], [out], vc(cols(out), half(out)))
@@ -289,11 +295,11 @@ def rank_program(g, core, T, topo):
             if isap(bias):
                 rd.append(bias)
         src = a[4] if off is None else a[4].indirect(off[4])
-        op("s", lambda: S.activation(out[4], src, f, **kw), rd, [out], FS + cols(out) * CY * (1 if off is None else GA))
+        op("s", lambda: S.activation(out[4], src, f, **kw), rd, [out], FS + cols(out) * CY * CS if off is None else FI + cols(out) * CY * CS * GA)
 
     def mm(out, l, r, start=True, stop=True, f32=False, ext=None, also=None):
         n = max(min(64, cols(l)), cols(r))
-        op("t", lambda: TE.matmul(out[4], l[4], r[4], start, stop), [l, r] + ([also] if also else []), [out], FT + n * (4 if f32 else 1) * CY, "c", ext)
+        op("t", lambda: TE.matmul(out[4], l[4], r[4], start, stop), [l, r] + ([also] if also else []), [out], FT + n * (4 if f32 else 1) * CY * CT, "c", ext)
 
     def dma(q, out, src, reads, writes, us):
         eng = g.sync if q == "y" else g.scalar
@@ -342,23 +348,23 @@ def rank_program(g, core, T, topo):
     P15, P4, P3 = [b("pf", k, k + 1) for k in range(1, 4)]
     cp(b("LI", 0, 16), b("li", 0, 16))
     cp(b("LI", 16, 72), b("li", 16, 72))
-    BC16, BC8, BC15, BH, DUP = b("LI", 0, 16), b("LI", 0, 8), b("LI", 16, 24), b("LI", 72, 80), b("LI", 80, 81)
-    PICK = [b("LI", 82 + 2 * h, 83 + 2 * h) for h in range(2)]
+    BC16, BC8, BC15, BH = b("LI", 0, 16), b("LI", 0, 8), b("LI", 16, 24), b("LI", 72, 80)
+    BC4, BC3 = b("LI", 96, 112), b("LI", 112, 136)
     BCS = [b("LI", 24 + 8 * s, 32 + 8 * s) for s in range(6)]
     ts(b("LC"), b("c8"), P4, OP.is_equal)
     cp(b("wf", 0, 1), b("wi", 0, 1))
     ts(b("WB"), b("LC"), b("wf", 0, 1), OP.mult)
     ts(b("DM"), b("j15"), P15, OP.is_equal)
-    for name, x in (("LCB", 1.0), ("BLK", 65536.0), ("BLKU", 65536.0 * U), ("LC2", 2.0)):
+    for name, x in (("LCB", 1.0), ("BLK", 65536.0), ("BLKU", 65536.0 * U), ("BLKW", WIDE), ("LC2", 2.0)):
         act(b(name), b("LC"), AF.Copy, scale=x)
     act(b("NIDB"), b("IDB"), AF.Copy, scale=-1.0)
     act(b("IDF"), b("IDB"), AF.Copy)
-    act(b("RAMP"), b("j15"), AF.Copy, scale=16.0)
-    act(b("RAMQ"), b("j15", 0, 128), AF.Identity, scale=16.0, bias=RND)
+    ts(b("GO"), b("j15"), 1.0, OP.min)
+    fill(b("DS"), -16.0)
     fill(b("MX"), -BIG)
     fill(b("MX", 0, 128, 16), BIG)
     act(b("bias", 0, 1), P15, AF.Identity, scale=4096.0 * U, bias=CO * U)
-    act(b("bias", 1, 2), P15, AF.Identity, scale=4096.0, bias=CO + 32768)
+    act(b("bias", 1, 2), P15, AF.Copy, scale=4096.0)
     cp(b("r0f", rows=48), b("r0i", rows=48))
     mm(b("MB", 0, 48), b("r0f", rows=48), b("IDF", 0, 48, rows=48), f32=True)
     const(b("FR"), 0)
@@ -366,7 +372,7 @@ def rank_program(g, core, T, topo):
     for h in range(2):
         act(b("RKS", 64 * h + 2, 64 * h + 64, 8), b("MB", h, 48, 6), AF.Identity, scale=65536.0 * U, bias=CO * U)
     for k in range(2, 6):
-        act(b("FR", 16 * k, 16 * k + 16, 2), b("MB", k, 48, 6), AF.Identity, scale=16.0, bias=128.0)
+        act(b("FR", 32 * k, 32 * k + 32, 4), b("MB", k, 48, 6), AF.Copy, scale=16.0)
     act(b("CH", M, ROOM), b("ONES", 0, ROOM - M), AF.Copy, scale=0.0)
     cp(b("CH", 0, 128), b("CHI", 0, 128))
     fill(b("PT", 0, 1), 2048.0)
@@ -390,30 +396,36 @@ def rank_program(g, core, T, topo):
         mm(b("MB", 80, 81), b("WD"), b("ONES", 0, 1))
         act(b("WL", 0, 1), b("MB", 80, 81), AF.Copy, scale=-0.4)
         act(b("WL", 1, 2), b("MB", 80, 81), AF.Copy, scale=0.4)
+        send(T.wn[:, 0:1], b("wi", 0, 1), -1, VI - 1)
+        ts(b("RL", 0, 8), b("c8"), P4, OP.is_gt, -1.0, OP.mult)
+        act(b("RL", 8, 16), b("LC"), AF.Copy, scale=-1.0)
+        iota(b("li", 80, 96), [[4, 16]], 3)
+        iota(b("li", 96, 120), [[0, 3], [1, 8]], 0)
+        cp(b("LI", 96, 136), b("li", 80, 120))
         for h in range(2):
-            x = b("LTD%d" % h)
-            iota(x, [[0, 128]], 256 * (h + 1), 2 * (h + 1))
-            keep(x, x, DIAG, OP.is_equal, 0.0)
-            keep(x, x, DIAG, OP.is_ge, -1.0)
-            iota(b("bias", 6 + h, 7 + h), [[0, 1]], 128 * h, 1)
+            iota(b("bias", 2 + h, 3 + h), [[0, 1]], 256 * (h + 1), 2 * (h + 1))
+            act(b("RL", 16 + 8 * h, 24 + 8 * h), b("LC"), AF.Copy, scale=b("bias", 2 + h, 3 + h))
             const(b("PK%d" % h), FLAG)
             const(b("SND%d" % h, 0, CAP), 0)
             const(b("RCV%d" % h, CAP, L), 0)
         const(b("SEL"), 1)
-        keep(b("SEL"), b("SEL"), [[-16, 8], [-1, 2]], OP.is_equal, 0.0)
+        keep(b("SEL"), b("SEL"), [[-16, 8], [-4, 4]], OP.is_equal, 0.0)
         x = b("bias", 4, 5)
         const(x, 0)
         keep(x, x, [[0, 1]], OP.is_ge, c0, -16)
-        keep(x, x, [[0, 1]], OP.is_ge, -8.0, -8)
+        keep(x, x, [[0, 1]], OP.is_ge, 0.0, -8)
         cp(b("thf", 0, 1), b("thi", 0, 1))
-        ts(b("TB"), b("SEL", 0, 16, 2), b("thf", 0, 1), OP.mult)
+        ts(b("TB"), b("SEL", 0, 32, 4), b("thf", 0, 1), OP.mult)
         mm(b("MB", 64, 72), b("ONES", 0, 128), b("TB"))
-        act(b("THK"), b("MB", 64, 72), AF.Identity, scale=65536.0, bias=8.0 * 65536)
+        act(b("THK"), b("MB", 64, 72), AF.Identity, scale=WIDE, bias=4096.0)
+        tg(b("THX", 0, 128), b("THK"), BC8, b("ONES", 0, 128), OP.mult)
+        ts(b("EF", 512, 640), b("j15", 0, 128), P15, OP.is_gt)
+        tg(b("THX", 128, 256), b("THK"), BC8, b("EF", 512, 640), OP.mult)
+        tg(b("THX", 256, 384), b("THK"), BC8, b("DM", 0, 128), OP.mult)
+        act(b("THX"), b("THX"), AF.Identity, bias=-8192.0)
         iota(b("K4096", 0, 2), [[-128, 2]], -4096, -1)
         iota(b("KC"), [[16, 16]], 0)
         act(b("bias", 5, 6), P15, AF.Identity, bias=4096.0)
-        for h in range(2):
-            act(b("bias", 2 + h, 3 + h), b("bias", 5, 6), AF.Identity, scale=-1.0, bias=b("bias", 6 + h, 7 + h))
         x = b("SELG", rows=16)
         keep(x, b("ONES", 0, 1024, rows=16), [[-2, 8], [0, 128]], OP.is_ge, 0.0)
         keep(x, x, [[2, 8], [0, 128]], OP.is_ge, 0.0, 1, -1)
@@ -422,10 +434,6 @@ def rank_program(g, core, T, topo):
         for k in range(4):
             keep(b("DGB", 128 * k, 128 * k + 128), b("IDB"), DIAG, OP.not_equal, float(M + 128 * k))
         ts(BH, b("li", 72, 80), P3, OP.add)
-        ts(b("pi", 4, 5), b("pi", 0, 1), 7, OP.bitwise_and)
-        cp(DUP, b("pi", 4, 5))
-        act(b("pf", 4, 5), P3, AF.Identity, scale=8.0, bias=P15)
-        ts(b("LI", 82, 86), b("li", 72, 76), 2.0, OP.mult, b("pf", 4, 5), OP.add)
 
     def share(t, p, h):
         return NVL[h] if (t, p) == (VI - 1, 4) else NV0[p][h] if t == 0 and p < 2 else NV[p][h]
@@ -437,18 +445,27 @@ def rank_program(g, core, T, topo):
         if t:
             r = "RCV%d" % (t - 1)
             mm(b("KP0", 0, CAP), b("IDB"), b("PT", q0, q0 + CAP))
+            for h in range(2):
+                mm(b("MA", 64 + 32 * h, 96 + 32 * h), b(r, 128 * h, 128 * h + 128), b("SEL"), f32=True, ext=t - 1)
+            tt(b("PM"), b("MA", 64, 128), b("FR", 64 * t, 64 * t + 64), OP.max)
+            ts(b("PD"), b("PM"), 4, OP.arith_shift_right, 2 ** 18 - 1, OP.bitwise_and)
+            tg(b("ZR"), b("PD"), BC4, b("DM"), OP.mult)
             tt(b("MI"), b(r, 0, CAP), b("KP0", 0, CAP), OP.max, ext=t - 1)
             ts(b("QI"), b("MI"), 15, OP.bitwise_and)
             cp(b("PT", q0, q0 + CAP), b("QI"))
+            root = b("PD", 3, 64, 4)
+            act(b("RKS", 2, 128, 8), b("PD", 0, 64, 4), AF.Identity, scale=65536.0 * U, bias=CO * U)
+        else:
+            for h in range(2):
+                mm(b("KP0", 256 + 8 * h, 264 + 8 * h), Qh[h], b("WB"))
+            cp(b("sm"), b("KP0", 256, 272))
+            root = b("sn")
+            ts(root, b("sm"), 63, OP.bitwise_and)
+            tg(b("ZR"), root, BC16, b("DM"), OP.mult)
         for h in range(2):
-            mm(b("KP0", 256 + 8 * h, 264 + 8 * h), Qh[h], b("WB"))
-        cp(b("si"), b("KP0", 256, 272))
-        ts(b("sj"), b("si"), 63, OP.bitwise_and)
-        tg(b("ZR"), b("sj"), BC16, b("DM"), OP.mult)
-        for h in range(2):
-            mm(b("KP0", 272 + 8 * h, 280 + 8 * h), b("ZR", 128 * h, 128 * h + 128), b("LCB"))
-        ts(b("OFF"), b("KP0", 272, 288), 1.0, OP.add)
-        lo = 128 - max(share(t, p, 0) for p in range(5))
+            mm(b("KP1", 272 + 8 * h, 280 + 8 * h), b("ZR", 128 * h, 128 * h + 128), b("LCB"))
+        ts(b("OFF"), b("KP1", 272, 288), 1.0, OP.add)
+        lo = 96 - max(share(t, p, 0) for p in range(5))
         hi = 128 + max(share(t, p, 1) for p in range(5))
         for i in range(16):
             o, q = b("Q16", 16 * lo + i, 16 * hi, 16), b("PT", q0 + lo, q0 + hi)
@@ -467,23 +484,16 @@ def rank_program(g, core, T, topo):
             mm(b("SP3", 0, 256), b("NIDB"), Q, True, False)
             mm(b("SP3", 0, 256), b("IDB"), b("DRB"), False, True)
             act(b("DRB"), b("SP3", 0, 256), AF.Abs)
-        if t:
-            for h in range(2):
-                mm(b("MA", 16 * h, 16 * h + 16), b(r, 128 * h, 128 * h + 128), b("SEL"), f32=True, ext=t - 1)
-            tt(b("PM"), b("MA", 0, 32), b("FR", 32 * t, 32 * t + 32), OP.max)
-            ts(b("PD"), b("PM"), 4, OP.arith_shift_right, 2 ** 18 - 1, OP.bitwise_and)
-            ts(b("B0C"), b("PD"), -c0, OP.add)
-            act(b("RKS", 2, 128, 8), b("B0C", 0, 32, 2), AF.Identity, scale=65536.0 * U, bias=(c0 - 0.5) * 65536 * U)
-        cp(b("RT"), b("sj"))
+        act(b("RT"), root, AF.Copy)
         for h in range(2):
             mm(b("MA", 48 + 8 * h, 56 + 8 * h), b("DRB", 128 * h, 128 * h + 128), b("LCB"))
-        act(b("D0"), b("MA", 48, 64), AF.Copy)
+        act(b("DS", 0, 256, 16), b("MA", 48, 64), AF.Copy)
         for h in range(2):
             mm(b("MA", 32 + 8 * h, 40 + 8 * h), b("DRB", 128 * h, 128 * h + 128), b("BLK"), True, False)
             mm(b("MA", 32 + 8 * h, 40 + 8 * h), b("IDB"), b("RT", 8 * h, 8 * h + 8), False, True)
         act(b("K0U"), b("MA", 32, 48), AF.Identity, scale=U, bias=(CO + 1) * U)
         act(b("K0"), b("MA", 32, 48), AF.Identity, bias=CO + 32768 + 1)
-        tg(b("E"), b("D0"), BC16, b("RAMP"), OP.subtract)
+        scan(b("E"), b("GO"), b("DS"), OP.mult, OP.add)
         act(b("A"), b("E"), AF.Abs, scale=65536.0 * U, bias=-CO * U)
         tt(b("RKS", 3, 128, 8), b("RKS", 2, 128, 8), b("K0U"), OP.min)
 
@@ -496,7 +506,10 @@ def rank_program(g, core, T, topo):
         off = b("OFF", 8 * h, 8 * h + 8)
         A = b("A", 128 * h, 128 * h + 128)
         pt = b("PT", 0, 4096)
-        op("v", lambda: V.tensor_copy(n("PU")[4], ch[4].indirect(off[4])), [ch, off], [n("PU")], FV + 128 * GA * CY)
+        if PUS:
+            act(n("PU"), ch, AF.Copy, off=off)
+        else:
+            op("v", lambda: V.tensor_copy(n("PU")[4], ch[4].indirect(off[4])), [ch, off], [n("PU")], FV + 128 * GA * CY)
         act(n("Pf"), ch, AF.Identity, bias=b("bias", p // 4, p // 4 + 1), scale=1.0 if p == 4 else U, off=off)
         rks = b("RKS", 64 * h, 64 * h + 64)
         tg(n("M1"), rks, BCS[p + 1 if p else 0], A, OP.is_lt)
@@ -505,38 +518,39 @@ def rank_program(g, core, T, topo):
         if p in (2, 3):
             mm(kp, b("IDB"), n("ST"), False, False)
         nv = share(t, p, h)
-        v0 = 128 - nv if h == 0 else 0
-        s0 = 0 if h == 0 else nv
-        c = 16 * (128 - nv)
-        r0 = 1536 - c if h == 0 else 1536
-        cut = [r0] + [x for x in range(512, 3072, 512) if r0 < x < r0 + c] + [r0 + c]
-        parts = [[k] for k in range(len(cut) - 1)] if SP > 2 else [list(range(len(cut) - 1))] if SP == 1 else [[0], list(range(1, len(cut) - 1))]
-        if h == 0 and SP == 2:
-            parts = [list(range(len(cut) - 2)), [len(cut) - 2]]
-        for k, part in enumerate(x for x in parts if x):
-            at = lambda x: 16 * s0 + x - r0
-            lo, hi = cut[part[0]], cut[part[-1] + 1]
-            d = b("DIFF", 2048 * h + at(lo), 2048 * h + at(hi))
+        v0 = 96 - nv if h == 0 else 0
+        c = 16 * (96 - nv)
+        for k, (s0, lo, hi) in enumerate(((0, 1024 - c, 1024), (96, 1024, 1536)) if h == 0 else ((nv, 2048, 2048 + c), (96, 1536, 2048))):
+            cut = [lo] + [x for x in range(512, 3072, 512) if lo < x < hi] + [hi]
+            at = [16 * s0 + x - lo for x in cut]
+            d = b("DIFF", 2048 * h + at[0], 2048 * h + at[-1])
             slot[2] = "get%d" % k
-            act(d, pt, AF.Copy, off=n("PU", at(lo) // 16, at(hi) // 16))
-            banks = [b(RING[cut[j] // 512], cut[j] % 512, cut[j] % 512 + cut[j + 1] - cut[j]) for j in part]
-            for j, ps in zip(part, banks):
-                slot[2] = "get%d" % k
-                mm(ps, b("NQT", 128 * h, 128 * h + 128), b("R", at(cut[j]), at(cut[j + 1])), True, False)
+            act(d, pt, AF.Copy, off=n("PU", at[0] // 16, at[-1] // 16))
+            banks = [b(RING[x // 512], x % 512, x % 512 + y - x) for x, y in zip(cut, cut[1:])]
+            for j, ps in enumerate(banks):
+                mm(ps, b("NQT", 128 * h, 128 * h + 128), b("R", at[j], at[j + 1]), True, False)
             slot[2] = "abs%d" % k
-            for j, ps in zip(part, banks):
-                mm(ps, b("IDB"), b("DIFF", 2048 * h + at(cut[j]), 2048 * h + at(cut[j + 1])), False, True)
-            op("s", lambda d=d, lo=lo, hi=hi: S.activation(d[4], T.RING[:, lo:hi], AF.Abs), banks, [d], FS + (hi - lo) * CY)
+            for j, ps in enumerate(banks):
+                mm(ps, b("IDB"), b("DIFF", 2048 * h + at[j], 2048 * h + at[j + 1]), False, True)
+            op("s", lambda d=d, lo=lo, hi=hi: S.activation(d[4], T.RING[:, lo:hi], AF.Abs), banks, [d], FS + (hi - lo) * CY * CS)
         cut = [v0 + nv * k // VP // 2 * 2 for k in range(VP)] + [v0 + nv]
-        for k in range(VP if nv else 0):
+        for k in range(VP):
             lo, hi = cut[k], cut[k + 1]
             d = b("DIFF", 2048 * h + 16 * lo, 2048 * h + 16 * hi)
             slot[2] = "vec%d" % k
             tg(d, pt, n("PU", lo, hi), b("Q16", 2048 * h + 16 * lo, 2048 * h + 16 * hi), OP.subtract)
-            act(d, d, AF.Abs)
-        slot[2] = "key"
-        for i in range(16):
-            mm(b(KP, i, 128, 16), b("DIFF", 2048 * h + i, 2048 * h + 2048, 16), b("BLK" if p == 4 else "BLKU"), False, i == 15)
+            if (k + 1) % VA == 0:
+                d = b("DIFF", 2048 * h + 16 * cut[k + 1 - VA], 2048 * h + 16 * hi)
+                slot[2] = "vec%d" % (k // VA)
+                act(d, d, AF.Abs)
+        blk = b("BLKW" if p == 4 else "BLKU")
+        for lo, hi in ((0, 96), (96, 128)) if KSP else ((0, 128),):
+            slot[2] = "key" if lo or not KSP else "kez"
+            for i0 in range(0, 16, KG):
+                def sums(lo=lo, hi=hi, i0=i0):
+                    return [TE.matmul(b(KP, i, 128, 16, hi - lo, lo)[4], b("DIFF", 2048 * h + 16 * lo + i, 2048 * h + 16 * hi, 16)[4],
+                                      blk[4], False, i == 15 and hi == 128) for i in range(i0, i0 + KG)][-1]
+                op("t", sums, [b("DIFF", 2048 * h + 16 * lo, 2048 * h + 16 * hi), blk], [kp], KG * (FT + min(64, hi - lo) * CY * CT))
         scan(n("KS"), b("MX"), kp, OP.max, OP.min)
         if p == 4:
             return
@@ -557,19 +571,22 @@ def rank_program(g, core, T, topo):
         tg(n("Z"), n("NN"), BC8, b("DM", 0, 128), OP.mult)
         slot[2] = "list"
         mm(b(KP, 128, 136), n("Z"), b("LC"), f32=True)
-        cp(off, b(KP, 128, 136))
+        if OFS:
+            act(off, b(KP, 128, 136), AF.Copy)
+        else:
+            cp(off, b(KP, 128, 136))
         if p in (1, 2):
             ts(dk, sk, 16, OP.arith_shift_right, 255, OP.bitwise_and)
             ts(n("RB"), n("FB") if p == 1 else n("SK", 8, 16), 0xF000, OP.bitwise_and)
             tt(n("RP"), sk, n("RB"), OP.min)
             tg(n("ST"), n("RP"), BC8, b("ROWB"), OP.is_equal)
         else:
-            dk = b("D0", 8 * h, 8 * h + 8)
-            act(dk, n("MS", 15, 128, 16), AF.Identity, scale=1 / (65536 * U), bias=RND)
+            ts(dk, n("MS", 15, 128, 16), 1 / (65536 * U), OP.mult)
         if p == 0:
             ts(n("FB"), sk, 32768.0, OP.add)
         e = b("E", 128 * h, 128 * h + 128)
-        tg(e, dk, BC8, b("RAMP", 0, 128) if p in (1, 2) else b("RAMQ"), OP.subtract)
+        cp(b("DS", 128 * h, 128 * h + 128, 16), dk)
+        scan(e, b("GO", 0, 128), b("DS", 128 * h, 128 * h + 128), OP.mult, OP.add)
         act(A, e, AF.Abs, scale=65536.0 * U, bias=-15.5 * 65536 * U)
         if (p, h) == (3, 1):
             ts(b("Tp"), b("RKS", 7, 128, 8), 1 / U, OP.mult, 32768.0, OP.add)
@@ -578,21 +595,47 @@ def rank_program(g, core, T, topo):
             tg(b("m", 8, 136), b("thr"), BH, b("RKS"), OP.is_gt)
             scan(b("sc"), b("m", 7, 135), b("RKS"), OP.mult, OP.max)
             ts(b("ki"), b("sc", 7, 128, 8), 1 / U, OP.mult)
-            ts(b("W", 16, 32), b("ki"), 4095, OP.bitwise_and)
+            ts(b("W"), b("ki"), 4095, OP.bitwise_and)
+            ts(b("y"), b("T3"), WIDE / 65536, OP.mult, -8 * WIDE - 4096, OP.add)
+            tt(b("Y"), b("y"), b("W"), OP.add)
+        if (p, h) == (1, 0):
+            slot[2] = "out"
             if t:
-                ts(b("y"), b("W", 16, 32), 0.0, OP.is_equal)
-                tt(b("y"), b("y"), b("B0C", 1, 32, 2), OP.mult)
-            else:
-                ts(b("y"), b("W", 16, 32), 0.0, OP.is_equal, -c0, OP.mult)
-            tt(b("W", 0, 16), b("y"), b("W", 16, 32), OP.add)
-        if (p, h) == (1, 0) and t:
-            outputs(t - 1)
+                outputs(t - 1)
+                cb = 4096.0 * ((rank - 1) % N)
+                act(b("y"), b("PD", 2, 64, 4), AF.Relu, scale=-1.0, bias=1.0)
+                act(b("thr"), b("PD", 1, 64, 4), AF.Identity, bias=-cb)
+                tt(b("y"), b("y"), b("thr"), OP.mult)
+                act(b("thr"), b("PD", 2, 64, 4), AF.Identity, bias=cb - c0)
+                tt(b("B0C"), b("y"), b("thr"), OP.add)
+                for k in range(2 if t < VI - 1 else 0):
+                    act(b("PK%d" % k, 4, 128, 16), b("B0C", 8 * k, 8 * k + 8), AF.Identity, scale=16.0, bias=FLAG + 16 * c0)
+            if t < VI - 1:
+                roots(t, "WN", VI - 1 if t == 0 else None)
+                for k in range(2):
+                    act(b("PK%d" % k, 12, 128, 16), b("sn", 8 * k, 8 * k + 8), AF.Identity, scale=16.0, bias=FLAG)
+            for k in range(1, VI if t == 0 else 0):
+                roots(k, "WB")
+                act(b("FR", 64 * k + 3, 64 * k + 64, 4), b("sn"), AF.Copy, scale=16.0)
+
+    def roots(t, w, ext=None):
+        if ext is not None:
+            op("s", lambda: S.activation(b("wf", 1, 2)[4], b("wn", 0, 1)[4], AF.Copy), [], [b("wf", 1, 2)], FS, "c", ext)
+            act(b("WN"), b("LC"), AF.Copy, scale=b("wf", 1, 2))
+        for k in range(2):
+            mm(b("KP1", 160 + 8 * k, 168 + 8 * k), b("PT", M + L * t + 128 * k, M + L * t + 128 * k + 128), b(w))
+        act(b("sm"), b("KP1", 160, 176), AF.Copy)
+        ts(b("sn"), b("sm"), 63, OP.bitwise_and)
+
+    def send(out, src, step, k):
+        dst = T.cores[(rank + step) % N]
+        rid, pid, _x = topo.addr(dst)
+        op("g", lambda: g.remote_dma(out, src[4], T.sem["arr%d" % k], T.sem["sent%d" % k], pid, rid, topo.mask(core, dst)), [src], [], 0.1, "r", k)
 
     def outputs(t):
-        slot[2] = "out"
         for k in range(2):
-            mm(b("MB", 128 * k, 128 * k + 128, 1, 32), b("OUT%d" % k), b("IDF"), f32=True, also=b("KS0"))
-        act(b("OB%d" % t, 0, L, 1, 32), b("MB", 0, L, 1, 32), AF.Identity, bias=b("bias", 4, 5, 1, 32))
+            mm(b("KP1", 256 + 128 * k, 384 + 128 * k, 1, 32), b("OUT%d" % k), b("IDF"), f32=True)
+        act(b("OB%d" % t, 0, L, 1, 32), b("KP1", 256, 512, 1, 32), AF.Identity, bias=b("bias", 4, 5, 1, 32))
         for k, out in ((0, T.yr), (1, T.yb), (3, T.yp)):
             o = b("OB%d" % t, 0, L, 1, 8, 8 * k)
             dma("y", out[:, t * L:(t + 1) * L], o[4], [o], [o], 2.0)
@@ -603,21 +646,36 @@ def rank_program(g, core, T, topo):
         pa, pb, po, pg = (("KP0", "SP0", 0, "SP1"), ("KP1", "SP2", 0, "SP3"))[h]
         pairs = ("MA", "MB")
         q = b("PT", M + L * t + 128 * h, M + L * t + 128 * h + 128)
-        Rr, node = n("RI", 0, 8), n("OUT", 16, 24)
-        tt(n("V4"), n("KS", 15, 128, 16), b("T3", 8 * h, 8 * h + 8), OP.min)
+        Rr, node = n("RI", 0, 16, 2), n("RI", 1, 16, 2)
+        tt(n("V4"), n("KS", 15, 128, 16), b("Y", 8 * h, 8 * h + 8), OP.min)
+        kc = b("KC", 8 * h, 8 * h + 8)
+        ts(node, n("V4"), 4095, OP.bitwise_and)
+        ts(n("n4"), n("V4"), -4096, OP.bitwise_and)
+        ts(Rr, n("n4"), -7 * 4096.0, OP.add, 1 / WIDE, OP.mult)
         if t < VI - 1:
-            tt(n("near"), n("V4"), b("THK"), OP.is_lt)
-            mm(b(pa, 136, 144), b("LTD" + hs), n("near"), True, h == 0)
+            act(n("PK", 0, 128, 8), n("RI"), AF.Identity, scale=16.0, bias=FLAG)
+            mm(b(pb, po, po + 128), b("IDB"), q, True, False)
+            mm(b(pb, po, po + 128), n("PK"), b("IDF"), False, True, f32=True)
+            act(n("XS"), b(pb, po, po + 128), AF.Copy)
+            tg(n("NB"), n("V4"), BC3, b("THX"), OP.is_lt)
+            mm(b(pa, 144, 152), b("IDB"), kc, True, False)
             if h:
-                mm(b(pa, 136, 144), b("NONE"), b("near0"), False, True)
-            act(n("DG", 0, 8), b(pa, 136, 144), AF.Identity, bias=b("bias", 2 + h, 3 + h))
-        ts(Rr, n("V4"), 16, OP.arith_shift_right)
-        op("v", lambda: V.tensor_scalar(n("n4")[4], n("V4")[4].indirect(DUP[4]), 4095, None, OP.bitwise_and),
-           [n("V4"), DUP], [n("n4")], FV + 16 * GA * CY)
-        ts(n("z"), n("n4"), 0.0, OP.is_equal)
-        tg(n("zw"), b("W"), PICK[h], n("z"), OP.mult)
-        tt(n("OUT", 8, 24), n("zw"), n("n4"), OP.add)
-        cp(n("OUT", 0, 8), Rr)
+                mm(b(pa, 144, 152), b("NB0", 0, 128), b("NONE", 0, 8), False, False)
+            for k in range(3):
+                mm(b(pa, 144, 152), n("NB", 128 * k, 128 * k + 128), b("RL", 8 * (k + h * (k // 2)), 8 * (k + h * (k // 2)) + 8), False, k == 2)
+            ts(n("OP"), b(pa, 144, 152), P15, OP.add)
+            snd, rcv = "SND%d" % t, "RCV%d" % t
+            op("v", lambda: V.tensor_copy(b(snd)[4].indirect(n("OP")[4]), n("XS")[4]), [n("XS"), n("OP")], [b(snd)], FV + 128 * SCA * CY)
+            if h:
+                send(T[rcv][:, 0:CAP], b(snd, 0, CAP), 1, t)
+            tag[0] = "g" + tag[0][1:]
+        if t:
+            ts(n("z"), node, 0.0, OP.is_equal)
+            tt(n("z"), n("z"), b("B0C", 8 * h, 8 * h + 8), OP.mult)
+        else:
+            ts(n("z"), node, 0.0, OP.is_equal, -c0, OP.mult)
+        tt(n("OUT", 8, 16), n("z"), node, OP.add)
+        act(n("OUT", 0, 8), Rr, AF.Copy)
         ob = b("OB%d" % t, 128 * h, 128 * h + 128, 1, 32 if t < VI - 1 else 16)
         if t == VI - 1:
             mm(b(pa, 256, 384, 1, 16), n("OUT", 0, 16), b("IDF"), f32=True)
@@ -626,35 +684,20 @@ def rank_program(g, core, T, topo):
                 o = b(ob[0], ob[1], ob[2], 1, 8, 8 * k)
                 dma(qn, out[:, t * L + 128 * h:t * L + 128 * h + 128], o[4], [o], [], 2.0)
             return
-        kc = b("KC", 8 * h, 8 * h + 8)
-        z1 = n("ZZ", 128, 256)
-        act(n("DG", 8, 16), node, AF.Identity, bias=b("K4096", h, h + 1))
-        tg(n("ZZ"), n("DG"), BC16, b("DM"), OP.mult)
-        mm(b(pa, 144, 152), n("ZZ", 0, 128), b("LC"), f32=True)
+        z1 = n("Z1")
+        act(n("OUT", 16, 24), node, AF.Copy)
+        ts(n("gq"), node, b("K4096", h, h + 1), OP.add)
+        tg(z1, n("gq"), BC8, b("DM", 0, 128), OP.mult)
         mm(b(pa, 152, 160), b("IDB"), kc, True, False)
         mm(b(pa, 152, 160), z1, b("LC"), False, True, f32=True)
-        ts(n("OG"), b(pa, 144, 160), b("bias", 5, 6), OP.add)
-        act(n("PK", 0, 128, 16), n("OUT", 0, 8), AF.Identity, scale=16.0, bias=FLAG)
-        act(n("PK", 1, 128, 16), n("OUT", 8, 16), AF.Identity, scale=16.0, bias=FLAG + 16 * c0)
-        mm(b(pb, po, po + 128), b("IDB"), q, True, False)
-        mm(b(pb, po, po + 128), n("PK"), b("IDF"), False, True, f32=True)
-        act(n("XS"), b(pb, po, po + 128), AF.Copy)
-        snd, rcv = "SND%d" % t, "RCV%d" % t
-        og = n("OG", 0, 8)
-        op("v", lambda: V.tensor_copy(b(snd)[4].indirect(og[4]), n("XS")[4]), [n("XS"), og], [b(snd)], FV + 128 * SCA * CY)
-        if h:
-            dst = T.cores[(rank + 1) % N]
-            rid, pid, _x = topo.addr(dst)
-            op("g", lambda: g.remote_dma(T[rcv][:, 0:CAP], T[snd][:, 0:CAP], T.sem["arr%d" % t], T.sem["sent%d" % t], pid, rid, topo.mask(core, dst)),
-               [b(snd, 0, CAP)], [], 0.1, "r", t)
-        tag[0] = "g" + tag[0][1:]
-        act(n("GC"), b("CH", 0, 4096), AF.Copy, off=n("OG", 8, 16))
+        ts(n("G1"), b(pa, 152, 160), b("bias", 5, 6), OP.add)
+        act(n("GC"), b("CH", 0, 4096), AF.Copy, off=n("G1"))
         act(n("NQ", 0, 16, 2), node, AF.Copy)
         tt(n("NQ", 1, 16, 2), node, n("NQ", 0, 16, 2), OP.subtract)
         mm(b(pg, 0, 128, 1, 16), n("NQ"), b("IDB"))
         nt = b("NT" + hs, 0, 128, 1, 16)
         act(nt, b(pg, 0, 128, 1, 16), AF.Copy)
-        ts(n("bb"), Rr, 0.0625, OP.mult, -0.96875, OP.add)
+        act(n("bb"), Rr, AF.Identity, scale=0.0625, bias=-0.46875)
         tg(n("OH"), n("bb"), BC8, b("j15", 0, 128), OP.is_equal)
         mm(b(pb, po + 128, po + 256), n("OH"), b("DGB", 128 * (2 * t + h), 128 * (2 * t + h) + 128), True, False)
         mm(b(pb, po + 128, po + 256), n("OH"), b("DGL"), False, True)
@@ -674,7 +717,7 @@ def rank_program(g, core, T, topo):
             hi = min(ns, lo + 4)
             act(n("EQ", 128 * lo, 128 * hi), b("EF", 128 * lo, 128 * hi), AF.Relu, scale=nwl, bias=wl)
         tt(n("OC"), b(pb, po + 128, po + 256), n("GC"), OP.mult)
-        mm(b(pg, 160, 168), b("WI"), n("near"), True, False)
+        mm(b(pg, 160, 168), b("WI"), n("NB", 0, 128, 16), True, False)
         if h:
             act(b("CG"), n("GC"), AF.Relu, bias=1.0 - M - L * t)
             mm(b(pg, 160, 168), b("CG"), b("BLK"), False, False)
@@ -709,7 +752,7 @@ def rank_program(g, core, T, topo):
 
     n = len(ops)
     cost = [o["cost"] for o in ops]
-    more = [o["ext"] if o["kind"] == "d" else 3.0 if o["kind"] == "r" else 0.0 for o in ops]
+    more = [o["ext"] if o["kind"] == "d" else FAR if o["kind"] == "r" else 0.0 for o in ops]
     fwd = [[] for _ in range(n)]
     bwd = [[] for _ in range(n)]
     for i, o in enumerate(ops):
@@ -766,7 +809,7 @@ def rank_program(g, core, T, topo):
         ops[i]["t0"] = ORDER["at"][i]
 
     QS = {"v": V, "t": TE, "s": S, "g": g, "y": g.sync}
-    CS = {"v": "cv", "t": "ct", "s": "cs", "g": "cg"}
+    CQ = {"v": "cv", "t": "ct", "s": "cs", "g": "cg"}
     done = {}
     total = {"v": 0, "t": 0, "s": 0, "g": 0}
     know = {x: {} for x in QS}
@@ -793,8 +836,8 @@ def rank_program(g, core, T, topo):
                     k[a] = c
         if o["kind"] == "c":
             total[qn] += 1
-            o["call"]().then_inc(T.sem[CS[qn]], 1)
-            done[i] = (CS[qn], total[qn], dict(k))
+            o["call"]().then_inc(T.sem[CQ[qn]], 1)
+            done[i] = (CQ[qn], total[qn], dict(k))
         elif o["kind"] == "d":
             o["call"]().then_inc(T.sem[o["sem"]], 16)
             done[i] = (o["sem"], 16, dict(k))
@@ -802,10 +845,10 @@ def rank_program(g, core, T, topo):
             o["call"]()
             done[i] = ("sent%d" % o["ext"], nout, dict(k))
     for x in "vtsg":
-        g.wait_ge(T.sem[CS[x]], total[x])
+        g.wait_ge(T.sem[CQ[x]], total[x])
     for i in range(ndma[0]):
         g.wait_ge(T.sem["d%d" % i], 16)
-    for t in range(VI - 1):
+    for t in range(VI):
         g.wait_ge(T.sem["sent%d" % t], nout)
         g.wait_ge(T.sem["arr%d" % t], nin)
     return ops, order

@@ -5,40 +5,33 @@ U = 2.0 ** -26
 WIDE = 17.0 * 4096
 BIG = float(2 ** 60)
 CO = 7.5 * 65536
+RND = 1.5 * 2.0 ** 39
 FLAG = float(2 ** 22)
 ROOM = 4096 + 256
 SNDW = 1280
-NV = ((60, 52), (46, 42), (42, 42), (42, 46), (40, 64))
-NV0 = ((66, 54), (46, 42))
-DRV = True
-PUS = False
-OFS = False
-NVL = (50, 76)
-VA, KSP, KG = 2, False, 8
-VP = 2
-SP = 2
-QV = 8
-GSC = (4, 6)
-HALF, GAP, LOOK, EARLY = 4.97, 18.0, 0.07, 2.3
-WHEN = {'vPU0': 0.83, 'vvec0': 2.6, 'vvec1': 2.85, 'vM0': 2.48, 'vKS0': 6.82, 'vRKS0': 7.81, 'vM1': 3.2, 'vKM0': 11.11, 'vMS0': 7.1, 'vz0': 7.44, 'vSK0': 5.26, 'vNN0': 7.1, 'vZ0': 5.7, 'vDK0': 8.03, 'vE0': 12.79, 'vOFF0': 8.24, 'vRB0': 7.77, 'vRP0': 9.84, 'vST0': 7.42, 'vFB0': 13.5, 'sget0': -0.16, 'sget1': 2.04, 'sPf0': 3.05, 'svec0': 2.69, 'sabs0': 3.0, 'sabs1': 1.92, 'svec1': 3.67, 'sA0': 12.3, 'tget0': 5.37, 'tabs0': 0.41, 'tget1': 2.4, 'tabs1': 5.16, 'tPf': 3.47, 'tkey': 2.85, 'tlist': 3.84, 'sD0': 4.51,
-        "tkez": 2.8, "vvec2": 3.0, "vvec3": 3.2, "vvec4": 3.4, "vvec5": 3.6, "svec2": 3.8, "sDK0": 8.0, "sDS0": 8.5, "sOFF0": 8.2, "sy0": 8.0, "sFB0": 12.0, "vTp0": 6.0, "vT0": 6.0, "vthr0": 6.0, "vm0": 6.0, "vsc0": 6.0, "vki0": 6.0, "vW0": 6.0, "vy0": 6.0, "vy1": 6.0, "vW1": 6.0}
-WHEN = {'sA0': 14.05, 'sPf0': 2.05, 'sabs0': 3.39, 'sabs1': -15.79, 'sget0': -2.15, 'sget1': 3.3, 'svec0': 2.89, 'tPf': 2.12, 'tabs0': 1.27, 'tabs1': 6.58, 'tget0': 2.43, 'tget1': -0.73, 'tkey': 3.6, 'tlist': -1.05, 'vDK0': 9.61, 'vDS0': 9.82, 'vE0': 23.88, 'vFB0': 24.54, 'vKM0': 10.8, 'vKS0': 9.72, 'vM0': 1.82, 'vM1': -12.36, 'vMS0': -17.94, 'vNN0': 8.71, 'vOFF0': -19.34, 'vPU0': -1.82, 'vRB0': 11.03, 'vRKS0': 2.41, 'vRP0': 24.86, 'vSK0': 1.07, 'vST0': 11.0, 'vT0': 8.99, 'vTp0': 0.57, 'vW0': 9.0, 'vY0': 9.24, 'vZ0': 0.62, 'vki0': -8.34, 'vm0': -13.12, 'vsc0': 5.83, 'vthr0': 9.0, 'vvec0': 2.73, 'vvec1': 3.79, 'vy0': 9.0, 'vz0': 12.31}
-WHEN = {'sA0': 10.3, 'sPf0': -2.94, 'sabs0': 5.99, 'sabs1': -16.03, 'sget0': -3.36, 'sget1': 0.91, 'svec0': 4.87, 'tPf': 1.92, 'tabs0': 5.5, 'tabs1': 9.09, 'tget0': 1.71, 'tget1': 0.33, 'tkey': -0.55, 'tlist': 2.81, 'vDK0': 12.77, 'vDS0': 9.52, 'vE0': 17.18, 'vFB0': 36.43, 'vKM0': 5.46, 'vKS0': 12.54, 'vM0': 0.41, 'vM1': -6.44, 'vMS0': -19.19, 'vNN0': 12.0, 'vOFF0': -36.48, 'vPU0': -0.93, 'vRB0': 17.61, 'vRKS0': 2.22, 'vRP0': 36.68, 'vSK0': 2.61, 'vST0': 5.41, 'vT0': 10.68, 'vTp0': 5.99, 'vW0': 19.94, 'vY0': 19.51, 'vZ0': 3.84, 'vki0': -30.94, 'vm0': -18.97, 'vsc0': 0.84, 'vthr0': 17.12, 'vvec0': 4.0, 'vvec1': 2.9, 'vy0': 1.69, 'vz0': 17.89}
-HALF, GAP, LOOK, EARLY = 9.66, 46.6, 0.1, -2.05
-ROUNDS = 30000
-CY, GA, GT, SCA, CS, CT, FI = 0.00089, 1.56, 1.6, 3.8, 0.83, 0.88, 0.065
-FIX, WAKE, FAR = (0.05, 0.09, 0.0), 0.145, 3.0
-WHEN0 = {"vPU0": 0.0, "vvec0": 0.25, "vvec1": 1.6, "vvec2": 2.0, "vvec3": 2.3, "vM0": 1.2, "vKS0": 5.9, "vRKS0": 6.1, "vM1": 6.2, "vKM0": 6.9, "vMS0": 7.2,
-        "vz0": 7.4, "vSK0": 7.5, "vNN0": 7.7, "vZ0": 7.9, "vDK0": 8.1, "vE0": 8.3, "vOFF0": 8.6, "vRB0": 7.3, "vRP0": 8.4, "vST0": 10.0,
-        "vFB0": 10.0, "sget0": 0.3, "sget1": 0.9, "sget2": 1.5, "sget3": 2.0, "sPf0": 2.0, "svec0": 2.2, "sabs0": 2.6, "sabs1": 3.0,
-        "svec1": 3.3, "svec2": 3.5, "svec3": 3.6, "sabs2": 3.8, "sabs3": 4.0, "sA0": 8.8,
-        "tget0": 1.4, "tabs0": 1.6, "tget1": 1.9, "tabs1": 2.1, "tget2": 2.4, "tabs2": 2.6, "tget3": 2.9, "tabs3": 3.0,
-        "tPf": 3.5, "tkey": 4.4, "tlist": 3.0}
+NV = [[48, 38], [38, 38], [38, 38], [40, 40], [48, 54]]
+CUT = (96,)
+RELU = (1, 1, 1, 1, 1)
+VP = 5
+KSP = ()
+PFQ, DSQ, PUQ, OFQ = "h", "g", "s", "s"
+JD, JS = False, False
+GQS = "gggg"
+PHQ = "v"
+JUNK = 0
+EQQ = "SVVV"
+PLQ, PTQ, ZRS, JM, DRQ = "s", "s", False, True, "s"
+LSQ = ("G1", "G2", "OP", "Rr")
+WHEN = {'gDS': -6.55, 'sPh': 1, 'vPh': 1, 'vEQ': 8, 'vvec4': 0, 'sA': 5.79, 'sOFF': 14.06, 'sPU': -7.09, 'sabs0': -37.07, 'sabs1': 0.02, 'sabs2': -5.01, 'sget0': -0.17, 'sget1': 0.02, 'sget2': 3.8, 'tM1': 5.86, 'tPf': 4.21, 'tST': -2.24, 'tabs0': -8.84, 'tabs1': -10.62, 'tabs2': -4.57, 'tget0': 4.22, 'tget1': 4.41, 'tget2': 6.38, 'tkey': -4.03, 'tlist': 15.26, 'tneg': -6.17, 'trow': 7.16, 'vDK': -3.14, 'vDS': 3.51, 'vE': 17.62, 'vFB': -5.22, 'vKM': 4.73, 'vKS': -8.32, 'vM1': 18.97, 'vM2': 9.05, 'vMS': 10.12, 'vNN': 8.65, 'vRB': 3.14, 'vRKS': 9.05, 'vRP': 14.11, 'vSK': 11.45, 'vST': -14.78, 'vZL': -30.62, 'vrelu': 5.91, 'vvec0': 2.63, 'vvec1': -7.15, 'vvec2': 3.52, 'vvec3': -5.87, 'vz3': -89.99}
+HALF, GAP = 6.72, 39.09
+ROUNDS, SPAN, HEAT = 130000, 120, 0.0001
+MODELS = ((0.00089, 1.56, 3.8, 0.83, 0.6, 0.145), (0.00089, 1.9, 3.8, 0.83, 0.6, 0.22), (0.00089, 1.2, 3.8, 0.83, 0.79, 0.145))
+FAR = 3.0
 
 SCRATCH = {}
 PS = set()
 VIRT = {}
-POOL = {"float32": ["poolf", 0], "int32": ["pooli", 0], "bfloat16": ["poolb", 0], "uint16": ["poolu", 0]}
+POOL = {"float32": ["poolf", 0], "int32": ["pooli", 0], "bfloat16": ["poolb", 0], "uint16": ["poolu", 0], "float16": ["poolh", 0]}
 
 
 def _own(name, cols, dt="float32"):
@@ -63,70 +56,173 @@ for _k, _n in enumerate(RING):
     PS.add(_n)
 _own("PT", M + VI * L, "bfloat16"); _own("CHI", M, "int32"); _own("CH", ROOM)
 _own("wi", 8, "int32"); _own("wn", 8, "int32"); _own("thi", 8, "int32"); _own("r0i", 128, "int32")
-_own("Q16", 4096, "bfloat16"); _own("DIFF", 4096, "bfloat16")
+_own("Q16", 2048, "bfloat16"); _own("QS", 2048, "bfloat16"); _own("DIFF", 4096, "bfloat16"); _own("RAW", 2048, "bfloat16")
 for _t in "01":
     _own("SND" + _t, SNDW); _own("RCV" + _t, L)
 for _t in "012":
     _own("OB" + _t, 256)
 for _n, _c in (("r0f", 128), ("wf", 2), ("thf", 2), ("pf", 8), ("j15", 256), ("c8", 8), ("IDF", 128), ("DM", 256),
-               ("LC", 8), ("MX", 128), ("ROWB", 128), ("bias", 8), ("THK", 8), ("K4096", 16),
-               ("SEL", 32), ("FR", 192), ("THX", 384), ("A", 256), ("K0", 16), ("K0U", 16), ("WL", 2), ("B0C", 16), ("EF", 1024),
-               ("RKS", 128), ("thr", 16), ("m", 136), ("sc", 128), ("y", 16), ("Y", 16)):
+               ("LC", 8), ("MX", 128), ("ROWB", 256), ("bias", 8), ("THK", 16), ("K4096", 16),
+               ("SEL", 32), ("FR", 192), ("A", 256), ("K0", 16), ("K0U", 16), ("WL", 2), ("B0C", 16), ("EF", 384),
+               ("RKS", 128), ("KS", 256), ("MS", 256), ("IDU", 128), ("T3", 16), ("thr", 16), ("m", 136), ("sc", 128), ("y", 16), ("Y", 16)):
     _s(_n, _c)
-for _n, _c in (("pi", 8), ("li", 120), ("sm", 16), ("sn", 16), ("DK", 16), ("MI", 192), ("QI", 192), ("PM", 64), ("PD", 64),
-               ("Tp", 16), ("T3", 16), ("ki", 16), ("W", 16)):
+for _n, _c in (("pi", 8), ("li", 176), ("sm", 16), ("sn", 16), ("DK", 16), ("MI", 192), ("QI", 192), ("PM", 64), ("PD", 64),
+               ("ki", 16), ("W", 16), ("SK", 64), ("FB", 16), ("RB", 16), ("RP", 16)):
     _s(_n, _c, "int32")
-for _n, _c in [("IDB", 128), ("NIDB", 128), ("WI", 128), ("BLKU", 8), ("BLKW", 8), ("BLK", 8), ("LCB", 8), ("LC2", 8), ("WB", 8), ("WD", 128), ("RT", 16),
-               ("RL", 32), ("WN", 8), ("ONES", 2048), ("R", 2048), ("TB", 8), ("SELG", 1024), ("ZR", 256), ("E", 256), ("GO", 256), ("DS", 256),
+for _n, _c in [("IDB", 128), ("NIDB", 128), ("WI", 128), ("BLKU", 8), ("NBLKU", 8), ("NBLKW", 8), ("BLKW", 8), ("BLK", 8), ("LCB", 8), ("LC2", 8),
+               ("WB", 8), ("ROWC", 256), ("ST", 256), ("M1", 256), ("GQ", 1024), ("WD", 128), ("RT", 16),
+               ("RL", 32), ("WN", 8), ("ONES", 512), ("R", 1536), ("TB", 8), ("SELG", 1024), ("ZR", 256), ("E", 512), ("GO", 256), ("DS", 512),
                ("DRB", 256), ("NQT", 256), ("DGL", 128), ("DGB", 128 * 4), ("NONE", 128), ("KC", 16), ("CG", 128)]:
     _s(_n, _c, "bfloat16")
-_s("LI", 136, "uint16"); _s("OFF", 16, "uint16")
+_s("LI", 176, "uint16"); _s("OFF", 16, "uint16")
+_s("IDH", 256, "float16"); _s("ROWH", 256, "float16"); _s("Ph0", 128, "float16"); _s("Ph1", 128, "float16")
 for _h in "01":
-    for _n, _c, _d in (("PU", 128, "uint16"), ("Pf", 128, "float32"), ("M1", 128, "bfloat16"), ("M2", 128, "bfloat16"),
-                       ("ST", 128, "bfloat16"), ("KS", 128, "float32"), ("KM", 128, "float32"), ("MS", 128, "float32"),
-                       ("SK", 32, "int32"), ("NN", 8, "int32"), ("FB", 8, "int32"),
-                       ("Z", 128, "float32"), ("RB", 8, "int32"), ("RP", 8, "int32"),
-                       ("z3", 8, "float32"), ("V4", 8, "int32"),
-                       ("n4", 8, "int32"), ("z", 8, "float32"), ("RI", 16, "int32"), ("OUT", 32, "float32"), ("NB", 384, "bfloat16"),
-                       ("gq", 8, "float32"), ("Z1", 128, "float32"), ("OP", 8, "uint16"), ("G1", 8, "uint16"), ("PK", 128, "float32"), ("XS", 128, "float32"),
-                       ("GC", 128, "float32"),
-                       ("bb", 8, "int32"), ("OH", 128, "bfloat16"), ("ON", 128, "float32"), ("OC", 128, "bfloat16"), ("can", 8, "bfloat16"),
-                       ("win", 8, "float32"), ("Z2", 128, "float32"), ("G2", 8, "uint16"), ("NQ", 16, "bfloat16"),
-                       ("NT", 128, "bfloat16"), ("EQ", 2048, "bfloat16")):
+    for _n, _c, _d in (("PU", 128, "uint16"), ("Pf", 128, "float32"), ("M2", 128, "bfloat16"),
+                       ("NN", 8, "int32"), ("z3", 8, "float32"), ("KM", 128, "float32"), ("ZL", 128, "float32")):
         _s(_n + _h, _c, _d)
+for _n, _c, _d in (("V4", 16, "int32"), ("n4", 16, "int32"), ("z", 16, "float32"), ("RI", 32, "int32"), ("OUT", 96, "float32"),
+                   ("near", 16, "bfloat16"), ("PL", 16, "float32"), ("ZP", 256, "float32"), ("OP", 16, "uint16"), ("PK", 256, "float32"),
+                   ("XS", 256, "float32"), ("gq", 16, "float32"), ("Z1", 256, "float32"), ("G1", 16, "uint16"), ("GC", 256, "float32"),
+                   ("bb", 16, "int32"), ("OH", 256, "bfloat16"), ("ON", 256, "float32"), ("OC", 256, "bfloat16"), ("can", 16, "bfloat16"),
+                   ("win", 16, "float32"), ("Z2", 256, "float32"), ("G2", 16, "uint16"), ("NQ", 32, "bfloat16"),
+                   ("NT", 256, "bfloat16"), ("EQ", 2048, "bfloat16"), ("TRS", 256, "bfloat16"), ("NSELG", 1024, "bfloat16")):
+    _s(_n, _c, _d)
 for _d in POOL:
     SCRATCH[POOL[_d][0]] = ("sbuf", [128, POOL[_d][1]], _d)
 
-NDMA = 24
+NDMA = 27
 SEMAPHORES = ["cv", "ct", "cs", "cg"] + ["d%d" % i for i in range(NDMA)] + ["arr0", "arr1", "arr2", "sent0", "sent1", "sent2"]
 
 
 ORDER = {}
 
 
-def improve(order, q, cost, more, fwd):
-    n = len(order)
-    reach, pre, suc = [0] * n, [[] for _ in range(n)], [[] for _ in range(n)]
-    for i in range(n - 1, -1, -1):
-        for j, x in sorted(fwd[i]):
-            if not (reach[i] >> j) & 1 or more[i] > 0:
-                pre[j].append((i, x))
-                suc[i].append(j)
-                reach[i] |= reach[j] | (1 << j)
+def links(ops, model):
+    cy, ga, sca, cs, ct, wake = model
+    n = len(ops)
+    cost = [o["cost"][0] + o["cost"][1] * cy * {"v": 1, "s": cs, "t": ct, "V": ga, "S": ga * cs, "W": sca}[o["cost"][2]] for o in ops]
+    more = [o["ext"] if o["kind"] == "d" else FAR if o["kind"] == "r" else 0.0 for o in ops]
+    fwd = [[] for _ in range(n)]
+    far = {o["ext"]: j for j, o in enumerate(ops) if o["kind"] == "r"}
+    for i, o in enumerate(ops):
+        dd = set(o["deps"])
+        if o["kind"] == "c" and o["ext"] is not None:
+            dd.add(far[o["ext"]])
+        for d in dd:
+            fwd[d].append((i, cost[d] + more[d] + wake))
+        for d in o["after"] - dd:
+            fwd[d].append((i, cost[d]))
+    return cost, more, fwd
 
-    def run(order):
-        at, why, free, last, end = [0.0] * n, [None] * n, {}, {}, (0.0, 0)
+
+def place(ops, cost, more, fwd, when, half, gap, passes=2):
+    n = len(ops)
+    due = [0.0] * n
+    for i in range(n - 1, -1, -1):
+        o = ops[i]
+        if o["slot"] is not None and o["lab"] in when:
+            t, p, h = o["slot"]
+            due[i] = (10 * half + gap) * t + (2 * p + h) * half + when[o["lab"]]
+        else:
+            due[i] = min([due[j] - x for j, x in fwd[i]] or [3 * (10 * half + gap)])
+    pre = [[] for _ in range(n)]
+    for i in range(n):
+        for j, x in fwd[i]:
+            pre[j].append((i, x))
+            due[j] = max(due[j], due[i])
+    back = [[(j, x - cost[i] + cost[j]) for j, x in fwd[i]] for i in range(n)]
+
+    def fit(order, pre, first):
+        at, st, en = [0.0] * n, {x: [] for x in "vstgy"}, {x: [] for x in "vstgy"}
         for i in order:
-            t, w = 0.0, None
+            t, s, e = first[i], st[ops[i]["q"]], en[ops[i]["q"]]
             for d, x in pre[i]:
                 if at[d] + x > t:
-                    t, w = at[d] + x, (d, False)
-            if free.get(q[i], 0.0) > t + 1e-9:
-                t, w = free[q[i]], (last[q[i]], True)
-            at[i], why[i], free[q[i]], last[q[i]] = t, w, t + cost[i], i
-            if t + cost[i] + more[i] > end[0]:
-                end = (t + cost[i] + more[i], i)
-        return end, at, why
+                    t = at[d] + x
+            k = len(e)
+            while k and e[k - 1] > t:
+                k -= 1
+            while k < len(s) and s[k] < t + cost[i] - 1e-9:
+                t, k = e[k], k + 1
+            s.insert(k, t)
+            e.insert(k, t + cost[i])
+            at[i] = t
+        return at
+
+    order = sorted(range(n), key=lambda i: (due[i], i))
+    for k in range(passes):
+        at = fit(order, pre, [0.0] * n)
+        if k < passes - 1:
+            at = fit(sorted(range(n), key=lambda i: (-at[i] - cost[i], -i)), back, more)
+            at = [-at[i] - cost[i] for i in range(n)]
+        order = sorted(range(n), key=lambda i: (at[i], i))
+    return order
+
+
+def improve(order, ops, rounds):
+    n = len(order)
+    q = ["vstgy".index(o["q"]) for o in ops]
+    sets = []
+    for model in MODELS:
+        cost, more, fwd = links(ops, model)
+        reach, pre, suc = [0] * n, [[] for _ in range(n)], [[] for _ in range(n)]
+        for i in range(n - 1, -1, -1):
+            for j, x in sorted(fwd[i]):
+                if not (reach[i] >> j) & 1 or more[i] > 0:
+                    pre[j].append((i, x))
+                    suc[i].append((j, x))
+                    reach[i] |= reach[j] | (1 << j)
+        sets.append((cost, more, pre, suc))
+
+    def ahead(order, k, at, lo, hi, calm):
+        cost, more, pre, suc = sets[k]
+        free, same = [None] * 5, 0
+        for j in range(lo - 1, -1, -1):
+            i = order[j]
+            if free[q[i]] is None:
+                free[q[i]] = at[i] + cost[i]
+                if None not in free:
+                    break
+        free = [x or 0.0 for x in free]
+        for j in range(lo, hi):
+            i = order[j]
+            x = q[i]
+            t = free[x]
+            for d, y in pre[i]:
+                if at[d] + y > t:
+                    t = at[d] + y
+            free[x] = t + cost[i]
+            if at[i] != t:
+                at[i], same = t, 0
+            elif j > calm:
+                same += 1
+                if same > SPAN:
+                    break
+
+    def behind(order, k, rest, hi, calm):
+        cost, more, pre, suc = sets[k]
+        nxt, same = [None] * 5, 0
+        for j in range(hi + 1, n):
+            i = order[j]
+            if nxt[q[i]] is None:
+                nxt[q[i]] = rest[i]
+                if None not in nxt:
+                    break
+        nxt = [x or 0.0 for x in nxt]
+        for j in range(hi, -1, -1):
+            i = order[j]
+            x = q[i]
+            t = cost[i] + max(nxt[x], more[i])
+            for d, y in suc[i]:
+                if rest[d] + y > t:
+                    t = rest[d] + y
+            nxt[x] = t
+            if rest[i] != t:
+                rest[i], same = t, 0
+            elif j < calm:
+                same += 1
+                if same > SPAN:
+                    break
 
     seed = [12345]
 
@@ -134,16 +230,31 @@ def improve(order, q, cost, more, fwd):
         seed[0] = (seed[0] * 1103515245 + 12345) % 2 ** 31
         return (seed[0] >> 8) % k
 
-    cur = run(order)
-    best = (cur[0][0], order, cur[1])
-    for it in range(ROUNDS):
-        i, pairs = cur[0][1], []
-        while cur[2][i]:
-            if cur[2][i][1]:
-                pairs.append((cur[2][i][0], i))
-            i = cur[2][i][0]
-        x, y = pairs[draw(len(pairs))]
-        lo, hi, step = order.index(x), order.index(y), 2 * draw(2) - 1
+    K = range(len(MODELS))
+    at, rest = [[0.0] * n for k in K], [[0.0] * n for k in K]
+    for k in K:
+        ahead(order, k, at[k], 0, n, n)
+        behind(order, k, rest[k], n - 1, -1)
+    end = [max(rest[k]) for k in K]
+    best = (sum(end), order, end)
+    pre, suc = sets[0][2:]
+    for it in range(rounds):
+        k = draw(len(K))
+        a, r, c, e = at[k], rest[k], sets[k][0], end[k] - 1e-6
+        hi = draw(n)
+        while hi < n:
+            y = order[hi]
+            if a[y] + r[y] > e:
+                lo = hi - 1
+                while lo >= 0 and q[order[lo]] != q[y]:
+                    lo -= 1
+                x = order[lo]
+                if lo >= 0 and a[x] + r[x] > e and a[x] + c[x] > a[y] - 1e-6:
+                    break
+            hi += 1
+        if hi == n:
+            continue
+        step = 2 * draw(2) - 1
         k = lo if step < 0 else hi
         for _ in range((0, 0, 1, 2, 4)[draw(5)]):
             j = k + step
@@ -154,7 +265,7 @@ def improve(order, q, cost, more, fwd):
             lo, go = k, {y}
             seg = order[lo:hi + 1]
             for v in reversed(seg):
-                if any(s in go for s in suc[v]):
+                if any(s in go for s, _x in suc[v]):
                     go.add(v)
             new = [v for v in seg if v in go] + [v for v in seg if v not in go]
         else:
@@ -164,15 +275,23 @@ def improve(order, q, cost, more, fwd):
                 if any(d in go for d, _x in pre[v]):
                     go.add(v)
             new = [v for v in seg if v not in go] + [v for v in seg if v in go]
-        if x in go and y in go:
+        if new == seg:
             continue
         new = order[:lo] + new + order[hi + 1:]
-        r = run(new)
-        if r[0][0] <= cur[0][0] + 0.0001 * draw(1000) * (1 - it / ROUNDS):
-            cur, order = r, new
-            if r[0][0] < best[0]:
-                best = (r[0][0], new, r[1])
-    return best[1], best[2]
+        far = min(n, hi + 1 + SPAN)
+        a2, e2 = [a[:] for a in at], []
+        for k in K:
+            ahead(new, k, a2[k], lo, far, n)
+            c, m = sets[k][:2]
+            e2.append(max([a2[k][i] + rest[k][i] for i in new[hi + 1:far]] + [a2[k][i] + c[i] + m[i] for i in seg]))
+        if sum(e2) <= sum(end) + HEAT * len(K) * draw(1000) * (1 - it / rounds):
+            order, at, end = new, a2, e2
+            for k in K:
+                ahead(order, k, at[k], far, n, far)
+                behind(order, k, rest[k], hi, lo)
+            if sum(end) < best[0]:
+                best = (sum(end), order, end)
+    return best[1], [[e] for e in best[2]]
 
 
 def rank_program(g, core, T, topo):
@@ -182,7 +301,6 @@ def rank_program(g, core, T, topo):
     ops = []
     hist = {}
     ndma = [0]
-    rot = [0]
     tag = [""]
     slot = [None, {}, ""]
     c0 = 4096.0 * rank
@@ -230,29 +348,23 @@ def rank_program(g, core, T, topo):
             h.append((r, w, n))
         d = {"q": q, "call": call, "deps": deps, "after": after - deps, "cost": cost, "kind": kind, "ext": ext,
              "tag": tag[0] + " " + (writes[0][0] if writes else "")}
-        d["slot"] = slot[0]
-        if slot[0] is not None:
-            lab = q + writes[0][0].rstrip("0123")
-            slot[1][lab] = slot[1].get(lab, -1) + 1
-            d["lab"] = lab + str(slot[1][lab])
-            if lab in ("tKP", "tSP", "tMA", "tMB", "sDIFF", "vDIFF"):
-                d["lab"] = q + slot[2]
-            if slot[2] == "out":
-                d["slot"] = None
+        d["slot"] = slot[0] if slot[2] != "out" else None
+        if d["slot"] is not None:
+            x = writes[0][0]
+            d["lab"] = q + (slot[2] if q == "t" or x in ("DIFF", "RAW") or q + x + slot[2] == "vDSRP" else x[:-1] if x[:-1] + "0" in VIRT and x[:-1] + "1" in VIRT else x)
         if kind == "d":
             d["sem"] = "d%d" % ndma[0]
             ndma[0] += 1
         ops.append(d)
         return n
 
-    FV, FS, FT = FIX
-    two = ("poolb", "poolu", "PT", "Q16", "DIFF")
+    two = ("poolb", "poolu", "poolh", "PT", "Q16", "QS", "DIFF", "RAW")
 
     def cols(o):
         return (o[2] - o[1] + o[3] - 1) // o[3]
 
     def vc(n, k=1.0):
-        return FV + max(64, n * k) * CY
+        return (0.05, max(64, n * k), "v")
 
     def half(*xs):
         return 0.5 if all(VIRT[x[0]][0] in two for x in xs) else 1.0
@@ -267,7 +379,7 @@ def rank_program(g, core, T, topo):
         op("v", lambda: V.tensor_tensor(out[4], a[4], c[4], o), [a, c], [out], vc(cols(out), k), "c", ext)
 
     def tg(out, win, off, c, o):
-        op("v", lambda: V.tensor_tensor(out[4], win[4].indirect(off[4]), c[4], o), [win, off, c], [out], FV + cols(out) * GT * CY)
+        op("v", lambda: V.tensor_tensor(out[4], win[4].indirect(off[4]), c[4], o), [win, off, c], [out], (0.05, cols(out), "V"))
 
     def ts(out, a, s1, o1, s2=None, o2=None):
         x1 = s1[4] if isap(s1) else s1
@@ -295,39 +407,48 @@ def rank_program(g, core, T, topo):
             if isap(bias):
                 rd.append(bias)
         src = a[4] if off is None else a[4].indirect(off[4])
-        op("s", lambda: S.activation(out[4], src, f, **kw), rd, [out], FS + cols(out) * CY * CS if off is None else FI + cols(out) * CY * CS * GA)
+        op("s", lambda: S.activation(out[4], src, f, **kw), rd, [out], (0.09, cols(out), "s") if off is None else (0.065, cols(out), "S"))
 
-    def mm(out, l, r, start=True, stop=True, f32=False, ext=None, also=None):
+    def mm(out, l, r, start=True, stop=True, f32=False, ext=None):
         n = max(min(64, cols(l)), cols(r))
-        op("t", lambda: TE.matmul(out[4], l[4], r[4], start, stop), [l, r] + ([also] if also else []), [out], FT + n * (4 if f32 else 1) * CY * CT, "c", ext)
+        op("t", lambda: TE.matmul(out[4], l[4], r[4], start, stop), [l, r], [out], (0.0, n * (4 if f32 else 1), "t"), "c", ext)
 
     def dma(q, out, src, reads, writes, us):
         eng = g.sync if q == "y" else g.scalar
-        op(q, lambda: eng.dma_start(out, src), reads, writes, 0.06, "d", us)
+        op(q, lambda: eng.dma_start(out, src), reads, writes, (0.06, 0, "v"), "d", us)
 
     def iota(out, pat, base, cm=0):
         kw = {} if VIRT[out[0]][0] == "pooli" else {"allow_small_or_imprecise_dtypes": True}
-        op("g", lambda: g.iota(out[4], pat, base, cm, **kw), [], [out], 0.13 + 2 * cols(out) * CY)
+        op("g", lambda: g.iota(out[4], pat, base, cm, **kw), [], [out], (0.13, 2 * cols(out), "v"))
 
     def const(out, x):
         iota(out, [[0, cols(out)]], int(x))
 
-    def keep(out, a, pat, o, other, base=0, cm=1):
-        op("g", lambda: g.affine_select(out[4], a[4], pat, o, other, base, cm), [a], [out], 0.17 + 2 * cols(out) * CY)
+    def keep(out, a, pat, o, other, base=0, cm=1, also=()):
+        op("g", lambda: g.affine_select(out[4], a[4], pat, o, other, base, cm), [a] + list(also), [out], (0.17, 2 * cols(out), "v"))
+
+    def copy(q, out, a):
+        if q == "g":
+            keep(out, a, [[0, cols(out)]], OP.is_ge, 0.0, 0, 0)
+        elif q == "s":
+            act(out, a, AF.Copy)
+        else:
+            cp(out, a)
 
     def load(q, name, lo, hi, src, us, rows=None):
         o = b(name, lo, hi, 1, rows)
         dma(q, o[4], src, [], [o], us)
+        ops[-1]["after"] = set([i for i, x in enumerate(ops[:-1]) if x["q"] == q][-1:])
 
-    load("y", "PT", M, M + VI * L, T.q[:], 2.0)
+    load("y", "PT", M, M + L, T.q[:, 0:L], 2.0)
     load("s", "wi", 0, 1, T.w[:], 2.0)
-    load("y", "PT", 0, M, T.pt[:], 4.5)
-    load("s", "CHI", 0, 128, T.ch[:, 0:128], 2.2)
+    load("y", "CHI", 0, 128, T.ch[:, 0:128], 2.2)
+    load("s", "PT", 0, 128, T.pt[:, 0:128], 2.2)
     load("s", "r0i", 0, 128, T.r0[:], 2.2, 48)
-    CHP = (128, 1536, 2944, M)
-    for k in range(3):
-        load("y", "CHI", CHP[k], CHP[k + 1], T.ch[:, CHP[k]:CHP[k + 1]], 6.0 + 1.5 * k)
-    load("s", "thi", 0, 1, T.th[:], 2.5)
+    load("y", "PT", 128, M, T.pt[:, 128:M], 5.0)
+    load("y", "CHI", 128, M, T.ch[:, 128:M], 10.0)
+    load("y", "PT", M + L, M + VI * L, T.q[:, L:VI * L], 10.5)
+    load("s", "thi", 0, 1, T.th[:], 10.5)
 
     DIAG = [[-1, 128]]
     fill(b("ONES"), 1.0)
@@ -337,55 +458,68 @@ def rank_program(g, core, T, topo):
     iota(b("j15"), [[0, 16], [1, 16]], 0)
     keep(b("IDB"), b("ONES", 0, 128), DIAG, OP.is_equal, 0.0)
     iota(b("li", 16, 24), [[16, 8]], 15)
-    iota(b("li", 24, 72), [[1, 6], [8, 8]], 2)
-    iota(b("li", 72, 80), [[2, 8]], 0)
-    op("g", lambda: g.affine_select(b("R")[4], b("ONES")[4], [[-1, 128], [0, 16]], OP.is_equal, 0.0, 0, 1),
-       [b("ONES"), b("IDB"), b("li", 0, 72)], [b("R")], 0.17 + 2 * 2048 * CY)
+    iota(b("li", 24, 120), [[1, 6], [8, 16]], 2)
+    iota(b("li", 120, 128), [[2, 8]], 0)
+    for k in (1, 2, 0):
+        keep(b("R", 512 * k, 512 * k + 512), b("ONES"), [[-1, 32], [0, 16]], OP.is_equal, 0.0, -32 - 32 * k, 1, [b("IDB"), b("li", 0, 120)])
     ts(b("pi", 1, 2), b("pi", 0, 1), 15, OP.bitwise_and)
     ts(b("pi", 2, 3), b("pi", 0, 1), 4, OP.arith_shift_right)
     ts(b("pi", 3, 4), b("pi", 0, 1), 3, OP.arith_shift_right, 1, OP.bitwise_and)
     cp(b("pf", 0, 4), b("pi", 0, 4))
     P15, P4, P3 = [b("pf", k, k + 1) for k in range(1, 4)]
     cp(b("LI", 0, 16), b("li", 0, 16))
-    cp(b("LI", 16, 72), b("li", 16, 72))
-    BC16, BC8, BC15, BH = b("LI", 0, 16), b("LI", 0, 8), b("LI", 16, 24), b("LI", 72, 80)
-    BC4, BC3 = b("LI", 96, 112), b("LI", 112, 136)
-    BCS = [b("LI", 24 + 8 * s, 32 + 8 * s) for s in range(6)]
+    cp(b("LI", 16, 120), b("li", 16, 120))
+    BC16, BC8, BC15, BH = b("LI", 0, 16), b("LI", 0, 8), b("LI", 16, 24), b("LI", 120, 128)
+    BC4 = b("LI", 128, 144)
+    BCS = lambda s, k: b("LI", 24 + 16 * s, 24 + 16 * s + 8 * k)
     ts(b("LC"), b("c8"), P4, OP.is_equal)
     cp(b("wf", 0, 1), b("wi", 0, 1))
     ts(b("WB"), b("LC"), b("wf", 0, 1), OP.mult)
     ts(b("DM"), b("j15"), P15, OP.is_equal)
-    for name, x in (("LCB", 1.0), ("BLK", 65536.0), ("BLKU", 65536.0 * U), ("BLKW", WIDE), ("LC2", 2.0)):
+    for name, x in (("LCB", 1.0), ("BLK", 65536.0), ("BLKU", 65536.0 * U), ("NBLKU", -65536.0 * U), ("BLKW", WIDE), ("NBLKW", -WIDE), ("LC2", 2.0)):
         act(b(name), b("LC"), AF.Copy, scale=x)
     act(b("NIDB"), b("IDB"), AF.Copy, scale=-1.0)
     act(b("IDF"), b("IDB"), AF.Copy)
     ts(b("GO"), b("j15"), 1.0, OP.min)
-    fill(b("DS"), -16.0)
+    fill(b("DS", 128, 384), -16.0 * 65536)
+    for k in range(2):
+        act(b("GQ", 512 * k, 512 * k + 512), b("ONES"), AF.Copy)
+        fill(b("QS", 1024 * k, 1024 * k + 16 * NV[0][k]), 0.0)
+    fill(b("GQ", 0, 1024, 16), 0.0)
     fill(b("MX"), -BIG)
     fill(b("MX", 0, 128, 16), BIG)
-    act(b("bias", 0, 1), P15, AF.Identity, scale=4096.0 * U, bias=CO * U)
-    act(b("bias", 1, 2), P15, AF.Copy, scale=4096.0)
+    if PFQ == "h":
+        act(b("ROWH", 0, 128), b("j15", 0, 128), AF.Identity, scale=4096.0 * U, bias=(CO + 2048) * U)
+        act(b("ROWH", 128, 256), b("j15", 0, 128), AF.Identity, scale=4096.0, bias=2048.0)
+        act(b("IDH", 0, 128), b("IDB"), AF.Copy, scale=2.0 ** -14)
+        act(b("IDH", 128, 256), b("IDB"), AF.Copy)
+    elif PFQ == "g":
+        act(b("ROWC", 0, 128), b("j15", 0, 128), AF.Identity, scale=4096.0 * U, bias=CO * U)
+        act(b("IDU"), b("IDB"), AF.Copy, scale=U)
+    else:
+        act(b("bias", 0, 1), P15, AF.Identity, scale=4096.0 * U, bias=CO * U)
+        act(b("bias", 1, 2), P15, AF.Copy, scale=4096.0)
     cp(b("r0f", rows=48), b("r0i", rows=48))
     mm(b("MB", 0, 48), b("r0f", rows=48), b("IDF", 0, 48, rows=48), f32=True)
     const(b("FR"), 0)
     act(b("RKS"), b("ONES", 0, 128), AF.Copy)
     for h in range(2):
-        act(b("RKS", 64 * h + 2, 64 * h + 64, 8), b("MB", h, 48, 6), AF.Identity, scale=65536.0 * U, bias=CO * U)
+        act(b("RKS", 64 * h + 2, 64 * h + 64, 8), b("MB", h, 48, 6), AF.Identity, scale=65536.0 * U, bias=8 * 65536.0 * U)
     for k in range(2, 6):
         act(b("FR", 32 * k, 32 * k + 32, 4), b("MB", k, 48, 6), AF.Copy, scale=16.0)
-    act(b("CH", M, ROOM), b("ONES", 0, ROOM - M), AF.Copy, scale=0.0)
-    cp(b("CH", 0, 128), b("CHI", 0, 128))
-    fill(b("PT", 0, 1), 2048.0)
+    fill(b("PT", 0, 1), 128.0)
 
     def late_constants():
-        for k in range(3):
-            if k == 2:
-                cp(b("CH", CHP[k], CHP[k + 1]), b("CHI", CHP[k], CHP[k + 1]))
-            else:
-                keep(b("CH", CHP[k], CHP[k + 1]), b("CHI", CHP[k], CHP[k + 1]), [[0, CHP[k + 1] - CHP[k]]], OP.is_ge, 0.0, 0, 0)
+        for k in range(0, M, 448):
+            copy("g", b("CH", k, k + 448), b("CHI", k, k + 448))
+        for k in range(M, ROOM, 384):
+            const(b("CH", k, k + 384), 0)
         const(b("NONE"), -1)
-        iota(b("ROWB"), [[0, 8], [4096, 16]], 0)
-        keep(b("WI"), b("IDB"), DIAG, OP.not_equal, 2.0 ** 26)
+        for k in (0, 384):
+            const(b("DS", k, k + 128), -4096)
+        act(b("WI"), b("IDB"), AF.Copy, scale=2.0 ** 26)
+        if PFQ == "g":
+            act(b("ROWC", 128, 256), b("j15", 0, 128), AF.Copy, scale=4096.0)
         const(b("m", 0, 8), 0)
         x = b("EF", 0, 128)
         fill(x, 0.5)
@@ -393,50 +527,42 @@ def rank_program(g, core, T, topo):
            [x, b("NONE")], [b("EF", 128, 256)], vc(128))
         keep(b("EF", 256, 384), b("EF", 128, 256), DIAG, OP.is_equal, 0.0)
         act(b("WD"), b("EF", 256, 384), AF.Copy, scale=-2.5)
-        mm(b("MB", 80, 81), b("WD"), b("ONES", 0, 1))
-        act(b("WL", 0, 1), b("MB", 80, 81), AF.Copy, scale=-0.4)
-        act(b("WL", 1, 2), b("MB", 80, 81), AF.Copy, scale=0.4)
         send(T.wn[:, 0:1], b("wi", 0, 1), -1, VI - 1)
-        ts(b("RL", 0, 8), b("c8"), P4, OP.is_gt, -1.0, OP.mult)
-        act(b("RL", 8, 16), b("LC"), AF.Copy, scale=-1.0)
-        iota(b("li", 80, 96), [[4, 16]], 3)
-        iota(b("li", 96, 120), [[0, 3], [1, 8]], 0)
-        cp(b("LI", 96, 136), b("li", 80, 120))
+        iota(b("li", 128, 144), [[4, 16]], 3)
+        cp(b("LI", 128, 144), b("li", 128, 144))
+        const(b("PK"), FLAG)
+        const(b("OUT", 48, 96), 0)
         for h in range(2):
-            iota(b("bias", 2 + h, 3 + h), [[0, 1]], 256 * (h + 1), 2 * (h + 1))
-            act(b("RL", 16 + 8 * h, 24 + 8 * h), b("LC"), AF.Copy, scale=b("bias", 2 + h, 3 + h))
-            const(b("PK%d" % h), FLAG)
+            x = b("TRS", 128 * h, 128 * h + 128)
+            iota(x, [[0, 128]], 256 * (h + 1), 2 * (h + 1))
+            keep(x, x, DIAG, OP.is_equal, 0.0)
+            keep(x, x, DIAG, OP.is_ge, -1.0)
             const(b("SND%d" % h, 0, CAP), 0)
             const(b("RCV%d" % h, CAP, L), 0)
         const(b("SEL"), 1)
         keep(b("SEL"), b("SEL"), [[-16, 8], [-4, 4]], OP.is_equal, 0.0)
         x = b("bias", 4, 5)
         const(x, 0)
-        keep(x, x, [[0, 1]], OP.is_ge, c0, -16)
-        keep(x, x, [[0, 1]], OP.is_ge, 0.0, -8)
+        keep(x, x, [[0, 1]], OP.is_ge, c0, -32)
+        keep(x, x, [[0, 1]], OP.is_ge, 0.0, -16)
         cp(b("thf", 0, 1), b("thi", 0, 1))
         ts(b("TB"), b("SEL", 0, 32, 4), b("thf", 0, 1), OP.mult)
-        mm(b("MB", 64, 72), b("ONES", 0, 128), b("TB"))
-        act(b("THK"), b("MB", 64, 72), AF.Identity, scale=WIDE, bias=4096.0)
-        tg(b("THX", 0, 128), b("THK"), BC8, b("ONES", 0, 128), OP.mult)
-        ts(b("EF", 512, 640), b("j15", 0, 128), P15, OP.is_gt)
-        tg(b("THX", 128, 256), b("THK"), BC8, b("EF", 512, 640), OP.mult)
-        tg(b("THX", 256, 384), b("THK"), BC8, b("DM", 0, 128), OP.mult)
-        act(b("THX"), b("THX"), AF.Identity, bias=-8192.0)
-        iota(b("K4096", 0, 2), [[-128, 2]], -4096, -1)
+        iota(b("K4096"), [[-128, 2], [0, 8]], -4096, -1)
         iota(b("KC"), [[16, 16]], 0)
         act(b("bias", 5, 6), P15, AF.Identity, bias=4096.0)
-        x = b("SELG", rows=16)
-        keep(x, b("ONES", 0, 1024, rows=16), [[-2, 8], [0, 128]], OP.is_ge, 0.0)
-        keep(x, x, [[2, 8], [0, 128]], OP.is_ge, 0.0, 1, -1)
+        for k in range(2):
+            x = b("SELG", 512 * k, 512 * k + 512, rows=16)
+            keep(x, b("ONES", rows=16), [[-2, 4], [0, 128]], OP.is_ge, 0.0, -8 * k)
+            keep(x, x, [[2, 4], [0, 128]], OP.is_ge, 0.0, 1 + 8 * k, -1)
+            x = b("NSELG", 512 * k, 512 * k + 512, rows=16)
+            const(x, -1)
+            keep(x, x, [[-2, 4], [0, 128]], OP.is_ge, 0.0, -8 * k)
+            keep(x, x, [[2, 4], [0, 128]], OP.is_ge, 0.0, 1 + 8 * k, -1)
         iota(b("DGL"), [[0, 128]], 0, 1)
         keep(b("DGL"), b("DGL"), DIAG, OP.is_equal, 0.0)
         for k in range(4):
             keep(b("DGB", 128 * k, 128 * k + 128), b("IDB"), DIAG, OP.not_equal, float(M + 128 * k))
-        ts(BH, b("li", 72, 80), P3, OP.add)
-
-    def share(t, p, h):
-        return NVL[h] if (t, p) == (VI - 1, 4) else NV0[p][h] if t == 0 and p < 2 else NV[p][h]
+        ts(BH, b("li", 120, 128), P3, OP.add)
 
     def begin(t):
         q0 = M + L * t
@@ -449,12 +575,13 @@ def rank_program(g, core, T, topo):
                 mm(b("MA", 64 + 32 * h, 96 + 32 * h), b(r, 128 * h, 128 * h + 128), b("SEL"), f32=True, ext=t - 1)
             tt(b("PM"), b("MA", 64, 128), b("FR", 64 * t, 64 * t + 64), OP.max)
             ts(b("PD"), b("PM"), 4, OP.arith_shift_right, 2 ** 18 - 1, OP.bitwise_and)
-            tg(b("ZR"), b("PD"), BC4, b("DM"), OP.mult)
+            for lo, hi in ((0, 1), (1, 2)) if ZRS else ((0, 2),):
+                tg(b("ZR", 128 * lo, 128 * hi), b("PD"), b("LI", 128 + 8 * lo, 128 + 8 * hi), b("DM", 128 * lo, 128 * hi), OP.mult)
             tt(b("MI"), b(r, 0, CAP), b("KP0", 0, CAP), OP.max, ext=t - 1)
             ts(b("QI"), b("MI"), 15, OP.bitwise_and)
-            cp(b("PT", q0, q0 + CAP), b("QI"))
+            copy(PTQ, b("PT", q0, q0 + CAP), b("QI"))
             root = b("PD", 3, 64, 4)
-            act(b("RKS", 2, 128, 8), b("PD", 0, 64, 4), AF.Identity, scale=65536.0 * U, bias=CO * U)
+            act(b("RKS", 2, 128, 8), b("PD", 0, 64, 4), AF.Identity, scale=65536.0 * U, bias=8 * 65536.0 * U)
         else:
             for h in range(2):
                 mm(b("KP0", 256 + 8 * h, 264 + 8 * h), Qh[h], b("WB"))
@@ -462,145 +589,186 @@ def rank_program(g, core, T, topo):
             root = b("sn")
             ts(root, b("sm"), 63, OP.bitwise_and)
             tg(b("ZR"), root, BC16, b("DM"), OP.mult)
+        for lo, hi in ((0, 1), (1, 2)) if ZRS and t else ((0, 2),):
+            for h in range(lo, hi):
+                mm(b("KP1", 272 + 8 * h, 280 + 8 * h), b("ZR", 128 * h, 128 * h + 128), b("LCB"))
+            ts(b("OFF", 8 * lo, 8 * hi), b("KP1", 272 + 8 * lo, 272 + 8 * hi), 1.0, OP.add)
         for h in range(2):
-            mm(b("KP1", 272 + 8 * h, 280 + 8 * h), b("ZR", 128 * h, 128 * h + 128), b("LCB"))
-        ts(b("OFF"), b("KP1", 272, 288), 1.0, OP.add)
-        lo = 96 - max(share(t, p, 0) for p in range(5))
-        hi = 128 + max(share(t, p, 1) for p in range(5))
-        for i in range(16):
-            o, q = b("Q16", 16 * lo + i, 16 * hi, 16), b("PT", q0 + lo, q0 + hi)
-            if i < QV:
-                cp(o, q)
-            else:
-                act(o, q, AF.Copy)
+            nv = max(x[h] for x in NV)
+            x, y, z = 1024 * h, 1024 * h + 16 * NV[0][h], 1024 * h + 16 * nv
+            copy(GQS[2 + h], b("QS", x, y, 16), b("PT", q0 + 128 * h, q0 + 128 * h + NV[0][h]))
+            scan(b("Q16", x, y), b("GQ", 0, y - x), b("QS", x, y), OP.mult, OP.add)
+            for i in range(16 if y < z else 0):
+                copy("g", b("Q16", y + i, z, 16), b("PT", q0 + 128 * h + NV[0][h], q0 + 128 * h + nv))
         for h in range(2):
             mm(b("SP2", 128 * h, 128 * h + 128), Qh[h], b("NIDB"))
         act(b("NQT"), b("SP2", 0, 256), AF.Copy)
-        if DRV:
+        if DRQ == "v":
             tg(b("DRB"), b("PT", 0, 128), b("OFF"), Q, OP.subtract)
             act(b("DRB"), b("DRB"), AF.Abs)
         else:
             act(b("DRB"), b("PT", 0, 128), AF.Copy, off=b("OFF"))
-            mm(b("SP3", 0, 256), b("NIDB"), Q, True, False)
-            mm(b("SP3", 0, 256), b("IDB"), b("DRB"), False, True)
-            act(b("DRB"), b("SP3", 0, 256), AF.Abs)
-        act(b("RT"), root, AF.Copy)
+            mm(b("KP0", 256, 512), b("NIDB"), Q, True, False)
+            mm(b("KP0", 256, 512), b("IDB"), b("DRB"), False, True)
+            act(b("DRB"), b("KP0", 256, 512), AF.Abs)
+        copy(GQS[0], b("RT"), root)
         for h in range(2):
-            mm(b("MA", 48 + 8 * h, 56 + 8 * h), b("DRB", 128 * h, 128 * h + 128), b("LCB"))
-        act(b("DS", 0, 256, 16), b("MA", 48, 64), AF.Copy)
+            mm(b("KP1", 336 + 8 * h, 344 + 8 * h), b("DRB", 128 * h, 128 * h + 128), b("BLK"))
         for h in range(2):
-            mm(b("MA", 32 + 8 * h, 40 + 8 * h), b("DRB", 128 * h, 128 * h + 128), b("BLK"), True, False)
-            mm(b("MA", 32 + 8 * h, 40 + 8 * h), b("IDB"), b("RT", 8 * h, 8 * h + 8), False, True)
-        act(b("K0U"), b("MA", 32, 48), AF.Identity, scale=U, bias=(CO + 1) * U)
-        act(b("K0"), b("MA", 32, 48), AF.Identity, bias=CO + 32768 + 1)
-        scan(b("E"), b("GO"), b("DS"), OP.mult, OP.add)
-        act(b("A"), b("E"), AF.Abs, scale=65536.0 * U, bias=-CO * U)
+            mm(b("KP1", 352 + 8 * h, 360 + 8 * h), b("DRB", 128 * h, 128 * h + 128), b("BLK"), True, False)
+            mm(b("KP1", 352 + 8 * h, 360 + 8 * h), b("IDB"), b("RT", 8 * h, 8 * h + 8), False, True)
+        act(b("DS", 128, 384, 16), b("KP1", 336, 352), AF.Copy)
+        act(b("K0U"), b("KP1", 352, 368), AF.Identity, scale=U, bias=(CO + 1) * U)
+        act(b("K0"), b("KP1", 352, 368), AF.Identity, bias=CO + 32768 + 1)
+        scan(b("E", 128, 384), b("GO"), b("DS", 128, 384), OP.mult, OP.add)
+        act(b("A"), b("E", 128, 384), AF.Abs, scale=U, bias=-CO * U)
+        for lo, hi in ((0, 2),) if JM else ((0, 1), (1, 2)):
+            first_mask(0, lo, hi)
         tt(b("RKS", 3, 128, 8), b("RKS", 2, 128, 8), b("K0U"), OP.min)
+
+    def first_mask(p, lo, hi):
+        tg(b("M1", 128 * lo, 128 * hi), b("RKS", 64 * lo, 64 * hi), BCS(p + 1 if p else 0, hi - lo), b("A", 128 * lo, 128 * hi), OP.is_lt)
+
+    def ramp(p, h):
+        d, r = 128 + 128 * h, 384 * h
+        sk = b("SK", 16 * p + 8 * h, 16 * p + 8 * h + 8)
+        if p in (1, 2):
+            ts(b("DK", 8 * h, 8 * h + 8), sk, 0xFF0000, OP.bitwise_and)
+            copy(DSQ, b("DS", d, d + 128, 16), b("DK", 8 * h, 8 * h + 8))
+            slot[2] = "RP"
+            tt(b("DS", r, r + 128, 16), sk, b("RB", 8 * h, 8 * h + 8), OP.min)
+            scan(b("E", 256 * h, 256 * h + 256), b("GO"), b("DS", 256 * h, 256 * h + 256), OP.mult, OP.add)
+            ts(b("ST", 128 * h, 128 * h + 128), b("E", r, r + 128), 0.0, OP.is_equal)
+        else:
+            ts(b("DS", d, d + 128, 16), sk, RND, OP.add, RND, OP.subtract)
+            scan(b("E", d, d + 128), b("GO", 0, 128), b("DS", d, d + 128), OP.mult, OP.add)
+        act(b("A", 128 * h, 128 * h + 128), b("E", d, d + 128), AF.Abs, scale=U, bias=-15.5 * 65536 * U)
+        first_mask(p + 1, h, h + 1)
 
     def push(t, h, p):
         hs = str(h)
         n = lambda x, *a: b(x + hs, *a)
         KP = "KP" + hs
         kp = b(KP, 0, 128)
-        ch = b("CH", 0, 128 if p == 0 else 4096)
+        ch = b("CH" if t else "CHI", 0, 128 if p == 0 else 4096 if t else M)
         off = b("OFF", 8 * h, 8 * h + 8)
-        A = b("A", 128 * h, 128 * h + 128)
-        pt = b("PT", 0, 4096)
-        if PUS:
+        A, KS, MS = [b(x, 128 * h, 128 * h + 128) for x in ("A", "KS", "MS")]
+        last = lambda x: b(x, 128 * h + 15, 128 * h + 128, 16)
+        pt = b("PT", 0, M + L * t)
+        if PUQ == "s":
             act(n("PU"), ch, AF.Copy, off=off)
         else:
-            op("v", lambda: V.tensor_copy(n("PU")[4], ch[4].indirect(off[4])), [ch, off], [n("PU")], FV + 128 * GA * CY)
-        act(n("Pf"), ch, AF.Identity, bias=b("bias", p // 4, p // 4 + 1), scale=1.0 if p == 4 else U, off=off)
-        rks = b("RKS", 64 * h, 64 * h + 64)
-        tg(n("M1"), rks, BCS[p + 1 if p else 0], A, OP.is_lt)
-        mm(kp, n("Pf"), b("IDF"), True, False, f32=True)
-        mm(kp, b("WI" if p == 4 else "IDB"), n("M1"), False, False)
-        if p in (2, 3):
-            mm(kp, b("IDB"), n("ST"), False, False)
-        nv = share(t, p, h)
-        v0 = 96 - nv if h == 0 else 0
-        c = 16 * (96 - nv)
-        for k, (s0, lo, hi) in enumerate(((0, 1024 - c, 1024), (96, 1024, 1536)) if h == 0 else ((nv, 2048, 2048 + c), (96, 1536, 2048))):
-            cut = [lo] + [x for x in range(512, 3072, 512) if lo < x < hi] + [hi]
-            at = [16 * s0 + x - lo for x in cut]
-            d = b("DIFF", 2048 * h + at[0], 2048 * h + at[-1])
-            slot[2] = "get%d" % k
-            act(d, pt, AF.Copy, off=n("PU", at[0] // 16, at[-1] // 16))
-            banks = [b(RING[x // 512], x % 512, x % 512 + y - x) for x, y in zip(cut, cut[1:])]
-            for j, ps in enumerate(banks):
-                mm(ps, b("NQT", 128 * h, 128 * h + 128), b("R", at[j], at[j + 1]), True, False)
-            slot[2] = "abs%d" % k
-            for j, ps in enumerate(banks):
-                mm(ps, b("IDB"), b("DIFF", 2048 * h + at[j], 2048 * h + at[j + 1]), False, True)
-            op("s", lambda d=d, lo=lo, hi=hi: S.activation(d[4], T.RING[:, lo:hi], AF.Abs), banks, [d], FS + (hi - lo) * CY * CS)
-        cut = [v0 + nv * k // VP // 2 * 2 for k in range(VP)] + [v0 + nv]
-        for k in range(VP):
-            lo, hi = cut[k], cut[k + 1]
+            op("v", lambda: V.tensor_copy(n("PU")[4], ch[4].indirect(off[4])), [ch, off], [n("PU")], (0.05, 128, "V"))
+        if PFQ == "h":
+            x = 1.0 if p == 4 else 2.0 ** -12
+            if PHQ == "s":
+                act(n("Ph"), n("PU"), AF.Identity, bias=-2048 * x, scale=x)
+            else:
+                ts(n("Ph"), n("PU"), -2048.0, OP.add, x, OP.mult)
+            slot[2] = "row"
+            mm(kp, b("IDH", 128, 256), b("ROWH", 128 * (p // 4), 128 * (p // 4) + 128), True, False)
+            slot[2] = "Pf"
+            mm(kp, n("Ph"), b("IDH", 128 * (p // 4), 128 * (p // 4) + 128), False, False)
+        else:
+            if PFQ == "s":
+                act(n("Pf"), n("PU"), AF.Identity, bias=b("bias", p // 4, p // 4 + 1), scale=1.0 if p == 4 else U)
+            else:
+                copy("g", n("Pf"), n("PU"))
+                slot[2] = "row"
+                mm(kp, b("IDB"), b("ROWC", 128 * (p // 4), 128 * (p // 4) + 128), True, False)
+            slot[2] = "Pf"
+            mm(kp, n("Pf"), b("IDU" if p < 4 and PFQ == "g" else "IDF"), PFQ != "g", False, f32=True)
+        nv = NV[p][h]
+        cut = [nv] + [x for x in CUT if x > nv] + [128]
+        for k, (lo, hi) in enumerate(zip(cut, cut[1:])):
             d = b("DIFF", 2048 * h + 16 * lo, 2048 * h + 16 * hi)
+            slot[2] = "get%d" % k
+            act(d, pt, AF.Copy, off=n("PU", lo, hi))
+            bc = [lo] + [x for x in (64, 96) if lo < x < hi] + [hi]
+            banks = [b(RING[3 * h + x // 32 - 1], 16 * (x % 32), 16 * (x % 32 + y - x)) for x, y in zip(bc, bc[1:])]
+            for ps, x, y in zip(banks, bc, bc[1:]):
+                mm(ps, b("NQT", 128 * h, 128 * h + 128), b("R", 16 * x - 512, 16 * y - 512), True, False)
+            slot[2] = "abs%d" % k
+            for ps, x, y in zip(banks, bc, bc[1:]):
+                mm(ps, b("IDB"), b("DIFF", 2048 * h + 16 * x, 2048 * h + 16 * y), False, True)
+            c = 1536 * h - 512
+            op("s", lambda d=d, lo=c + 16 * lo, hi=c + 16 * hi: S.activation(d[4], T.RING[:, lo:hi], AF.Abs), banks, [d], (0.09, 16 * (hi - lo), "s"))
+        cut = [nv * k // VP // 2 * 2 for k in range(VP)] + [nv]
+        for k in range(VP):
+            lo, hi = 16 * cut[k], 16 * cut[k + 1]
             slot[2] = "vec%d" % k
-            tg(d, pt, n("PU", lo, hi), b("Q16", 2048 * h + 16 * lo, 2048 * h + 16 * hi), OP.subtract)
-            if (k + 1) % VA == 0:
-                d = b("DIFF", 2048 * h + 16 * cut[k + 1 - VA], 2048 * h + 16 * hi)
-                slot[2] = "vec%d" % (k // VA)
-                act(d, d, AF.Abs)
-        blk = b("BLKW" if p == 4 else "BLKU")
-        for lo, hi in ((0, 96), (96, 128)) if KSP else ((0, 128),):
-            slot[2] = "key" if lo or not KSP else "kez"
-            for i0 in range(0, 16, KG):
-                def sums(lo=lo, hi=hi, i0=i0):
-                    return [TE.matmul(b(KP, i, 128, 16, hi - lo, lo)[4], b("DIFF", 2048 * h + 16 * lo + i, 2048 * h + 16 * hi, 16)[4],
-                                      blk[4], False, i == 15 and hi == 128) for i in range(i0, i0 + KG)][-1]
-                op("t", sums, [b("DIFF", 2048 * h + 16 * lo, 2048 * h + 16 * hi), blk], [kp], KG * (FT + min(64, hi - lo) * CY * CT))
-        scan(n("KS"), b("MX"), kp, OP.max, OP.min)
+            tg(b("RAW", 1024 * h + lo, 1024 * h + hi), pt, n("PU", cut[k], cut[k + 1]), b("Q16", 1024 * h + lo, 1024 * h + hi), OP.subtract)
+        if JUNK:
+            x = (b("EQ", 0, JUNK), b("RAW", 1024 * h, 1024 * h + JUNK), b("Q16", 1024 * h, 1024 * h + JUNK))
+            op("v", lambda: V.tensor_tensor(x[0][4], x[1][4], x[2][4], OP.max), [x[1], x[2]], [x[0]], vc(JUNK, 1.5))
+        slot[2] = "relu"
+        if RELU[p]:
+            ts(b("DIFF", 2048 * h, 2048 * h + 16 * nv), b("RAW", 1024 * h, 1024 * h + 16 * nv), 0.0, OP.max, 2.0, OP.mult)
+        else:
+            act(b("DIFF", 2048 * h, 2048 * h + 16 * nv), b("RAW", 1024 * h, 1024 * h + 16 * nv), AF.Abs)
+
+        def sums(lab, src, at, lo, hi, blk, stop=False):
+            slot[2] = lab
+            op("t", lambda: [TE.matmul(b(KP, i, 128, 16, hi - lo, lo)[4], b(src, at + 16 * lo + i, at + 16 * hi, 16)[4], blk[4], False, stop and i == 15)
+                             for i in range(16)][-1], [b(src, at + 16 * lo, at + 16 * hi), blk], [kp], (0.0, 16 * min(64, hi - lo), "t"))
+        w = "W" if p == 4 else "U"
+        if RELU[p]:
+            sums("neg", "RAW", 1024 * h, 0, nv, b("NBLK" + w))
+        cut = (0,) + KSP
+        for k in range(len(KSP)):
+            sums("key%d" % k, "DIFF", 2048 * h, cut[k], cut[k + 1], b("BLK" + w))
+        if p in (2, 3):
+            slot[2] = "ST"
+            mm(kp, b("IDB"), b("ST", 128 * h, 128 * h + 128), False, False)
+        if KSP:
+            sums("key", "DIFF", 2048 * h, cut[-1], 128, b("BLK" + w))
+        slot[2] = "M1"
+        mm(kp, b("WI" if p == 4 else "IDB"), b("M1", 128 * h, 128 * h + 128), False, bool(KSP))
+        if not KSP:
+            sums("key", "DIFF", 2048 * h, 0, 128, b("BLK" + w), True)
+        scan(KS, b("MX"), kp, OP.max, OP.min)
         if p == 4:
             return
-        tt(b("RKS", 64 * h + p + 4, 64 * h + 64, 8), b("RKS", 64 * h + p + 3, 64 * h + 64, 8), n("KS", 15, 128, 16), OP.min)
         if p == 0:
-            tg(n("M2"), rks, BCS[2], A, OP.is_lt)
+            tt(b("RKS", 64 * h + 4, 64 * h + 64, 8), b("RKS", 64 * h + 3, 64 * h + 64, 8), last("KS"), OP.min)
+            tg(n("M2"), b("RKS", 64 * h, 64 * h + 64), BCS(2, 1), A, OP.is_lt)
         else:
-            tg(n("M2"), n("KS"), BC15, A, OP.is_lt)
+            tg(n("M2"), KS, BC15, A, OP.is_lt)
         tt(n("KM"), kp, n("M2"), OP.add)
-        scan(n("MS"), b("MX"), n("KM"), OP.max, OP.min)
-        sk, dk = n("SK", 8 * p, 8 * p + 8), b("DK", 8 * h, 8 * h + 8)
-        if p in (0, 3):
-            ts(sk, n("MS", 15, 128, 16), 0.25, OP.min, 1 / U, OP.mult)
-        else:
-            ts(n("z3"), n("MS", 15, 128, 16), 32768.0 * U - 0.25, OP.add, 1 / U, OP.mult)
-            tt(sk, n("z3"), b("K0", 8 * h, 8 * h + 8) if p == 1 else n("FB"), OP.min)
-        ts(n("NN"), sk, 4095, OP.bitwise_and)
-        tg(n("Z"), n("NN"), BC8, b("DM", 0, 128), OP.mult)
-        slot[2] = "list"
-        mm(b(KP, 128, 136), n("Z"), b("LC"), f32=True)
-        if OFS:
-            act(off, b(KP, 128, 136), AF.Copy)
-        else:
-            cp(off, b(KP, 128, 136))
+        scan(MS, b("MX"), n("KM"), OP.max, OP.min)
+        sk = b("SK", 16 * p + 8 * h, 16 * p + 8 * h + 8)
         if p in (1, 2):
-            ts(dk, sk, 16, OP.arith_shift_right, 255, OP.bitwise_and)
-            ts(n("RB"), n("FB") if p == 1 else n("SK", 8, 16), 0xF000, OP.bitwise_and)
-            tt(n("RP"), sk, n("RB"), OP.min)
-            tg(n("ST"), n("RP"), BC8, b("ROWB"), OP.is_equal)
+            ts(n("z3"), last("MS"), 32768.0 * U - 0.25, OP.add, 1 / U, OP.mult)
+            tt(sk, n("z3"), b("K0" if p == 1 else "FB", 8 * h, 8 * h + 8), OP.min)
         else:
-            ts(dk, n("MS", 15, 128, 16), 1 / (65536 * U), OP.mult)
-        if p == 0:
-            ts(n("FB"), sk, 32768.0, OP.add)
-        e = b("E", 128 * h, 128 * h + 128)
-        cp(b("DS", 128 * h, 128 * h + 128, 16), dk)
-        scan(e, b("GO", 0, 128), b("DS", 128 * h, 128 * h + 128), OP.mult, OP.add)
-        act(A, e, AF.Abs, scale=65536.0 * U, bias=-15.5 * 65536 * U)
+            ts(sk, last("MS"), 0.25, OP.min, 1 / U, OP.mult)
+        ts(n("NN"), sk, 4095, OP.bitwise_and)
+        tg(n("ZL"), n("NN"), BC8, b("DM", 0, 128), OP.mult)
+        slot[2] = "list"
+        mm(b(KP, 128, 136), n("ZL"), b("LC"), f32=True)
+        copy(OFQ, off, b(KP, 128, 136))
+        if h and p:
+            tt(b("RKS", p + 4, 128, 8), b("RKS", p + 3, 128, 8), b("KS", 15, 256, 16), OP.min)
+        if h and p == 0:
+            ts(b("FB"), b("SK", 0, 16), 32768.0, OP.add)
+        if h and p in (1, 2):
+            ts(b("RB"), b("FB") if p == 1 else b("SK", 16, 32), 0xF000, OP.bitwise_and)
+        for k in range(2 * h):
+            slot[0] = (t, p, k)
+            ramp(p, k)
         if (p, h) == (3, 1):
-            ts(b("Tp"), b("RKS", 7, 128, 8), 1 / U, OP.mult, 32768.0, OP.add)
-            ts(b("T3"), b("Tp"), -65536, OP.bitwise_and)
-            ts(b("thr"), b("T3"), 32768.0, OP.add, U, OP.mult)
+            ts(b("T3"), b("RKS", 7, 128, 8), RND * U, OP.add, RND * U, OP.subtract)
+            act(b("thr"), b("T3"), AF.Identity, bias=32768.0 * U)
             tg(b("m", 8, 136), b("thr"), BH, b("RKS"), OP.is_gt)
             scan(b("sc"), b("m", 7, 135), b("RKS"), OP.mult, OP.max)
             ts(b("ki"), b("sc", 7, 128, 8), 1 / U, OP.mult)
             ts(b("W"), b("ki"), 4095, OP.bitwise_and)
-            ts(b("y"), b("T3"), WIDE / 65536, OP.mult, -8 * WIDE - 4096, OP.add)
+            act(b("y"), b("T3"), AF.Identity, scale=WIDE / 65536 / U, bias=-8 * WIDE - 4096)
             tt(b("Y"), b("y"), b("W"), OP.add)
         if (p, h) == (1, 0):
             slot[2] = "out"
             if t:
+                stayed()
                 outputs(t - 1)
                 cb = 4096.0 * ((rank - 1) % N)
                 act(b("y"), b("PD", 2, 64, 4), AF.Relu, scale=-1.0, bias=1.0)
@@ -608,19 +776,25 @@ def rank_program(g, core, T, topo):
                 tt(b("y"), b("y"), b("thr"), OP.mult)
                 act(b("thr"), b("PD", 2, 64, 4), AF.Identity, bias=cb - c0)
                 tt(b("B0C"), b("y"), b("thr"), OP.add)
-                for k in range(2 if t < VI - 1 else 0):
-                    act(b("PK%d" % k, 4, 128, 16), b("B0C", 8 * k, 8 * k + 8), AF.Identity, scale=16.0, bias=FLAG + 16 * c0)
+                if t < VI - 1:
+                    act(b("PK", 4, 256, 16), b("B0C"), AF.Identity, scale=16.0, bias=FLAG + 16 * c0)
+            else:
+                mm(b("KP1", 320, 321), b("WD"), b("ONES", 0, 1))
+                act(b("WL", 0, 1), b("KP1", 320, 321), AF.Copy, scale=-0.4)
+                act(b("WL", 1, 2), b("KP1", 320, 321), AF.Copy, scale=0.4)
+                for k in range(2):
+                    mm(b("KP1", 304 + 8 * k, 312 + 8 * k), b("ONES", 0, 128), b("TB"))
+                act(b("THK"), b("KP1", 304, 320), AF.Identity, scale=WIDE, bias=-4096.0)
             if t < VI - 1:
                 roots(t, "WN", VI - 1 if t == 0 else None)
-                for k in range(2):
-                    act(b("PK%d" % k, 12, 128, 16), b("sn", 8 * k, 8 * k + 8), AF.Identity, scale=16.0, bias=FLAG)
+                act(b("PK", 12, 256, 16), b("sn"), AF.Identity, scale=16.0, bias=FLAG)
             for k in range(1, VI if t == 0 else 0):
                 roots(k, "WB")
                 act(b("FR", 64 * k + 3, 64 * k + 64, 4), b("sn"), AF.Copy, scale=16.0)
 
     def roots(t, w, ext=None):
         if ext is not None:
-            op("s", lambda: S.activation(b("wf", 1, 2)[4], b("wn", 0, 1)[4], AF.Copy), [], [b("wf", 1, 2)], FS, "c", ext)
+            op("s", lambda: S.activation(b("wf", 1, 2)[4], b("wn", 0, 1)[4], AF.Copy), [], [b("wf", 1, 2)], (0.09, 1, "s"), "c", ext)
             act(b("WN"), b("LC"), AF.Copy, scale=b("wf", 1, 2))
         for k in range(2):
             mm(b("KP1", 160 + 8 * k, 168 + 8 * k), b("PT", M + L * t + 128 * k, M + L * t + 128 * k + 128), b(w))
@@ -630,110 +804,121 @@ def rank_program(g, core, T, topo):
     def send(out, src, step, k):
         dst = T.cores[(rank + step) % N]
         rid, pid, _x = topo.addr(dst)
-        op("g", lambda: g.remote_dma(out, src[4], T.sem["arr%d" % k], T.sem["sent%d" % k], pid, rid, topo.mask(core, dst)), [src], [], 0.1, "r", k)
+        op("g", lambda: g.remote_dma(out, src[4], T.sem["arr%d" % k], T.sem["sent%d" % k], pid, rid, topo.mask(core, dst)), [src], [], (0.1, 0, "v"), "r", k)
 
     def outputs(t):
-        for k in range(2):
-            mm(b("KP1", 256 + 128 * k, 384 + 128 * k, 1, 32), b("OUT%d" % k), b("IDF"), f32=True)
-        act(b("OB%d" % t, 0, L, 1, 32), b("KP1", 256, 512, 1, 32), AF.Identity, bias=b("bias", 4, 5, 1, 32))
-        for k, out in ((0, T.yr), (1, T.yb), (3, T.yp)):
-            o = b("OB%d" % t, 0, L, 1, 8, 8 * k)
-            dma("y", out[:, t * L:(t + 1) * L], o[4], [o], [o], 2.0)
+        k = 48 if t < VI - 1 else 32
+        ps, ob = b("KP1", 256, 384, 1, k), "OB%d" % t
+        mm(ps, b("OUT", 48, 48 + k), b("IDF"), True, False, f32=True)
+        mm(ps, b("OUT", 0, k), b("IDF"), False, True, f32=True)
+        act(b(ob, 0, 128, 1, k), ps, AF.Identity, bias=b("bias", 4, 5, 1, k))
+        for j in range(k // 8):
+            o = b(ob, 0, 128, 1, 8, 8 * j)
+            x = t * L + 128 * (j % 2)
+            dma("s" if t == VI - 1 and j % 2 else "y", (T.yr, T.yb, T.yp)[j // 2][:, x:x + 128], o[4], [o], [], 2.0)
 
-    def finish(t, h):
-        hs = str(h)
-        n = lambda x, *a: b(x + hs, *a)
-        pa, pb, po, pg = (("KP0", "SP0", 0, "SP1"), ("KP1", "SP2", 0, "SP3"))[h]
-        pairs = ("MA", "MB")
-        q = b("PT", M + L * t + 128 * h, M + L * t + 128 * h + 128)
-        Rr, node = n("RI", 0, 16, 2), n("RI", 1, 16, 2)
-        tt(n("V4"), n("KS", 15, 128, 16), b("Y", 8 * h, 8 * h + 8), OP.min)
-        kc = b("KC", 8 * h, 8 * h + 8)
-        ts(node, n("V4"), 4095, OP.bitwise_and)
-        ts(n("n4"), n("V4"), -4096, OP.bitwise_and)
-        ts(Rr, n("n4"), -7 * 4096.0, OP.add, 1 / WIDE, OP.mult)
+    def listed(ps, z, out, add):
+        mm(b(ps[0], ps[1], ps[1] + 16), b("IDB"), b("KC"), True, False)
+        for h in range(2):
+            mm(b(ps[0], ps[1] + 8 * h, ps[1] + 8 * h + 8), b(z, 128 * h, 128 * h + 128), b("LC"), False, h == 1, f32=True)
+        if out in LSQ:
+            act(b(out), b(ps[0], ps[1], ps[1] + 16), AF.Identity, bias=add)
+        else:
+            ts(b(out), b(ps[0], ps[1], ps[1] + 16), add, OP.add)
+
+    def finish(t):
+        q0 = M + L * t
+        H = lambda x, h, k=128: b(x, k * h, k * h + k)
+        Rr, node = b("RI", 0, 32, 2), b("RI", 1, 32, 2)
+        tt(b("V4"), b("KS", 15, 256, 16), b("Y"), OP.min)
+        ts(node, b("V4"), 4095, OP.bitwise_and)
+        ts(b("n4"), b("V4"), -4096, OP.bitwise_and)
+        if "Rr" in LSQ:
+            act(Rr, b("n4"), AF.Identity, scale=1 / WIDE, bias=-7 * 4096.0 / WIDE)
+        else:
+            ts(Rr, b("n4"), -7 * 4096.0, OP.add, 1 / WIDE, OP.mult)
         if t < VI - 1:
-            act(n("PK", 0, 128, 8), n("RI"), AF.Identity, scale=16.0, bias=FLAG)
-            mm(b(pb, po, po + 128), b("IDB"), q, True, False)
-            mm(b(pb, po, po + 128), n("PK"), b("IDF"), False, True, f32=True)
-            act(n("XS"), b(pb, po, po + 128), AF.Copy)
-            tg(n("NB"), n("V4"), BC3, b("THX"), OP.is_lt)
-            mm(b(pa, 144, 152), b("IDB"), kc, True, False)
-            if h:
-                mm(b(pa, 144, 152), b("NB0", 0, 128), b("NONE", 0, 8), False, False)
-            for k in range(3):
-                mm(b(pa, 144, 152), n("NB", 128 * k, 128 * k + 128), b("RL", 8 * (k + h * (k // 2)), 8 * (k + h * (k // 2)) + 8), False, k == 2)
-            ts(n("OP"), b(pa, 144, 152), P15, OP.add)
-            snd, rcv = "SND%d" % t, "RCV%d" % t
-            op("v", lambda: V.tensor_copy(b(snd)[4].indirect(n("OP")[4]), n("XS")[4]), [n("XS"), n("OP")], [b(snd)], FV + 128 * SCA * CY)
-            if h:
-                send(T[rcv][:, 0:CAP], b(snd, 0, CAP), 1, t)
+            act(b("PK", 0, 256, 8), b("RI"), AF.Identity, scale=16.0, bias=FLAG)
+            mm(b("SP2", 0, L), b("IDB"), b("PT", q0, q0 + L), True, False)
+            for h in range(2):
+                mm(H("SP2", h), H("PK", h), b("IDF"), False, h == 1, f32=True)
+            act(b("XS"), b("SP2", 0, L), AF.Copy)
+            tt(b("near"), b("V4"), b("THK"), OP.is_lt)
+            mm(b("KP0", 144, 152), H("TRS", 0), H("near", 0, 8))
+            mm(b("KP0", 152, 160), b("NONE"), H("near", 0, 8), True, False)
+            mm(b("KP0", 152, 160), H("TRS", 1), H("near", 1, 8), False, True)
+            copy(PLQ, b("PL"), b("KP0", 144, 160))
+            tg(b("ZP"), b("PL"), BC16, b("DM"), OP.mult)
+            listed(("KP0", 160), "ZP", "OP", P15)
+            snd = b("SND%d" % t)
+            op("v", lambda: V.tensor_copy(snd[4].indirect(b("OP")[4]), b("XS")[4]), [b("XS"), b("OP")], [snd], (0.05, L, "W"))
+            send(T["RCV%d" % t][:, 0:CAP], b(snd[0], 0, CAP), 1, t)
             tag[0] = "g" + tag[0][1:]
         if t:
-            ts(n("z"), node, 0.0, OP.is_equal)
-            tt(n("z"), n("z"), b("B0C", 8 * h, 8 * h + 8), OP.mult)
+            act(b("z"), node, AF.Relu, scale=-1.0, bias=1.0)
+            tt(b("OUT", 16, 32), b("z"), b("B0C"), OP.mult)
         else:
-            ts(n("z"), node, 0.0, OP.is_equal, -c0, OP.mult)
-        tt(n("OUT", 8, 16), n("z"), node, OP.add)
-        act(n("OUT", 0, 8), Rr, AF.Copy)
-        ob = b("OB%d" % t, 128 * h, 128 * h + 128, 1, 32 if t < VI - 1 else 16)
+            ts(b("OUT", 16, 32), node, 0.0, OP.is_equal, -c0, OP.mult)
+        copy(GQS[1] if t < VI - 1 else "s", b("OUT", 0, 16), Rr)
+        act(b("OUT", 64, 80), node, AF.Copy)
         if t == VI - 1:
-            mm(b(pa, 256, 384, 1, 16), n("OUT", 0, 16), b("IDF"), f32=True)
-            act(ob, b(pa, 256, 384, 1, 16), AF.Identity, bias=b("bias", 4, 5, 1, 16))
-            for k, (qn, out) in enumerate((("y", T.yr), ("s" if h else "y", T.yb))):
-                o = b(ob[0], ob[1], ob[2], 1, 8, 8 * k)
-                dma(qn, out[:, t * L + 128 * h:t * L + 128 * h + 128], o[4], [o], [], 2.0)
-            return
-        z1 = n("Z1")
-        act(n("OUT", 16, 24), node, AF.Copy)
-        ts(n("gq"), node, b("K4096", h, h + 1), OP.add)
-        tg(z1, n("gq"), BC8, b("DM", 0, 128), OP.mult)
-        mm(b(pa, 152, 160), b("IDB"), kc, True, False)
-        mm(b(pa, 152, 160), z1, b("LC"), False, True, f32=True)
-        ts(n("G1"), b(pa, 152, 160), b("bias", 5, 6), OP.add)
-        act(n("GC"), b("CH", 0, 4096), AF.Copy, off=n("G1"))
-        act(n("NQ", 0, 16, 2), node, AF.Copy)
-        tt(n("NQ", 1, 16, 2), node, n("NQ", 0, 16, 2), OP.subtract)
-        mm(b(pg, 0, 128, 1, 16), n("NQ"), b("IDB"))
-        nt = b("NT" + hs, 0, 128, 1, 16)
-        act(nt, b(pg, 0, 128, 1, 16), AF.Copy)
-        act(n("bb"), Rr, AF.Identity, scale=0.0625, bias=-0.46875)
-        tg(n("OH"), n("bb"), BC8, b("j15", 0, 128), OP.is_equal)
-        mm(b(pb, po + 128, po + 256), n("OH"), b("DGB", 128 * (2 * t + h), 128 * (2 * t + h) + 128), True, False)
-        mm(b(pb, po + 128, po + 256), n("OH"), b("DGL"), False, True)
-        act(n("ON"), b(pb, po + 128, po + 256), AF.Copy)
-        ns = GSC[h]
-        for gg in range(8):
-            ps = b(pairs[gg // 4], 128 * (gg % 4), 128 * (gg % 4) + 128)
-            mm(ps, b("SELG", 128 * gg, 128 * gg + 128, 1, 16), nt)
+            return outputs(t)
+        tt(b("gq"), node, b("K4096"), OP.add)
+        tg(b("Z1"), b("gq"), BC16, b("DM"), OP.mult)
+        listed(("KP1", 144), "Z1", "G1", b("bias", 5, 6))
+        act(b("GC"), b("CH", 0, 4096), AF.Copy, off=b("G1"))
+        act(b("NQ", 0, 32, 2), node, AF.Copy)
+        tt(b("NQ", 1, 32, 2), node, b("NQ", 0, 32, 2), OP.subtract)
+        for h in range(2):
+            mm(b("SP3", 256 + 128 * h, 384 + 128 * h, 1, 16), H("NQ", h, 16), b("IDB"))
+        act(b("NT", rows=16), b("SP3", 256, 512, 1, 16), AF.Copy)
+        act(b("bb"), Rr, AF.Identity, scale=0.0625, bias=-0.46875)
+        tg(b("OH"), b("bb"), BC16, b("j15"), OP.is_equal)
+        for h in range(2):
+            mm(H("SP3", h), H("OH", h), H("DGB", 2 * t + h), True, False)
+            mm(H("SP3", h), H("OH", h), b("DGL"), False, True)
+        tt(b("OC"), b("SP3", 0, L), b("GC"), OP.mult)
+        act(b("ON"), b("SP3", 0, L), AF.Copy)
         wl, nwl = b("WL", 0, 1), b("WL", 1, 2)
-        for gg in range(8):
-            ps, cc = b(pairs[gg // 4], 128 * (gg % 4), 128 * (gg % 4) + 128), n("OUT", 16 + gg, 17 + gg)
-            if gg < ns:
-                act(b("EF", 128 * gg, 128 * gg + 128), ps, AF.Abs, scale=-1.0, bias=cc)
-            else:
-                ts(n("EQ", 128 * gg, 128 * gg + 128), ps, cc, OP.is_equal, wl, OP.mult)
-        for lo in range(0, ns, 4):
-            hi = min(ns, lo + 4)
-            act(n("EQ", 128 * lo, 128 * hi), b("EF", 128 * lo, 128 * hi), AF.Relu, scale=nwl, bias=wl)
-        tt(n("OC"), b(pb, po + 128, po + 256), n("GC"), OP.mult)
-        mm(b(pg, 160, 168), b("WI"), n("NB", 0, 128, 16), True, False)
-        if h:
-            act(b("CG"), n("GC"), AF.Relu, bias=1.0 - M - L * t)
-            mm(b(pg, 160, 168), b("CG"), b("BLK"), False, False)
-        mm(b(pg, 160, 168), n("OC"), b("LC2"), False, True)
-        tt(n("can"), node, b(pg, 160, 168), OP.is_gt)
-        mm(b(pg, 168, 176), b("WD"), n("can"), True, False)
-        for gg in range(8):
-            mm(b(pg, 168 + gg, 169 + gg), n("EQ", 128 * gg, 128 * gg + 128), n("can", gg, gg + 1), False, gg == 7)
-        mm(b(pa, 176, 184), b("IDB"), kc, True, False)
-        ts(n("win"), b(pg, 168, 176), 0.0, OP.is_lt)
-        tg(n("Z2"), n("win"), BC8, z1, OP.mult)
-        mm(b(pa, 176, 184), n("Z2"), b("LC"), False, True, f32=True)
-        ts(n("G2"), b(pa, 176, 184), b("bias", 5, 6), OP.add)
-        op("v", lambda: V.tensor_tensor(b("CH")[4].indirect(n("G2")[4]), n("GC")[4], n("ON")[4], OP.add),
-           [n("GC"), n("ON"), n("G2")], [b("CH")], FV + 128 * SCA * CY)
-        tt(n("OUT", 24, 32), n("win"), node, OP.mult)
+        for j, ps in enumerate(("MA", "SP0", "SP1", "MB")):
+            nt, x = b("NT", 128 * (j // 2), 128 * (j // 2) + 128, 1, 16), 512 * (j % 2)
+            sub = EQQ[j] in "sv"
+            if sub:
+                mm(b(ps), nt, b("NSELG", x, x + 512, 1, 16), True, False)
+            for k in range(4):
+                mm(H(ps, k), b("SELG", x + 128 * k, x + 128 * k + 128, 1, 16), nt, not sub, k == 3 or not sub)
+            eq = H("EQ", j, 512)
+            for k in range(0 if sub else 4):
+                own = b("OUT", 64 + 4 * j + k, 65 + 4 * j + k)
+                if EQQ[j] == "S":
+                    act(H("EQ", 4 * j + k), H(ps, k), AF.Abs, scale=-1.0, bias=own)
+                else:
+                    ts(H("EQ", 4 * j + k), H(ps, k), own, OP.is_equal, wl, OP.mult)
+            if EQQ[j] == "s":
+                act(eq, b(ps), AF.Abs)
+            if EQQ[j] in "sS":
+                act(eq, eq, AF.Relu, scale=nwl, bias=wl)
+            if EQQ[j] == "v":
+                ts(eq, b(ps), 0.0, OP.is_equal, wl, OP.mult)
+        mm(b("KP1", 160, 176), b("WI"), b("near"), True, False)
+        for h in range(2):
+            mm(b("KP1", 160 + 8 * h, 168 + 8 * h), H("OC", h), b("LC2"), False, h == 1)
+        tt(b("can"), node, b("KP1", 160, 176), OP.is_gt)
+        mm(b("KP1", 176, 192), b("WD"), b("can"), True, False)
+        for j in range(16):
+            mm(b("KP1", 176 + j, 177 + j), H("EQ", j), b("can", j, j + 1), False, j == 15)
+        ts(b("win"), b("KP1", 176, 192), 0.0, OP.is_lt)
+        tg(b("Z2"), b("win"), BC16, b("Z1"), OP.mult)
+        listed(("KP1", 192), "Z2", "G2", b("bias", 5, 6))
+        for h in (1, 0):
+            op("v", lambda h=h: V.tensor_tensor(b("CH")[4].indirect(H("G2", h, 8)[4]), H("GC", h)[4], H("ON", h)[4], OP.add),
+               [H("GC", h), H("ON", h), H("G2", h, 8)], [b("CH")], (0.05, 128, "W"))
+        tt(b("OUT", 32, 48), b("win"), node, OP.mult)
+        act(b("CG"), b("CH", 0, 4096), AF.Relu, bias=-127.0 - q0, off=H("G1", 1, 8))
+
+    def stayed():
+        mm(b("KP1", 208, 216), b("CG"), b("BLK"))
+        tt(b("OUT", 40, 48), b("OUT", 40, 48), b("KP1", 208, 216), OP.min)
 
     for t in range(VI):
         tag[0] = "b%d" % t
@@ -746,67 +931,12 @@ def rank_program(g, core, T, topo):
                 slot[:] = [(t, p, h), {}, "Pf"]
                 push(t, h, p)
         slot[0] = None
-        for h in range(2):
-            tag[0] = "f%d%s" % (t, "AB"[h])
-            finish(t, h)
+        tag[0] = "f%d" % t
+        finish(t)
 
-    n = len(ops)
-    cost = [o["cost"] for o in ops]
-    more = [o["ext"] if o["kind"] == "d" else FAR if o["kind"] == "r" else 0.0 for o in ops]
-    fwd = [[] for _ in range(n)]
-    bwd = [[] for _ in range(n)]
-    for i, o in enumerate(ops):
-        dd = set(o["deps"])
-        if o["kind"] == "c" and o["ext"] is not None:
-            dd.add([j for j in range(n) if ops[j]["kind"] == "r" and ops[j]["ext"] == o["ext"]][0])
-        for d in dd:
-            fwd[d].append((i, cost[d] + more[d] + WAKE))
-            bwd[i].append((d, cost[i] + more[d] + WAKE))
-        for d in o["after"] - dd:
-            fwd[d].append((i, cost[d]))
-            bwd[i].append((d, cost[i]))
-
-    def place(succ, pri, first):
-        cnt = [0] * n
-        for lst in succ:
-            for j, x in lst:
-                cnt[j] += 1
-        rt, at, free, order, byq = list(first), [0.0] * n, {}, [], {}
-        for i in range(n):
-            if cnt[i] == 0:
-                byq.setdefault(ops[i]["q"], []).append(i)
-        while len(order) < n:
-            t0, qn = min((max(free.get(x, 0.0), min(rt[i] for i in lst)), x) for x, lst in byq.items() if lst)
-            i = max((i for i in byq[qn] if rt[i] <= t0 + LOOK), key=lambda i: pri[i])
-            at[i] = max(t0, rt[i])
-            byq[qn].remove(i)
-            order.append(i)
-            free[qn] = at[i] + cost[i]
-            for j, x in succ[i]:
-                rt[j] = max(rt[j], at[i] + x)
-                cnt[j] -= 1
-                if cnt[j] == 0:
-                    byq.setdefault(ops[j]["q"], []).append(j)
-        return order, at
-
-    seen = {}
-    due = [0.0] * n
-    for i in range(n - 1, -1, -1):
-        due[i] = min([due[j] - x for j, x in fwd[i]] or [1000.0])
-        o = ops[i]
-        if o["slot"] is not None:
-            t, p, h = o["slot"]
-            if o["lab"] in WHEN:
-                due[i] = (10 * HALF + GAP) * t + (2 * p + h) * HALF + WHEN[o["lab"]]
-    for i in range(n):
-        if ops[i]["tag"][:1] in ("f", "g") and ops[i]["tag"][2] == "A":
-            due[i] -= EARLY
     if "order" not in ORDER:
-        at = place(fwd, [-x for x in due], [0.0] * n)[1]
-        ORDER["order"], ORDER["at"] = improve(sorted(range(n), key=lambda i: (at[i], i)), [o["q"] for o in ops], cost, more, fwd)
+        ORDER["order"], ORDER["runs"] = improve(place(ops, *links(ops, MODELS[0]), WHEN, HALF, GAP), ops, ROUNDS)
     order = ORDER["order"]
-    for i in range(n):
-        ops[i]["t0"] = ORDER["at"][i]
 
     QS = {"v": V, "t": TE, "s": S, "g": g, "y": g.sync}
     CQ = {"v": "cv", "t": "ct", "s": "cs", "g": "cg"}

from concourse.mybir import AluOpType as OP, ActivationFunctionType as AF

N, L, CAP, M, VI = 4, 256, 192, 3584, 3
U = 2.0 ** -26
WIDE = 17.0 * 4096
BIG = float(2 ** 60)
CO = 7.5 * 65536
RND = 1.5 * 2.0 ** 39
FLAG = float(2 ** 22)
ROOM = 4096 + 256
SNDW = 1280
NV = [[48, 38], [38, 38], [38, 38], [40, 40], [48, 54]]
CUT = (96,)
RELU = (1, 1, 1, 1, 1)
VP = 5
KSP = ()
PFQ, DSQ, PUQ, OFQ = "h", "g", "s", "s"
JD, JS = False, False
GQS = "gggg"
PHQ = "v"
JUNK = 0
EQQ = "SVVV"
PLQ, PTQ, ZRS, JM, DRQ = "s", "s", False, True, "s"
LSQ = ("G1", "G2", "OP", "Rr")
WHEN = {'gDS': -6.55, 'sPh': 1, 'vPh': 1, 'vEQ': 8, 'vvec4': 0, 'sA': 5.79, 'sOFF': 14.06, 'sPU': -7.09, 'sabs0': -37.07, 'sabs1': 0.02, 'sabs2': -5.01, 'sget0': -0.17, 'sget1': 0.02, 'sget2': 3.8, 'tM1': 5.86, 'tPf': 4.21, 'tST': -2.24, 'tabs0': -8.84, 'tabs1': -10.62, 'tabs2': -4.57, 'tget0': 4.22, 'tget1': 4.41, 'tget2': 6.38, 'tkey': -4.03, 'tlist': 15.26, 'tneg': -6.17, 'trow': 7.16, 'vDK': -3.14, 'vDS': 3.51, 'vE': 17.62, 'vFB': -5.22, 'vKM': 4.73, 'vKS': -8.32, 'vM1': 18.97, 'vM2': 9.05, 'vMS': 10.12, 'vNN': 8.65, 'vRB': 3.14, 'vRKS': 9.05, 'vRP': 14.11, 'vSK': 11.45, 'vST': -14.78, 'vZL': -30.62, 'vrelu': 5.91, 'vvec0': 2.63, 'vvec1': -7.15, 'vvec2': 3.52, 'vvec3': -5.87, 'vz3': -89.99}
HALF, GAP = 6.72, 39.09
ROUNDS, SPAN, HEAT = 130000, 120, 0.0001
MODELS = ((0.00089, 1.56, 3.8, 0.83, 0.6, 0.145), (0.00089, 1.9, 3.8, 0.83, 0.6, 0.22), (0.00089, 1.2, 3.8, 0.83, 0.79, 0.145))
FAR = 3.0

SCRATCH = {}
PS = set()
VIRT = {}
POOL = {"float32": ["poolf", 0], "int32": ["pooli", 0], "bfloat16": ["poolb", 0], "uint16": ["poolu", 0], "float16": ["poolh", 0]}


def _own(name, cols, dt="float32"):
    SCRATCH[name] = ("sbuf", [128, cols], dt)
    VIRT[name] = (name, 0, cols)


def _s(name, cols, dt="float32"):
    p = POOL[dt]
    VIRT[name] = (p[0], p[1], cols)
    p[1] += (cols + 15) // 16 * 16


for _n in ("KP0", "KP1"):
    SCRATCH[_n] = ("psum", [128, 512], "float32")
    VIRT[_n] = (_n, 0, 512)
    PS.add(_n)
RING = ("MA", "SP0", "SP1", "SP2", "SP3", "MB")
SCRATCH["RING"] = ("psum", [128, 3072], "float32")
for _k, _n in enumerate(RING):
    VIRT[_n] = ("RING", 512 * _k, 512)
    PS.add(_n)
_own("PT", M + VI * L, "bfloat16"); _own("CHI", M, "int32"); _own("CH", ROOM)
_own("wi", 8, "int32"); _own("wn", 8, "int32"); _own("thi", 8, "int32"); _own("r0i", 128, "int32")
_own("Q16", 2048, "bfloat16"); _own("QS", 2048, "bfloat16"); _own("DIFF", 4096, "bfloat16"); _own("RAW", 2048, "bfloat16")
for _t in "01":
    _own("SND" + _t, SNDW); _own("RCV" + _t, L)
for _t in "012":
    _own("OB" + _t, 256)
for _n, _c in (("r0f", 128), ("wf", 2), ("thf", 2), ("pf", 8), ("j15", 256), ("c8", 8), ("IDF", 128), ("DM", 256),
               ("LC", 8), ("MX", 128), ("ROWB", 256), ("bias", 8), ("THK", 16), ("K4096", 16),
               ("SEL", 32), ("FR", 192), ("A", 256), ("K0", 16), ("K0U", 16), ("WL", 2), ("B0C", 16), ("EF", 384),
               ("RKS", 128), ("KS", 256), ("MS", 256), ("IDU", 128), ("T3", 16), ("thr", 16), ("m", 136), ("sc", 128), ("y", 16), ("Y", 16)):
    _s(_n, _c)
for _n, _c in (("pi", 8), ("li", 176), ("sm", 16), ("sn", 16), ("DK", 16), ("MI", 192), ("QI", 192), ("PM", 64), ("PD", 64),
               ("ki", 16), ("W", 16), ("SK", 64), ("FB", 16), ("RB", 16), ("RP", 16)):
    _s(_n, _c, "int32")
for _n, _c in [("IDB", 128), ("NIDB", 128), ("WI", 128), ("BLKU", 8), ("NBLKU", 8), ("NBLKW", 8), ("BLKW", 8), ("BLK", 8), ("LCB", 8), ("LC2", 8),
               ("WB", 8), ("ROWC", 256), ("ST", 256), ("M1", 256), ("GQ", 1024), ("WD", 128), ("RT", 16),
               ("RL", 32), ("WN", 8), ("ONES", 512), ("R", 1536), ("TB", 8), ("SELG", 1024), ("ZR", 256), ("E", 512), ("GO", 256), ("DS", 512),
               ("DRB", 256), ("NQT", 256), ("DGL", 128), ("DGB", 128 * 4), ("NONE", 128), ("KC", 16), ("CG", 128)]:
    _s(_n, _c, "bfloat16")
_s("LI", 176, "uint16"); _s("OFF", 16, "uint16")
_s("IDH", 256, "float16"); _s("ROWH", 256, "float16"); _s("Ph0", 128, "float16"); _s("Ph1", 128, "float16")
for _h in "01":
    for _n, _c, _d in (("PU", 128, "uint16"), ("Pf", 128, "float32"), ("M2", 128, "bfloat16"),
                       ("NN", 8, "int32"), ("z3", 8, "float32"), ("KM", 128, "float32"), ("ZL", 128, "float32")):
        _s(_n + _h, _c, _d)
for _n, _c, _d in (("V4", 16, "int32"), ("n4", 16, "int32"), ("z", 16, "float32"), ("RI", 32, "int32"), ("OUT", 96, "float32"),
                   ("near", 16, "bfloat16"), ("PL", 16, "float32"), ("ZP", 256, "float32"), ("OP", 16, "uint16"), ("PK", 256, "float32"),
                   ("XS", 256, "float32"), ("gq", 16, "float32"), ("Z1", 256, "float32"), ("G1", 16, "uint16"), ("GC", 256, "float32"),
                   ("bb", 16, "int32"), ("OH", 256, "bfloat16"), ("ON", 256, "float32"), ("OC", 256, "bfloat16"), ("can", 16, "bfloat16"),
                   ("win", 16, "float32"), ("Z2", 256, "float32"), ("G2", 16, "uint16"), ("NQ", 32, "bfloat16"),
                   ("NT", 256, "bfloat16"), ("EQ", 2048, "bfloat16"), ("TRS", 256, "bfloat16"), ("NSELG", 1024, "bfloat16")):
    _s(_n, _c, _d)
for _d in POOL:
    SCRATCH[POOL[_d][0]] = ("sbuf", [128, POOL[_d][1]], _d)

NDMA = 27
SEMAPHORES = ["cv", "ct", "cs", "cg"] + ["d%d" % i for i in range(NDMA)] + ["arr0", "arr1", "arr2", "sent0", "sent1", "sent2"]


ORDER = {}


def links(ops, model):
    cy, ga, sca, cs, ct, wake = model
    n = len(ops)
    cost = [o["cost"][0] + o["cost"][1] * cy * {"v": 1, "s": cs, "t": ct, "V": ga, "S": ga * cs, "W": sca}[o["cost"][2]] for o in ops]
    more = [o["ext"] if o["kind"] == "d" else FAR if o["kind"] == "r" else 0.0 for o in ops]
    fwd = [[] for _ in range(n)]
    far = {o["ext"]: j for j, o in enumerate(ops) if o["kind"] == "r"}
    for i, o in enumerate(ops):
        dd = set(o["deps"])
        if o["kind"] == "c" and o["ext"] is not None:
            dd.add(far[o["ext"]])
        for d in dd:
            fwd[d].append((i, cost[d] + more[d] + wake))
        for d in o["after"] - dd:
            fwd[d].append((i, cost[d]))
    return cost, more, fwd


def place(ops, cost, more, fwd, when, half, gap, passes=2):
    n = len(ops)
    due = [0.0] * n
    for i in range(n - 1, -1, -1):
        o = ops[i]
        if o["slot"] is not None and o["lab"] in when:
            t, p, h = o["slot"]
            due[i] = (10 * half + gap) * t + (2 * p + h) * half + when[o["lab"]]
        else:
            due[i] = min([due[j] - x for j, x in fwd[i]] or [3 * (10 * half + gap)])
    pre = [[] for _ in range(n)]
    for i in range(n):
        for j, x in fwd[i]:
            pre[j].append((i, x))
            due[j] = max(due[j], due[i])
    back = [[(j, x - cost[i] + cost[j]) for j, x in fwd[i]] for i in range(n)]

    def fit(order, pre, first):
        at, st, en = [0.0] * n, {x: [] for x in "vstgy"}, {x: [] for x in "vstgy"}
        for i in order:
            t, s, e = first[i], st[ops[i]["q"]], en[ops[i]["q"]]
            for d, x in pre[i]:
                if at[d] + x > t:
                    t = at[d] + x
            k = len(e)
            while k and e[k - 1] > t:
                k -= 1
            while k < len(s) and s[k] < t + cost[i] - 1e-9:
                t, k = e[k], k + 1
            s.insert(k, t)
            e.insert(k, t + cost[i])
            at[i] = t
        return at

    order = sorted(range(n), key=lambda i: (due[i], i))
    for k in range(passes):
        at = fit(order, pre, [0.0] * n)
        if k < passes - 1:
            at = fit(sorted(range(n), key=lambda i: (-at[i] - cost[i], -i)), back, more)
            at = [-at[i] - cost[i] for i in range(n)]
        order = sorted(range(n), key=lambda i: (at[i], i))
    return order


def improve(order, ops, rounds):
    n = len(order)
    q = ["vstgy".index(o["q"]) for o in ops]
    sets = []
    for model in MODELS:
        cost, more, fwd = links(ops, model)
        reach, pre, suc = [0] * n, [[] for _ in range(n)], [[] for _ in range(n)]
        for i in range(n - 1, -1, -1):
            for j, x in sorted(fwd[i]):
                if not (reach[i] >> j) & 1 or more[i] > 0:
                    pre[j].append((i, x))
                    suc[i].append((j, x))
                    reach[i] |= reach[j] | (1 << j)
        sets.append((cost, more, pre, suc))

    def ahead(order, k, at, lo, hi, calm):
        cost, more, pre, suc = sets[k]
        free, same = [None] * 5, 0
        for j in range(lo - 1, -1, -1):
            i = order[j]
            if free[q[i]] is None:
                free[q[i]] = at[i] + cost[i]
                if None not in free:
                    break
        free = [x or 0.0 for x in free]
        for j in range(lo, hi):
            i = order[j]
            x = q[i]
            t = free[x]
            for d, y in pre[i]:
                if at[d] + y > t:
                    t = at[d] + y
            free[x] = t + cost[i]
            if at[i] != t:
                at[i], same = t, 0
            elif j > calm:
                same += 1
                if same > SPAN:
                    break

    def behind(order, k, rest, hi, calm):
        cost, more, pre, suc = sets[k]
        nxt, same = [None] * 5, 0
        for j in range(hi + 1, n):
            i = order[j]
            if nxt[q[i]] is None:
                nxt[q[i]] = rest[i]
                if None not in nxt:
                    break
        nxt = [x or 0.0 for x in nxt]
        for j in range(hi, -1, -1):
            i = order[j]
            x = q[i]
            t = cost[i] + max(nxt[x], more[i])
            for d, y in suc[i]:
                if rest[d] + y > t:
                    t = rest[d] + y
            nxt[x] = t
            if rest[i] != t:
                rest[i], same = t, 0
            elif j < calm:
                same += 1
                if same > SPAN:
                    break

    seed = [12345]

    def draw(k):
        seed[0] = (seed[0] * 1103515245 + 12345) % 2 ** 31
        return (seed[0] >> 8) % k

    K = range(len(MODELS))
    at, rest = [[0.0] * n for k in K], [[0.0] * n for k in K]
    for k in K:
        ahead(order, k, at[k], 0, n, n)
        behind(order, k, rest[k], n - 1, -1)
    end = [max(rest[k]) for k in K]
    best = (sum(end), order, end)
    pre, suc = sets[0][2:]
    for it in range(rounds):
        k = draw(len(K))
        a, r, c, e = at[k], rest[k], sets[k][0], end[k] - 1e-6
        hi = draw(n)
        while hi < n:
            y = order[hi]
            if a[y] + r[y] > e:
                lo = hi - 1
                while lo >= 0 and q[order[lo]] != q[y]:
                    lo -= 1
                x = order[lo]
                if lo >= 0 and a[x] + r[x] > e and a[x] + c[x] > a[y] - 1e-6:
                    break
            hi += 1
        if hi == n:
            continue
        step = 2 * draw(2) - 1
        k = lo if step < 0 else hi
        for _ in range((0, 0, 1, 2, 4)[draw(5)]):
            j = k + step
            while 0 <= j < n and q[order[j]] != q[y]:
                j += step
            k = j if 0 <= j < n else k
        if step < 0:
            lo, go = k, {y}
            seg = order[lo:hi + 1]
            for v in reversed(seg):
                if any(s in go for s, _x in suc[v]):
                    go.add(v)
            new = [v for v in seg if v in go] + [v for v in seg if v not in go]
        else:
            hi, go = k, {x}
            seg = order[lo:hi + 1]
            for v in seg:
                if any(d in go for d, _x in pre[v]):
                    go.add(v)
            new = [v for v in seg if v not in go] + [v for v in seg if v in go]
        if new == seg:
            continue
        new = order[:lo] + new + order[hi + 1:]
        far = min(n, hi + 1 + SPAN)
        a2, e2 = [a[:] for a in at], []
        for k in K:
            ahead(new, k, a2[k], lo, far, n)
            c, m = sets[k][:2]
            e2.append(max([a2[k][i] + rest[k][i] for i in new[hi + 1:far]] + [a2[k][i] + c[i] + m[i] for i in seg]))
        if sum(e2) <= sum(end) + HEAT * len(K) * draw(1000) * (1 - it / rounds):
            order, at, end = new, a2, e2
            for k in K:
                ahead(order, k, at[k], far, n, far)
                behind(order, k, rest[k], hi, lo)
            if sum(end) < best[0]:
                best = (sum(end), order, end)
    return best[1], [[e] for e in best[2]]


def rank_program(g, core, T, topo):
    rank = T.rank_of(core)
    if rank is None:
        return
    ops = []
    hist = {}
    ndma = [0]
    tag = [""]
    slot = [None, {}, ""]
    c0 = 4096.0 * rank

    def b(name, lo=0, hi=None, st=1, rows=None, row0=0):
        buf, o, c = VIRT[name]
        hi = c if hi is None else hi
        p = slice(None) if rows is None else slice(row0, row0 + rows)
        return (name, lo, hi, st, T[buf][p, o + lo:o + hi:st] if st > 1 else T[buf][p, o + lo:o + hi])

    def clash(x, y):
        if x[1] <= y[0] or y[1] <= x[0]:
            return False
        return not (x[2] == y[2] and x[2] > 1 and (x[0] - y[0]) % x[2])

    def op(q, call, reads, writes, cost, kind="c", ext=None):
        n = len(ops)
        deps = set()
        after = set()
        both = [(False, o) for o in reads] + [(True, o) for o in writes]
        for w, o in both:
            r = (o[1], o[2], o[3])
            if o[0] in PS:
                runs = hist.setdefault(o[0], [])
                if not runs or runs[-1][0] != q:
                    runs.append((q, []))
                if len(runs) > 1:
                    deps.update(runs[-2][1][-1:] if runs[-2][0] == "t" else runs[-2][1])
                if q == "t":
                    after.update(runs[-1][1][-1:])
                elif w:
                    deps.update(runs[-1][1])
                runs[-1][1].append(n)
                continue
            for (r2, w2, n2) in hist.get(o[0], ()):
                if (w or w2) and clash(r, r2):
                    deps.add(n2)
        for w, o in both:
            if o[0] in PS:
                continue
            r = (o[1], o[2], o[3])
            h = hist.setdefault(o[0], [])
            if w:
                h[:] = [e for e in h if not (e[2] != n and r[0] <= e[0][0] and e[0][1] <= r[1] and (r[2] == 1 or r == e[0]))]
            h.append((r, w, n))
        d = {"q": q, "call": call, "deps": deps, "after": after - deps, "cost": cost, "kind": kind, "ext": ext,
             "tag": tag[0] + " " + (writes[0][0] if writes else "")}
        d["slot"] = slot[0] if slot[2] != "out" else None
        if d["slot"] is not None:
            x = writes[0][0]
            d["lab"] = q + (slot[2] if q == "t" or x in ("DIFF", "RAW") or q + x + slot[2] == "vDSRP" else x[:-1] if x[:-1] + "0" in VIRT and x[:-1] + "1" in VIRT else x)
        if kind == "d":
            d["sem"] = "d%d" % ndma[0]
            ndma[0] += 1
        ops.append(d)
        return n

    two = ("poolb", "poolu", "poolh", "PT", "Q16", "QS", "DIFF", "RAW")

    def cols(o):
        return (o[2] - o[1] + o[3] - 1) // o[3]

    def vc(n, k=1.0):
        return (0.05, max(64, n * k), "v")

    def half(*xs):
        return 0.5 if all(VIRT[x[0]][0] in two for x in xs) else 1.0

    V, S, TE = g.vector, g.scalar, g.tensor

    def isap(x):
        return isinstance(x, tuple)

    def tt(out, a, c, o, ext=None):
        k = 1.0 if (a[0] in PS or c[0] in PS) else 2.0
        op("v", lambda: V.tensor_tensor(out[4], a[4], c[4], o), [a, c], [out], vc(cols(out), k), "c", ext)

    def tg(out, win, off, c, o):
        op("v", lambda: V.tensor_tensor(out[4], win[4].indirect(off[4]), c[4], o), [win, off, c], [out], (0.05, cols(out), "V"))

    def ts(out, a, s1, o1, s2=None, o2=None):
        x1 = s1[4] if isap(s1) else s1
        x2 = s2[4] if isap(s2) else s2
        rd = [a] + [s for s in (s1, s2) if isap(s)]
        if o2 is None:
            op("v", lambda: V.tensor_scalar(out[4], a[4], x1, None, o1), rd, [out], vc(cols(out), half(out, a)))
        else:
            op("v", lambda: V.tensor_scalar(out[4], a[4], x1, x2, o1, o2), rd, [out], vc(cols(out), half(out, a)))

    def cp(out, a):
        op("v", lambda: V.tensor_copy(out[4], a[4]), [a], [out], vc(cols(out), half(out, a)))

    def scan(out, d0, d1, o0, o1):
        op("v", lambda: V.tensor_tensor_scan(out[4], d0[4], d1[4], 0.0, o0, o1), [d0, d1], [out], vc(cols(out), half(out, d0, d1)))

    def fill(out, x):
        op("v", lambda: V.memset(out[4], x), [], [out], vc(cols(out), half(out)))

    def act(out, a, f, bias=None, scale=1.0, off=None):
        kw = {"scale": scale[4] if isap(scale) else scale}
        rd = ([a] if off is None else [a, off]) + ([scale] if isap(scale) else [])
        if bias is not None:
            kw["bias"] = bias[4] if isap(bias) else bias
            if isap(bias):
                rd.append(bias)
        src = a[4] if off is None else a[4].indirect(off[4])
        op("s", lambda: S.activation(out[4], src, f, **kw), rd, [out], (0.09, cols(out), "s") if off is None else (0.065, cols(out), "S"))

    def mm(out, l, r, start=True, stop=True, f32=False, ext=None):
        n = max(min(64, cols(l)), cols(r))
        op("t", lambda: TE.matmul(out[4], l[4], r[4], start, stop), [l, r], [out], (0.0, n * (4 if f32 else 1), "t"), "c", ext)

    def dma(q, out, src, reads, writes, us):
        eng = g.sync if q == "y" else g.scalar
        op(q, lambda: eng.dma_start(out, src), reads, writes, (0.06, 0, "v"), "d", us)

    def iota(out, pat, base, cm=0):
        kw = {} if VIRT[out[0]][0] == "pooli" else {"allow_small_or_imprecise_dtypes": True}
        op("g", lambda: g.iota(out[4], pat, base, cm, **kw), [], [out], (0.13, 2 * cols(out), "v"))

    def const(out, x):
        iota(out, [[0, cols(out)]], int(x))

    def keep(out, a, pat, o, other, base=0, cm=1, also=()):
        op("g", lambda: g.affine_select(out[4], a[4], pat, o, other, base, cm), [a] + list(also), [out], (0.17, 2 * cols(out), "v"))

    def copy(q, out, a):
        if q == "g":
            keep(out, a, [[0, cols(out)]], OP.is_ge, 0.0, 0, 0)
        elif q == "s":
            act(out, a, AF.Copy)
        else:
            cp(out, a)

    def load(q, name, lo, hi, src, us, rows=None):
        o = b(name, lo, hi, 1, rows)
        dma(q, o[4], src, [], [o], us)
        ops[-1]["after"] = set([i for i, x in enumerate(ops[:-1]) if x["q"] == q][-1:])

    load("y", "PT", M, M + L, T.q[:, 0:L], 2.0)
    load("s", "wi", 0, 1, T.w[:], 2.0)
    load("y", "CHI", 0, 128, T.ch[:, 0:128], 2.2)
    load("s", "PT", 0, 128, T.pt[:, 0:128], 2.2)
    load("s", "r0i", 0, 128, T.r0[:], 2.2, 48)
    load("y", "PT", 128, M, T.pt[:, 128:M], 5.0)
    load("y", "CHI", 128, M, T.ch[:, 128:M], 10.0)
    load("y", "PT", M + L, M + VI * L, T.q[:, L:VI * L], 10.5)
    load("s", "thi", 0, 1, T.th[:], 10.5)

    DIAG = [[-1, 128]]
    fill(b("ONES"), 1.0)
    iota(b("pi", 0, 1), [[0, 1]], 0, 1)
    iota(b("c8"), [[1, 8]], 0)
    iota(b("li", 0, 16), [[1, 16]], 0)
    iota(b("j15"), [[0, 16], [1, 16]], 0)
    keep(b("IDB"), b("ONES", 0, 128), DIAG, OP.is_equal, 0.0)
    iota(b("li", 16, 24), [[16, 8]], 15)
    iota(b("li", 24, 120), [[1, 6], [8, 16]], 2)
    iota(b("li", 120, 128), [[2, 8]], 0)
    for k in (1, 2, 0):
        keep(b("R", 512 * k, 512 * k + 512), b("ONES"), [[-1, 32], [0, 16]], OP.is_equal, 0.0, -32 - 32 * k, 1, [b("IDB"), b("li", 0, 120)])
    ts(b("pi", 1, 2), b("pi", 0, 1), 15, OP.bitwise_and)
    ts(b("pi", 2, 3), b("pi", 0, 1), 4, OP.arith_shift_right)
    ts(b("pi", 3, 4), b("pi", 0, 1), 3, OP.arith_shift_right, 1, OP.bitwise_and)
    cp(b("pf", 0, 4), b("pi", 0, 4))
    P15, P4, P3 = [b("pf", k, k + 1) for k in range(1, 4)]
    cp(b("LI", 0, 16), b("li", 0, 16))
    cp(b("LI", 16, 120), b("li", 16, 120))
    BC16, BC8, BC15, BH = b("LI", 0, 16), b("LI", 0, 8), b("LI", 16, 24), b("LI", 120, 128)
    BC4 = b("LI", 128, 144)
    BCS = lambda s, k: b("LI", 24 + 16 * s, 24 + 16 * s + 8 * k)
    ts(b("LC"), b("c8"), P4, OP.is_equal)
    cp(b("wf", 0, 1), b("wi", 0, 1))
    ts(b("WB"), b("LC"), b("wf", 0, 1), OP.mult)
    ts(b("DM"), b("j15"), P15, OP.is_equal)
    for name, x in (("LCB", 1.0), ("BLK", 65536.0), ("BLKU", 65536.0 * U), ("NBLKU", -65536.0 * U), ("BLKW", WIDE), ("NBLKW", -WIDE), ("LC2", 2.0)):
        act(b(name), b("LC"), AF.Copy, scale=x)
    act(b("NIDB"), b("IDB"), AF.Copy, scale=-1.0)
    act(b("IDF"), b("IDB"), AF.Copy)
    ts(b("GO"), b("j15"), 1.0, OP.min)
    fill(b("DS", 128, 384), -16.0 * 65536)
    for k in range(2):
        act(b("GQ", 512 * k, 512 * k + 512), b("ONES"), AF.Copy)
        fill(b("QS", 1024 * k, 1024 * k + 16 * NV[0][k]), 0.0)
    fill(b("GQ", 0, 1024, 16), 0.0)
    fill(b("MX"), -BIG)
    fill(b("MX", 0, 128, 16), BIG)
    if PFQ == "h":
        act(b("ROWH", 0, 128), b("j15", 0, 128), AF.Identity, scale=4096.0 * U, bias=(CO + 2048) * U)
        act(b("ROWH", 128, 256), b("j15", 0, 128), AF.Identity, scale=4096.0, bias=2048.0)
        act(b("IDH", 0, 128), b("IDB"), AF.Copy, scale=2.0 ** -14)
        act(b("IDH", 128, 256), b("IDB"), AF.Copy)
    elif PFQ == "g":
        act(b("ROWC", 0, 128), b("j15", 0, 128), AF.Identity, scale=4096.0 * U, bias=CO * U)
        act(b("IDU"), b("IDB"), AF.Copy, scale=U)
    else:
        act(b("bias", 0, 1), P15, AF.Identity, scale=4096.0 * U, bias=CO * U)
        act(b("bias", 1, 2), P15, AF.Copy, scale=4096.0)
    cp(b("r0f", rows=48), b("r0i", rows=48))
    mm(b("MB", 0, 48), b("r0f", rows=48), b("IDF", 0, 48, rows=48), f32=True)
    const(b("FR"), 0)
    act(b("RKS"), b("ONES", 0, 128), AF.Copy)
    for h in range(2):
        act(b("RKS", 64 * h + 2, 64 * h + 64, 8), b("MB", h, 48, 6), AF.Identity, scale=65536.0 * U, bias=8 * 65536.0 * U)
    for k in range(2, 6):
        act(b("FR", 32 * k, 32 * k + 32, 4), b("MB", k, 48, 6), AF.Copy, scale=16.0)
    fill(b("PT", 0, 1), 128.0)

    def late_constants():
        for k in range(0, M, 448):
            copy("g", b("CH", k, k + 448), b("CHI", k, k + 448))
        for k in range(M, ROOM, 384):
            const(b("CH", k, k + 384), 0)
        const(b("NONE"), -1)
        for k in (0, 384):
            const(b("DS", k, k + 128), -4096)
        act(b("WI"), b("IDB"), AF.Copy, scale=2.0 ** 26)
        if PFQ == "g":
            act(b("ROWC", 128, 256), b("j15", 0, 128), AF.Copy, scale=4096.0)
        const(b("m", 0, 8), 0)
        x = b("EF", 0, 128)
        fill(x, 0.5)
        op("v", lambda: V.tensor_tensor_scan(b("EF", 128, 256)[4], b("EF", 0, 128)[4], b("NONE")[4], 2.0 ** 64, OP.mult, OP.max),
           [x, b("NONE")], [b("EF", 128, 256)], vc(128))
        keep(b("EF", 256, 384), b("EF", 128, 256), DIAG, OP.is_equal, 0.0)
        act(b("WD"), b("EF", 256, 384), AF.Copy, scale=-2.5)
        send(T.wn[:, 0:1], b("wi", 0, 1), -1, VI - 1)
        iota(b("li", 128, 144), [[4, 16]], 3)
        cp(b("LI", 128, 144), b("li", 128, 144))
        const(b("PK"), FLAG)
        const(b("OUT", 48, 96), 0)
        for h in range(2):
            x = b("TRS", 128 * h, 128 * h + 128)
            iota(x, [[0, 128]], 256 * (h + 1), 2 * (h + 1))
            keep(x, x, DIAG, OP.is_equal, 0.0)
            keep(x, x, DIAG, OP.is_ge, -1.0)
            const(b("SND%d" % h, 0, CAP), 0)
            const(b("RCV%d" % h, CAP, L), 0)
        const(b("SEL"), 1)
        keep(b("SEL"), b("SEL"), [[-16, 8], [-4, 4]], OP.is_equal, 0.0)
        x = b("bias", 4, 5)
        const(x, 0)
        keep(x, x, [[0, 1]], OP.is_ge, c0, -32)
        keep(x, x, [[0, 1]], OP.is_ge, 0.0, -16)
        cp(b("thf", 0, 1), b("thi", 0, 1))
        ts(b("TB"), b("SEL", 0, 32, 4), b("thf", 0, 1), OP.mult)
        iota(b("K4096"), [[-128, 2], [0, 8]], -4096, -1)
        iota(b("KC"), [[16, 16]], 0)
        act(b("bias", 5, 6), P15, AF.Identity, bias=4096.0)
        for k in range(2):
            x = b("SELG", 512 * k, 512 * k + 512, rows=16)
            keep(x, b("ONES", rows=16), [[-2, 4], [0, 128]], OP.is_ge, 0.0, -8 * k)
            keep(x, x, [[2, 4], [0, 128]], OP.is_ge, 0.0, 1 + 8 * k, -1)
            x = b("NSELG", 512 * k, 512 * k + 512, rows=16)
            const(x, -1)
            keep(x, x, [[-2, 4], [0, 128]], OP.is_ge, 0.0, -8 * k)
            keep(x, x, [[2, 4], [0, 128]], OP.is_ge, 0.0, 1 + 8 * k, -1)
        iota(b("DGL"), [[0, 128]], 0, 1)
        keep(b("DGL"), b("DGL"), DIAG, OP.is_equal, 0.0)
        for k in range(4):
            keep(b("DGB", 128 * k, 128 * k + 128), b("IDB"), DIAG, OP.not_equal, float(M + 128 * k))
        ts(BH, b("li", 120, 128), P3, OP.add)

    def begin(t):
        q0 = M + L * t
        Q = b("PT", q0, q0 + L)
        Qh = [b("PT", q0 + 128 * h, q0 + 128 * h + 128) for h in range(2)]
        if t:
            r = "RCV%d" % (t - 1)
            mm(b("KP0", 0, CAP), b("IDB"), b("PT", q0, q0 + CAP))
            for h in range(2):
                mm(b("MA", 64 + 32 * h, 96 + 32 * h), b(r, 128 * h, 128 * h + 128), b("SEL"), f32=True, ext=t - 1)
            tt(b("PM"), b("MA", 64, 128), b("FR", 64 * t, 64 * t + 64), OP.max)
            ts(b("PD"), b("PM"), 4, OP.arith_shift_right, 2 ** 18 - 1, OP.bitwise_and)
            for lo, hi in ((0, 1), (1, 2)) if ZRS else ((0, 2),):
                tg(b("ZR", 128 * lo, 128 * hi), b("PD"), b("LI", 128 + 8 * lo, 128 + 8 * hi), b("DM", 128 * lo, 128 * hi), OP.mult)
            tt(b("MI"), b(r, 0, CAP), b("KP0", 0, CAP), OP.max, ext=t - 1)
            ts(b("QI"), b("MI"), 15, OP.bitwise_and)
            copy(PTQ, b("PT", q0, q0 + CAP), b("QI"))
            root = b("PD", 3, 64, 4)
            act(b("RKS", 2, 128, 8), b("PD", 0, 64, 4), AF.Identity, scale=65536.0 * U, bias=8 * 65536.0 * U)
        else:
            for h in range(2):
                mm(b("KP0", 256 + 8 * h, 264 + 8 * h), Qh[h], b("WB"))
            cp(b("sm"), b("KP0", 256, 272))
            root = b("sn")
            ts(root, b("sm"), 63, OP.bitwise_and)
            tg(b("ZR"), root, BC16, b("DM"), OP.mult)
        for lo, hi in ((0, 1), (1, 2)) if ZRS and t else ((0, 2),):
            for h in range(lo, hi):
                mm(b("KP1", 272 + 8 * h, 280 + 8 * h), b("ZR", 128 * h, 128 * h + 128), b("LCB"))
            ts(b("OFF", 8 * lo, 8 * hi), b("KP1", 272 + 8 * lo, 272 + 8 * hi), 1.0, OP.add)
        for h in range(2):
            nv = max(x[h] for x in NV)
            x, y, z = 1024 * h, 1024 * h + 16 * NV[0][h], 1024 * h + 16 * nv
            copy(GQS[2 + h], b("QS", x, y, 16), b("PT", q0 + 128 * h, q0 + 128 * h + NV[0][h]))
            scan(b("Q16", x, y), b("GQ", 0, y - x), b("QS", x, y), OP.mult, OP.add)
            for i in range(16 if y < z else 0):
                copy("g", b("Q16", y + i, z, 16), b("PT", q0 + 128 * h + NV[0][h], q0 + 128 * h + nv))
        for h in range(2):
            mm(b("SP2", 128 * h, 128 * h + 128), Qh[h], b("NIDB"))
        act(b("NQT"), b("SP2", 0, 256), AF.Copy)
        if DRQ == "v":
            tg(b("DRB"), b("PT", 0, 128), b("OFF"), Q, OP.subtract)
            act(b("DRB"), b("DRB"), AF.Abs)
        else:
            act(b("DRB"), b("PT", 0, 128), AF.Copy, off=b("OFF"))
            mm(b("KP0", 256, 512), b("NIDB"), Q, True, False)
            mm(b("KP0", 256, 512), b("IDB"), b("DRB"), False, True)
            act(b("DRB"), b("KP0", 256, 512), AF.Abs)
        copy(GQS[0], b("RT"), root)
        for h in range(2):
            mm(b("KP1", 336 + 8 * h, 344 + 8 * h), b("DRB", 128 * h, 128 * h + 128), b("BLK"))
        for h in range(2):
            mm(b("KP1", 352 + 8 * h, 360 + 8 * h), b("DRB", 128 * h, 128 * h + 128), b("BLK"), True, False)
            mm(b("KP1", 352 + 8 * h, 360 + 8 * h), b("IDB"), b("RT", 8 * h, 8 * h + 8), False, True)
        act(b("DS", 128, 384, 16), b("KP1", 336, 352), AF.Copy)
        act(b("K0U"), b("KP1", 352, 368), AF.Identity, scale=U, bias=(CO + 1) * U)
        act(b("K0"), b("KP1", 352, 368), AF.Identity, bias=CO + 32768 + 1)
        scan(b("E", 128, 384), b("GO"), b("DS", 128, 384), OP.mult, OP.add)
        act(b("A"), b("E", 128, 384), AF.Abs, scale=U, bias=-CO * U)
        for lo, hi in ((0, 2),) if JM else ((0, 1), (1, 2)):
            first_mask(0, lo, hi)
        tt(b("RKS", 3, 128, 8), b("RKS", 2, 128, 8), b("K0U"), OP.min)

    def first_mask(p, lo, hi):
        tg(b("M1", 128 * lo, 128 * hi), b("RKS", 64 * lo, 64 * hi), BCS(p + 1 if p else 0, hi - lo), b("A", 128 * lo, 128 * hi), OP.is_lt)

    def ramp(p, h):
        d, r = 128 + 128 * h, 384 * h
        sk = b("SK", 16 * p + 8 * h, 16 * p + 8 * h + 8)
        if p in (1, 2):
            ts(b("DK", 8 * h, 8 * h + 8), sk, 0xFF0000, OP.bitwise_and)
            copy(DSQ, b("DS", d, d + 128, 16), b("DK", 8 * h, 8 * h + 8))
            slot[2] = "RP"
            tt(b("DS", r, r + 128, 16), sk, b("RB", 8 * h, 8 * h + 8), OP.min)
            scan(b("E", 256 * h, 256 * h + 256), b("GO"), b("DS", 256 * h, 256 * h + 256), OP.mult, OP.add)
            ts(b("ST", 128 * h, 128 * h + 128), b("E", r, r + 128), 0.0, OP.is_equal)
        else:
            ts(b("DS", d, d + 128, 16), sk, RND, OP.add, RND, OP.subtract)
            scan(b("E", d, d + 128), b("GO", 0, 128), b("DS", d, d + 128), OP.mult, OP.add)
        act(b("A", 128 * h, 128 * h + 128), b("E", d, d + 128), AF.Abs, scale=U, bias=-15.5 * 65536 * U)
        first_mask(p + 1, h, h + 1)

    def push(t, h, p):
        hs = str(h)
        n = lambda x, *a: b(x + hs, *a)
        KP = "KP" + hs
        kp = b(KP, 0, 128)
        ch = b("CH" if t else "CHI", 0, 128 if p == 0 else 4096 if t else M)
        off = b("OFF", 8 * h, 8 * h + 8)
        A, KS, MS = [b(x, 128 * h, 128 * h + 128) for x in ("A", "KS", "MS")]
        last = lambda x: b(x, 128 * h + 15, 128 * h + 128, 16)
        pt = b("PT", 0, M + L * t)
        if PUQ == "s":
            act(n("PU"), ch, AF.Copy, off=off)
        else:
            op("v", lambda: V.tensor_copy(n("PU")[4], ch[4].indirect(off[4])), [ch, off], [n("PU")], (0.05, 128, "V"))
        if PFQ == "h":
            x = 1.0 if p == 4 else 2.0 ** -12
            if PHQ == "s":
                act(n("Ph"), n("PU"), AF.Identity, bias=-2048 * x, scale=x)
            else:
                ts(n("Ph"), n("PU"), -2048.0, OP.add, x, OP.mult)
            slot[2] = "row"
            mm(kp, b("IDH", 128, 256), b("ROWH", 128 * (p // 4), 128 * (p // 4) + 128), True, False)
            slot[2] = "Pf"
            mm(kp, n("Ph"), b("IDH", 128 * (p // 4), 128 * (p // 4) + 128), False, False)
        else:
            if PFQ == "s":
                act(n("Pf"), n("PU"), AF.Identity, bias=b("bias", p // 4, p // 4 + 1), scale=1.0 if p == 4 else U)
            else:
                copy("g", n("Pf"), n("PU"))
                slot[2] = "row"
                mm(kp, b("IDB"), b("ROWC", 128 * (p // 4), 128 * (p // 4) + 128), True, False)
            slot[2] = "Pf"
            mm(kp, n("Pf"), b("IDU" if p < 4 and PFQ == "g" else "IDF"), PFQ != "g", False, f32=True)
        nv = NV[p][h]
        cut = [nv] + [x for x in CUT if x > nv] + [128]
        for k, (lo, hi) in enumerate(zip(cut, cut[1:])):
            d = b("DIFF", 2048 * h + 16 * lo, 2048 * h + 16 * hi)
            slot[2] = "get%d" % k
            act(d, pt, AF.Copy, off=n("PU", lo, hi))
            bc = [lo] + [x for x in (64, 96) if lo < x < hi] + [hi]
            banks = [b(RING[3 * h + x // 32 - 1], 16 * (x % 32), 16 * (x % 32 + y - x)) for x, y in zip(bc, bc[1:])]
            for ps, x, y in zip(banks, bc, bc[1:]):
                mm(ps, b("NQT", 128 * h, 128 * h + 128), b("R", 16 * x - 512, 16 * y - 512), True, False)
            slot[2] = "abs%d" % k
            for ps, x, y in zip(banks, bc, bc[1:]):
                mm(ps, b("IDB"), b("DIFF", 2048 * h + 16 * x, 2048 * h + 16 * y), False, True)
            c = 1536 * h - 512
            op("s", lambda d=d, lo=c + 16 * lo, hi=c + 16 * hi: S.activation(d[4], T.RING[:, lo:hi], AF.Abs), banks, [d], (0.09, 16 * (hi - lo), "s"))
        cut = [nv * k // VP // 2 * 2 for k in range(VP)] + [nv]
        for k in range(VP):
            lo, hi = 16 * cut[k], 16 * cut[k + 1]
            slot[2] = "vec%d" % k
            tg(b("RAW", 1024 * h + lo, 1024 * h + hi), pt, n("PU", cut[k], cut[k + 1]), b("Q16", 1024 * h + lo, 1024 * h + hi), OP.subtract)
        if JUNK:
            x = (b("EQ", 0, JUNK), b("RAW", 1024 * h, 1024 * h + JUNK), b("Q16", 1024 * h, 1024 * h + JUNK))
            op("v", lambda: V.tensor_tensor(x[0][4], x[1][4], x[2][4], OP.max), [x[1], x[2]], [x[0]], vc(JUNK, 1.5))
        slot[2] = "relu"
        if RELU[p]:
            ts(b("DIFF", 2048 * h, 2048 * h + 16 * nv), b("RAW", 1024 * h, 1024 * h + 16 * nv), 0.0, OP.max, 2.0, OP.mult)
        else:
            act(b("DIFF", 2048 * h, 2048 * h + 16 * nv), b("RAW", 1024 * h, 1024 * h + 16 * nv), AF.Abs)

        def sums(lab, src, at, lo, hi, blk, stop=False):
            slot[2] = lab
            op("t", lambda: [TE.matmul(b(KP, i, 128, 16, hi - lo, lo)[4], b(src, at + 16 * lo + i, at + 16 * hi, 16)[4], blk[4], False, stop and i == 15)
                             for i in range(16)][-1], [b(src, at + 16 * lo, at + 16 * hi), blk], [kp], (0.0, 16 * min(64, hi - lo), "t"))
        w = "W" if p == 4 else "U"
        if RELU[p]:
            sums("neg", "RAW", 1024 * h, 0, nv, b("NBLK" + w))
        cut = (0,) + KSP
        for k in range(len(KSP)):
            sums("key%d" % k, "DIFF", 2048 * h, cut[k], cut[k + 1], b("BLK" + w))
        if p in (2, 3):
            slot[2] = "ST"
            mm(kp, b("IDB"), b("ST", 128 * h, 128 * h + 128), False, False)
        if KSP:
            sums("key", "DIFF", 2048 * h, cut[-1], 128, b("BLK" + w))
        slot[2] = "M1"
        mm(kp, b("WI" if p == 4 else "IDB"), b("M1", 128 * h, 128 * h + 128), False, bool(KSP))
        if not KSP:
            sums("key", "DIFF", 2048 * h, 0, 128, b("BLK" + w), True)
        scan(KS, b("MX"), kp, OP.max, OP.min)
        if p == 4:
            return
        if p == 0:
            tt(b("RKS", 64 * h + 4, 64 * h + 64, 8), b("RKS", 64 * h + 3, 64 * h + 64, 8), last("KS"), OP.min)
            tg(n("M2"), b("RKS", 64 * h, 64 * h + 64), BCS(2, 1), A, OP.is_lt)
        else:
            tg(n("M2"), KS, BC15, A, OP.is_lt)
        tt(n("KM"), kp, n("M2"), OP.add)
        scan(MS, b("MX"), n("KM"), OP.max, OP.min)
        sk = b("SK", 16 * p + 8 * h, 16 * p + 8 * h + 8)
        if p in (1, 2):
            ts(n("z3"), last("MS"), 32768.0 * U - 0.25, OP.add, 1 / U, OP.mult)
            tt(sk, n("z3"), b("K0" if p == 1 else "FB", 8 * h, 8 * h + 8), OP.min)
        else:
            ts(sk, last("MS"), 0.25, OP.min, 1 / U, OP.mult)
        ts(n("NN"), sk, 4095, OP.bitwise_and)
        tg(n("ZL"), n("NN"), BC8, b("DM", 0, 128), OP.mult)
        slot[2] = "list"
        mm(b(KP, 128, 136), n("ZL"), b("LC"), f32=True)
        copy(OFQ, off, b(KP, 128, 136))
        if h and p:
            tt(b("RKS", p + 4, 128, 8), b("RKS", p + 3, 128, 8), b("KS", 15, 256, 16), OP.min)
        if h and p == 0:
            ts(b("FB"), b("SK", 0, 16), 32768.0, OP.add)
        if h and p in (1, 2):
            ts(b("RB"), b("FB") if p == 1 else b("SK", 16, 32), 0xF000, OP.bitwise_and)
        for k in range(2 * h):
            slot[0] = (t, p, k)
            ramp(p, k)
        if (p, h) == (3, 1):
            ts(b("T3"), b("RKS", 7, 128, 8), RND * U, OP.add, RND * U, OP.subtract)
            act(b("thr"), b("T3"), AF.Identity, bias=32768.0 * U)
            tg(b("m", 8, 136), b("thr"), BH, b("RKS"), OP.is_gt)
            scan(b("sc"), b("m", 7, 135), b("RKS"), OP.mult, OP.max)
            ts(b("ki"), b("sc", 7, 128, 8), 1 / U, OP.mult)
            ts(b("W"), b("ki"), 4095, OP.bitwise_and)
            act(b("y"), b("T3"), AF.Identity, scale=WIDE / 65536 / U, bias=-8 * WIDE - 4096)
            tt(b("Y"), b("y"), b("W"), OP.add)
        if (p, h) == (1, 0):
            slot[2] = "out"
            if t:
                stayed()
                outputs(t - 1)
                cb = 4096.0 * ((rank - 1) % N)
                act(b("y"), b("PD", 2, 64, 4), AF.Relu, scale=-1.0, bias=1.0)
                act(b("thr"), b("PD", 1, 64, 4), AF.Identity, bias=-cb)
                tt(b("y"), b("y"), b("thr"), OP.mult)
                act(b("thr"), b("PD", 2, 64, 4), AF.Identity, bias=cb - c0)
                tt(b("B0C"), b("y"), b("thr"), OP.add)
                if t < VI - 1:
                    act(b("PK", 4, 256, 16), b("B0C"), AF.Identity, scale=16.0, bias=FLAG + 16 * c0)
            else:
                mm(b("KP1", 320, 321), b("WD"), b("ONES", 0, 1))
                act(b("WL", 0, 1), b("KP1", 320, 321), AF.Copy, scale=-0.4)
                act(b("WL", 1, 2), b("KP1", 320, 321), AF.Copy, scale=0.4)
                for k in range(2):
                    mm(b("KP1", 304 + 8 * k, 312 + 8 * k), b("ONES", 0, 128), b("TB"))
                act(b("THK"), b("KP1", 304, 320), AF.Identity, scale=WIDE, bias=-4096.0)
            if t < VI - 1:
                roots(t, "WN", VI - 1 if t == 0 else None)
                act(b("PK", 12, 256, 16), b("sn"), AF.Identity, scale=16.0, bias=FLAG)
            for k in range(1, VI if t == 0 else 0):
                roots(k, "WB")
                act(b("FR", 64 * k + 3, 64 * k + 64, 4), b("sn"), AF.Copy, scale=16.0)

    def roots(t, w, ext=None):
        if ext is not None:
            op("s", lambda: S.activation(b("wf", 1, 2)[4], b("wn", 0, 1)[4], AF.Copy), [], [b("wf", 1, 2)], (0.09, 1, "s"), "c", ext)
            act(b("WN"), b("LC"), AF.Copy, scale=b("wf", 1, 2))
        for k in range(2):
            mm(b("KP1", 160 + 8 * k, 168 + 8 * k), b("PT", M + L * t + 128 * k, M + L * t + 128 * k + 128), b(w))
        act(b("sm"), b("KP1", 160, 176), AF.Copy)
        ts(b("sn"), b("sm"), 63, OP.bitwise_and)

    def send(out, src, step, k):
        dst = T.cores[(rank + step) % N]
        rid, pid, _x = topo.addr(dst)
        op("g", lambda: g.remote_dma(out, src[4], T.sem["arr%d" % k], T.sem["sent%d" % k], pid, rid, topo.mask(core, dst)), [src], [], (0.1, 0, "v"), "r", k)

    def outputs(t):
        k = 48 if t < VI - 1 else 32
        ps, ob = b("KP1", 256, 384, 1, k), "OB%d" % t
        mm(ps, b("OUT", 48, 48 + k), b("IDF"), True, False, f32=True)
        mm(ps, b("OUT", 0, k), b("IDF"), False, True, f32=True)
        act(b(ob, 0, 128, 1, k), ps, AF.Identity, bias=b("bias", 4, 5, 1, k))
        for j in range(k // 8):
            o = b(ob, 0, 128, 1, 8, 8 * j)
            x = t * L + 128 * (j % 2)
            dma("s" if t == VI - 1 and j % 2 else "y", (T.yr, T.yb, T.yp)[j // 2][:, x:x + 128], o[4], [o], [], 2.0)

    def listed(ps, z, out, add):
        mm(b(ps[0], ps[1], ps[1] + 16), b("IDB"), b("KC"), True, False)
        for h in range(2):
            mm(b(ps[0], ps[1] + 8 * h, ps[1] + 8 * h + 8), b(z, 128 * h, 128 * h + 128), b("LC"), False, h == 1, f32=True)
        if out in LSQ:
            act(b(out), b(ps[0], ps[1], ps[1] + 16), AF.Identity, bias=add)
        else:
            ts(b(out), b(ps[0], ps[1], ps[1] + 16), add, OP.add)

    def finish(t):
        q0 = M + L * t
        H = lambda x, h, k=128: b(x, k * h, k * h + k)
        Rr, node = b("RI", 0, 32, 2), b("RI", 1, 32, 2)
        tt(b("V4"), b("KS", 15, 256, 16), b("Y"), OP.min)
        ts(node, b("V4"), 4095, OP.bitwise_and)
        ts(b("n4"), b("V4"), -4096, OP.bitwise_and)
        if "Rr" in LSQ:
            act(Rr, b("n4"), AF.Identity, scale=1 / WIDE, bias=-7 * 4096.0 / WIDE)
        else:
            ts(Rr, b("n4"), -7 * 4096.0, OP.add, 1 / WIDE, OP.mult)
        if t < VI - 1:
            act(b("PK", 0, 256, 8), b("RI"), AF.Identity, scale=16.0, bias=FLAG)
            mm(b("SP2", 0, L), b("IDB"), b("PT", q0, q0 + L), True, False)
            for h in range(2):
                mm(H("SP2", h), H("PK", h), b("IDF"), False, h == 1, f32=True)
            act(b("XS"), b("SP2", 0, L), AF.Copy)
            tt(b("near"), b("V4"), b("THK"), OP.is_lt)
            mm(b("KP0", 144, 152), H("TRS", 0), H("near", 0, 8))
            mm(b("KP0", 152, 160), b("NONE"), H("near", 0, 8), True, False)
            mm(b("KP0", 152, 160), H("TRS", 1), H("near", 1, 8), False, True)
            copy(PLQ, b("PL"), b("KP0", 144, 160))
            tg(b("ZP"), b("PL"), BC16, b("DM"), OP.mult)
            listed(("KP0", 160), "ZP", "OP", P15)
            snd = b("SND%d" % t)
            op("v", lambda: V.tensor_copy(snd[4].indirect(b("OP")[4]), b("XS")[4]), [b("XS"), b("OP")], [snd], (0.05, L, "W"))
            send(T["RCV%d" % t][:, 0:CAP], b(snd[0], 0, CAP), 1, t)
            tag[0] = "g" + tag[0][1:]
        if t:
            act(b("z"), node, AF.Relu, scale=-1.0, bias=1.0)
            tt(b("OUT", 16, 32), b("z"), b("B0C"), OP.mult)
        else:
            ts(b("OUT", 16, 32), node, 0.0, OP.is_equal, -c0, OP.mult)
        copy(GQS[1] if t < VI - 1 else "s", b("OUT", 0, 16), Rr)
        act(b("OUT", 64, 80), node, AF.Copy)
        if t == VI - 1:
            return outputs(t)
        tt(b("gq"), node, b("K4096"), OP.add)
        tg(b("Z1"), b("gq"), BC16, b("DM"), OP.mult)
        listed(("KP1", 144), "Z1", "G1", b("bias", 5, 6))
        act(b("GC"), b("CH", 0, 4096), AF.Copy, off=b("G1"))
        act(b("NQ", 0, 32, 2), node, AF.Copy)
        tt(b("NQ", 1, 32, 2), node, b("NQ", 0, 32, 2), OP.subtract)
        for h in range(2):
            mm(b("SP3", 256 + 128 * h, 384 + 128 * h, 1, 16), H("NQ", h, 16), b("IDB"))
        act(b("NT", rows=16), b("SP3", 256, 512, 1, 16), AF.Copy)
        act(b("bb"), Rr, AF.Identity, scale=0.0625, bias=-0.46875)
        tg(b("OH"), b("bb"), BC16, b("j15"), OP.is_equal)
        for h in range(2):
            mm(H("SP3", h), H("OH", h), H("DGB", 2 * t + h), True, False)
            mm(H("SP3", h), H("OH", h), b("DGL"), False, True)
        tt(b("OC"), b("SP3", 0, L), b("GC"), OP.mult)
        act(b("ON"), b("SP3", 0, L), AF.Copy)
        wl, nwl = b("WL", 0, 1), b("WL", 1, 2)
        for j, ps in enumerate(("MA", "SP0", "SP1", "MB")):
            nt, x = b("NT", 128 * (j // 2), 128 * (j // 2) + 128, 1, 16), 512 * (j % 2)
            sub = EQQ[j] in "sv"
            if sub:
                mm(b(ps), nt, b("NSELG", x, x + 512, 1, 16), True, False)
            for k in range(4):
                mm(H(ps, k), b("SELG", x + 128 * k, x + 128 * k + 128, 1, 16), nt, not sub, k == 3 or not sub)
            eq = H("EQ", j, 512)
            for k in range(0 if sub else 4):
                own = b("OUT", 64 + 4 * j + k, 65 + 4 * j + k)
                if EQQ[j] == "S":
                    act(H("EQ", 4 * j + k), H(ps, k), AF.Abs, scale=-1.0, bias=own)
                else:
                    ts(H("EQ", 4 * j + k), H(ps, k), own, OP.is_equal, wl, OP.mult)
            if EQQ[j] == "s":
                act(eq, b(ps), AF.Abs)
            if EQQ[j] in "sS":
                act(eq, eq, AF.Relu, scale=nwl, bias=wl)
            if EQQ[j] == "v":
                ts(eq, b(ps), 0.0, OP.is_equal, wl, OP.mult)
        mm(b("KP1", 160, 176), b("WI"), b("near"), True, False)
        for h in range(2):
            mm(b("KP1", 160 + 8 * h, 168 + 8 * h), H("OC", h), b("LC2"), False, h == 1)
        tt(b("can"), node, b("KP1", 160, 176), OP.is_gt)
        mm(b("KP1", 176, 192), b("WD"), b("can"), True, False)
        for j in range(16):
            mm(b("KP1", 176 + j, 177 + j), H("EQ", j), b("can", j, j + 1), False, j == 15)
        ts(b("win"), b("KP1", 176, 192), 0.0, OP.is_lt)
        tg(b("Z2"), b("win"), BC16, b("Z1"), OP.mult)
        listed(("KP1", 192), "Z2", "G2", b("bias", 5, 6))
        for h in (1, 0):
            op("v", lambda h=h: V.tensor_tensor(b("CH")[4].indirect(H("G2", h, 8)[4]), H("GC", h)[4], H("ON", h)[4], OP.add),
               [H("GC", h), H("ON", h), H("G2", h, 8)], [b("CH")], (0.05, 128, "W"))
        tt(b("OUT", 32, 48), b("win"), node, OP.mult)
        act(b("CG"), b("CH", 0, 4096), AF.Relu, bias=-127.0 - q0, off=H("G1", 1, 8))

    def stayed():
        mm(b("KP1", 208, 216), b("CG"), b("BLK"))
        tt(b("OUT", 40, 48), b("OUT", 40, 48), b("KP1", 208, 216), OP.min)

    for t in range(VI):
        tag[0] = "b%d" % t
        begin(t)
        if t == 0:
            late_constants()
        for p in range(5):
            for h in range(2):
                tag[0] = "%d%d%s" % (t, p, "AB"[h])
                slot[:] = [(t, p, h), {}, "Pf"]
                push(t, h, p)
        slot[0] = None
        tag[0] = "f%d" % t
        finish(t)

    if "order" not in ORDER:
        ORDER["order"], ORDER["runs"] = improve(place(ops, *links(ops, MODELS[0]), WHEN, HALF, GAP), ops, ROUNDS)
    order = ORDER["order"]

    QS = {"v": V, "t": TE, "s": S, "g": g, "y": g.sync}
    CQ = {"v": "cv", "t": "ct", "s": "cs", "g": "cg"}
    done = {}
    total = {"v": 0, "t": 0, "s": 0, "g": 0}
    know = {x: {} for x in QS}
    nout = len(topo.engines(core, T.cores[(rank + 1) % N]))
    nin = len(topo.engines(T.cores[(rank - 1) % N], core))
    for i in order:
        o = ops[i]
        qn = o["q"]
        k = know[qn]
        need = {}
        for d in o["deps"]:
            sem, val, kn = done[d]
            if need.get(sem, (0,))[0] < val:
                need[sem] = (val, kn)
        if o["kind"] == "c" and o["ext"] is not None:
            need["arr%d" % o["ext"]] = (nin, {})
        for sem, (val, kn) in sorted(need.items(), key=lambda e: -len(e[1][1])):
            if k.get(sem, 0) >= val:
                continue
            QS[qn].wait_ge(T.sem[sem], val)
            k[sem] = val
            for a, c in kn.items():
                if k.get(a, 0) < c:
                    k[a] = c
        if o["kind"] == "c":
            total[qn] += 1
            o["call"]().then_inc(T.sem[CQ[qn]], 1)
            done[i] = (CQ[qn], total[qn], dict(k))
        elif o["kind"] == "d":
            o["call"]().then_inc(T.sem[o["sem"]], 16)
            done[i] = (o["sem"], 16, dict(k))
        else:
            o["call"]()
            done[i] = ("sent%d" % o["ext"], nout, dict(k))
    for x in "vtsg":
        g.wait_ge(T.sem[CQ[x]], total[x])
    for i in range(ndma[0]):
        g.wait_ge(T.sem["d%d" % i], 16)
    for t in range(VI):
        g.wait_ge(T.sem["sent%d" % t], nout)
        g.wait_ge(T.sem["arr%d" % t], nin)
    return ops, order
